import numpy as np, ml_dtypes
CORES = [23,119,17,113]
N = 4
BF = ml_dtypes.bfloat16
def gentries(a):
    return np.ascontiguousarray(a.reshape(8, 16, -1).transpose(0, 2, 1)).reshape(8, -1)
def gtable(e):
    e = np.asarray(e); return np.ascontiguousarray(e.reshape(8, -1, 16).transpose(0, 2, 1)).reshape(128, -1).astype(np.int32)
V, Q, T, S, HOP = 4096, 256, 3, 1, 1
TH, TAU = 1020, (1020, 1530, 1275)
def toward(rng, shape, hub, share):
    h = hub[np.arange(8).reshape((1, 8) + (1,) * (len(shape) - 2)), rng.integers(0, hub.shape[1], shape)]
    return np.where(rng.random(shape) < share, h, rng.integers(0, V, shape))
def parts(rng):
    hub = rng.integers(0, V, (8, 32))
    X = rng.integers(0, 256, (N, 8, 16, V)); E = toward(rng, (N, 8, 16, V), hub, 0.1)
    v = toward(rng, (N, 8, Q), hub, 0.2); z = rng.integers(0, 256, (N, 8, 16, Q)); L = toward(rng, (N, 8, 16, Q), hub, 0.3)
    return X, E, v, z, L
def pack(X, E, v, z, L):
    return {"X": np.ascontiguousarray(X.reshape(N, 128, V)).astype(np.float32).astype(BF), "E": np.ascontiguousarray(E.reshape(N, 128, V)).astype(np.int32),
            "v0": np.stack([gtable(a) for a in v]), "z0": np.ascontiguousarray(z.reshape(N, 128, Q)).astype(np.float32).astype(BF), "L0": np.ascontiguousarray(L.reshape(N, 128, Q)).astype(np.int32)}
def setup_inputs(rng):
    return pack(*parts(rng))
def skew(rng, shape):
    col = shape[:2] + (1, shape[3])
    x = np.minimum((np.exp2(8 * rng.random(col)) * rng.random(shape)).astype(np.int64), 255)
    return np.where(rng.random(shape) < 0.5 * rng.integers(0, 2, col), 255 - x, x)
def lean(rng, shape):
    u = rng.random(shape); i = np.minimum((V * u * u * u).astype(np.int64), V - 1)
    return np.where(rng.random(shape[:2] + (1,) * (len(shape) - 2)) < 0.5, V - 1 - i, i)
def setup_inputs_spread(rng):
    return pack(skew(rng, (N, 8, 16, V)), lean(rng, (N, 8, 16, V)), lean(rng, (N, 8, Q)), skew(rng, (N, 8, 16, Q)), lean(rng, (N, 8, 16, Q)))
def setup_inputs_ends(rng):
    X, E, v, z, L = parts(rng)
    X = 255 * (rng.random(X.shape) < rng.choice(np.array([0.1, 0.5, 0.9]), (N, 8, 1, V))).astype(np.int64)
    z = 255 * (rng.random(z.shape) < rng.choice(np.array([0.0, 0.25, 0.5, 0.75, 1.0]), (N, 8, 1, Q))).astype(np.int64)
    E, v, L = [np.where(rng.random(a.shape) < 0.75, (V - 1) * rng.integers(0, 2, a.shape), a) for a in (E, v, L)]
    X[..., [0, 1, V - 3]] = 0; X[..., [2, V - 2, V - 1]] = 255
    for g in range(8):
        tie, full = (V - 1, V - 2) if g % 2 == 0 else (V - 2, V - 1)
        E[:, g, :, tie] = np.array([2, V - 1, V - 2, V - 1] * 4); E[:, g, :, full] = V - 1
        E[:, g, :, 1] = np.array([V - 3, 0, 1, 0] * 4); E[:, g, :, V - 3] = 0; E[:, g, :, 2] = np.array([V - 1, 2] * 8)
        if g % 4 != 2: E[:, g, 0, 0] = V - 1; E[:, g, 1, 0] = 0
    v[..., Q - 1] = V - 1; v[..., Q - 2] = V - 2; z[..., Q - 2:] = 0; L[..., Q - 2:] = V - 1; L[:, :, 15, Q - 2:] = 0
    v[..., 0] = 1; z[..., 0] = 255; v[..., 1] = 1; z[..., 1] = 0
    return pack(X, E, v, z, L)
def setup_inputs_corners(rng):
    X, E, v, z, L = parts(rng); own = np.arange(V); kinds = rng.permutation(8); h = V // 2
    for g in range(8):
        e, l, k = E[:, g], L[:, g], int(kinds[g])
        if k == 0: e[:] = own
        elif k == 1: e[:, 0::2] = (own + 1) % V; e[:, 1::2] = (own - 1) % V
        elif k == 2: e[:] = 0; e[:, 0] = V - 1
        elif k == 3:
            w = int(rng.choice(np.array([0, V - 1, h]))); l[:] = w; z[:, g] = 0
            e[:, 1] = e[:, 0]
            e[:, 0::2, w] = 5; e[:, 1::2, w] = 6; X[:, g, :, 5] = 255; X[:, g, :, 6] = 0
        elif k == 4: v[:, g] = V - 1; l[:] = V - 1
        elif k == 5:
            few = rng.permutation(h)[:64]; x = X[:, g]; x[:] = rng.integers(70, 256, x.shape)
            x[:, :, few[:32]] = rng.integers(240, 256, (N, 16, 32)); x[:, :, few[32:]] = rng.integers(70, 81, (N, 16, 32))
            e[:] = rng.integers(0, h, e.shape); e[:, 1, :h] = e[:, 0, :h]; z[:, g] = 0
            e[:, 0, h:] = few[rng.integers(0, 32, (N, V - h))]; e[:, 1, h:] = few[rng.integers(32, 64, (N, V - h))]
            l[:, :15] = rng.integers(0, h, (N, 15, Q)); l[:, 15] = rng.integers(h, V, (N, Q))
        elif k == 6: z[:, g] = 255; z[int(rng.integers(0, N)), g] = 0
        else:
            c = V // 4; o = rng.permutation(V).reshape(4, c); x = X[:, g]; z[:, g] = 255
            for i in range(4): e[:, :, o[i]] = o[i][rng.integers(0, c, (N, 16, c))]
            x[:, :, o[0]] = rng.integers(0, 64, (N, 16, c))
            x[:, :, o[1]] = rng.integers(252, 256, (N, 16, c)); x[:, :5, o[1]] = rng.integers(0, 16, (N, 5, c))
            x[:, :, o[2]] = np.array([0] * 5 + [255] * 2 + [215] * 2 + [255] * 7)[:, None]
            x[:, :, o[3]] = np.array([0] * 4 + [254] + [255] * 11)[:, None]
    v[..., 0] = 0; v[..., Q - 1] = V - 1
    return pack(X, E, v, z, L)
def setup_inputs_crowd(rng):
    X, E, v, z, L = parts(rng); A = T * S
    kinds = np.stack([rng.permutation(np.array([0, 1, 2, 4])), rng.permutation(np.array([0, 1, 3, 4]))], axis=1).reshape(-1)
    for g in range(8):
        k = int(kinds[g])
        if k == 4: continue
        h = V // 2; four = np.array([0, V - 1, 1 + 2 * int(rng.integers(0, V // 4)), h + 2 * int(rng.integers(0, V // 4))])
        o = rng.permutation(np.setdiff1d(np.arange(V), four))
        hi = np.concatenate([four, o[:h - 4]]); lo = o[h - 4:]
        w = X[:, g]; w[:, :, hi] = rng.integers(240, 256, (N, 16, h)); w[:, :, lo] = rng.integers(70, 81, (N, 16, h))
        z[:, g] = rng.integers(0, 4, (N, 16, Q))
        e = E[:, g]; e[:, :2] = lo[rng.integers(0, h, (N, 2, V))]
        if k < 2:
            hs = hi[:4]; names = np.repeat(hs[(np.arange(N) + int(rng.integers(0, 4))) % 4][:, None], Q, axis=1)
            if k == 1:
                miss = rng.integers(0, Q, N); miss[int(rng.integers(0, N))] = Q - 1; names[np.arange(N), miss] = -1
        elif k == 2:
            hs = hi[:4]; names = rng.choice(hs, (N, Q))
        else:
            hs = hi[rng.permutation(h)[:Q]]; names = np.stack([rng.permutation(hs) for _ in range(N)])
        n = len(hs)
        a = e[:, 0::2]; a[:, :, hs] = hi[rng.integers(4 if k < 2 else 0, h, (N, 8, n))]
        b = e[:, 1::2]; b[:, :, hs] = lo[rng.integers(0, h, (N, 8, n))]
        l = lo[rng.integers(0, h, (N, 16, Q))]
        here = np.argsort(np.argsort(rng.random((N, 16 - A, Q)), axis=1), axis=1) < T
        l[:, A:] = np.where(here & (names >= 0)[:, None], names[:, None], l[:, A:])
        L[:, g] = l
    return pack(X, E, v, z, L)
def setup_inputs_ties(rng):
    X, E, v, z, L = parts(rng); h = V // 2; o = rng.permutation(V); tw = np.zeros(V, np.int64); tw[o[:h]] = o[h:]; tw[o[h:]] = o[:h]
    X = 51 * rng.integers(0, 6, X.shape); z = 51 * rng.integers(0, 6, z.shape); X[..., o[:h]] = X[..., o[h:]]
    E[:, :, 8:] = tw[E[:, :, :8]]; E = np.ascontiguousarray(E[:, :, rng.permutation(16)])
    X[..., V - 2] = 0; X[:, :, 12:, V - 2] = 255; X[..., V - 4] = 0
    E[..., V - 1] = V - 2; E[..., V - 2] = V - 2; E[..., V - 3] = V - 4; E[:, :, 0, V - 3] = V - 2
    v[..., Q - 2:] = V - 1; z[..., Q - 2:] = 0; z[:, :, 0, Q - 2] = 51; L[..., Q - 2:] = V - 3
    return pack(X, E, v, z, L)
def check_inputs(d):
    bad = []
    for k, lo, hi in (("X", 0, 255), ("E", 0, V - 1), ("v0", 0, V - 1), ("z0", 0, 255), ("L0", 0, V - 1)):
        a = np.asarray(d[k]).astype(np.float64)
        if not (np.min(a) >= lo and np.max(a) <= hi and np.all(a == np.floor(a))): bad.append("range of " + k)
    return bad
def pick(tab, ix):
    return np.take_along_axis(tab, ix[:, None, :], 2)
def reference(X, E, v0, z0, L0):
    x = X.astype(np.float32).astype(np.int64).reshape(N, 8, 16, V); e = E.astype(np.int64).reshape(N, 8, 16, V)
    v = np.stack([gentries(a) for a in v0]).astype(np.int64)
    z = z0.astype(np.float32).astype(np.int64).reshape(N, 8, 16, Q); L = L0.astype(np.int64).reshape(N, 8, 16, Q)
    wt = (2 * np.arange(16) + 1)[None, :, None]
    for t in range(T):
        mark = np.zeros((N, 8, V), bool)
        for r in range(N):
            p = (r + HOP * t) % N; s = (p + HOP) % N; zr = z[r].copy(); vr = v[r].copy(); ll = L[r].copy()
            for step in range(S):
                c = pick(e[p], vr)
                far = np.add.reduce(np.abs(pick(x[p], c.reshape(8, -1)).reshape(8, 16, 16, Q) - zr[:, :, None, :]), axis=1)
                k = np.argmin(far, axis=1)
                vr = np.take_along_axis(c, k[:, None, :], 1)[:, 0]; ll[:, S * t + step] = vr
            like = np.min(far, axis=1) <= TH; xv = pick(x[p], vr)
            flat = ll.reshape(8, -1); a = np.take_along_axis(e[s][:, 0], flat, 1); b = np.take_along_axis(e[s][:, 1], flat, 1)
            zz = np.tile(zr, (1, 1, 16))
            gap = np.add.reduce(np.abs(np.maximum(pick(x[s], a), zz) - np.maximum(pick(x[s], b), zz)), axis=1).reshape(8, 16, Q)
            fail = gap > TAU[t]; some = np.any(fail, axis=1); f = np.argmax(fail, axis=1)
            cut = ~like & some; none = ~like & ~some
            u = np.take_along_axis(ll, f[:, None, :], 1)[:, 0]; base = np.take_along_axis(a.reshape(8, 16, Q), f[:, None, :], 1)[:, 0]
            gi, qi = np.nonzero(cut)
            mark[s, gi, u[gi, qi]] = True; ll[gi, f[gi, qi], qi] = base[gi, qi]
            half = (zr + xv) >> 1; h = np.add.reduce(half * wt, axis=1) & (V - 1)
            L[r] = ll; v[r] = np.where(cut, base, np.where(none, h, vr))
            z[r] = np.where(like[:, None, :], np.abs(zr - xv), np.where(none[:, None, :], half, zr))
        e = np.where(mark[:, :, None, :], np.roll(e, -1, axis=2), e)
    ya = np.add.reduce(e * (np.arange(16) + 1)[None, None, :, None], axis=2)
    return {"yv": v.astype(np.float32), "yz": z.reshape(N, 128, Q).astype(np.float32), "yl": L.reshape(N, 128, Q).astype(np.float32), "ya": ya.astype(np.float32)}

@@ -1,0 +1,643 @@
+from concourse.bass import DstId, RemoteDMATransfer
+from concourse.mybir import dt, AluOpType, AxisListType, ActivationFunctionType
+
+A = AluOpType
+F = ActivationFunctionType
+V_, Q_, NV = 4096, 256, 3
+TH, TAU = 1020, (1020, 1530, 1275)
+WN = V_ + 16
+H16 = "float16"
+WALK_ON_V = (2, 3, 3)
+CUT_ON_S = (3, 3, 3)
+
+
+def _sb(n, d):
+    return ("sbuf", [128, n], d)
+
+
+SCRATCH = {
+    "Xs": _sb(V_, "bfloat16"), "Eraw": _sb(V_, "int32"), "Win": _sb(4 * WN, "float32"), "ident": _sb(WN, "float32"),
+    "xg": _sb(V_, "bfloat16"), "absd": _sb(V_, "bfloat16"), "zz": _sb(V_, "bfloat16"), "mH": _sb(V_, "bfloat16"),
+    "mL": _sb(V_, "bfloat16"), "tmp": _sb(V_, "bfloat16"),
+    "R1": _sb(2048, "bfloat16"), "nI": _sb(128, "bfloat16"), "keyT": _sb(256, "float32"), "I32": _sb(128, "float32"), "ones": _sb(256, "bfloat16"), "I": _sb(128, "bfloat16"),
+    "pi": _sb(8, "int32"), "col": _sb(32, "float32"), "cols": _sb(144, "float32"),
+    "WK": _sb(144, "bfloat16"), "WP": _sb(144, "bfloat16"), "WM": _sb(144, "bfloat16"), "Wh": _sb(144, "bfloat16"),
+    "W1": _sb(144, H16), "Wr0": _sb(144, H16), "Wr1": _sb(144, H16), "Wr2": _sb(144, H16), "Ws": _sb(144, H16),
+    "Rot": _sb(128, H16), "W32": _sb(144, "float32"), "d16": _sb(16, "float32"),
+    "kc": _sb(256, "float32"), "kcP": _sb(256, "float32"), "kcM": _sb(256, "float32"), "rK": _sb(256, "float32"),
+    "rG": _sb(256, "float32"), "rD": _sb(256, "float32"), "jc": _sb(256, "bfloat16"), "pb": _sb(256, "bfloat16"),
+    "c16b": _sb(256, "bfloat16"), "cSb": _sb(256, "bfloat16"), "ctau": _sb(768, "bfloat16"),
+    "fi": _sb(288, "int32"), "lists": _sb(288, "uint16"), "qc": _sb(16, "float32"),
+    "raw": _sb(768, "int32"), "t1": _sb(768, "float32"), "t2": _sb(768, "float32"), "offE": _sb(512, "uint16"),
+    "v0i": _sb(16, "int32"), "S0": _sb(256, "float32"),
+    "cf": _sb(256, "float32"), "c16": _sb(256, "uint16"), "zs": _sb(256, "bfloat16"), "nzW": _sb(256, "bfloat16"),
+    "scK": _sb(256, "float32"), "ki": _sb(48, "int32"), "k16": _sb(32, "uint16"),
+    "selc": _sb(256, H16), "sum": _sb(256, "float32"), "hi": _sb(256, "float32"),
+    "Lf": _sb(256, "float32"), "key": _sb(256, "float32"), "scG": _sb(256, "float32"), "Ht": _sb(512, "bfloat16"),
+    "sm": _sb(320, "float32"), "si": _sb(80, "int32"), "s16": _sb(96, "uint16"), "ech": _sb(256, H16),
+    "eq": _sb(256, "float32"), "dl": _sb(256, "float32"), "Ln": _sb(256, "float32"), "Lp": _sb(256, "float32"),
+    "ur": _sb(256, "float32"), "eq2": _sb(256, "float32"), "scD": _sb(256, "float32"),
+    "o16": _sb(64, "uint16"), "An": _sb(768, "bfloat16"),
+    "vals": _sb(1024, "float32"), "zo": _sb(256, "float32"), "Lo": _sb(256, "float32"), "vo": _sb(256, "float32"),
+    "vin": _sb(16, "uint16"), "ec": _sb(256, "float32"),
+}
+for _t in range(NV + 1):
+    SCRATCH["zq%d" % _t] = _sb(256, "bfloat16")
+    SCRATCH["Lq%d" % _t] = _sb(256, "uint16")
+    SCRATCH["vq%d" % _t] = _sb(16, "uint16")
+    SCRATCH["zin%d" % _t] = _sb(1024 if _t < NV else 256, "bfloat16")
+    SCRATCH["Lin%d" % _t] = _sb(256, "uint16")
+for _t in range(NV):
+    SCRATCH["a%d" % _t] = _sb(32, "uint16")
+    SCRATCH["ain%d" % _t] = _sb(32, "uint16")
+    SCRATCH["b%d" % _t] = _sb(512, "bfloat16")
+for _n in ("pA0", "pA1", "pB0", "pB1", "pK", "pG", "pM0", "pM1"):
+    SCRATCH[_n] = ("psum", [128, 512], "float32")
+
+SEMAPHORES = (["cV", "cS", "cT", "cG", "sent"] + ["dma%d" % _i for _i in range(20)]
+              + ["m1_%d" % _i for _i in range(4)] + ["mz_%d" % _i for _i in range(4)] + ["m2a_%d" % _i for _i in range(3)] + ["m2b_%d" % _i for _i in range(3)] + ["mv"])
+
+CYC, CG, CS, TC = 0.00104, 1.56, 3.8, 0.0005
+HOLD, FIT, EDGE, ROUNDS = 0.3, 0.05, 2.0, 6
+OFF = [0, 0, 0, 0]
+SUMS_AT = 0
+KEPT = {}
+COUNTER = {"V": "cV", "S": "cS", "T": "cT", "G": "cG"}
+
+
+def build_ops(g, T, topo, core, nxt):
+    ops = []
+    v, s, te = g.vector, g.scalar, g.tensor
+    rid, pid, _ = topo.addr(nxt)
+    eng = topo.engines(core, nxt)
+    mask_all = topo.mask(core, nxt)
+    half = len(eng) // 2
+    mask_lo = sum(1 << e for e in eng[:half])
+    mask_hi = sum(1 << e for e in eng[half:])
+    nd = [0]
+
+    def op(q, fn, rd, wr, dur, kind="c", sem=None, n=1, lat=0.0, loose=False):
+        ops.append(dict(q=q, fn=fn, rd=list(rd), wr=list(wr), dur=dur, kind=kind, sem=sem, n=n, lat=lat, loose=loose))
+
+    def vd(n, c=1.0):
+        return 0.06 + max(64, n * c) * CYC
+
+    def ts(out, in0, s1, s2, o0, o1, rd, wr, n=16, c=1.0):
+        if o1 is None:
+            op("V", lambda: v.tensor_scalar(out, in0, s1, None, o0), rd, wr, vd(n, c))
+        else:
+            op("V", lambda: v.tensor_scalar(out, in0, s1, s2, o0, o1), rd, wr, vd(n, c))
+
+    def tt(out, in0, in1, o, rd, wr, n=16, c=2.0):
+        op("V", lambda: v.tensor_tensor(out, in0, in1, o), rd, wr, vd(n, c))
+
+    def cp(out, in_, rd, wr, n=16, c=1.0, loose=False):
+        op("V", lambda: v.tensor_copy(out, in_), rd, wr, vd(n, c), loose=loose)
+
+    def ms(ap, val, wr, n=16, c=1.0):
+        op("V", lambda: v.memset(ap, val), [], wr, vd(n, c))
+
+    def scan(out, d0, d1, o0, o1, rd, wr):
+        op("V", lambda: v.tensor_tensor_scan(out, d0, d1, 0.0, o0, o1), rd, wr, vd(256))
+
+    def act(out, in_, f, rd, wr, n, c=1.0, scale=1.0, bias=0.0):
+        op("S", lambda: s.activation(out, in_, f, bias=bias, scale=scale), rd, wr, 0.08 + max(64, n * c) * CYC)
+
+    def mm(items, rd, wr, first=True, last=True, x=1):
+        def fn():
+            ins = None
+            for i, (o, l, r, _n) in enumerate(items):
+                ins = te.matmul(o, l, r, first and i == 0, last and i == len(items) - 1)
+            return ins
+        op("T", fn, rd, wr, 0.05 + sum(max(64, it[3]) * x for it in items) * TC)
+
+    def iota(out, pat, base, cm, wr, n, small=False):
+        if small:
+            op("G", lambda: g.iota(out, pat, base, cm, allow_small_or_imprecise_dtypes=True), [], wr, 0.16 + 2 * n * CYC)
+        else:
+            op("G", lambda: g.iota(out, pat, base, cm), [], wr, 0.16 + 2 * n * CYC)
+
+    def gcopy(out, in_, rd, wr, n):
+        op("G", lambda: g.affine_select(out, in_, [[0, n]], A.is_equal, 0.0, 0, 0), rd, wr, 0.21 + 2 * n * CYC)
+
+    def dma(q, pairs, rd, wr, lat):
+        name = "dma%d" % nd[0]
+        nd[0] += 1
+        queue = g.sync if q == "Y" else s
+
+        def fn():
+            for o, i in pairs:
+                queue.dma_start(o, i).then_inc(T.sem[name], 16)
+        op(q, fn, rd, wr, 0.06 * len(pairs), "d", name, 16 * len(pairs), lat)
+
+    def send(pairs, sem, rd, wr, nbytes):
+        def fn():
+            if len(pairs) == 1:
+                g.remote_dma(pairs[0][0], pairs[0][1], T.sem[sem], T.sem.sent, pid, rid, mask_all)
+            else:
+                g.remote_dma_fused([RemoteDMATransfer(dst_ids=[DstId(rid=rid, pnc=pid)], dma_engine_mask=m, remote_sem=T.sem[sem], src=i, dst=o)
+                                    for (o, i), m in zip(pairs, (mask_lo, mask_hi))], local_sem=T.sem.sent)
+        op("G", fn, rd, wr, 0.5, "r", sem, len(eng), 2.0 + nbytes / 40000.0)
+
+    def ch(name, n=8):
+        return ["%s%d" % (name, i) for i in range(n)]
+
+    def wsl(w, b):
+        return w[:, 15 - b:143 - b]
+
+    def win(r):
+        return T.Win[:, r * WN:(r + 1) * WN]
+
+    dma("S", [(T.raw[32 * (gi // 2):32 * (gi // 2) + 32, 128 * (gi % 2):128 * (gi % 2) + 128], T.L0[16 * gi:16 * gi + 16, :]) for gi in range(8)], [], ["rawL"], 2.2)
+    dma("Y", [(T.raw[:, 256 * (1 + r) + 128 * u:256 * (1 + r) + 128 * u + 128], T.E[16 * u + r::32, :]) for r in range(2) for u in range(2)], [], ["rawE"], 2.2)
+    dma("Y", [(T.Xs[:], T.X[:, :])], [], ["X"], 5.0)
+    dma("S", [(T.zq0[:], T.z0[:, :])], [], ["z0"], 2.2)
+    dma("S", [(T.v0i[:], T.v0[:, :])], [], ["v0i"], 2.2)
+    for c in range(4):
+        dma("Y", [(T.Eraw[:, 1024 * c:1024 * c + 1024], T.E[:, 1024 * c:1024 * c + 1024])], [], ["Eraw%d" % c], 6.5 + 1.5 * c)
+
+    col = T.col
+    iota(T.pi[:, 0:1], [[0, 1]], 0, 1, ["pi0"], 1)
+    ms(T.ones[:, 0:256], 1.0, ["onesa"], 256, 0.5)
+    op("G", lambda: g.affine_select(T.I[:], T.ones[:, 0:128], [[-1, 128]], A.is_equal, 0.0, 0, 1), ["onesa"], ["I"], 0.2 + 256 * CYC)
+    ts(T.pi[:, 1:2], T.pi[:, 0:1], 15, None, A.bitwise_and, None, ["pi0"], ["pi1"])
+    for j in range(1, 4):
+        ts(T.pi[:, 1 + j:2 + j], T.pi[:, 1:2], j, None, A.arith_shift_right, None, ["pi1"], ["pi%d" % (1 + j)])
+    cp(col[:, 0:5], T.pi[:, 0:5], ch("pi", 5), ["colb"])
+    cP, cB, cB1, cB2, cB3 = [col[:, j:j + 1] for j in range(5)]
+    made = [5]
+
+    def column(in0, s1, s2, o0, o1, rd=()):
+        j = made[0]
+        made[0] += 1
+        if o0 == A.mult and o1 in (None, A.add):
+            act(col[:, j:j + 1], in0, F.Identity, ["colb"] + list(rd), ["col%d" % j], 1, 1.0, s1, 0.0 if s2 is None else s2)
+        elif o0 == A.add and o1 is None:
+            act(col[:, j:j + 1], in0, F.Identity, ["colb"] + list(rd), ["col%d" % j], 1, 1.0, 1.0, s1)
+        else:
+            ts(col[:, j:j + 1], in0, s1, s2, o0, o1, ["colb"] + list(rd), ["col%d" % j])
+        return col[:, j:j + 1], "col%d" % j
+
+    c16b, k16b = column(cB, 16.0, None, A.mult, None)
+    c32b, k32b = column(cB, 32.0, None, A.mult, None)
+    cE, kE = column(cB3, -255.0, c32b, A.mult, A.add, [k32b])
+    c8b, k8b = column(cB, 8.0, None, A.mult, None)
+    cn2, kn2 = column(cB1, -2.0, cB, A.mult, A.add)
+    c8o, k8o = column(cn2, 8.0, None, A.mult, None, [kn2])
+    cG15, kG15 = column(cP, cB, 15.0, A.subtract, A.add)
+    cz, kz = column(cB, 0.0, None, A.is_equal, None)
+    c1, k1 = column(cB, 1.0, None, A.is_equal, None)
+    c2, k2 = column(cB, 2.0, None, A.is_equal, None)
+    cw, kw = column(cz, 16.0, cB, A.mult, A.add, [kz])
+    crot, krot = column(cw, cG15, -16.0, A.add, A.add, [kw, kG15])
+    ch_, kh = column(cB, 2.0 / 4096, 1.0 / 4096, A.mult, A.add)
+    cs, ks = column(cB, 1.0 / 4096, 1.0 / 4096, A.mult, A.add)
+    cdum, kdum = column(cB, float(V_), None, A.add, None)
+    cclamp, kclamp = column(cB, float(16 * 8192 + V_), None, A.add, None)
+    c256, k256 = column(cB, 256.0, None, A.mult, None)
+    cbig, kbig = column(cB, 0.0, -0.75 * 2.0 ** 24, A.mult, A.add)
+    cmid, kmid = column(cB, 0.0, -2048.0, A.mult, A.add)
+
+    iota(T.cols[:], [[1, 144]], 0, 0, ["cols"], 144, True)
+    for name, val, kk in (("WK", 4096.0, None), ("W1", 1.0, None), ("Wr0", cz, kz), ("Wr1", c1, k1), ("Wr2", c2, k2), ("Ws", cw, kw)):
+        ts(T[name][:], T.cols[:], cG15, val, A.is_equal, A.mult, ["cols", kG15] + ([kk] if kk else []), [name], 144)
+    act(T.WP[:], T.WK[:], F.Copy, ["WK"], ["WP"], 144, 1.0, 128.0)
+    act(T.WM[:], T.WK[:], F.Copy, ["WK"], ["WM"], 144, 1.0, -128.0)
+    act(T.Wh[:], T.WK[:], F.Copy, ["WK", kh], ["Wh"], 144, 1.0, ch_)
+    act(T.W32[:], T.WK[:], F.Copy, ["WK", ks], ["W32"], 144, 1.0, cs)
+    ts(T.Rot[:], T.cols[:, 0:128], crot, None, A.is_equal, None, ["cols", krot], ["Rot"], 128)
+    ts(T.d16[:], T.cols[:, 0:16], cB, None, A.is_equal, None, ["cols", "colb"], ["d16"])
+    iota(T.kc[:], [[0, 16], [1, 16]], 0, 0, ["kc"], 256, True)
+    iota(T.kcP[:], [[0, 8], [1, 16], [0, 2]], 0, 0, ["kcP"], 256, True)
+    iota(T.jc[:], [[1, 256]], 0, 0, ["jc"], 256, True)
+    for c in range(4):
+        w = WN // 4
+        iota(T.ident[:, c * w:c * w + w], [[1, w]], c * w, 0, ["id%d" % c], w, True)
+    ts(T.rK[:], T.kc[:], 0.0, 2.0 ** 25, A.is_equal, A.mult, ["kc"], ["rK"], 256)
+    act(T.rG[:], T.rK[:], F.Identity, ["rK"], ["rG"], 256, 1.0, 512.0, -8192.0)
+    act(T.rD[:], T.rK[:], F.Identity, ["rK"], ["rD"], 256, 1.0, -2.0 ** -24, 2.0)
+    act(T.pb[:], T.ones[:, 0:256], F.Copy, ["onesa", k256], ["pb"], 256, 1.0, c256)
+
+    def fill(ap, val, wr, n):
+        act(ap, T.ones[:, 0:n] if ap.shape[0] == 128 else T.ones[0:ap.shape[0], 0:n], F.Copy, ["onesa"], wr, n, 1.0, float(val))
+    fill(T.c16b[:], 16.0, ["c16b"], 256)
+    fill(T.cSb[:], 17.0 * 128, ["cSb"], 256)
+    for t in range(NV):
+        top = 16 * ((2 * TAU[t] + 1 + 15) // 16)
+        fill(T.ctau[:, 256 * t:256 * t + 256], 4096.0 * (2 * TAU[t] + 1 - top), ["ctau%d" % t, "ctaub%d" % t], 256)
+        fill(T.ctau[0:64, 256 * t:256 * t + 256], 4096.0 * top, ["ctau%d" % t], 256)
+        fill(T.ctau[0:64, 256 * t + 16 * t:256 * t + 16 * t + 16], 4096.0 * 16384, ["ctau%d" % t], 16)
+    iota(T.mH[:, 0:256], [[0, 256]], 0, 0, ["mH0"], 256, True)
+    iota(T.mL[:, 0:256], [[0, 256]], 0, 0, ["mL0"], 256, True)
+    act(T.nI[:], T.I[:], F.Copy, ["I"], ["nI"], 128, 1.0, -1.0)
+    act(T.I32[:], T.I[:], F.Copy, ["I"], ["I32"], 128)
+    iota(T.kcM[:], [[1, 16], [0, 16]], 0, 0, ["kcM"], 256, True)
+    for r in range(4):
+        iota(T.Win[:, r * WN + V_:(r + 1) * WN], [[0, 16]], 0, 0, ["dum%d" % r], 16, True)
+
+    lists = {}
+    at = [0]
+
+    def clist(name, pat, n, cadd, kadd):
+        a = at[0]
+        at[0] += n
+        iota(T.fi[:, a:a + n], pat, 0, 0, ["fi" + name], n)
+        if cadd is None:
+            cp(T.lists[:, a:a + n], T.fi[:, a:a + n], ["fi" + name], ["l" + name], n)
+        else:
+            ts(T.lists[:, a:a + n], T.fi[:, a:a + n], cadd, None, A.add, None, ["fi" + name, kadd], ["l" + name], n)
+        lists[name] = T.lists[:, a:a + n]
+        return a
+
+    clist("p1", [[16, 8], [128, 2]], 16, cB, "colb")
+    clist("pE", [[2, 16]], 16, cE, kE)
+    clist("sig", [[1, 16]], 16, c16b, k16b)
+    clist("x16", [[1, 16]], 16, None, None)
+    clist("xm", [[0, 16]], 16, cB, "colb")
+    clist("iL", [[1, 8], [128, 2]], 16, c8b, k8b)
+    clist("xP", [[1, 8], [0, 2]], 16, c8o, k8o)
+    clist("p2", [[16, 2], [32, 8]], 16, cB, "colb")
+    a_r1 = clist("r1", [[1, 128]], 128, None, None)
+    for c in range(4):
+        act(T.R1[:, 512 * c:512 * c + 512], T.I[:].indirect(T.lists[:, a_r1 + 32 * c:a_r1 + 32 * c + 32]), F.Copy, ["I", "lr1"], ["R1%d" % c], 512, CG)
+    ts(T.qc[:], T.cols[:, 0:16], 16.0, cB, A.mult, A.add, ["cols", "colb"], ["qc"])
+    ts(T.sum[:, 0:16], T.cols[:, 0:16], cB, 1.0, A.is_ge, A.add, ["cols", "colb"], ["sum"])
+    op("V", lambda: v.tensor_reduce(col[:, 31:32], T.sum[:, 0:16], AxisListType.X, A.mult), ["sum"], ["pow"], vd(16))
+
+    for r, src, lst, out, ko in ((0, "rawL", "pE", T.Lq0[:], "L0"), (1, "rawE", "pE", T.offE[:, 0:256], "offE0"), (2, "rawE", "pE", T.offE[:, 256:512], "offE1")):
+        sl = slice(256 * r, 256 * r + 256)
+        cp(T.t1[:, sl], T.raw[:, sl].indirect(lists["p1"]), [src, "lp1"], ["t1%d" % r], 256, CG)
+        op("V", lambda sl=sl: v.transpose(T.t2[:, sl], T.t1[:, sl]), ["t1%d" % r], ["t2%d" % r], vd(256))
+        cp(out, T.t2[:, sl].indirect(lists[lst]), ["t2%d" % r, "l" + lst], [ko], 256, CG)
+    cp(T.vq0[:], T.v0i[:], ["v0i"], ["v0"])
+
+    for c in range(8):
+        act(T.tmp[:, 512 * c:512 * c + 512], T.Xs[:].indirect(T.offE[:, 32 * c:32 * c + 32]), F.Copy, ["X", "offE0"], ["tmp%d" % c], 512, CG)
+    for c0, c1_ in ((0, 1), (1, 2), (2, 4), (4, 6), (6, 8)):
+        for r, o, kk in ((1, A.max, "H"), (2, A.min, "Lw")):
+            tt(T.Win[:, r * WN + 512 * c0:r * WN + 512 * c1_], T.Xs[:].indirect(T.offE[:, 256 + 32 * c0:256 + 32 * c1_]), T.tmp[:, 512 * c0:512 * c1_], o,
+               ["X", "offE1"] + ["tmp%d" % c for c in range(c0, c1_)], ["%s%d" % (kk, c) for c in range(c0, c1_)], 512 * (c1_ - c0), CG)
+    for c in range(8):
+        gcopy(T.Win[:, 512 * c:512 * c + 512], T.Eraw[:, 512 * c:512 * c + 512], ["Eraw%d" % (c // 2)], ["E%d" % c], 512)
+    kE_, kH, kL, kS = ch("E") + ["dum0"], ch("H") + ["dum1"], ch("Lw") + ["dum2"], ["S", "dum3"]
+
+    def edge_sums():
+        for b in range(16):
+            mm([(T.pM1[:, 0:256], wsl(T.W32, b), T.Win[:, 256 * b:256 * b + 256], 256)], ["W32", "E%d" % (b // 2)], ["pM1"], b == 0, b == 15, 4)
+        act(T.S0[:], T.pM1[:, 0:256], F.Copy, ["pM1"], ["S0"], 256)
+        dma("Y", [(T.Win[16 * gi:16 * gi + 1, 3 * WN:3 * WN + V_], T.S0[16 * gi:16 * gi + 16, :]) for gi in range(8)], ["S0"], ["S"], 2.5)
+    if SUMS_AT == 0:
+        edge_sums()
+
+    def sm(i):
+        return T.sm[:, 16 * i:16 * i + 16]
+
+    def si(i):
+        return T.si[:, 16 * i:16 * i + 16]
+
+    def s16(i, n=1):
+        return T.s16[:, 16 * i:16 * (i + n)]
+
+    def n2l(out, w, kw_, src, ksrc, bank, const, kconst, contiguous=False, a0=0):
+        items = [(out, T.ones[:, 0:128], const[:, 0:16], 16)] if const is not None else []
+        for b in range(16):
+            items.append((out, wsl(w, b), src[:, a0 + 16 * b:a0 + 16 * b + 16] if contiguous else src[:, a0 + b:a0 + 256:16], 16))
+        mm(items, [kw_, ksrc, "onesa"] + ([kconst] if kconst else []), [bank])
+
+    for t in range(NV):
+        z, L16, v16 = T["zq%d" % t], T["Lq%d" % t], T["vq%d" % t]
+        zw, Lin, ain, ma, mb = T["zin%d" % t], T["Lin%d" % t], T["ain%d" % t], T["a%d" % t], T["b%d" % t]
+        zin0, zin1, zin2 = zw[:, 256:512], zw[:, 512:1024], zw[:, 256:1024]
+        kz_, kzi, kLi, kai, kbi = "z%d" % t, "zin%d" % t, "Lin%d" % t, "ain%d" % t, "bin%d" % t
+        last = t == NV - 1
+        send([(zin0, z[:])], "mz_%d" % t, [kz_], [kzi], 65536)
+        send([(Lin[:], L16[:])], "m1_%d" % t, ["L%d" % t], [kLi], 65536)
+
+        if t == 0:
+            ts(T.cf[:], T.Eraw[:].indirect(v16[:]), -2048.0, None, A.add, None, ch("Eraw", 4) + ["v0"], ["cf"], 256, CG)
+        else:
+            act(T.cf[:], win(0).indirect(v16[:]), F.Identity, kE_ + ["v%d" % t, kmid], ["cf"], 256, CG, 1.0, cmid)
+        ts(T.c16[:], T.cf[:].indirect(lists["sig"]), 2048.0, None, A.add, None, ["cf", "lsig"], ["c16"], 256, CG)
+        act(T.zs[:], z[:].indirect(lists["sig"]), F.Copy, [kz_, "lsig"], ["zs"], 256, CG)
+        for h in range(2):
+            mm([(T.pA1[:, 128 * h:128 * h + 128], T.zs[:, 128 * h:128 * h + 128], T.I[:], 128)], ["zs", "I"], ["pA1"])
+        act(T.nzW[:], T.pA1[:, 0:256], F.Copy, ["pA1"], ["nzW"], 256, 1.0, -1.0)
+        mm([(T.pK[:, 0:256], T.I[:], T.jc[:], 256), (T.pK[:, 0:256], T.I[:], T.pb[:], 256)], ["I", "jc", "pb"], ["pK"], True, False)
+        order = [c for c in range(8)]
+        for c in order:
+            sl = slice(512 * c, 512 * c + 512)
+            bank = "pA%d" % (c % 2)
+            src = T.Xs[:].indirect(T.c16[:, 32 * c:32 * c + 32])
+            if (c * WALK_ON_V[t]) % 8 < WALK_ON_V[t]:
+                cp(T.xg[:, sl], src, ["X", "c16"], ["xg%d" % c], 512, CG)
+            else:
+                act(T.xg[:, sl], src, F.Copy, ["X", "c16"], ["xg%d" % c], 512, CG)
+            h, cc = c // 4, c % 4
+            mm([(T[bank][:], T.nzW[:, 128 * h:128 * h + 128], T.R1[:, 512 * cc:512 * cc + 512], 512), (T[bank][:], T.I[:], T.xg[:, sl], 512)],
+               ["nzW", "R1%d" % cc, "I", "xg%d" % c], [bank])
+            act(T.absd[:, sl], T[bank][:], F.Abs, [bank], ["ab%d" % c], 512)
+            mm([(T.pK[:, 0:256], wsl(T.WK, b), T.absd[:, 256 * b:256 * b + 256], 256) for b in (2 * c, 2 * c + 1)], ["WK", "ab%d" % c], ["pK"], False, c == order[-1])
+        scan(T.scK[:], T.rK[:], T.pK[:, 0:256], A.add, A.min, ["rK", "pK"], ["scK"])
+        cp(T.ki[:, 32:48], T.scK[:, 15::16], ["scK"], ["ki"])
+        ts(T.ki[:, 16:32], T.ki[:, 32:48], 15, None, A.bitwise_and, None, ["ki"], ["kik"])
+        cp(T.k16[:, 16:32], T.ki[:, 16:32], ["kik"], ["k16k"])
+        tt(T.selc[:], T.d16[:].indirect(T.k16[:, 16:32]), T.cf[:], A.mult, ["d16", "k16k", "cf"], ["selc"], 256, CG)
+        n2l(T.pK[:, 256:272], T.W1, "W1", T.selc, "selc", "pK", T.c16b, "c16b")
+        ts(ma[:, 16:32], T.scK[:, 15::16], float(TH * 4096 + 4095), None, A.is_le, None, ["scK"], ["mab%d" % t])
+        cp(ma[:, 0:16], T.pK[:, 256:272], ["pK"], ["maa%d" % t])
+        send([(ain[:], ma[:])], "m2a_%d" % t, ["maa%d" % t, "mab%d" % t], [kai], 8192)
+        ts(T.ki[:, 0:16], T.ki[:, 32:48], 4095, None, A.bitwise_and, None, ["ki"], ["kio"])
+        (gcopy if OFF[2] else cp)(T.k16[:, 0:16], T.ki[:, 0:16], ["kio"], ["k16o"], 16)
+        act(mb[:, 0:256], T.absd[:].indirect(T.k16[:, 0:16]), F.Copy, ch("ab") + ["k16o"], ["mba%d" % t], 256, CG)
+        tt(T.sum[:], T.xg[:].indirect(T.k16[:, 0:16]), z[:], A.add, ch("xg") + ["k16o", kz_], ["sum"], 256, CG)
+        ts(T.hi[:], T.sum[:], -0.5, 1.5 * 2.0 ** 24, A.add, A.add, ["sum"], ["hi"], 256)
+        act(mb[:, 256:512], T.hi[:], F.Identity, ["hi", kbig], ["mbb%d" % t], 256, 1.0, 0.5, cbig)
+        send([(zin1, mb[:])], "m2b_%d" % t, ["mba%d" % t, "mbb%d" % t], [kbi], 131072)
+
+        gcopy(zw[:, 0:256], zin0, [kzi], ["zd%d" % t], 256)
+        gcopy(T.Lf[:], Lin[:], [kLi], ["Lf"], 256)
+        mm([(T.pG[:, 0:256], T.ones[:, 0:128], T.ctau[:, 256 * t:256 * t + 256], 256)], ["onesa", "ctau%d" % t, "ctaub%d" % t], ["pG"], True, False)
+        flip = [0]
+
+        def nb():
+            flip[0] ^= 1
+            return "pB%d" % (1 - flip[0])
+        on_s = [c for c in range(8) if c >= 8 - CUT_ON_S[t]]
+        for c in range(8):
+            k0, k1_ = 2 * c + (2 * c == t), 2 * c + 2 - (2 * c + 1 == t)
+            w_ = 256 * (k1_ - k0)
+            sl = slice(256 * k0, 256 * k1_)
+            offs = Lin[:, 16 * k0:16 * k1_]
+            zt, zrd = zw[:, 512 - w_:512], [kzi] + (["zd%d" % t] if w_ > 256 else [])
+            if c in on_s:
+                for r, kr, mid, km, out, ko in ((1, kH, T.zz, "zz", T.mH, "mH"), (2, kL, T.tmp, "tmp", T.mL, "mL")):
+                    bank = nb()
+                    act(mid[:, sl], win(r).indirect(offs), F.Copy, kr + [kLi], ["%s%d" % (km, c)], w_, CG)
+                    mm([(T[bank][:, 0:w_], T.nI[:], zt, w_), (T[bank][:, 0:w_], T.I[:], mid[:, sl], w_)], zrd + ["I", "nI", "%s%d" % (km, c)], [bank])
+                    act(out[:, sl], T[bank][:, 0:w_], F.Relu, [bank], ["%s%d" % (ko, c)], w_)
+            else:
+                tt(T.mH[:, sl], win(1).indirect(offs), zt, A.max, kH + [kLi] + zrd, ["mH%d" % c], w_, CG)
+                tt(T.mL[:, sl], win(2).indirect(offs), zt, A.max, kL + [kLi] + zrd, ["mL%d" % c], w_, CG)
+            if c % 2 == 1:
+                qd = c // 2
+                for w, kw_, src, ks_ in ((T.WM, "WM", T.mH, "mH"), (T.WP, "WP", T.mL, "mL")):
+                    mm([(T.pG[:, 64 * qd:64 * qd + 64], wsl(w, b), src[:, 1024 * qd + b:1024 * qd + 1024:16], 64) for b in range(16)],
+                       [kw_, "%s%d" % (ks_, c - 1), "%s%d" % (ks_, c)], ["pG"], False, c == 7 and kw_ == "WP")
+        tt(T.key[:], T.pG[:, 0:256], T.Lf[:], A.max, ["pG", "Lf"], ["key"], 256, 1.0)
+        act(T.keyT[:], T.key[:].indirect(lists["sig"]), F.Copy, ["key", "lsig"], ["keyT"], 256, CG)
+        scan(T.scG[:], T.rG[:], T.keyT[:], A.add, A.min, ["rG", "keyT"], ["scG"])
+
+
+        vw = ain[:, 0:16]
+        tt(T.Ht[:, 0:256], win(1).indirect(vw), zin0, A.max, kH + [kai, kzi], ["Hta"], 256, CG)
+        tt(T.Ht[:, 256:512], win(2).indirect(vw), zin0, A.max, kL + [kai, kzi], ["Htb"], 256, CG)
+        o = (t + 1) % 16
+        items = [(T.pM0[:, 0:16], T.ones[:, 0:128], T.ctau[:, 256 * t + 16 * o:256 * t + 16 * o + 16], 16)]
+        items += [(T.pM0[:, 0:16], wsl(T.WM, b), T.Ht[:, b:256:16], 16) for b in range(16)]
+        mm(items, ["onesa", "ctau%d" % t, "ctaub%d" % t, "WM", "Hta"], ["pM0"], True, False)
+        mm([(T.pM0[:, 0:16], wsl(T.WP, b), T.Ht[:, 256 + b:512:16], 16) for b in range(16)], ["WP", "Htb"], ["pM0"], False, True)
+        ts(sm(1), ain[:, 16:32], 2.0 ** 22, -2.0 ** 21, A.mult, A.add, [kai], ["sm1"])
+        vwf = T.Lf[:, 16 * t:16 * t + 16]
+        (gcopy if OFF[2] else cp)(vwf, vw, [kai], ["Lf"], 16)
+        ts(sm(2), vw, -8192.0 * (15 - t), None, A.add, None, [kai], ["sm2"])
+        tt(sm(3), sm(2), sm(1), A.max, ["sm1", "sm2"], ["sm3"])
+        tt(sm(4), T.scG[:, 15::16], sm(1), A.max, ["scG", "sm1"], ["sm4"])
+        tt(sm(5), T.pM0[:, 0:16], sm(3), A.max, ["pM0", "sm3"], ["sm5"])
+        tt(sm(6), sm(5), sm(4), A.min, ["sm4", "sm5"], ["sm6"])
+        ts(si(0), sm(6), 8192.0 * 15, cclamp, A.add, A.min, ["sm6", kclamp], ["si0"])
+        ts(si(1), si(0), 8191, None, A.bitwise_and, None, ["si0"], ["u"])
+        cp(s16(0), si(1), ["u"], ["u16"])
+        if OFF[1] and not last:
+            act(T.ec[:], win(0).indirect(s16(0)), F.Identity, kE_ + ["u16", kmid], ["ec"], 256, CG, 1.0, cmid)
+            gcopy(T.ech[:], T.ec[:], ["ec"], ["ech"], 256)
+        else:
+            ts(T.ech[:], win(0).indirect(s16(0)), -2048.0, None, A.add, None, kE_ + ["u16"], ["ech"], 256, CG)
+        n2l(T.pM0[:, 16:32], T.Wr0, "Wr0", T.ech, "ech", "pM0", T.c16b, "c16b")
+        ts(si(2), si(0), 13, None, A.arith_shift_right, None, ["si0"], ["f"])
+        ts(sm(7), si(0), 16.0 * 8192, None, A.is_ge, None, ["si0"], ["ncut"])
+        ts(sm(8), si(0), 16.0 * 8192, None, A.is_lt, None, ["si0"], ["cut"])
+        n2l(T.pA0[:, 0:16], T.Wh, "Wh", zw, kbi, "pA0", None, None, False, 768)
+        cp(si(3), T.pA0[:, 0:16], ["pA0"], ["si3"])
+        ts(si(4), si(3), 4095, None, A.bitwise_and, None, ["si3"], ["hash"])
+        tt(sm(9), si(4), sm(1), A.max, ["hash", "sm1"], ["sm9"])
+        act(sm(10), sm(1), F.Identity, ["sm1"], ["sm10"], 16, 1.0, -1.0)
+        tt(sm(11), sm(10), vwf, A.max, ["sm10", "Lf"], ["sm11"])
+        tt(sm(12), sm(9), sm(11), A.min, ["sm9", "sm11"], ["sm12"])
+        tt(sm(13), sm(12), sm(7), A.mult, ["sm12", "ncut"], ["sm13"])
+        tt(sm(14), T.pM0[:, 16:32], sm(8), A.mult, ["pM0", "cut"], ["sm14"])
+        tt(sm(15), sm(14), sm(13), A.add, ["sm13", "sm14"], ["sm15"])
+        vn, zn, Ln16 = T["vq%d" % (t + 1)], T["zq%d" % (t + 1)], T["Lq%d" % (t + 1)]
+        (gcopy if OFF[3] else cp)(vn[:], sm(15), ["sm15"], ["v%d" % (t + 1)], 16)
+        if last:
+            send([(T.vin[:], vn[:])], "mv", ["v3"], ["vin"], 4096)
+
+        act(sm(16), sm(1), F.Identity, ["sm1"], ["sm16"], 16, 1.0, -2.0 ** -14, 384.0)
+        tt(sm(17), sm(16), sm(7), A.mult, ["sm16", "ncut"], ["sm17"])
+        tt(sm(18), sm(17), T.qc[:], A.add, ["sm17", "qc"], ["sm18"])
+        (gcopy if OFF[2] else cp)(s16(1), sm(18), ["sm18"], ["zo16"], 16)
+        act(zn[:], zin2.indirect(s16(1)), F.Copy, [kzi, kbi, "zo16"], ["z%d" % (t + 1)], 256, CG)
+
+        xl, kx, kc, kkc = ("xP", "lxP", T.kcP, "kcP") if last else ("xm", "lxm", T.kcM, "kcM")
+        tt(T.eq[:], si(2).indirect(lists[xl]), kc[:], A.is_equal, ["f", kx, kkc], ["eq"], 256, CG)
+        tt(sm(19), T.pM0[:, 16:32], si(1), A.subtract, ["pM0", "u"], ["sm19"])
+        tt(T.dl[:], sm(19).indirect(lists[xl]), T.eq[:], A.mult, ["sm19", kx, "eq"], ["dl"], 256, CG)
+        if not last:
+            mm([(T.pB0[:, 0:256], T.I32[:], T.Lf[:], 256)], ["I32", "Lf"], ["pB0"], True, False, 4)
+            mm([(T.pB0[:, 0:256], T.I32[:], T.dl[:], 256)], ["I32", "dl"], ["pB0"], False, True, 4)
+            if OFF[0]:
+                act(T.Ln[:], T.pB0[:, 0:256], F.Copy, ["pB0"], ["Ln"], 256)
+                gcopy(Ln16[:], T.Ln[:], ["Ln"], ["L%d" % (t + 1)], 256)
+            else:
+                cp(Ln16[:], T.pB0[:, 0:256], ["pB0"], ["L%d" % (t + 1)], 256)
+        else:
+            tt(T.Ln[:], T.Lf[:].indirect(lists["iL"]), T.dl[:], A.add, ["Lf", "liL", "dl"], ["Ln"], 256, CG)
+            op("V", lambda: v.transpose(T.Lp[:], T.Ln[:]), ["Ln"], ["Lp"], vd(256))
+            cp(Ln16[:], T.Lp[:].indirect(lists["p2"]), ["Lp", "lp2"], ["L3"], 256, CG)
+
+        act(T.ur[:], T.ident[:].indirect(s16(0)), F.Copy, ch("id", 4) + ["u16"], ["ur"], 256, CG)
+        tt(T.eq2[:], si(1).indirect(lists["x16"]), T.ur[:], A.is_equal, ["u", "lx16", "ur"], ["eq2"], 256, CG)
+        scan(T.scD[:], T.rD[:], T.eq2[:], A.mult, A.add, ["rD", "eq2"], ["scD"])
+        ts(sm(0), T.scD[:, 15::16], col[:, 31:32], cdum, A.is_ge, A.mult, ["scD", kdum, "pow"], ["sm0"])
+        tt(sm(3), sm(0), si(1), A.max, ["sm0", "u"], ["sm3"])
+        cp(T.o16[:, 0:64:4], sm(3), ["sm3"], ["oE"])
+        if not last:
+            mm([(T.pA1[:, 256:512], T.ones[:, 0:128], T.c16b[:], 256), (T.pA1[:, 256:512], T.Rot[:], T.ech[:], 256)], ["onesa", "c16b", "Rot", "ech"], ["pA1"])
+            act(T.vals[:, 0:256], T.pA1[:, 256:512], F.Copy, ["pA1"], ["val0"], 256)
+            for m in range(16):
+                cp(win(0).indirect(T.o16[:, 4 * m:4 * m + 1]), T.vals[:, 16 * m:16 * m + 16], ["val0", "oE"], kE_, 16, CS)
+            n2l(T.pG[:, 256:272], T.Wr1, "Wr1", T.ech, "ech", "pG", T.c16b, "c16b", True)
+            n2l(T.pG[:, 272:288], T.Wr2, "Wr2", T.ech, "ech", "pG", T.c16b, "c16b", True)
+            cp(s16(2, 2), T.pG[:, 256:288], ["pG"], ["ab16"])
+            act(T.An[:, 0:512], T.Xs[:].indirect(s16(2, 2)), F.Copy, ["X", "ab16"], ["An"], 512, CG)
+            An, Bn, Rn = T.An[:, 0:256], T.An[:, 256:512], T.An[:, 512:768]
+            mm([(T.pB1[:, 0:256], T.I[:], Bn, 256), (T.pB1[:, 0:256], T.nI[:], An, 256)], ["I", "nI", "An"], ["pB1"])
+            act(Rn, T.pB1[:, 0:256], F.Relu, ["pB1"], ["Rn"], 256)
+            mm([(T.pB1[:, 0:256], T.I[:], An, 256), (T.pB1[:, 0:256], T.I[:], Rn, 256)], ["I", "An", "Rn"], ["pB1"])
+            mm([(T.pB1[:, 256:512], T.I[:], Bn, 256), (T.pB1[:, 256:512], T.nI[:], Rn, 256)], ["I", "nI", "An", "Rn"], ["pB1"])
+            act(T.vals[:, 256:768], T.pB1[:], F.Copy, ["pB1"], ["val1"], 512)
+            ts(T.o16[:, 1:64:4], sm(3), float(WN), None, A.add, None, ["sm3"], ["o16b"])
+            if t >= SUMS_AT:
+                items = [(T.pK[:, 256:512], T.ones[:, 0:128], T.cSb[:], 256)]
+                items += [(T.pK[:, 256 + m:512:16], wsl(T.Ws, 0), T.ech[:, 16 * m:16 * m + 16], 16) for m in range(16)]
+                mm(items, ["onesa", "cSb", "Ws", "ech"], ["pK"])
+                act(T.vals[:, 768:1024], T.pK[:, 256:512], F.Copy, ["pK"], ["val3"], 256)
+                ts(T.o16[:, 2:64:4], sm(3), float(2 * WN), None, A.add, None, ["sm3"], ["o16c"])
+                for m in range(16):
+                    cp(T.Win[:, WN:4 * WN].indirect(T.o16[:, 4 * m:4 * m + 3]), T.vals[:, 256 + m:1024:16], ["val1", "val3", "oE", "o16b", "o16c"], kH + kL + kS, 48, CS)
+            else:
+                for m in range(16):
+                    cp(T.Win[:, WN:3 * WN].indirect(T.o16[:, 4 * m:4 * m + 2]), T.vals[:, 256 + m:768:16], ["val1", "oE", "o16b"], kH + kL, 32, CS)
+            if t + 1 == SUMS_AT:
+                edge_sums()
+        else:
+            mm([(T.pK[:, 256:512], T.ones[:, 0:128], T.cSb[:], 256), (T.pK[:, 256:512], wsl(T.Ws, 0), T.ech[:], 256)], ["onesa", "cSb", "Ws", "ech"], ["pK"])
+            act(T.vals[:, 768:1024], T.pK[:, 256:512], F.Copy, ["pK"], ["val3"], 256)
+            for m in range(16):
+                cp(win(3).indirect(T.o16[:, 4 * m:4 * m + 1]), T.vals[:, 768 + 16 * m:784 + 16 * m], ["val3", "oE"], kS, 16, CS)
+            dma("Y", [(T.ya[gi:gi + 1, :], T.Win[16 * gi:16 * gi + 1, 3 * WN:3 * WN + V_]) for gi in range(8)], kS, ["ya"], 2.5)
+
+    send([(T.zin3[:, 0:256], T.zq3[:])], "mz_3", ["z3"], ["zin3"], 65536)
+    send([(T.Lin3[:], T.Lq3[:])], "m1_3", ["L3"], ["Lin3"], 65536)
+    act(T.vo[:], T.ident[:].indirect(T.vin[:]), F.Copy, ch("id", 4) + ["vin"], ["vo"], 256, CG)
+    dma("Y", [(T.yv[gi:gi + 1, :], T.vo[16 * gi:16 * gi + 1, :]) for gi in range(8)], ["vo"], ["yv"], 2.0)
+    act(T.zo[:], T.zin3[:, 0:256], F.Copy, ["zin3"], ["zo"], 256)
+    dma("S", [(T.yz[:, :], T.zo[:])], ["zo"], ["yz"], 2.0)
+    cp(T.Lo[:], T.Lin3[:], ["Lin3"], ["Lo"], 256)
+    dma("Y", [(T.yl[16 * gi:16 * gi + 16, :], T.Lo[32 * (gi // 2):32 * (gi // 2) + 32, 128 * (gi % 2):128 * (gi % 2) + 128]) for gi in range(8)], ["Lo"], ["yl"], 2.0)
+    return ops
+
+
+def is_bank(k):
+    return k in ("pA0", "pA1", "pB0", "pB1", "pK", "pG", "pM0", "pM1")
+
+
+def order_ops(ops):
+    writer, readers = {}, {}
+    for i, o in enumerate(ops):
+        deps = set()
+        wr = set(o["wr"]) | set(k for k in o["rd"] if is_bank(k))
+        for k in o["rd"]:
+            if k in writer:
+                deps.add(writer[k])
+        for k in wr:
+            if k in writer:
+                deps.add(writer[k])
+            deps.update(readers.get(k, ()))
+        deps.discard(i)
+        for k in o["rd"]:
+            readers.setdefault(k, []).append(i)
+        for k in wr:
+            writer[k] = i
+            readers[k] = []
+        o["deps"] = sorted(deps)
+    n = len(ops)
+    succ = [[] for _ in range(n)]
+    for i, o in enumerate(ops):
+        for d in o["deps"]:
+            succ[d].append(i)
+    gap = 0.12
+    prio = [0.0] * n
+    for i in range(n - 1, -1, -1):
+        prio[i] = ops[i]["dur"] + ops[i]["lat"] + max([gap + prio[j] for j in succ[i]] + [0.0])
+    if "seq" in KEPT:
+        return KEPT["seq"]
+    pred = [o["deps"] for o in ops]
+    best = None
+    for _ in range(ROUNDS):
+        for i in range(n):
+            if ops[i]["kind"] == "d" and not ops[i]["deps"]:
+                prio[i] = 1e6 - i
+        seq, start = place(ops, pred, succ, prio, gap, False)
+        end = max(start[i] + ops[i]["dur"] + ops[i]["lat"] for i in range(n))
+        if best is None or end < best[0]:
+            best = (end, seq, start)
+        _s, back = place(ops, succ, pred, [start[i] + ops[i]["dur"] for i in range(n)], gap, True)
+        prio = [back[i] + ops[i]["dur"] for i in range(n)]
+    for i in range(n):
+        ops[i]["start"] = best[2][i]
+    KEPT["seq"] = best[1]
+    return best[1]
+
+
+def place(ops, pred, succ, prio, gap, backwards):
+    n = len(ops)
+    start = [0.0] * n
+    left = [len(p) for p in pred]
+    ready_at = [o["lat"] if backwards else 0.0 for o in ops]
+    ready = [i for i in range(n) if left[i] == 0]
+    free = {q: 0.0 for q in "VSTGY"}
+    seq = []
+    while ready:
+        first = min(ready, key=lambda i: (max(ready_at[i], free[ops[i]["q"]]), -prio[i], i))
+        q = ops[first]["q"]
+        t0 = max(ready_at[first], free[q])
+        i = max((i for i in ready if ops[i]["q"] == q and ready_at[i] <= t0 + HOLD), key=lambda i: (prio[i], -i))
+        if ready_at[i] > t0:
+            fit = [j for j in ready if ops[j]["q"] == q and max(ready_at[j], t0) + ops[j]["dur"] <= ready_at[i] + FIT]
+            now = max((j for j in ready if ops[j]["q"] == q and ready_at[j] <= t0), key=lambda j: (prio[j], -j))
+            if fit:
+                i = max(fit, key=lambda j: (prio[j], -j))
+            elif prio[i] - prio[now] < EDGE:
+                i = now
+        st = max(ready_at[i], free[q])
+        ready.remove(i)
+        o = ops[i]
+        start[i] = st
+        free[o["q"]] = st + o["dur"]
+        seq.append(i)
+        for j in succ[i]:
+            soft = ops[j]["q"] == "T" and o["q"] == "T"
+            ready_at[j] = max(ready_at[j], st + o["dur"] + (ops[j]["lat"] if backwards else o["lat"]) + (0.0 if soft else gap))
+            left[j] -= 1
+            if left[j] == 0:
+                ready.append(j)
+    return seq, start
+
+
+def rank_program(g, core, T, topo):
+    rank = T.rank_of(core)
+    if rank is None:
+        return
+    nxt = T.cores[(rank + 1) % len(T.cores)]
+    ops = build_ops(g, T, topo, core, nxt)
+    seq = order_ops(ops)
+    queue = {"V": g.vector, "S": g.scalar, "T": g.tensor, "G": g, "Y": g.sync}
+
+    def needs_wait(d, o):
+        p = ops[d]
+        if p["q"] == "T" and o["q"] == "T":
+            return False
+        if o["loose"] and p["q"] == o["q"] and set(p["wr"]) == set(o["wr"]):
+            return False
+        return True
+
+    signals = set(d for o in ops for d in o["deps"] if needs_wait(d, o))
+    count = {q: 0 for q in COUNTER}
+    seen = {q: {} for q in queue}
+    total = {}
+    for i in seq:
+        o = ops[i]
+        want = {}
+        for d in o["deps"]:
+            if needs_wait(d, o):
+                name, val = ops[d]["mark"]
+                want[name] = max(want.get(name, 0), val)
+        for name in sorted(want):
+            if seen[o["q"]].get(name, 0) < want[name]:
+                queue[o["q"]].wait_ge(T.sem[name], want[name])
+                seen[o["q"]][name] = want[name]
+        ins = o["fn"]()
+        if o["kind"] == "c":
+            if i in signals:
+                count[o["q"]] += 1
+                ins.then_inc(T.sem[COUNTER[o["q"]]], 1)
+                o["mark"] = (COUNTER[o["q"]], count[o["q"]])
+                total[COUNTER[o["q"]]] = count[o["q"]]
+        else:
+            o["mark"] = (o["sem"], o["n"])
+            total[o["sem"]] = o["n"]
+            if o["kind"] == "r":
+                total["sent"] = total.get("sent", 0) + o["n"]
+    for name in sorted(total):
+        if seen["G"].get(name, 0) < total[name]:
+            g.wait_ge(T.sem[name], total[name])

@@ -7,8 +7,8 @@ V_, Q_, NV = 4096, 256, 3
 TH, TAU = 1020, (1020, 1530, 1275)
 WN = V_ + 16
 H16 = "float16"
-WALK_ON_V = (2, 3, 3)
-CUT_ON_S = (3, 3, 3)
+WALK_ON_V = (2, 4, 3)
+CUT_ON_S = (2, 3, 3)
 
 
 def _sb(n, d):
@@ -57,8 +57,11 @@ for _n in ("pA0", "pA1", "pB0", "pB1", "pK", "pG", "pM0", "pM1"):
 SEMAPHORES = (["cV", "cS", "cT", "cG", "sent"] + ["dma%d" % _i for _i in range(20)]
               + ["m1_%d" % _i for _i in range(4)] + ["mz_%d" % _i for _i in range(4)] + ["m2a_%d" % _i for _i in range(3)] + ["m2b_%d" % _i for _i in range(3)] + ["mv"])
 
-CYC, CG, CS, TC = 0.00104, 1.56, 3.8, 0.0005
-HOLD, FIT, EDGE, ROUNDS = 0.3, 0.05, 2.0, 6
+CYC, CG, CS, TC = 0.00104, 1.56, 3.8, 0.0006
+HOLD, FIT, EDGE, ROUNDS = 0.3, 0.05, 1.0, 6
+GAP, RI, RL, DI = 0.15, 0.5, 2.0, 0.15
+JITTER, SEED, MB = 0.0, 1, 3.0
+BUILD_ON_S = 0
 OFF = [0, 0, 0, 0]
 SUMS_AT = 0
 KEPT = {}
@@ -128,7 +131,7 @@ def build_ops(g, T, topo, core, nxt):
         def fn():
             for o, i in pairs:
                 queue.dma_start(o, i).then_inc(T.sem[name], 16)
-        op(q, fn, rd, wr, 0.06 * len(pairs), "d", name, 16 * len(pairs), lat)
+        op(q, fn, rd, wr, DI * len(pairs), "d", name, 16 * len(pairs), lat)
 
     def send(pairs, sem, rd, wr, nbytes):
         def fn():
@@ -137,7 +140,7 @@ def build_ops(g, T, topo, core, nxt):
             else:
                 g.remote_dma_fused([RemoteDMATransfer(dst_ids=[DstId(rid=rid, pnc=pid)], dma_engine_mask=m, remote_sem=T.sem[sem], src=i, dst=o)
                                     for (o, i), m in zip(pairs, (mask_lo, mask_hi))], local_sem=T.sem.sent)
-        op("G", fn, rd, wr, 0.5, "r", sem, len(eng), 2.0 + nbytes / 40000.0)
+        op("G", fn, rd, wr, RI, "r", sem, len(eng), RL + nbytes / 40000.0)
 
     def ch(name, n=8):
         return ["%s%d" % (name, i) for i in range(n)]
@@ -148,13 +151,14 @@ def build_ops(g, T, topo, core, nxt):
     def win(r):
         return T.Win[:, r * WN:(r + 1) * WN]
 
-    dma("S", [(T.raw[32 * (gi // 2):32 * (gi // 2) + 32, 128 * (gi % 2):128 * (gi % 2) + 128], T.L0[16 * gi:16 * gi + 16, :]) for gi in range(8)], [], ["rawL"], 2.2)
-    dma("Y", [(T.raw[:, 256 * (1 + r) + 128 * u:256 * (1 + r) + 128 * u + 128], T.E[16 * u + r::32, :]) for r in range(2) for u in range(2)], [], ["rawE"], 2.2)
-    dma("Y", [(T.Xs[:], T.X[:, :])], [], ["X"], 5.0)
-    dma("S", [(T.zq0[:], T.z0[:, :])], [], ["z0"], 2.2)
-    dma("S", [(T.v0i[:], T.v0[:, :])], [], ["v0i"], 2.2)
-    for c in range(4):
-        dma("Y", [(T.Eraw[:, 1024 * c:1024 * c + 1024], T.E[:, 1024 * c:1024 * c + 1024])], [], ["Eraw%d" % c], 6.5 + 1.5 * c)
+    dma("Y", [(T.raw[:, 256 + 128 * u:256 + 128 * u + 128], T.E[16 * u::32, :]) for u in range(2)], [], ["rawE0"], 2.2)
+    dma("S", [(T.raw[:, 512 + 128 * u:512 + 128 * u + 128], T.E[16 * u + 1::32, :]) for u in range(2)], [], ["rawE1"], 2.2)
+    dma("Y", [(T.Xs[:], T.X[:, :])], [], ["X"], 2.0 + MB)
+    dma("S", [(T.zq0[:], T.z0[:, :])], [], ["z0"], 2.0 + MB)
+    dma("Y", [(T.v0i[:], T.v0[:, :])], [], ["v0i"], 2.0 + MB)
+    for c in range(2):
+        dma("Y", [(T.Eraw[:, 2048 * c:2048 * c + 2048], T.E[:, 2048 * c:2048 * c + 2048])], [], ["Eraw%d" % (2 * c), "Eraw%d" % (2 * c + 1)], 2.0 + MB * (2 + c))
+    dma("Y", [(T.raw[32 * (gi // 2):32 * (gi // 2) + 32, 128 * (gi % 2):128 * (gi % 2) + 128], T.L0[16 * gi:16 * gi + 16, :]) for gi in range(8)], [], ["rawL"], 2.0 + 3 * MB)
 
     col = T.col
     iota(T.pi[:, 0:1], [[0, 1]], 0, 1, ["pi0"], 1)
@@ -264,7 +268,7 @@ def build_ops(g, T, topo, core, nxt):
     ts(T.sum[:, 0:16], T.cols[:, 0:16], cB, 1.0, A.is_ge, A.add, ["cols", "colb"], ["sum"])
     op("V", lambda: v.tensor_reduce(col[:, 31:32], T.sum[:, 0:16], AxisListType.X, A.mult), ["sum"], ["pow"], vd(16))
 
-    for r, src, lst, out, ko in ((0, "rawL", "pE", T.Lq0[:], "L0"), (1, "rawE", "pE", T.offE[:, 0:256], "offE0"), (2, "rawE", "pE", T.offE[:, 256:512], "offE1")):
+    for r, src, lst, out, ko in ((0, "rawL", "pE", T.Lq0[:], "L0"), (1, "rawE0", "pE", T.offE[:, 0:256], "offE0"), (2, "rawE1", "pE", T.offE[:, 256:512], "offE1")):
         sl = slice(256 * r, 256 * r + 256)
         cp(T.t1[:, sl], T.raw[:, sl].indirect(lists["p1"]), [src, "lp1"], ["t1%d" % r], 256, CG)
         op("V", lambda sl=sl: v.transpose(T.t2[:, sl], T.t1[:, sl]), ["t1%d" % r], ["t2%d" % r], vd(256))
@@ -273,7 +277,19 @@ def build_ops(g, T, topo, core, nxt):
 
     for c in range(8):
         act(T.tmp[:, 512 * c:512 * c + 512], T.Xs[:].indirect(T.offE[:, 32 * c:32 * c + 32]), F.Copy, ["X", "offE0"], ["tmp%d" % c], 512, CG)
+    for c in range(8 - BUILD_ON_S, 8):
+        sl = slice(512 * c, 512 * c + 512)
+        act(T.zz[:, sl], T.Xs[:].indirect(T.offE[:, 256 + 32 * c:256 + 32 * c + 32]), F.Copy, ["X", "offE1"], ["zz%d" % c], 512, CG)
+        mm([(T.pB0[:], T.I[:], T.zz[:, sl], 512), (T.pB0[:], T.nI[:], T.tmp[:, sl], 512)], ["I", "nI", "zz%d" % c, "tmp%d" % c], ["pB0"])
+        act(T.mL[:, sl], T.pB0[:], F.Relu, ["pB0"], ["mL%d" % c], 512)
+        mm([(T.pB1[:], T.I[:], T.tmp[:, sl], 512), (T.pB1[:], T.I[:], T.mL[:, sl], 512)], ["I", "tmp%d" % c, "mL%d" % c], ["pB1"])
+        act(T.Win[:, WN + 512 * c:WN + 512 * c + 512], T.pB1[:], F.Copy, ["pB1"], ["H%d" % c], 512)
+        mm([(T.pM0[:], T.I[:], T.zz[:, sl], 512), (T.pM0[:], T.nI[:], T.mL[:, sl], 512)], ["I", "nI", "zz%d" % c, "mL%d" % c], ["pM0"])
+        act(T.Win[:, 2 * WN + 512 * c:2 * WN + 512 * c + 512], T.pM0[:], F.Copy, ["pM0"], ["Lw%d" % c], 512)
     for c0, c1_ in ((0, 1), (1, 2), (2, 4), (4, 6), (6, 8)):
+        c1_ = min(c1_, 8 - BUILD_ON_S)
+        if c1_ <= c0:
+            continue
         for r, o, kk in ((1, A.max, "H"), (2, A.min, "Lw")):
             tt(T.Win[:, r * WN + 512 * c0:r * WN + 512 * c1_], T.Xs[:].indirect(T.offE[:, 256 + 32 * c0:256 + 32 * c1_]), T.tmp[:, 512 * c0:512 * c1_], o,
                ["X", "offE1"] + ["tmp%d" % c for c in range(c0, c1_)], ["%s%d" % (kk, c) for c in range(c0, c1_)], 512 * (c1_ - c0), CG)
@@ -285,7 +301,7 @@ def build_ops(g, T, topo, core, nxt):
         for b in range(16):
             mm([(T.pM1[:, 0:256], wsl(T.W32, b), T.Win[:, 256 * b:256 * b + 256], 256)], ["W32", "E%d" % (b // 2)], ["pM1"], b == 0, b == 15, 4)
         act(T.S0[:], T.pM1[:, 0:256], F.Copy, ["pM1"], ["S0"], 256)
-        dma("Y", [(T.Win[16 * gi:16 * gi + 1, 3 * WN:3 * WN + V_], T.S0[16 * gi:16 * gi + 16, :]) for gi in range(8)], ["S0"], ["S"], 2.5)
+        dma("Y", [(T.Win[0::16, 3 * WN:3 * WN + V_], T.S0[:])], ["S0"], ["S"], 2.5)
     if SUMS_AT == 0:
         edge_sums()
 
@@ -340,14 +356,13 @@ def build_ops(g, T, topo, core, nxt):
         scan(T.scK[:], T.rK[:], T.pK[:, 0:256], A.add, A.min, ["rK", "pK"], ["scK"])
         cp(T.ki[:, 32:48], T.scK[:, 15::16], ["scK"], ["ki"])
         ts(T.ki[:, 16:32], T.ki[:, 32:48], 15, None, A.bitwise_and, None, ["ki"], ["kik"])
-        cp(T.k16[:, 16:32], T.ki[:, 16:32], ["kik"], ["k16k"])
+        ts(T.ki[:, 0:16], T.ki[:, 32:48], 4095, None, A.bitwise_and, None, ["ki"], ["kio"])
+        cp(T.k16[:, 0:32], T.ki[:, 0:32], ["kik", "kio"], ["k16k", "k16o"], 32)
         tt(T.selc[:], T.d16[:].indirect(T.k16[:, 16:32]), T.cf[:], A.mult, ["d16", "k16k", "cf"], ["selc"], 256, CG)
         n2l(T.pK[:, 256:272], T.W1, "W1", T.selc, "selc", "pK", T.c16b, "c16b")
         ts(ma[:, 16:32], T.scK[:, 15::16], float(TH * 4096 + 4095), None, A.is_le, None, ["scK"], ["mab%d" % t])
         cp(ma[:, 0:16], T.pK[:, 256:272], ["pK"], ["maa%d" % t])
         send([(ain[:], ma[:])], "m2a_%d" % t, ["maa%d" % t, "mab%d" % t], [kai], 8192)
-        ts(T.ki[:, 0:16], T.ki[:, 32:48], 4095, None, A.bitwise_and, None, ["ki"], ["kio"])
-        (gcopy if OFF[2] else cp)(T.k16[:, 0:16], T.ki[:, 0:16], ["kio"], ["k16o"], 16)
         act(mb[:, 0:256], T.absd[:].indirect(T.k16[:, 0:16]), F.Copy, ch("ab") + ["k16o"], ["mba%d" % t], 256, CG)
         tt(T.sum[:], T.xg[:].indirect(T.k16[:, 0:16]), z[:], A.add, ch("xg") + ["k16o", kz_], ["sum"], 256, CG)
         ts(T.hi[:], T.sum[:], -0.5, 1.5 * 2.0 ** 24, A.add, A.add, ["sum"], ["hi"], 256)
@@ -494,16 +509,17 @@ def build_ops(g, T, topo, core, nxt):
             act(T.vals[:, 768:1024], T.pK[:, 256:512], F.Copy, ["pK"], ["val3"], 256)
             for m in range(16):
                 cp(win(3).indirect(T.o16[:, 4 * m:4 * m + 1]), T.vals[:, 768 + 16 * m:784 + 16 * m], ["val3", "oE"], kS, 16, CS)
-            dma("Y", [(T.ya[gi:gi + 1, :], T.Win[16 * gi:16 * gi + 1, 3 * WN:3 * WN + V_]) for gi in range(8)], kS, ["ya"], 2.5)
+            dma("Y", [(T.ya[:, :], T.Win[0::16, 3 * WN:3 * WN + V_])], kS, ["ya"], 2.5)
 
     send([(T.zin3[:, 0:256], T.zq3[:])], "mz_3", ["z3"], ["zin3"], 65536)
     send([(T.Lin3[:], T.Lq3[:])], "m1_3", ["L3"], ["Lin3"], 65536)
     act(T.vo[:], T.ident[:].indirect(T.vin[:]), F.Copy, ch("id", 4) + ["vin"], ["vo"], 256, CG)
-    dma("Y", [(T.yv[gi:gi + 1, :], T.vo[16 * gi:16 * gi + 1, :]) for gi in range(8)], ["vo"], ["yv"], 2.0)
+    dma("S", [(T.yv[:, :], T.vo[0::16, :])], ["vo"], ["yv"], 2.0)
     act(T.zo[:], T.zin3[:, 0:256], F.Copy, ["zin3"], ["zo"], 256)
     dma("S", [(T.yz[:, :], T.zo[:])], ["zo"], ["yz"], 2.0)
     cp(T.Lo[:], T.Lin3[:], ["Lin3"], ["Lo"], 256)
-    dma("Y", [(T.yl[16 * gi:16 * gi + 16, :], T.Lo[32 * (gi // 2):32 * (gi // 2) + 32, 128 * (gi % 2):128 * (gi % 2) + 128]) for gi in range(8)], ["Lo"], ["yl"], 2.0)
+    for u, q in ((0, "Y"), (1, "S")):
+        dma(q, [(T.yl[32 * a + 16 * u:32 * a + 16 * u + 16, :], T.Lo[32 * a:32 * a + 32, 128 * u:128 * u + 128]) for a in range(4)], ["Lo"], ["yl%d" % u], 2.0)
     return ops
 
 
@@ -535,7 +551,7 @@ def order_ops(ops):
     for i, o in enumerate(ops):
         for d in o["deps"]:
             succ[d].append(i)
-    gap = 0.12
+    gap = GAP
     prio = [0.0] * n
     for i in range(n - 1, -1, -1):
         prio[i] = ops[i]["dur"] + ops[i]["lat"] + max([gap + prio[j] for j in succ[i]] + [0.0])
@@ -552,7 +568,7 @@ def order_ops(ops):
         if best is None or end < best[0]:
             best = (end, seq, start)
         _s, back = place(ops, succ, pred, [start[i] + ops[i]["dur"] for i in range(n)], gap, True)
-        prio = [back[i] + ops[i]["dur"] for i in range(n)]
+        prio = [back[i] + ops[i]["dur"] + JITTER * (((i + 1) * SEED * 2654435761 + _ * 40503) % 1000) / 1000.0 for i in range(n)]
     for i in range(n):
         ops[i]["start"] = best[2][i]
     KEPT["seq"] = best[1]

@@ -6,9 +6,19 @@ F = ActivationFunctionType
 V_, Q_, NV = 4096, 256, 3
 TH, TAU = 1020, (1020, 1530, 1275)
 WN = V_ + 16
-H16 = "float16"
-WALK_ON_V = (2, 4, 3)
-CUT_ON_S = (2, 3, 3)
+WE = WN + 512
+BASE = (0, WE + WN, WE + 2 * WN, WE)
+AT = (0, 2, 3, 1)
+SPLIT = False
+LOG_BY_S = False
+NC = 8192 + WN - 256
+H16, B16, F32 = "float16", "bfloat16", "float32"
+WALK_ON_V = ((1,), (0, 1), (0, 1))
+CUT_ON_S = (3, 2, 2)
+BUILD_ON_S = 0
+PAIR_ON_V = False
+FIN = ("Lg", "Ln", "Lp", "Lr", "Lrow", "msk", "m1", "m2", "zo", "Lo", "vo")
+SUMQ = 2
 
 
 def _sb(n, d):
@@ -16,95 +26,95 @@ def _sb(n, d):
 
 
 SCRATCH = {
-    "Xs": _sb(V_, "bfloat16"), "Eraw": _sb(V_, "int32"), "Win": _sb(4 * WN, "float32"), "ident": _sb(WN, "float32"),
-    "xg": _sb(V_, "bfloat16"), "absd": _sb(V_, "bfloat16"), "zz": _sb(V_, "bfloat16"), "mH": _sb(V_, "bfloat16"),
-    "mL": _sb(V_, "bfloat16"), "tmp": _sb(V_, "bfloat16"),
-    "R1": _sb(2048, "bfloat16"), "nI": _sb(128, "bfloat16"), "keyT": _sb(256, "float32"), "I32": _sb(128, "float32"), "ones": _sb(256, "bfloat16"), "I": _sb(128, "bfloat16"),
-    "pi": _sb(8, "int32"), "col": _sb(32, "float32"), "cols": _sb(144, "float32"),
-    "WK": _sb(144, "bfloat16"), "WP": _sb(144, "bfloat16"), "WM": _sb(144, "bfloat16"), "Wh": _sb(144, "bfloat16"),
-    "W1": _sb(144, H16), "Wr0": _sb(144, H16), "Wr1": _sb(144, H16), "Wr2": _sb(144, H16), "Ws": _sb(144, H16),
-    "Rot": _sb(128, H16), "W32": _sb(144, "float32"), "d16": _sb(16, "float32"),
-    "kc": _sb(256, "float32"), "kcP": _sb(256, "float32"), "kcM": _sb(256, "float32"), "rK": _sb(256, "float32"),
-    "rG": _sb(256, "float32"), "rD": _sb(256, "float32"), "jc": _sb(256, "bfloat16"), "pb": _sb(256, "bfloat16"),
-    "c16b": _sb(256, "bfloat16"), "cSb": _sb(256, "bfloat16"), "ctau": _sb(768, "bfloat16"),
-    "fi": _sb(288, "int32"), "lists": _sb(288, "uint16"), "qc": _sb(16, "float32"),
-    "raw": _sb(768, "int32"), "t1": _sb(768, "float32"), "t2": _sb(768, "float32"), "offE": _sb(512, "uint16"),
-    "v0i": _sb(16, "int32"), "S0": _sb(256, "float32"),
-    "cf": _sb(256, "float32"), "c16": _sb(256, "uint16"), "zs": _sb(256, "bfloat16"), "nzW": _sb(256, "bfloat16"),
-    "scK": _sb(256, "float32"), "ki": _sb(48, "int32"), "k16": _sb(32, "uint16"),
-    "selc": _sb(256, H16), "sum": _sb(256, "float32"), "hi": _sb(256, "float32"),
-    "Lf": _sb(256, "float32"), "key": _sb(256, "float32"), "scG": _sb(256, "float32"), "Ht": _sb(512, "bfloat16"),
-    "sm": _sb(320, "float32"), "si": _sb(80, "int32"), "s16": _sb(96, "uint16"), "ech": _sb(256, H16),
-    "eq": _sb(256, "float32"), "dl": _sb(256, "float32"), "Ln": _sb(256, "float32"), "Lp": _sb(256, "float32"),
-    "ur": _sb(256, "float32"), "eq2": _sb(256, "float32"), "scD": _sb(256, "float32"),
-    "o16": _sb(64, "uint16"), "An": _sb(768, "bfloat16"),
-    "vals": _sb(1024, "float32"), "zo": _sb(256, "float32"), "Lo": _sb(256, "float32"), "vo": _sb(256, "float32"),
-    "vin": _sb(16, "uint16"), "ec": _sb(256, "float32"),
+    "Xs": _sb(V_, B16), "Eraw": _sb(V_, "int32"), "Win": _sb(WE + 3 * WN, F32), "ident": _sb(WE, F32),
+    "xg": _sb(V_, B16), "absd": ("sbuf", [128, 16, 256], B16), "mH": _sb(V_, B16), "mL": _sb(V_, B16),
+    "mid": _sb(2048, B16), "R1": _sb(512, B16), "Wt": _sb(2048, B16),
+    "nI": _sb(128, B16), "hI": _sb(128, H16), "I32": _sb(128, F32), "I": _sb(128, B16), "ones": _sb(256, B16),
+    "pi": _sb(8, "int32"), "col": _sb(40, F32), "cols": _sb(144, F32),
+    "WK": _sb(144, B16), "WP": _sb(144, B16), "WM": _sb(144, B16), "Wh": _sb(144, B16), "Wf": _sb(144, B16),
+    "W1": _sb(144, B16), "Wr0": _sb(144, B16), "Wr1": _sb(144, B16), "Wr2": _sb(144, B16), "Ws": _sb(144, B16),
+    "Rot": _sb(128, B16), "W32": _sb(144, F32), "Wp0": _sb(144, F32), "Wp1": _sb(144, F32),
+    "dm": _sb(528, F32), "dn": _sb(32, F32),
+    "kcb": _sb(256, B16), "kcM": _sb(256, F32), "rK": _sb(256, F32), "rG": _sb(256, F32),
+    "c16": _sb(256, "uint16"), "cmid": _sb(128, B16), "csum": _sb(128, B16), "ctau": _sb(384, B16), "cneg": _sb(16, B16), "nc": _sb(80, F32),
+    "fi": _sb(192, "int32"), "lists": _sb(112, "uint16"),
+    "raw": _sb(768, "int32"), "t1": _sb(768, F32), "t2": _sb(768, F32), "offE": _sb(512, "uint16"), "S0": _sb(256, F32),
+    "cf": _sb(256, F32), "cfr": _sb(256, F32), "nzW": _sb(256, B16), "neq": _sb(256, B16),
+    "scK": _sb(256, F32), "ki": _sb(80, "int32"), "k16": _sb(16, "uint16"), "selc": _sb(256, H16), "xv": _sb(256, B16),
+    "Lf": _sb(256, F32), "key": _sb(256, F32), "keyT": _sb(256, F32), "scG": _sb(256, F32), "Ht": _sb(512, B16),
+    "sm": _sb(160, F32), "si": _sb(48, "int32"), "s16": _sb(64, "uint16"), "ech": _sb(256, H16),
+    "eq": _sb(256, F32), "dl": _sb(256, F32), "ur": _sb(256, F32), "eq2": _sb(256, B16),
+    "o16": _sb(64, "uint16"), "An": _sb(768, B16), "vals": ("sbuf", [128, 16, 64], F32),
+    "fin": _sb(256 * len(FIN), F32),
+    "Lfin": _sb(256, F32), "zfin": _sb(768, B16), "fz": _sb(32, "uint16"), "fzin": _sb(32, "uint16"), "vin": _sb(16, "uint16"),
 }
 for _t in range(NV + 1):
-    SCRATCH["zq%d" % _t] = _sb(256, "bfloat16")
-    SCRATCH["Lq%d" % _t] = _sb(256, "uint16")
     SCRATCH["vq%d" % _t] = _sb(16, "uint16")
-    SCRATCH["zin%d" % _t] = _sb(1024 if _t < NV else 256, "bfloat16")
-    SCRATCH["Lin%d" % _t] = _sb(256, "uint16")
 for _t in range(NV):
-    SCRATCH["a%d" % _t] = _sb(32, "uint16")
-    SCRATCH["ain%d" % _t] = _sb(32, "uint16")
-    SCRATCH["b%d" % _t] = _sb(512, "bfloat16")
-for _n in ("pA0", "pA1", "pB0", "pB1", "pK", "pG", "pM0", "pM1"):
-    SCRATCH[_n] = ("psum", [128, 512], "float32")
+    SCRATCH["zq%d" % _t] = _sb(256, B16)
+    SCRATCH["Lq%d" % _t] = _sb(256, "uint16")
+    SCRATCH["zin%d" % _t] = _sb(1024, B16)
+    SCRATCH["Lin%d" % _t] = _sb(256, "uint16")
+    SCRATCH["a%d" % _t] = _sb(16, "uint16")
+    SCRATCH["ain%d" % _t] = _sb(16, "uint16")
+    SCRATCH["lb%d" % _t] = _sb(16, B16)
+    SCRATCH["lbin%d" % _t] = _sb(16, B16)
+    SCRATCH["h%d" % _t] = _sb(16, "uint16")
+    SCRATCH["hin%d" % _t] = _sb(16, "uint16")
+    SCRATCH["b%d" % _t] = _sb(512, B16)
+BANKS = ("pA0", "pA1", "pB0", "pB1", "pK", "pG", "pM0", "pM1")
+for _n in BANKS:
+    SCRATCH[_n] = ("psum", [128, 512], F32)
 
-SEMAPHORES = (["cV", "cS", "cT", "cG", "sent"] + ["dma%d" % _i for _i in range(20)]
-              + ["m1_%d" % _i for _i in range(4)] + ["mz_%d" % _i for _i in range(4)] + ["m2a_%d" % _i for _i in range(3)] + ["m2b_%d" % _i for _i in range(3)] + ["mv"])
+SEMAPHORES = (["cV", "cS", "cT", "cG", "sent", "mv", "mf", "mzo", "mLo"] + ["dma%d" % _i for _i in range(16)]
+              + ["%s_%d" % (_n, _i) for _n in ("m1", "mz", "m2a", "m2b", "mh") for _i in range(NV)])
 
-CYC, CG, CS, TC = 0.00104, 1.56, 3.8, 0.0006
-HOLD, FIT, EDGE, ROUNDS = 0.3, 0.05, 1.0, 6
-GAP, RI, RL, DI = 0.15, 0.5, 2.0, 0.15
-JITTER, SEED, MB = 0.0, 1, 3.0
-BUILD_ON_S = 0
-OFF = [0, 0, 0, 0]
-SUMS_AT = 0
+ROUGH = ((0.0009, 1.5, 3.6, 0.00046, 0.12, 0.55, 2.0, 25.0, 2.8),
+         (0.00085, 1.1, 2.0, 0.00042, 0.1, 0.5, 1.8, 20.0, 2.5),
+         (0.001, 1.3, 4.5, 0.0005, 0.18, 0.7, 2.4, 30.0, 2.8),
+         (0.0012, 1.9, 5.0, 0.0006, 0.1, 0.5, 2.0, 22.0, 3.3))
+HOLD, FIT, EDGE, ROUNDS, TRIES, JITTER = 0.3, 0.05, 1.0, 4, 4, 0.6
+STEPS, SLACK = 4000, 0.001
+CG, CS, DI = "gather", "scatter", 0.15
 KEPT = {}
 COUNTER = {"V": "cV", "S": "cS", "T": "cT", "G": "cG"}
 
 
-def build_ops(g, T, topo, core, nxt):
+def build_ops(g, T, topo, core, nxt, own):
     ops = []
     v, s, te = g.vector, g.scalar, g.tensor
-    rid, pid, _ = topo.addr(nxt)
     eng = topo.engines(core, nxt)
-    mask_all = topo.mask(core, nxt)
-    half = len(eng) // 2
-    mask_lo = sum(1 << e for e in eng[:half])
-    mask_hi = sum(1 << e for e in eng[half:])
+    free = [e for e in topo.engines(core, own) if e not in eng]
+    eng_own = free if len(free) == len(eng) else [e for e in topo.engines(core, own) if e in eng]
     nd = [0]
+    early = [False]
 
-    def op(q, fn, rd, wr, dur, kind="c", sem=None, n=1, lat=0.0, loose=False):
-        ops.append(dict(q=q, fn=fn, rd=list(rd), wr=list(wr), dur=dur, kind=kind, sem=sem, n=n, lat=lat, loose=loose))
-
-    def vd(n, c=1.0):
-        return 0.06 + max(64, n * c) * CYC
+    def op(q, fn, rd, wr, fix, n=0, c=1.0, kind="c", sem=None, inc=1, mb=0.0):
+        ops.append(dict(q=q, fn=fn, rd=list(rd), wr=list(wr), fix=fix, cyc=n if c in (CG, CS) else max(64, n * c), c=c, kind=kind, sem=sem, n=inc, mb=mb, early=early[0]))
 
     def ts(out, in0, s1, s2, o0, o1, rd, wr, n=16, c=1.0):
         if o1 is None:
-            op("V", lambda: v.tensor_scalar(out, in0, s1, None, o0), rd, wr, vd(n, c))
+            op("V", lambda: v.tensor_scalar(out, in0, s1, None, o0), rd, wr, 0.05, n, c)
         else:
-            op("V", lambda: v.tensor_scalar(out, in0, s1, s2, o0, o1), rd, wr, vd(n, c))
+            op("V", lambda: v.tensor_scalar(out, in0, s1, s2, o0, o1), rd, wr, 0.05, n, c)
 
     def tt(out, in0, in1, o, rd, wr, n=16, c=2.0):
-        op("V", lambda: v.tensor_tensor(out, in0, in1, o), rd, wr, vd(n, c))
+        op("V", lambda: v.tensor_tensor(out, in0, in1, o), rd, wr, 0.05, n, c)
 
-    def cp(out, in_, rd, wr, n=16, c=1.0, loose=False):
-        op("V", lambda: v.tensor_copy(out, in_), rd, wr, vd(n, c), loose=loose)
+    def cp(out, in_, rd, wr, n=16, c=1.0):
+        op("V", lambda: v.tensor_copy(out, in_), rd, wr, 0.05, n, c)
 
     def ms(ap, val, wr, n=16, c=1.0):
-        op("V", lambda: v.memset(ap, val), [], wr, vd(n, c))
+        op("V", lambda: v.memset(ap, val), [], wr, 0.05, n, c)
+
+    def turn(out, in_, rd, wr):
+        op("V", lambda: v.transpose(out, in_), rd, wr, 0.05, 256)
 
     def scan(out, d0, d1, o0, o1, rd, wr):
-        op("V", lambda: v.tensor_tensor_scan(out, d0, d1, 0.0, o0, o1), rd, wr, vd(256))
+        op("V", lambda: v.tensor_tensor_scan(out, d0, d1, 0.0, o0, o1), rd, wr, 0.05, 256)
 
     def act(out, in_, f, rd, wr, n, c=1.0, scale=1.0, bias=0.0):
-        op("S", lambda: s.activation(out, in_, f, bias=bias, scale=scale), rd, wr, 0.08 + max(64, n * c) * CYC)
+        op("S", lambda: s.activation(out, in_, f, bias=bias, scale=scale), rd, wr, 0.065, n, c)
 
     def mm(items, rd, wr, first=True, last=True, x=1):
         def fn():
@@ -112,18 +122,21 @@ def build_ops(g, T, topo, core, nxt):
             for i, (o, l, r, _n) in enumerate(items):
                 ins = te.matmul(o, l, r, first and i == 0, last and i == len(items) - 1)
             return ins
-        op("T", fn, rd, wr, 0.05 + sum(max(64, it[3]) * x for it in items) * TC)
+        op("T", fn, rd, wr, 0.02, sum(max(64, it[3]) * x for it in items))
 
-    def iota(out, pat, base, cm, wr, n, small=False):
+    def iota(out, pat, base, cm, wr, n, small=True):
         if small:
-            op("G", lambda: g.iota(out, pat, base, cm, allow_small_or_imprecise_dtypes=True), [], wr, 0.16 + 2 * n * CYC)
+            op("G", lambda: g.iota(out, pat, base, cm, allow_small_or_imprecise_dtypes=True), [], wr, 0.08, 2 * n + 64)
         else:
-            op("G", lambda: g.iota(out, pat, base, cm), [], wr, 0.16 + 2 * n * CYC)
+            op("G", lambda: g.iota(out, pat, base, cm), [], wr, 0.08, 2 * n + 64)
+
+    def sel(out, in_, pat, o, fill, base, cm, rd, wr, n):
+        op("G", lambda: g.affine_select(out, in_, pat, o, fill, base, cm), rd, wr, 0.12, 2 * n + 64)
 
     def gcopy(out, in_, rd, wr, n):
-        op("G", lambda: g.affine_select(out, in_, [[0, n]], A.is_equal, 0.0, 0, 0), rd, wr, 0.21 + 2 * n * CYC)
+        sel(out, in_, [[0, n]], A.is_equal, 0.0, 0, 0, rd, wr, n)
 
-    def dma(q, pairs, rd, wr, lat):
+    def dma(q, pairs, rd, wr, mb):
         name = "dma%d" % nd[0]
         nd[0] += 1
         queue = g.sync if q == "Y" else s
@@ -131,16 +144,21 @@ def build_ops(g, T, topo, core, nxt):
         def fn():
             for o, i in pairs:
                 queue.dma_start(o, i).then_inc(T.sem[name], 16)
-        op(q, fn, rd, wr, DI * len(pairs), "d", name, 16 * len(pairs), lat)
+        op(q, fn, rd, wr, DI * len(pairs), 0, 1.0, "d", name, 16 * len(pairs), mb)
 
-    def send(pairs, sem, rd, wr, nbytes):
+    def send(pairs, sem, rd, wr, mb, to=nxt):
+        rid, pid, _ = topo.addr(to)
+        es = eng if to == nxt else eng_own
+        k = len(es) // len(pairs)
+        masks = [sum(1 << e for e in es[k * j:k * j + k]) for j in range(len(pairs))]
+
         def fn():
             if len(pairs) == 1:
-                g.remote_dma(pairs[0][0], pairs[0][1], T.sem[sem], T.sem.sent, pid, rid, mask_all)
+                g.remote_dma(pairs[0][0], pairs[0][1], T.sem[sem], T.sem.sent, pid, rid, masks[0])
             else:
                 g.remote_dma_fused([RemoteDMATransfer(dst_ids=[DstId(rid=rid, pnc=pid)], dma_engine_mask=m, remote_sem=T.sem[sem], src=i, dst=o)
-                                    for (o, i), m in zip(pairs, (mask_lo, mask_hi))], local_sem=T.sem.sent)
-        op("G", fn, rd, wr, RI, "r", sem, len(eng), RL + nbytes / 40000.0)
+                                    for (o, i), m in zip(pairs, masks)], local_sem=T.sem.sent)
+        op("G", fn, rd, wr, 0.0, 0, 1.0, "r", sem, len(es), mb)
 
     def ch(name, n=8):
         return ["%s%d" % (name, i) for i in range(n)]
@@ -148,162 +166,153 @@ def build_ops(g, T, topo, core, nxt):
     def wsl(w, b):
         return w[:, 15 - b:143 - b]
 
-    def win(r):
-        return T.Win[:, r * WN:(r + 1) * WN]
+    def win(r, n=WN):
+        return T.Win[:, BASE[r]:BASE[r] + n]
 
-    dma("Y", [(T.raw[:, 256 + 128 * u:256 + 128 * u + 128], T.E[16 * u::32, :]) for u in range(2)], [], ["rawE0"], 2.2)
-    dma("S", [(T.raw[:, 512 + 128 * u:512 + 128 * u + 128], T.E[16 * u + 1::32, :]) for u in range(2)], [], ["rawE1"], 2.2)
-    dma("Y", [(T.Xs[:], T.X[:, :])], [], ["X"], 2.0 + MB)
-    dma("S", [(T.zq0[:], T.z0[:, :])], [], ["z0"], 2.0 + MB)
-    dma("Y", [(T.v0i[:], T.v0[:, :])], [], ["v0i"], 2.0 + MB)
+    def fin(name, a=0, b=256):
+        return T.fin[:, 256 * FIN.index(name) + a:256 * FIN.index(name) + b]
+
+    dma("Y", [(T.raw[:, 256 + 128 * u:256 + 128 * u + 128], T.E[16 * u::32, :]) for u in range(2)], [], ["rawE0"], 0.15)
+    dma("S", [(T.raw[:, 512 + 128 * u:512 + 128 * u + 128], T.E[16 * u + 1::32, :]) for u in range(2)], [], ["rawE1"], 0.25)
+    dma("Y", [(T.Xs[:], T.X[:, :])], [], ["X"], 1.3)
+    dma("S", [(T.zq0[:], T.z0[:, :])], [], ["z0"], 1.3)
+    dma("Y", [(T.ki[:, 64:80], T.v0[:, :])], [], ["v0i"], 1.35)
     for c in range(2):
-        dma("Y", [(T.Eraw[:, 2048 * c:2048 * c + 2048], T.E[:, 2048 * c:2048 * c + 2048])], [], ["Eraw%d" % (2 * c), "Eraw%d" % (2 * c + 1)], 2.0 + MB * (2 + c))
-    dma("Y", [(T.raw[32 * (gi // 2):32 * (gi // 2) + 32, 128 * (gi % 2):128 * (gi % 2) + 128], T.L0[16 * gi:16 * gi + 16, :]) for gi in range(8)], [], ["rawL"], 2.0 + 3 * MB)
+        dma("Y", [(T.Eraw[:, 2048 * c:2048 * c + 2048], T.E[:, 2048 * c:2048 * c + 2048])], [], ["Eraw%d" % (2 * c), "Eraw%d" % (2 * c + 1)], 2.35 + c)
+    dma("Y", [(T.raw[32 * (gi // 2):32 * (gi // 2) + 32, 128 * (gi % 2):128 * (gi % 2) + 128], T.L0[16 * gi:16 * gi + 16, :]) for gi in range(8)], [], ["rawL"], 3.5)
 
+    early[0] = True
     col = T.col
-    iota(T.pi[:, 0:1], [[0, 1]], 0, 1, ["pi0"], 1)
-    ms(T.ones[:, 0:256], 1.0, ["onesa"], 256, 0.5)
-    op("G", lambda: g.affine_select(T.I[:], T.ones[:, 0:128], [[-1, 128]], A.is_equal, 0.0, 0, 1), ["onesa"], ["I"], 0.2 + 256 * CYC)
+    iota(T.pi[:, 0:1], [[0, 1]], 0, 1, ["pi0"], 1, False)
+    names = ("p1", "xm", "p2", "pE", "sig", "iL", "x16")
+    pats = ([[16, 8], [128, 2]], [[0, 16]], [[16, 2], [32, 8]], [[2, 16]], [[1, 16]], [[1, 8], [128, 2]], [[1, 16]])
+    lists = {name: T.lists[:, 16 * j:16 * j + 16] for j, name in enumerate(names)}
+    for j in (0, 3, 1, 2):
+        iota(T.fi[:, 16 * j:16 * j + 16], pats[j], 0, 0, ["fi" + names[j]], 16, False)
+    iota(T.cols[:], [[1, 144]], 0, 0, ["cols"], 144)
     ts(T.pi[:, 1:2], T.pi[:, 0:1], 15, None, A.bitwise_and, None, ["pi0"], ["pi1"])
-    for j in range(1, 4):
-        ts(T.pi[:, 1 + j:2 + j], T.pi[:, 1:2], j, None, A.arith_shift_right, None, ["pi1"], ["pi%d" % (1 + j)])
+    ts(T.pi[:, 2:3], T.pi[:, 0:1], 15, 1, A.bitwise_and, A.arith_shift_right, ["pi0"], ["pi2"])
+    ts(T.pi[:, 3:4], T.pi[:, 0:1], 4, 1, A.arith_shift_right, A.bitwise_and, ["pi0"], ["pi3"])
+    ts(T.pi[:, 4:5], T.pi[:, 0:1], 3, 1, A.arith_shift_right, A.bitwise_and, ["pi0"], ["pi4"])
     cp(col[:, 0:5], T.pi[:, 0:5], ch("pi", 5), ["colb"])
-    cP, cB, cB1, cB2, cB3 = [col[:, j:j + 1] for j in range(5)]
+    cP, cB, cB1, cU, cB3 = [col[:, j:j + 1] for j in range(5)]
+    ms(T.ones[:, 0:256], 1.0, ["onesa"], 256, 0.5)
     made = [5]
 
-    def column(in0, s1, s2, o0, o1, rd=()):
+    def column(in0, scale, bias, rd=()):
         j = made[0]
         made[0] += 1
-        if o0 == A.mult and o1 in (None, A.add):
-            act(col[:, j:j + 1], in0, F.Identity, ["colb"] + list(rd), ["col%d" % j], 1, 1.0, s1, 0.0 if s2 is None else s2)
-        elif o0 == A.add and o1 is None:
-            act(col[:, j:j + 1], in0, F.Identity, ["colb"] + list(rd), ["col%d" % j], 1, 1.0, 1.0, s1)
-        else:
-            ts(col[:, j:j + 1], in0, s1, s2, o0, o1, ["colb"] + list(rd), ["col%d" % j])
+        act(col[:, j:j + 1], in0, F.Identity, ["colb"] + list(rd), ["col%d" % j], 1, 1.0, scale, bias)
         return col[:, j:j + 1], "col%d" % j
 
-    c16b, k16b = column(cB, 16.0, None, A.mult, None)
-    c32b, k32b = column(cB, 32.0, None, A.mult, None)
-    cE, kE = column(cB3, -255.0, c32b, A.mult, A.add, [k32b])
-    c8b, k8b = column(cB, 8.0, None, A.mult, None)
-    cn2, kn2 = column(cB1, -2.0, cB, A.mult, A.add)
-    c8o, k8o = column(cn2, 8.0, None, A.mult, None, [kn2])
-    cG15, kG15 = column(cP, cB, 15.0, A.subtract, A.add)
-    cz, kz = column(cB, 0.0, None, A.is_equal, None)
-    c1, k1 = column(cB, 1.0, None, A.is_equal, None)
-    c2, k2 = column(cB, 2.0, None, A.is_equal, None)
-    cw, kw = column(cz, 16.0, cB, A.mult, A.add, [kz])
-    crot, krot = column(cw, cG15, -16.0, A.add, A.add, [kw, kG15])
-    ch_, kh = column(cB, 2.0 / 4096, 1.0 / 4096, A.mult, A.add)
-    cs, ks = column(cB, 1.0 / 4096, 1.0 / 4096, A.mult, A.add)
-    cdum, kdum = column(cB, float(V_), None, A.add, None)
-    cclamp, kclamp = column(cB, float(16 * 8192 + V_), None, A.add, None)
-    c256, k256 = column(cB, 256.0, None, A.mult, None)
-    cbig, kbig = column(cB, 0.0, -0.75 * 2.0 ** 24, A.mult, A.add)
-    cmid, kmid = column(cB, 0.0, -2048.0, A.mult, A.add)
-
-    iota(T.cols[:], [[1, 144]], 0, 0, ["cols"], 144, True)
-    for name, val, kk in (("WK", 4096.0, None), ("W1", 1.0, None), ("Wr0", cz, kz), ("Wr1", c1, k1), ("Wr2", c2, k2), ("Ws", cw, kw)):
-        ts(T[name][:], T.cols[:], cG15, val, A.is_equal, A.mult, ["cols", kG15] + ([kk] if kk else []), [name], 144)
-    act(T.WP[:], T.WK[:], F.Copy, ["WK"], ["WP"], 144, 1.0, 128.0)
-    act(T.WM[:], T.WK[:], F.Copy, ["WK"], ["WM"], 144, 1.0, -128.0)
-    act(T.Wh[:], T.WK[:], F.Copy, ["WK", kh], ["Wh"], 144, 1.0, ch_)
-    act(T.W32[:], T.WK[:], F.Copy, ["WK", ks], ["W32"], 144, 1.0, cs)
-    ts(T.Rot[:], T.cols[:, 0:128], crot, None, A.is_equal, None, ["cols", krot], ["Rot"], 128)
-    ts(T.d16[:], T.cols[:, 0:16], cB, None, A.is_equal, None, ["cols", "colb"], ["d16"])
-    iota(T.kc[:], [[0, 16], [1, 16]], 0, 0, ["kc"], 256, True)
-    iota(T.kcP[:], [[0, 8], [1, 16], [0, 2]], 0, 0, ["kcP"], 256, True)
-    iota(T.jc[:], [[1, 256]], 0, 0, ["jc"], 256, True)
-    for c in range(4):
-        w = WN // 4
-        iota(T.ident[:, c * w:c * w + w], [[1, w]], c * w, 0, ["id%d" % c], w, True)
-    ts(T.rK[:], T.kc[:], 0.0, 2.0 ** 25, A.is_equal, A.mult, ["kc"], ["rK"], 256)
+    c32b, k32b = column(cB, 32.0, 0.0)
+    cE, kE = column(cB3, -255.0, c32b, [k32b])
+    ts(T.lists[:, 0:48], T.fi[:, 0:48], cB, None, A.add, None, ["fip1", "fixm", "fip2", "colb"], ["lp1", "lxm", "lp2"], 48)
+    ts(lists["pE"], T.fi[:, 48:64], cE, None, A.add, None, ["fipE", kE], ["lpE"])
+    cg, kg = column(cB, -1.0, cP)
+    cG15, kG15 = column(cg, 1.0, 15.0, [kg])
+    ts(T.W1[:], T.cols[:], cG15, None, A.is_equal, None, ["cols", kG15], ["W1"], 144)
+    ts(T.dm[:, 0:32], T.cols[:, 0:32], cB, None, A.is_equal, None, ["cols", "colb"], ["dm0"], 32)
+    cz, c1, c2 = [T.dm[:, j:j + 1] for j in range(3)]
+    sel(T.I[:], T.ones[:, 0:128], [[-1, 128]], A.is_equal, 0.0, 0, 1, ["onesa"], ["I"], 128)
+    iota(T.kcb[:], [[0, 16], [1, 16]], 0, 0, ["kcb"], 256)
+    iota(T.mid[:, 0:512], [[1, 32], [0, 16]], 0, 0, ["mid0"], 512)
+    c32p, k32p = column(cU, 16.0, cB)
+    ts(T.R1[:], T.mid[:, 0:512], c32p, None, A.is_equal, None, ["mid0", k32p], ["R1"], 512, 0.5)
+    ms(T.mH[:, 0:256], 0.0, ["mH0"], 256, 0.5)
+    ts(T.rK[:], T.kcb[:], 0.0, 2.0 ** 25, A.is_equal, A.mult, ["kcb"], ["rK"], 256)
     act(T.rG[:], T.rK[:], F.Identity, ["rK"], ["rG"], 256, 1.0, 512.0, -8192.0)
-    act(T.rD[:], T.rK[:], F.Identity, ["rK"], ["rD"], 256, 1.0, -2.0 ** -24, 2.0)
-    act(T.pb[:], T.ones[:, 0:256], F.Copy, ["onesa", k256], ["pb"], 256, 1.0, c256)
-
-    def fill(ap, val, wr, n):
-        act(ap, T.ones[:, 0:n] if ap.shape[0] == 128 else T.ones[0:ap.shape[0], 0:n], F.Copy, ["onesa"], wr, n, 1.0, float(val))
-    fill(T.c16b[:], 16.0, ["c16b"], 256)
-    fill(T.cSb[:], 17.0 * 128, ["cSb"], 256)
-    for t in range(NV):
-        top = 16 * ((2 * TAU[t] + 1 + 15) // 16)
-        fill(T.ctau[:, 256 * t:256 * t + 256], 4096.0 * (2 * TAU[t] + 1 - top), ["ctau%d" % t, "ctaub%d" % t], 256)
-        fill(T.ctau[0:64, 256 * t:256 * t + 256], 4096.0 * top, ["ctau%d" % t], 256)
-        fill(T.ctau[0:64, 256 * t + 16 * t:256 * t + 16 * t + 16], 4096.0 * 16384, ["ctau%d" % t], 16)
-    iota(T.mH[:, 0:256], [[0, 256]], 0, 0, ["mH0"], 256, True)
-    iota(T.mL[:, 0:256], [[0, 256]], 0, 0, ["mL0"], 256, True)
+    for j in (4, 5, 6):
+        iota(T.fi[:, 16 * j:16 * j + 16], pats[j], 0, 0, ["fi" + names[j]], 16, False)
+    iota(T.fi[:, 112:144], [[-512, 2], [16, 16]], NC + 512, 0, ["finc0"], 32, False)
+    iota(T.fi[:, 144:192], [[-8192, NV], [16, 16]], NC + 256 + 8192 * 15, 0, ["finc1"], 48, False)
+    c16b, k16b = column(cB, 16.0, 0.0)
+    c8b, k8b = column(cB, 8.0, 0.0)
+    cn2, kn2 = column(cB1, -2.0, cB)
+    cev, kev = column(cn2, -1.0, 1.0, [kn2])
+    cw, kw = column(cz, 16.0, cB, ["dm0"])
+    cr1, kr1 = column(cw, 1.0, cg, [kw, kg])
+    crot, krot = column(cr1, 1.0, -1.0, [kr1])
+    ch_, kh = column(cB, 2.0, 1.0)
+    cs, ks = column(cB, 1.0, 1.0)
+    cdum, kdum = column(cB, 1.0, float(V_))
+    cmid, kmid = column(cB, 0.0, -2048.0)
+    cq1, kq1 = column(cU, -8.0, cg, [kg])
+    cq3, kq3 = column(cB1, 1.0, cq1, [kq1])
+    cq2, kq2 = column(cq3, 1.0, 16.0, [kq3])
+    for name, val, kk in (("WK", 1024.0, ()), ("WP", 2.0 ** 19, ()), ("WM", -2.0 ** 19, ()), ("Wf", 32.0, ()), ("Wh", ch_, [kh]), ("W32", cs, [ks]),
+                          ("Wr0", cz, ["dm0"]), ("Wr1", c1, ["dm0"]), ("Wr2", c2, ["dm0"]), ("Ws", cw, [kw])):
+        act(T[name][:], T.W1[:], F.Copy, ["W1"] + list(kk), [name], 144, 1.0, val)
+    ts(lists["sig"], T.fi[:, 64:80], c16b, None, A.add, None, ["fisig", k16b], ["lsig"])
+    ts(lists["iL"], T.fi[:, 80:96], c8b, None, A.add, None, ["fiiL", k8b], ["liL"])
+    cp(lists["x16"], T.fi[:, 96:112], ["fix16"], ["lx16"])
+    ts(T.nc[:], T.fi[:, 112:192], cB, None, A.add, None, ["finc0", "finc1", "colb"], ["nc"], 80)
+    for name, val, kk in (("Wp0", cev, kev), ("Wp1", cn2, kn2)):
+        ts(T[name][:], T.cols[:], cq2, val, A.is_equal, A.mult, ["cols", kq2, kk], [name], 144)
+    ts(T.Rot[:], T.cols[:, 0:128], crot, None, A.is_equal, None, ["cols", krot], ["Rot"], 128)
+    ts(T.hI[:], T.I[:], 0.5 - 2.0 ** -11, None, A.mult, None, ["I"], ["hI"], 128, 0.5)
     act(T.nI[:], T.I[:], F.Copy, ["I"], ["nI"], 128, 1.0, -1.0)
     act(T.I32[:], T.I[:], F.Copy, ["I"], ["I32"], 128)
-    iota(T.kcM[:], [[1, 16], [0, 16]], 0, 0, ["kcM"], 256, True)
-    for r in range(4):
-        iota(T.Win[:, r * WN + V_:(r + 1) * WN], [[0, 16]], 0, 0, ["dum%d" % r], 16, True)
-
-    lists = {}
-    at = [0]
-
-    def clist(name, pat, n, cadd, kadd):
-        a = at[0]
-        at[0] += n
-        iota(T.fi[:, a:a + n], pat, 0, 0, ["fi" + name], n)
-        if cadd is None:
-            cp(T.lists[:, a:a + n], T.fi[:, a:a + n], ["fi" + name], ["l" + name], n)
-        else:
-            ts(T.lists[:, a:a + n], T.fi[:, a:a + n], cadd, None, A.add, None, ["fi" + name, kadd], ["l" + name], n)
-        lists[name] = T.lists[:, a:a + n]
-        return a
-
-    clist("p1", [[16, 8], [128, 2]], 16, cB, "colb")
-    clist("pE", [[2, 16]], 16, cE, kE)
-    clist("sig", [[1, 16]], 16, c16b, k16b)
-    clist("x16", [[1, 16]], 16, None, None)
-    clist("xm", [[0, 16]], 16, cB, "colb")
-    clist("iL", [[1, 8], [128, 2]], 16, c8b, k8b)
-    clist("xP", [[1, 8], [0, 2]], 16, c8o, k8o)
-    clist("p2", [[16, 2], [32, 8]], 16, cB, "colb")
-    a_r1 = clist("r1", [[1, 128]], 128, None, None)
-    for c in range(4):
-        act(T.R1[:, 512 * c:512 * c + 512], T.I[:].indirect(T.lists[:, a_r1 + 32 * c:a_r1 + 32 * c + 32]), F.Copy, ["I", "lr1"], ["R1%d" % c], 512, CG)
-    ts(T.qc[:], T.cols[:, 0:16], 16.0, cB, A.mult, A.add, ["cols", "colb"], ["qc"])
-    ts(T.sum[:, 0:16], T.cols[:, 0:16], cB, 1.0, A.is_ge, A.add, ["cols", "colb"], ["sum"])
-    op("V", lambda: v.tensor_reduce(col[:, 31:32], T.sum[:, 0:16], AxisListType.X, A.mult), ["sum"], ["pow"], vd(16))
-
-    for r, src, lst, out, ko in ((0, "rawL", "pE", T.Lq0[:], "L0"), (1, "rawE0", "pE", T.offE[:, 0:256], "offE0"), (2, "rawE1", "pE", T.offE[:, 256:512], "offE1")):
-        sl = slice(256 * r, 256 * r + 256)
-        cp(T.t1[:, sl], T.raw[:, sl].indirect(lists["p1"]), [src, "lp1"], ["t1%d" % r], 256, CG)
-        op("V", lambda sl=sl: v.transpose(T.t2[:, sl], T.t1[:, sl]), ["t1%d" % r], ["t2%d" % r], vd(256))
-        cp(out, T.t2[:, sl].indirect(lists[lst]), ["t2%d" % r, "l" + lst], [ko], 256, CG)
-    cp(T.vq0[:], T.v0i[:], ["v0i"], ["v0"])
+    act(T.dn[:], T.dm[:, 0:32], F.Identity, ["dm0"], ["dn"], 32, 1.0, -1.0, 1.0)
+    ts(T.col[:, 24:40], T.cols[:, 0:16], cB, 2.0 ** 19, A.is_gt, A.mult, ["cols", "colb"], ["tri"])
+    for b in range(1, 16):
+        ts(T.Wt[:, 128 * b:128 * b + 128], wsl(T.W1, b), T.col[:, 24 + b:25 + b], None, A.mult, None, ["W1", "tri"], ["Wt%d" % b], 128, 0.5)
+    early[0] = False
 
     for c in range(8):
-        act(T.tmp[:, 512 * c:512 * c + 512], T.Xs[:].indirect(T.offE[:, 32 * c:32 * c + 32]), F.Copy, ["X", "offE0"], ["tmp%d" % c], 512, CG)
+        w = WE // 8
+        iota(T.ident[:, c * w:c * w + w], [[1, w]], c * w, 0, ["id%d" % c], w)
+    iota(T.dm[:, 32:528], [[0, 496]], 0, 0, ["dm"], 496)
+    act(T.dm[:, 32::32], T.ones[:, 0:16], F.Copy, ["onesa", "dm0"], ["dm"], 16, 1.0, cz)
+    iota(T.cmid[:], [[0, 128]], 16, 0, ["cmid"], 128)
+    iota(T.csum[:], [[0, 128]], 17 * 128, 0, ["csum"], 128)
+    iota(T.cneg[:], [[0, 16]], -2 ** 23, 0, ["cneg"], 16)
+    for t in range(NV):
+        top = 16 * ((2 * TAU[t] + 1 + 15) // 16)
+        iota(T.ctau[:, 128 * t:128 * t + 128], [[0, 128]], 4096 * (2 * TAU[t] + 1 - top), 0, ["ctau%d" % t], 128)
+        iota(T.ctau[0:64, 128 * t:128 * t + 128], [[0, 128]], 4096 * top, 0, ["ctau%d" % t], 128)
+    iota(T.kcM[:], [[1, 16], [0, 16]], -15, 0, ["kcM"], 256)
+    for r in range(4):
+        iota(T.Win[:, BASE[r] + V_:BASE[r] + WN], [[0, 16]], 0, 0, ["dum%d" % r], 16)
+
+    for r, src, out, ko in ((1, "rawE0", T.offE[:, 0:256], "offE0"), (2, "rawE1", T.offE[:, 256:512], "offE1"), (0, "rawL", T.Lq0[:], "L0")):
+        sl = slice(256 * r, 256 * r + 256)
+        early[0] = 2 if r else False
+        cp(T.t1[:, sl], T.raw[:, sl].indirect(lists["p1"]), [src, "lp1"], ["t1%d" % r], 256, CG)
+        turn(T.t2[:, sl], T.t1[:, sl], ["t1%d" % r], ["t2%d" % r])
+        cp(out, T.t2[:, sl].indirect(lists["pE"]), ["t2%d" % r, "lpE"], [ko], 256, CG)
+    cp(T.vq0[:], T.ki[:, 64:80], ["v0i"], ["v0"])
+
+    for c in range(8):
+        act(T.mL[:, 512 * c:512 * c + 512], T.Xs[:].indirect(T.offE[:, 32 * c:32 * c + 32]), F.Copy, ["X", "offE0"], ["mL%d" % c], 512, CG)
     for c in range(8 - BUILD_ON_S, 8):
         sl = slice(512 * c, 512 * c + 512)
-        act(T.zz[:, sl], T.Xs[:].indirect(T.offE[:, 256 + 32 * c:256 + 32 * c + 32]), F.Copy, ["X", "offE1"], ["zz%d" % c], 512, CG)
-        mm([(T.pB0[:], T.I[:], T.zz[:, sl], 512), (T.pB0[:], T.nI[:], T.tmp[:, sl], 512)], ["I", "nI", "zz%d" % c, "tmp%d" % c], ["pB0"])
-        act(T.mL[:, sl], T.pB0[:], F.Relu, ["pB0"], ["mL%d" % c], 512)
-        mm([(T.pB1[:], T.I[:], T.tmp[:, sl], 512), (T.pB1[:], T.I[:], T.mL[:, sl], 512)], ["I", "tmp%d" % c, "mL%d" % c], ["pB1"])
-        act(T.Win[:, WN + 512 * c:WN + 512 * c + 512], T.pB1[:], F.Copy, ["pB1"], ["H%d" % c], 512)
-        mm([(T.pM0[:], T.I[:], T.zz[:, sl], 512), (T.pM0[:], T.nI[:], T.mL[:, sl], 512)], ["I", "nI", "zz%d" % c, "mL%d" % c], ["pM0"])
-        act(T.Win[:, 2 * WN + 512 * c:2 * WN + 512 * c + 512], T.pM0[:], F.Copy, ["pM0"], ["Lw%d" % c], 512)
+        Bc, Rc = T.mid[:, 0:512], T.mid[:, 512:1024]
+        act(Bc, T.Xs[:].indirect(T.offE[:, 256 + 32 * c:256 + 32 * c + 32]), F.Copy, ["X", "offE1"], ["mid0"], 512, CG)
+        mm([(T.pB0[:], T.I[:], Bc, 512), (T.pB0[:], T.nI[:], T.mL[:, sl], 512)], ["I", "nI", "mid0", "mL%d" % c], ["pB0"])
+        act(Rc, T.pB0[:], F.Relu, ["pB0"], ["mid1"], 512)
+        mm([(T.pB1[:], T.I[:], T.mL[:, sl], 512), (T.pB1[:], T.I[:], Rc, 512)], ["I", "mL%d" % c, "mid1"], ["pB1"])
+        act(T.Win[:, BASE[1] + 512 * c:BASE[1] + 512 * c + 512], T.pB1[:], F.Copy, ["pB1"], ["H%d" % c], 512)
+        mm([(T.pB0[:], T.I[:], Bc, 512), (T.pB0[:], T.nI[:], Rc, 512)], ["I", "nI", "mid0", "mid1"], ["pB0"])
+        act(T.Win[:, BASE[2] + 512 * c:BASE[2] + 512 * c + 512], T.pB0[:], F.Copy, ["pB0"], ["Lw%d" % c], 512)
     for c0, c1_ in ((0, 1), (1, 2), (2, 4), (4, 6), (6, 8)):
         c1_ = min(c1_, 8 - BUILD_ON_S)
         if c1_ <= c0:
             continue
         for r, o, kk in ((1, A.max, "H"), (2, A.min, "Lw")):
-            tt(T.Win[:, r * WN + 512 * c0:r * WN + 512 * c1_], T.Xs[:].indirect(T.offE[:, 256 + 32 * c0:256 + 32 * c1_]), T.tmp[:, 512 * c0:512 * c1_], o,
-               ["X", "offE1"] + ["tmp%d" % c for c in range(c0, c1_)], ["%s%d" % (kk, c) for c in range(c0, c1_)], 512 * (c1_ - c0), CG)
+            tt(T.Win[:, BASE[r] + 512 * c0:BASE[r] + 512 * c1_], T.Xs[:].indirect(T.offE[:, 256 + 32 * c0:256 + 32 * c1_]), T.mL[:, 512 * c0:512 * c1_], o,
+               ["X", "offE1"] + ["mL%d" % c for c in range(c0, c1_)], ["%s%d" % (kk, c) for c in range(c0, c1_)], 512 * (c1_ - c0), CG)
     for c in range(8):
         gcopy(T.Win[:, 512 * c:512 * c + 512], T.Eraw[:, 512 * c:512 * c + 512], ["Eraw%d" % (c // 2)], ["E%d" % c], 512)
-    kE_, kH, kL, kS = ch("E") + ["dum0"], ch("H") + ["dum1"], ch("Lw") + ["dum2"], ["S", "dum3"]
+    kE_, kH, kL, kS = ch("E"), ch("H") + ["dum1"], ch("Lw") + ["dum2"], ["S", "dum3"]
+    kEall = kE_ + ["dum0", "VNh", "VNw"]
+    kid = ch("id", 8)
+    kdm = ["dm0", "dm"]
 
-    def edge_sums():
-        for b in range(16):
-            mm([(T.pM1[:, 0:256], wsl(T.W32, b), T.Win[:, 256 * b:256 * b + 256], 256)], ["W32", "E%d" % (b // 2)], ["pM1"], b == 0, b == 15, 4)
-        act(T.S0[:], T.pM1[:, 0:256], F.Copy, ["pM1"], ["S0"], 256)
-        dma("Y", [(T.Win[0::16, 3 * WN:3 * WN + V_], T.S0[:])], ["S0"], ["S"], 2.5)
-    if SUMS_AT == 0:
-        edge_sums()
+    for b in range(16):
+        mm([(T.pM1[:, 0:256], wsl(T.W32, b), T.Win[:, 256 * b:256 * b + 256], 256)], ["W32", "E%d" % (b // 2)], ["pM1"], b == 0, b == 15, 4)
+    act(T.S0[:], T.pM1[:, 0:256], F.Copy, ["pM1"], ["S0"], 256)
+    dma("Y", [(T.Win[0::16, BASE[3]:BASE[3] + V_], T.S0[:])], ["S0"], ["S"], 0.2)
 
     def sm(i):
         return T.sm[:, 16 * i:16 * i + 16]
@@ -311,84 +320,113 @@ def build_ops(g, T, topo, core, nxt):
     def si(i):
         return T.si[:, 16 * i:16 * i + 16]
 
+    def ki(i):
+        return T.ki[:, 16 * i:16 * i + 16]
+
     def s16(i, n=1):
         return T.s16[:, 16 * i:16 * (i + n)]
 
-    def n2l(out, w, kw_, src, ksrc, bank, const, kconst, contiguous=False, a0=0):
-        items = [(out, T.ones[:, 0:128], const[:, 0:16], 16)] if const is not None else []
-        for b in range(16):
-            items.append((out, wsl(w, b), src[:, a0 + 16 * b:a0 + 16 * b + 16] if contiguous else src[:, a0 + b:a0 + 256:16], 16))
-        mm(items, [kw_, ksrc, "onesa"] + ([kconst] if kconst else []), [bank])
+    def n2l(out, w, kw_, src, ksrc, bank, const=None, kconst=(), first=True, last=True, a0=0):
+        items = [(out, const, T.ones[:, 0:16], 16)] if const is not None else []
+        items += [(out, wsl(w, b), src[:, a0 + b:a0 + 256:16], 16) for b in range(16)]
+        mm(items, [kw_, ksrc, "onesa"] + list(kconst), [bank], first, last)
 
+    flip = [0]
+    mid2k = (T.cmid[:], ["cmid"])
     for t in range(NV):
         z, L16, v16 = T["zq%d" % t], T["Lq%d" % t], T["vq%d" % t]
         zw, Lin, ain, ma, mb = T["zin%d" % t], T["Lin%d" % t], T["ain%d" % t], T["a%d" % t], T["b%d" % t]
+        lb, lbin, hs, hin = T["lb%d" % t], T["lbin%d" % t], T["h%d" % t], T["hin%d" % t]
         zin0, zin1, zin2 = zw[:, 256:512], zw[:, 512:1024], zw[:, 256:1024]
-        kz_, kzi, kLi, kai, kbi = "z%d" % t, "zin%d" % t, "Lin%d" % t, "ain%d" % t, "bin%d" % t
+        kz_, kv, kzi, kLi, kai, kbi, khi = "z%d" % t, "v%d" % t, "zin%d" % t, "Lin%d" % t, "ain%d" % t, "bin%d" % t, "hin%d" % t
+        ctau, ktau = T.ctau[:, 128 * t:128 * t + 128], ["ctau%d" % t]
         last = t == NV - 1
-        send([(zin0, z[:])], "mz_%d" % t, [kz_], [kzi], 65536)
-        send([(Lin[:], L16[:])], "m1_%d" % t, ["L%d" % t], [kLi], 65536)
+        send([(zin0, z[:])], "mz_%d" % t, [kz_], [kzi], 0.065)
+        send([(Lin[:], L16[:])], "m1_%d" % t, ["L%d" % t], [kLi], 0.065)
+        if last:
+            send([(T.zfin[:, 0:256], z[:])], "mzo", [kz_], ["zfin0"], 0.03, own)
 
-        if t == 0:
-            ts(T.cf[:], T.Eraw[:].indirect(v16[:]), -2048.0, None, A.add, None, ch("Eraw", 4) + ["v0"], ["cf"], 256, CG)
-        else:
-            act(T.cf[:], win(0).indirect(v16[:]), F.Identity, kE_ + ["v%d" % t, kmid], ["cf"], 256, CG, 1.0, cmid)
-        ts(T.c16[:], T.cf[:].indirect(lists["sig"]), 2048.0, None, A.add, None, ["cf", "lsig"], ["c16"], 256, CG)
-        act(T.zs[:], z[:].indirect(lists["sig"]), F.Copy, [kz_, "lsig"], ["zs"], 256, CG)
         for h in range(2):
-            mm([(T.pA1[:, 128 * h:128 * h + 128], T.zs[:, 128 * h:128 * h + 128], T.I[:], 128)], ["zs", "I"], ["pA1"])
+            mm([(T.pA1[:, 128 * h:128 * h + 128], z[:, 128 * h:128 * h + 128], T.I[:], 128)], [kz_, "I"], ["pA1"])
         act(T.nzW[:], T.pA1[:, 0:256], F.Copy, ["pA1"], ["nzW"], 256, 1.0, -1.0)
-        mm([(T.pK[:, 0:256], T.I[:], T.jc[:], 256), (T.pK[:, 0:256], T.I[:], T.pb[:], 256)], ["I", "jc", "pb"], ["pK"], True, False)
-        order = [c for c in range(8)]
-        for c in order:
+        if t == 0:
+            cp(T.c16[:], T.Eraw[:].indirect(v16[:]), ch("Eraw", 4) + [kv], ["c16"], 256, CG)
+        gcopy(T.cfr[:], T.c16[:], ["c16"], ["cfr"], 256)
+        act(T.cf[:], T.cfr[:], F.Identity, ["cfr", kmid], ["cf"], 256, 1.0, 1.0, cmid)
+        if t > 0:
+            tt(T.neq[:], win(0, V_).indirect(v16[:]), T.cfr[:], A.not_equal, kE_ + [kv, "cfr"], ["neq"], 256, CG)
+        mm([(T.pK[:, 0:256], T.I[:], T.kcb[:], 256)], ["I", "kcb"], ["pK"], True, False)
+        for c in range(8):
             sl = slice(512 * c, 512 * c + 512)
             bank = "pA%d" % (c % 2)
             src = T.Xs[:].indirect(T.c16[:, 32 * c:32 * c + 32])
-            if (c * WALK_ON_V[t]) % 8 < WALK_ON_V[t]:
+            if c in WALK_ON_V[t]:
                 cp(T.xg[:, sl], src, ["X", "c16"], ["xg%d" % c], 512, CG)
             else:
                 act(T.xg[:, sl], src, F.Copy, ["X", "c16"], ["xg%d" % c], 512, CG)
             h, cc = c // 4, c % 4
-            mm([(T[bank][:], T.nzW[:, 128 * h:128 * h + 128], T.R1[:, 512 * cc:512 * cc + 512], 512), (T[bank][:], T.I[:], T.xg[:, sl], 512)],
-               ["nzW", "R1%d" % cc, "I", "xg%d" % c], [bank])
-            act(T.absd[:, sl], T[bank][:], F.Abs, [bank], ["ab%d" % c], 512)
-            mm([(T.pK[:, 0:256], wsl(T.WK, b), T.absd[:, 256 * b:256 * b + 256], 256) for b in (2 * c, 2 * c + 1)], ["WK", "ab%d" % c], ["pK"], False, c == order[-1])
+            mm([(T[bank][:], T.nzW[32 * cc:32 * cc + 32, 128 * h:128 * h + 128], T.R1[32 * cc:32 * cc + 32, :], 512), (T[bank][:], T.I[:], T.xg[:, sl], 512)],
+               ["nzW", "R1", "I", "xg%d" % c], [bank])
+            act(T.absd[:, 2 * c:2 * c + 2, :], T[bank][:], F.Abs, [bank], ["ab%d" % c], 512)
+            if (c + 1) % SUMQ == 0:
+                m0, m1 = 2 * (c + 1 - SUMQ), 2 * (c + 1)
+                if c == 7 and t > 0:
+                    n2l(T.pK[:, 0:256:16], T.Wf, "Wf", T.neq, "neq", "pK", None, (), False, False)
+                mm([(T.pK[:, 16 * m0:16 * m1], wsl(T.WK, b), T.absd[:, m0:m1, 16 * b:16 * b + 16], 32 * SUMQ) for b in range(16)],
+                   ["WK"] + ["ab%d" % j for j in range(c + 1 - SUMQ, c + 1)], ["pK"], False, c == 7)
         scan(T.scK[:], T.rK[:], T.pK[:, 0:256], A.add, A.min, ["rK", "pK"], ["scK"])
-        cp(T.ki[:, 32:48], T.scK[:, 15::16], ["scK"], ["ki"])
-        ts(T.ki[:, 16:32], T.ki[:, 32:48], 15, None, A.bitwise_and, None, ["ki"], ["kik"])
-        ts(T.ki[:, 0:16], T.ki[:, 32:48], 4095, None, A.bitwise_and, None, ["ki"], ["kio"])
-        cp(T.k16[:, 0:32], T.ki[:, 0:32], ["kik", "kio"], ["k16k", "k16o"], 32)
-        tt(T.selc[:], T.d16[:].indirect(T.k16[:, 16:32]), T.cf[:], A.mult, ["d16", "k16k", "cf"], ["selc"], 256, CG)
-        n2l(T.pK[:, 256:272], T.W1, "W1", T.selc, "selc", "pK", T.c16b, "c16b")
-        ts(ma[:, 16:32], T.scK[:, 15::16], float(TH * 4096 + 4095), None, A.is_le, None, ["scK"], ["mab%d" % t])
-        cp(ma[:, 0:16], T.pK[:, 256:272], ["pK"], ["maa%d" % t])
-        send([(ain[:], ma[:])], "m2a_%d" % t, ["maa%d" % t, "mab%d" % t], [kai], 8192)
-        act(mb[:, 0:256], T.absd[:].indirect(T.k16[:, 0:16]), F.Copy, ch("ab") + ["k16o"], ["mba%d" % t], 256, CG)
-        tt(T.sum[:], T.xg[:].indirect(T.k16[:, 0:16]), z[:], A.add, ch("xg") + ["k16o", kz_], ["sum"], 256, CG)
-        ts(T.hi[:], T.sum[:], -0.5, 1.5 * 2.0 ** 24, A.add, A.add, ["sum"], ["hi"], 256)
-        act(mb[:, 256:512], T.hi[:], F.Identity, ["hi", kbig], ["mbb%d" % t], 256, 1.0, 0.5, cbig)
-        send([(zin1, mb[:])], "m2b_%d" % t, ["mba%d" % t, "mbb%d" % t], [kbi], 131072)
+        cp(ki(0), T.scK[:, 15::16], ["scK"], ["ki0"])
+        ts(ki(1), ki(0), 1023, None, A.bitwise_and, None, ["ki0"], ["ki1"])
+        cp(T.k16[:], ki(1), ["ki1"], ["k16"])
+        tt(T.selc[:], T.dm[:, 0:528 if t else 32].indirect(T.k16[:]), T.cf[:], A.mult, kdm[0:2 if t else 1] + ["k16", "cf"], ["selc"], 256, CG)
+        n2l(T.pK[:, 256:272], T.W1, "W1", T.selc, "selc", "pK", *mid2k)
+        act(lb[:], T.scK[:, 15::16], F.Identity, ["scK"], ["lb%d" % t], 16, 1.0, -2.0 ** 19, (TH * 1024 + 1023.5) * 2.0 ** 19)
+        cp(ma[:], T.pK[:, 256:272], ["pK"], ["ma%d" % t])
+        send([(ain[:], ma[:]), (lbin[:], lb[:])], "m2a_%d" % t, ["ma%d" % t, "lb%d" % t], [kai], 0.02)
+        act(T.xv[:], T.Xs[:].indirect(ma[:]), F.Copy, ["X", "ma%d" % t], ["xv"], 256, CG)
+        mm([(T.pA1[:, 0:256], T.hI[:], z[:], 256), (T.pA1[:, 0:256], T.hI[:], T.xv[:], 256)], ["hI", kz_, "xv"], ["pA1"])
+        mm([(T.pA0[:, 0:256], T.I[:], z[:], 256), (T.pA0[:, 0:256], T.nI[:], T.xv[:], 256)], ["I", "nI", kz_, "xv"], ["pA0"])
+        ts(mb[:, 0:256], T.pA1[:, 0:256], 1.5 * 2.0 ** 23, -1.5 * 2.0 ** 23, A.add, A.add, ["pA1"], ["mba%d" % t], 256)
+        act(mb[:, 256:512], T.pA0[:, 0:256], F.Abs, ["pA0"], ["mbb%d" % t], 256)
+        n2l(T.pA1[:, 256:272], T.Wh, "Wh", mb, "mba%d" % t, "pA1")
+        cp(ki(2), T.pA1[:, 256:272], ["pA1"], ["ki2"])
+        ts(ki(3), ki(2), 4095, None, A.bitwise_and, None, ["ki2"], ["ki3"])
+        gcopy(hs[:], ki(3), ["ki3"], ["h%d" % t], 16)
+        send([(hin[:], hs[:])], "mh_%d" % t, ["h%d" % t], [khi], 0.01)
+        if not last:
+            send([(zin1, mb[:])], "m2b_%d" % t, ["mba%d" % t, "mbb%d" % t, "h%d" % t], [kbi], 0.13)
+        else:
+            send([(T.zfin[:, 256:768], mb[:])], "m2b_%d" % t, ["mba%d" % t, "mbb%d" % t, "h%d" % t], ["zfin1"], 0.06, own)
+            if not LOG_BY_S:
+                gcopy(fin("Lg"), L16[:], ["L%d" % t], ["Lg"], 256)
+            gcopy(fin("Lg", 16 * t, 16 * t + 16), ma[:], ["ma%d" % t], ["Lg"], 16)
+            act(fin("Ln"), fin("Lg").indirect(lists["iL"]), F.Copy, ["Lg", "liL"], ["Ln"], 256, CG)
+            turn(fin("Lp"), fin("Ln"), ["Ln"], ["Lp"])
+            act(fin("Lr"), fin("Lp").indirect(lists["p2"]), F.Copy, ["Lp", "lp2"], ["Lr"], 256, CG)
+            for sg, w in enumerate((T.Wp0, T.Wp1)):
+                mm([(T.pA0[:, 256 + 128 * sg:384 + 128 * sg], w[:, 16 - 16 * u:144 - 16 * u], fin("Lr", 128 * u, 128 * u + 128), 128) for u in range(2)],
+                   ["Wp0", "Wp1", "Lr"], ["pA0"], True, True, 4)
+            act(fin("Lrow"), T.pA0[:, 256:512], F.Copy, ["pA0"], ["Lrow"], 256)
+            send([(T.Lfin[:], fin("Lrow"))], "mLo", ["Lrow"], ["Lfin"], 0.06, own)
 
         gcopy(zw[:, 0:256], zin0, [kzi], ["zd%d" % t], 256)
         gcopy(T.Lf[:], Lin[:], [kLi], ["Lf"], 256)
-        mm([(T.pG[:, 0:256], T.ones[:, 0:128], T.ctau[:, 256 * t:256 * t + 256], 256)], ["onesa", "ctau%d" % t, "ctaub%d" % t], ["pG"], True, False)
-        flip = [0]
-
-        def nb():
-            flip[0] ^= 1
-            return "pB%d" % (1 - flip[0])
-        on_s = [c for c in range(8) if c >= 8 - CUT_ON_S[t]]
+        slot = T.Lf[:, 16 * t:16 * t + 16]
+        gcopy(slot, T.nc[:, 16 * (2 + t):16 * (3 + t)], ["nc"], ["Lf"], 16)
+        mm([(T.pG[:, 0:256], ctau, T.ones[:], 256), (T.pG[:, 16 * t:16 * t + 16], T.cmid[:], T.cneg[:], 16)], ["onesa", "cmid", "cneg"] + ktau, ["pG"], True, False)
         for c in range(8):
             k0, k1_ = 2 * c + (2 * c == t), 2 * c + 2 - (2 * c + 1 == t)
             w_ = 256 * (k1_ - k0)
             sl = slice(256 * k0, 256 * k1_)
             offs = Lin[:, 16 * k0:16 * k1_]
             zt, zrd = zw[:, 512 - w_:512], [kzi] + (["zd%d" % t] if w_ > 256 else [])
-            if c in on_s:
-                for r, kr, mid, km, out, ko in ((1, kH, T.zz, "zz", T.mH, "mH"), (2, kL, T.tmp, "tmp", T.mL, "mL")):
-                    bank = nb()
-                    act(mid[:, sl], win(r).indirect(offs), F.Copy, kr + [kLi], ["%s%d" % (km, c)], w_, CG)
-                    mm([(T[bank][:, 0:w_], T.nI[:], zt, w_), (T[bank][:, 0:w_], T.I[:], mid[:, sl], w_)], zrd + ["I", "nI", "%s%d" % (km, c)], [bank])
+            if c >= 8 - CUT_ON_S[t]:
+                for r, kr, out, ko in ((1, kH, T.mH, "mH"), (2, kL, T.mL, "mL")):
+                    j = flip[0] % 4
+                    flip[0] += 1
+                    bank, mid = "pB%d" % (j % 2), T.mid[:, 512 * j:512 * j + w_]
+                    act(mid, win(r).indirect(offs), F.Copy, kr + [kLi], ["mid%d" % j], w_, CG)
+                    mm([(T[bank][:, 0:w_], T.nI[:], zt, w_), (T[bank][:, 0:w_], T.I[:], mid, w_)], zrd + ["I", "nI", "mid%d" % j], [bank])
                     act(out[:, sl], T[bank][:, 0:w_], F.Relu, [bank], ["%s%d" % (ko, c)], w_)
             else:
                 tt(T.mH[:, sl], win(1).indirect(offs), zt, A.max, kH + [kLi] + zrd, ["mH%d" % c], w_, CG)
@@ -402,136 +440,131 @@ def build_ops(g, T, topo, core, nxt):
         act(T.keyT[:], T.key[:].indirect(lists["sig"]), F.Copy, ["key", "lsig"], ["keyT"], 256, CG)
         scan(T.scG[:], T.rG[:], T.keyT[:], A.add, A.min, ["rG", "keyT"], ["scG"])
 
-
-        vw = ain[:, 0:16]
-        tt(T.Ht[:, 0:256], win(1).indirect(vw), zin0, A.max, kH + [kai, kzi], ["Hta"], 256, CG)
-        tt(T.Ht[:, 256:512], win(2).indirect(vw), zin0, A.max, kL + [kai, kzi], ["Htb"], 256, CG)
-        o = (t + 1) % 16
-        items = [(T.pM0[:, 0:16], T.ones[:, 0:128], T.ctau[:, 256 * t + 16 * o:256 * t + 16 * o + 16], 16)]
-        items += [(T.pM0[:, 0:16], wsl(T.WM, b), T.Ht[:, b:256:16], 16) for b in range(16)]
-        mm(items, ["onesa", "ctau%d" % t, "ctaub%d" % t, "WM", "Hta"], ["pM0"], True, False)
-        mm([(T.pM0[:, 0:16], wsl(T.WP, b), T.Ht[:, 256 + b:512:16], 16) for b in range(16)], ["WP", "Htb"], ["pM0"], False, True)
-        ts(sm(1), ain[:, 16:32], 2.0 ** 22, -2.0 ** 21, A.mult, A.add, [kai], ["sm1"])
-        vwf = T.Lf[:, 16 * t:16 * t + 16]
-        (gcopy if OFF[2] else cp)(vwf, vw, [kai], ["Lf"], 16)
-        ts(sm(2), vw, -8192.0 * (15 - t), None, A.add, None, [kai], ["sm2"])
-        tt(sm(3), sm(2), sm(1), A.max, ["sm1", "sm2"], ["sm3"])
-        tt(sm(4), T.scG[:, 15::16], sm(1), A.max, ["scG", "sm1"], ["sm4"])
-        tt(sm(5), T.pM0[:, 0:16], sm(3), A.max, ["pM0", "sm3"], ["sm5"])
-        tt(sm(6), sm(5), sm(4), A.min, ["sm4", "sm5"], ["sm6"])
-        ts(si(0), sm(6), 8192.0 * 15, cclamp, A.add, A.min, ["sm6", kclamp], ["si0"])
+        tt(T.Ht[:, 0:256], win(1).indirect(ain[:]), zin0, A.max, kH + [kai, kzi], ["Hta"], 256, CG)
+        tt(T.Ht[:, 256:512], win(2).indirect(ain[:]), zin0, A.max, kL + [kai, kzi], ["Htb"], 256, CG)
+        n2l(T.pM0[:, 0:16], T.WM, "WM", T.Ht, "Hta", "pM0", ctau, ktau, True, False)
+        n2l(T.pM0[:, 0:16], T.WP, "WP", T.Ht, "Htb", "pM0", None, (), False, True, 256)
+        act(T.Win[:, WN + 256:WN + 512], T.ident[:].indirect(ain[:]), F.Copy, kid + [kai] , ["VNw"], 256, CG)
+        act(T.Win[:, WN:WN + 256], T.ident[:].indirect(hin[:]), F.Copy, kid + [khi], ["VNh"], 256, CG)
+        gcopy(sm(0), ain[:], [kai], ["sm0"], 16)
+        act(sm(1), sm(0), F.Identity, ["sm0"], ["sm1"], 16, 1.0, 1.0, -8192.0 * (15 - t))
+        tt(sm(2), sm(1), lbin[:], A.max, ["sm1", kai], ["sm2"])
+        tt(sm(3), lbin[:], T.nc[:, 0:16], A.min, [kai, "nc"], ["sm3"])
+        tt(sm(4), T.scG[:, 15::16], sm(3), A.max, ["scG", "sm3"], ["sm4"])
+        tt(sm(5), T.pM0[:, 0:16], sm(2), A.max, ["pM0", "sm2"], ["sm5"])
+        tt(si(0), sm(5), sm(4), A.min, ["sm4", "sm5"], ["si0"])
         ts(si(1), si(0), 8191, None, A.bitwise_and, None, ["si0"], ["u"])
         cp(s16(0), si(1), ["u"], ["u16"])
-        if OFF[1] and not last:
-            act(T.ec[:], win(0).indirect(s16(0)), F.Identity, kE_ + ["u16", kmid], ["ec"], 256, CG, 1.0, cmid)
-            gcopy(T.ech[:], T.ec[:], ["ec"], ["ech"], 256)
-        else:
-            ts(T.ech[:], win(0).indirect(s16(0)), -2048.0, None, A.add, None, kE_ + ["u16"], ["ech"], 256, CG)
-        n2l(T.pM0[:, 16:32], T.Wr0, "Wr0", T.ech, "ech", "pM0", T.c16b, "c16b")
+        ts(T.ech[:], win(0, WE).indirect(s16(0)), -2048.0, None, A.add, None, kEall + ["u16"], ["ech"], 256, CG)
+        n2l(T.pM0[:, 16:32], T.Wr0, "Wr0", T.ech, "ech", "pM0", *mid2k)
+        vn, kvn = T["vq%d" % (t + 1)], "v%d" % (t + 1)
+        cp(vn[:], T.pM0[:, 16:32], ["pM0"], [kvn])
         ts(si(2), si(0), 13, None, A.arith_shift_right, None, ["si0"], ["f"])
-        ts(sm(7), si(0), 16.0 * 8192, None, A.is_ge, None, ["si0"], ["ncut"])
-        ts(sm(8), si(0), 16.0 * 8192, None, A.is_lt, None, ["si0"], ["cut"])
-        n2l(T.pA0[:, 0:16], T.Wh, "Wh", zw, kbi, "pA0", None, None, False, 768)
-        cp(si(3), T.pA0[:, 0:16], ["pA0"], ["si3"])
-        ts(si(4), si(3), 4095, None, A.bitwise_and, None, ["si3"], ["hash"])
-        tt(sm(9), si(4), sm(1), A.max, ["hash", "sm1"], ["sm9"])
-        act(sm(10), sm(1), F.Identity, ["sm1"], ["sm10"], 16, 1.0, -1.0)
-        tt(sm(11), sm(10), vwf, A.max, ["sm10", "Lf"], ["sm11"])
-        tt(sm(12), sm(9), sm(11), A.min, ["sm9", "sm11"], ["sm12"])
-        tt(sm(13), sm(12), sm(7), A.mult, ["sm12", "ncut"], ["sm13"])
-        tt(sm(14), T.pM0[:, 16:32], sm(8), A.mult, ["pM0", "cut"], ["sm14"])
-        tt(sm(15), sm(14), sm(13), A.add, ["sm13", "sm14"], ["sm15"])
-        vn, zn, Ln16 = T["vq%d" % (t + 1)], T["zq%d" % (t + 1)], T["Lq%d" % (t + 1)]
-        (gcopy if OFF[3] else cp)(vn[:], sm(15), ["sm15"], ["v%d" % (t + 1)], 16)
+        tt(sm(6), si(0), T.nc[:, 16:32], A.max, ["si0", "nc"], ["sm6"])
         if last:
-            send([(T.vin[:], vn[:])], "mv", ["v3"], ["vin"], 4096)
-
-        act(sm(16), sm(1), F.Identity, ["sm1"], ["sm16"], 16, 1.0, -2.0 ** -14, 384.0)
-        tt(sm(17), sm(16), sm(7), A.mult, ["sm16", "ncut"], ["sm17"])
-        tt(sm(18), sm(17), T.qc[:], A.add, ["sm17", "qc"], ["sm18"])
-        (gcopy if OFF[2] else cp)(s16(1), sm(18), ["sm18"], ["zo16"], 16)
-        act(zn[:], zin2.indirect(s16(1)), F.Copy, [kzi, kbi, "zo16"], ["z%d" % (t + 1)], 256, CG)
-
-        xl, kx, kc, kkc = ("xP", "lxP", T.kcP, "kcP") if last else ("xm", "lxm", T.kcM, "kcM")
-        tt(T.eq[:], si(2).indirect(lists[xl]), kc[:], A.is_equal, ["f", kx, kkc], ["eq"], 256, CG)
-        tt(sm(19), T.pM0[:, 16:32], si(1), A.subtract, ["pM0", "u"], ["sm19"])
-        tt(T.dl[:], sm(19).indirect(lists[xl]), T.eq[:], A.mult, ["sm19", kx, "eq"], ["dl"], 256, CG)
-        if not last:
+            ts(T.fz[:, 0:16], si(2), 15.0, None, A.add, None, ["f"], ["fza"])
+            ts(T.fz[:, 16:32], sm(6), -float(NC), None, A.add, None, ["sm6"], ["fzb"])
+            send([(T.fzin[:], T.fz[:])], "mf", ["fza", "fzb"], ["fzin"], 0.01)
+            send([(T.vin[:], vn[:])], "mv", [kvn], ["vin"], 0.01)
+        else:
+            cp(T.c16[:], win(0, V_).indirect(vn[:]), kE_ + [kvn], ["c16"], 256, CG)
+            ts(s16(1), sm(6), -float(NC), None, A.add, None, ["sm6"], ["zo16"])
+            act(T["zq%d" % (t + 1)][:], zin2.indirect(s16(1)), F.Copy, [kzi, kbi, "zo16"], ["z%d" % (t + 1)], 256, CG)
+            gcopy(slot, ain[:], [kai], ["Lf"], 16)
+            tt(T.eq[:], si(2).indirect(lists["xm"]), T.kcM[:], A.is_equal, ["f", "lxm", "kcM"], ["eq"], 256, CG)
+            tt(sm(7), T.pM0[:, 16:32], si(1), A.subtract, ["pM0", "u"], ["sm7"])
+            tt(T.dl[:], sm(7).indirect(lists["xm"]), T.eq[:], A.mult, ["sm7", "lxm", "eq"], ["dl"], 256, CG)
             mm([(T.pB0[:, 0:256], T.I32[:], T.Lf[:], 256)], ["I32", "Lf"], ["pB0"], True, False, 4)
             mm([(T.pB0[:, 0:256], T.I32[:], T.dl[:], 256)], ["I32", "dl"], ["pB0"], False, True, 4)
-            if OFF[0]:
-                act(T.Ln[:], T.pB0[:, 0:256], F.Copy, ["pB0"], ["Ln"], 256)
-                gcopy(Ln16[:], T.Ln[:], ["Ln"], ["L%d" % (t + 1)], 256)
+            if LOG_BY_S:
+                act(fin("Lg"), T.pB0[:, 0:256], F.Copy, ["pB0"], ["Lg"], 256)
+                gcopy(T["Lq%d" % (t + 1)][:], fin("Lg"), ["Lg"], ["L%d" % (t + 1)], 256)
             else:
-                cp(Ln16[:], T.pB0[:, 0:256], ["pB0"], ["L%d" % (t + 1)], 256)
-        else:
-            tt(T.Ln[:], T.Lf[:].indirect(lists["iL"]), T.dl[:], A.add, ["Lf", "liL", "dl"], ["Ln"], 256, CG)
-            op("V", lambda: v.transpose(T.Lp[:], T.Ln[:]), ["Ln"], ["Lp"], vd(256))
-            cp(Ln16[:], T.Lp[:].indirect(lists["p2"]), ["Lp", "lp2"], ["L3"], 256, CG)
+                cp(T["Lq%d" % (t + 1)][:], T.pB0[:, 0:256], ["pB0"], ["L%d" % (t + 1)], 256)
 
-        act(T.ur[:], T.ident[:].indirect(s16(0)), F.Copy, ch("id", 4) + ["u16"], ["ur"], 256, CG)
+        act(T.ur[:], T.ident[:].indirect(s16(0)), F.Copy, kid + ["u16"], ["ur"], 256, CG)
         tt(T.eq2[:], si(1).indirect(lists["x16"]), T.ur[:], A.is_equal, ["u", "lx16", "ur"], ["eq2"], 256, CG)
-        scan(T.scD[:], T.rD[:], T.eq2[:], A.mult, A.add, ["rD", "eq2"], ["scD"])
-        ts(sm(0), T.scD[:, 15::16], col[:, 31:32], cdum, A.is_ge, A.mult, ["scD", kdum, "pow"], ["sm0"])
-        tt(sm(3), sm(0), si(1), A.max, ["sm0", "u"], ["sm3"])
-        cp(T.o16[:, 0:64:4], sm(3), ["sm3"], ["oE"])
+        gcopy(sm(8), s16(0), ["u16"], ["sm8"], 16)
+        y = T.pG[:, 288:304]
+        mm([(y, T.I32[:], sm(8), 16)], ["I32", "sm8"], ["pG"], True, False, 4)
+        mm([(y, T.Wt[:, 128 * b:128 * b + 128], T.eq2[:, b::16], 16) for b in range(1, 16)], ch("Wt", 16) + ["eq2"], ["pG"], False, True)
+        mm([(T.pM1[:, 256:512], T.csum[:], T.ones[:], 256), (T.pM1[:, 256:512], wsl(T.Ws, 0), T.ech[:], 256)], ["onesa", "csum", "Ws", "ech"], ["pM1"])
         if not last:
-            mm([(T.pA1[:, 256:512], T.ones[:, 0:128], T.c16b[:], 256), (T.pA1[:, 256:512], T.Rot[:], T.ech[:], 256)], ["onesa", "c16b", "Rot", "ech"], ["pA1"])
-            act(T.vals[:, 0:256], T.pA1[:, 256:512], F.Copy, ["pA1"], ["val0"], 256)
-            for m in range(16):
-                cp(win(0).indirect(T.o16[:, 4 * m:4 * m + 1]), T.vals[:, 16 * m:16 * m + 16], ["val0", "oE"], kE_, 16, CS)
-            n2l(T.pG[:, 256:272], T.Wr1, "Wr1", T.ech, "ech", "pG", T.c16b, "c16b", True)
-            n2l(T.pG[:, 272:288], T.Wr2, "Wr2", T.ech, "ech", "pG", T.c16b, "c16b", True)
-            cp(s16(2, 2), T.pG[:, 256:288], ["pG"], ["ab16"])
+            for r in range(4):
+                ts(T.o16[:, AT[r]:64:4], y, cdum, float(BASE[r] - (BASE[1] if SPLIT and AT[r] > 1 else 0)), A.min, A.add, ["pG", kdum], ["o%d" % r])
+            mm([(T.pM1[:, 0:256], T.cmid[:], T.ones[:], 256), (T.pM1[:, 0:256], T.Rot[:], T.ech[:], 256)], ["onesa", "cmid", "Rot", "ech"], ["pM1"])
+            act(T.vals[:, :, 0:16], T.pM1[:, 0:256], F.Copy, ["pM1"], ["val0"], 256)
+            act(T.vals[:, :, 16:32], T.pM1[:, 256:512], F.Copy, ["pM1"], ["val3"], 256)
+            n2l(T.pB1[:, 0:16], T.Wr1, "Wr1", T.ech, "ech", "pB1", *mid2k)
+            n2l(T.pB1[:, 16:32], T.Wr2, "Wr2", T.ech, "ech", "pB1", *mid2k)
+            cp(s16(2, 2), T.pB1[:, 0:32], ["pB1"], ["ab16"])
             act(T.An[:, 0:512], T.Xs[:].indirect(s16(2, 2)), F.Copy, ["X", "ab16"], ["An"], 512, CG)
             An, Bn, Rn = T.An[:, 0:256], T.An[:, 256:512], T.An[:, 512:768]
             mm([(T.pB1[:, 0:256], T.I[:], Bn, 256), (T.pB1[:, 0:256], T.nI[:], An, 256)], ["I", "nI", "An"], ["pB1"])
             act(Rn, T.pB1[:, 0:256], F.Relu, ["pB1"], ["Rn"], 256)
             mm([(T.pB1[:, 0:256], T.I[:], An, 256), (T.pB1[:, 0:256], T.I[:], Rn, 256)], ["I", "An", "Rn"], ["pB1"])
             mm([(T.pB1[:, 256:512], T.I[:], Bn, 256), (T.pB1[:, 256:512], T.nI[:], Rn, 256)], ["I", "nI", "An", "Rn"], ["pB1"])
-            act(T.vals[:, 256:768], T.pB1[:], F.Copy, ["pB1"], ["val1"], 512)
-            ts(T.o16[:, 1:64:4], sm(3), float(WN), None, A.add, None, ["sm3"], ["o16b"])
-            if t >= SUMS_AT:
-                items = [(T.pK[:, 256:512], T.ones[:, 0:128], T.cSb[:], 256)]
-                items += [(T.pK[:, 256 + m:512:16], wsl(T.Ws, 0), T.ech[:, 16 * m:16 * m + 16], 16) for m in range(16)]
-                mm(items, ["onesa", "cSb", "Ws", "ech"], ["pK"])
-                act(T.vals[:, 768:1024], T.pK[:, 256:512], F.Copy, ["pK"], ["val3"], 256)
-                ts(T.o16[:, 2:64:4], sm(3), float(2 * WN), None, A.add, None, ["sm3"], ["o16c"])
-                for m in range(16):
-                    cp(T.Win[:, WN:4 * WN].indirect(T.o16[:, 4 * m:4 * m + 3]), T.vals[:, 256 + m:1024:16], ["val1", "val3", "oE", "o16b", "o16c"], kH + kL + kS, 48, CS)
-            else:
-                for m in range(16):
-                    cp(T.Win[:, WN:3 * WN].indirect(T.o16[:, 4 * m:4 * m + 2]), T.vals[:, 256 + m:768:16], ["val1", "oE", "o16b"], kH + kL, 32, CS)
-            if t + 1 == SUMS_AT:
-                edge_sums()
-        else:
-            mm([(T.pK[:, 256:512], T.ones[:, 0:128], T.cSb[:], 256), (T.pK[:, 256:512], wsl(T.Ws, 0), T.ech[:], 256)], ["onesa", "cSb", "Ws", "ech"], ["pK"])
-            act(T.vals[:, 768:1024], T.pK[:, 256:512], F.Copy, ["pK"], ["val3"], 256)
+            act(T.vals[:, :, 32:48], T.pB1[:, 0:256], F.Copy, ["pB1"], ["val1"], 256)
+            act(T.vals[:, :, 48:64], T.pB1[:, 256:512], F.Copy, ["pB1"], ["val2"], 256)
             for m in range(16):
-                cp(win(3).indirect(T.o16[:, 4 * m:4 * m + 1]), T.vals[:, 768 + 16 * m:784 + 16 * m], ["val3", "oE"], kS, 16, CS)
-            dma("Y", [(T.ya[:, :], T.Win[0::16, 3 * WN:3 * WN + V_])], kS, ["ya"], 2.5)
+                if SPLIT:
+                    cp(T.Win[:, BASE[1]:].indirect(T.o16[:, 4 * m + 2:4 * m + 4]), T.vals[:, m, 32:64], ["val1", "val2", "o1", "o2"], kH + kL, 32, CS)
+                    cp(T.Win[:, 0:BASE[1]].indirect(T.o16[:, 4 * m:4 * m + 2]), T.vals[:, m, 0:32], ["val0", "val3", "o0", "o3"], kEall + kS, 32, CS)
+                else:
+                    cp(T.Win[:].indirect(T.o16[:, 4 * m:4 * m + 4]), T.vals[:, m, :], ch("val", 4) + ch("o", 4), kEall + kH + kL + kS, 64, CS)
+        else:
+            ts(T.o16[:, 0:64:4], y, cdum, None, A.min, None, ["pG", kdum], ["o0"])
+            act(T.vals[:, :, 48:64], T.pM1[:, 256:512], F.Copy, ["pM1"], ["val3"], 256)
+            for m in range(16):
+                cp(win(3).indirect(T.o16[:, 4 * m:4 * m + 1]), T.vals[:, m, 48:64], ["val3", "o0"], kS, 16, CS)
+            dma("Y", [(T.ya[:, :], T.Win[0::16, BASE[3]:BASE[3] + V_])], kS, ["ya"], 0.2)
 
-    send([(T.zin3[:, 0:256], T.zq3[:])], "mz_3", ["z3"], ["zin3"], 65536)
-    send([(T.Lin3[:], T.Lq3[:])], "m1_3", ["L3"], ["Lin3"], 65536)
-    act(T.vo[:], T.ident[:].indirect(T.vin[:]), F.Copy, ch("id", 4) + ["vin"], ["vo"], 256, CG)
-    dma("S", [(T.yv[:, :], T.vo[0::16, :])], ["vo"], ["yv"], 2.0)
-    act(T.zo[:], T.zin3[:, 0:256], F.Copy, ["zin3"], ["zo"], 256)
-    dma("S", [(T.yz[:, :], T.zo[:])], ["zo"], ["yz"], 2.0)
-    cp(T.Lo[:], T.Lin3[:], ["Lin3"], ["Lo"], 256)
-    for u, q in ((0, "Y"), (1, "S")):
-        dma(q, [(T.yl[32 * a + 16 * u:32 * a + 16 * u + 16, :], T.Lo[32 * a:32 * a + 32, 128 * u:128 * u + 128]) for a in range(4)], ["Lo"], ["yl%d" % u], 2.0)
+    fl, zl = T.fzin[:, 0:16], T.fzin[:, 16:32]
+    act(fin("zo"), T.zfin[:].indirect(zl), F.Copy, ["zfin0", "zfin1", "fzin"], ["zo"], 256, CG)
+    dma("Y", [(T.yz[:, :], fin("zo"))], ["zo"], ["yz"], 0.1)
+    act(fin("msk"), T.dm[:].indirect(fl), F.Copy, kdm + ["fzin"], ["msk"], 256, CG)
+    tt(fin("m2"), T.dn[:].indirect(fl), T.Lfin[:], A.mult, ["dn", "fzin", "Lfin"], ["m2"], 256, CG)
+    tt(fin("m1"), T.ident[:].indirect(T.vin[:]), fin("msk"), A.mult, kid + ["vin", "msk"], ["m1"], 256, CG)
+    tt(fin("Lo"), fin("m1"), fin("m2"), A.add, ["m1", "m2"], ["Lo"], 256)
+    dma("Y", [(T.yl[:, :], fin("Lo"))], ["Lo"], ["yl"], 0.1)
+    act(fin("vo"), T.ident[:].indirect(T.vin[:]), F.Copy, kid + ["vin"], ["vo"], 256, CG)
+    dma("S", [(T.yv[:, :], T.fin[0::16, 256 * FIN.index("vo"):256 * FIN.index("vo") + 256])], ["vo"], ["yv"], 0.05)
     return ops
 
 
-def is_bank(k):
-    return k in ("pA0", "pA1", "pB0", "pB1", "pK", "pG", "pM0", "pM1")
+def lengths(ops, row):
+    cyc, cg, cs, tc, gap, ri, rl, rmb, lmb = row
+    dur, lat = [], []
+    for o in ops:
+        if o["kind"] == "c":
+            dur.append(o["fix"] + o["cyc"] * (tc if o["q"] == "T" else cyc * {CG: cg, CS: cs}.get(o["c"], 1.0)))
+            lat.append(0.0)
+        elif o["kind"] == "r":
+            dur.append(ri)
+            lat.append(rl + rmb * o["mb"])
+        else:
+            dur.append(o["fix"])
+            lat.append(1.9 + lmb * o["mb"])
+    return dur, lat, gap
+
+
+def replay(ops, seq, size):
+    dur, lat, gap = size
+    free = {q: 0.0 for q in "VSTGY"}
+    done = [0.0] * len(ops)
+    for i in seq:
+        o = ops[i]
+        st = max([free[o["q"]]] + [done[d] + (0.0 if o["q"] == "T" == ops[d]["q"] else gap) for d in o["deps"]])
+        free[o["q"]] = st + dur[i]
+        done[i] = st + dur[i] + lat[i]
+    return max(done)
 
 
 def order_ops(ops):
     writer, readers = {}, {}
     for i, o in enumerate(ops):
         deps = set()
-        wr = set(o["wr"]) | set(k for k in o["rd"] if is_bank(k))
+        wr = set(o["wr"]) | set(k for k in o["rd"] if k in BANKS)
         for k in o["rd"]:
             if k in writer:
                 deps.add(writer[k])
@@ -546,40 +579,125 @@ def order_ops(ops):
             writer[k] = i
             readers[k] = []
         o["deps"] = sorted(deps)
+    if "seq" in KEPT:
+        return KEPT["seq"]
     n = len(ops)
     succ = [[] for _ in range(n)]
     for i, o in enumerate(ops):
         for d in o["deps"]:
             succ[d].append(i)
-    gap = GAP
-    prio = [0.0] * n
-    for i in range(n - 1, -1, -1):
-        prio[i] = ops[i]["dur"] + ops[i]["lat"] + max([gap + prio[j] for j in succ[i]] + [0.0])
-    if "seq" in KEPT:
-        return KEPT["seq"]
     pred = [o["deps"] for o in ops]
+    sizes = [lengths(ops, row) for row in ROUGH]
     best = None
-    for _ in range(ROUNDS):
-        for i in range(n):
-            if ops[i]["kind"] == "d" and not ops[i]["deps"]:
-                prio[i] = 1e6 - i
-        seq, start = place(ops, pred, succ, prio, gap, False)
-        end = max(start[i] + ops[i]["dur"] + ops[i]["lat"] for i in range(n))
-        if best is None or end < best[0]:
-            best = (end, seq, start)
-        _s, back = place(ops, succ, pred, [start[i] + ops[i]["dur"] for i in range(n)], gap, True)
-        prio = [back[i] + ops[i]["dur"] + JITTER * (((i + 1) * SEED * 2654435761 + _ * 40503) % 1000) / 1000.0 for i in range(n)]
-    for i in range(n):
-        ops[i]["start"] = best[2][i]
-    KEPT["seq"] = best[1]
+    for k in range(TRIES):
+        size = sizes[k % len(sizes)] if k >= TRIES // 2 else sizes[0]
+        dur, lat, gap = size
+        prio = [0.0] * n
+        for i in range(n - 1, -1, -1):
+            prio[i] = dur[i] + lat[i] + max([gap + prio[j] for j in succ[i]] + [0.0])
+        for r in range(ROUNDS):
+            for i in range(n):
+                if ops[i]["kind"] == "d" and not ops[i]["deps"]:
+                    prio[i] = 1e6 - i
+                elif ops[i]["early"]:
+                    prio[i] = 1e5 * ops[i]["early"] - i
+                elif k:
+                    prio[i] += JITTER * (((i + 1) * 2654435761 + (k * ROUNDS + r) * 40503 * (i + 7)) % 1000) / 1000.0
+            seq, start = place(ops, pred, succ, prio, size, False)
+            score = sum(replay(ops, seq, sz) / row[0] for sz, row in zip(sizes, ROUGH))
+            if best is None or score < best[0]:
+                best = (score, seq)
+            _s, back = place(ops, succ, pred, [start[i] + dur[i] for i in range(n)], size, True)
+            prio = [back[i] + dur[i] for i in range(n)]
+    KEPT["seq"] = improve(ops, best[1], succ, sizes)
+    return KEPT["seq"]
+
+
+def improve(ops, seq, succ, sizes):
+    n = len(ops)
+    direct = []
+    for o in ops:
+        far = set(e for d in o["deps"] for e in ops[d]["deps"] if ops[e]["kind"] == "c")
+        direct.append([(d, o["q"] == "T" == ops[d]["q"]) for d in o["deps"] if d not in far])
+    line = {q: [i for i in seq if ops[i]["q"] == q] for q in "VSTGY"}
+
+    def run():
+        before, after = [-1] * n, [-1] * n
+        for l in line.values():
+            for a, b in zip(l, l[1:]):
+                before[b], after[a] = a, b
+        left = [len(ops[i]["deps"]) + (before[i] >= 0) for i in range(n)]
+        order = [i for i in range(n) if left[i] == 0]
+        for i in order:
+            for j in succ[i]:
+                left[j] -= 1
+                if left[j] == 0:
+                    order.append(j)
+            j = after[i]
+            if j >= 0:
+                left[j] -= 1
+                if left[j] == 0:
+                    order.append(j)
+        if len(order) < n:
+            return None
+        score, paths = 0.0, []
+        for (dur, lat, gap), row in zip(sizes, ROUGH):
+            free, done, why = [0.0] * n, [0.0] * n, [-1] * n
+            for i in order:
+                w = before[i]
+                st = free[w] if w >= 0 else 0.0
+                for d, soft in direct[i]:
+                    x = done[d] if soft else done[d] + gap
+                    if x > st:
+                        st, w = x, d
+                why[i] = w
+                free[i] = st + dur[i]
+                done[i] = st + dur[i] + lat[i]
+            end = max(done)
+            score += end / row[0]
+            paths.append((why, done.index(end)))
+        return score, order, paths, before
+
+    now = run()
+    best = (now[0], now[1])
+    x = 12345
+    for step in range(STEPS):
+        x = (x * 1103515245 + 12345) % 2147483648
+        why, i = now[2][(x >> 8) % len(sizes)]
+        held = []
+        while i >= 0:
+            if why[i] >= 0 and why[i] == now[3][i] and why[i] not in ops[i]["deps"] and ops[i]["kind"] != "d":
+                held.append(i)
+            i = why[i]
+        if not held:
+            continue
+        x = (x * 1103515245 + 12345) % 2147483648
+        b = held[(x >> 8) % len(held)]
+        l = line[ops[b]["q"]]
+        p = l.index(b)
+        x = (x * 1103515245 + 12345) % 2147483648
+        k = 1 + (x >> 8) % 4
+        old = list(l)
+        if (x >> 16) % 2:
+            l.insert(max(0, p - k), l.pop(p))
+        else:
+            l.insert(min(len(l) - 1, p - 1 + k), l.pop(p - 1))
+        new = run()
+        if new is not None and new[0] <= now[0] * (1.0 + SLACK * (1.0 - step / STEPS)):
+            now = new
+            if now[0] < best[0]:
+                best = (now[0], now[1])
+        else:
+            l[:] = old
     return best[1]
 
 
-def place(ops, pred, succ, prio, gap, backwards):
+def place(ops, pred, succ, prio, size, backwards):
+    dur, lat, gap = size
     n = len(ops)
     start = [0.0] * n
     left = [len(p) for p in pred]
-    ready_at = [o["lat"] if backwards else 0.0 for o in ops]
+    ready_at = [lat[i] if backwards else 0.0 for i in range(n)]
     ready = [i for i in range(n) if left[i] == 0]
     free = {q: 0.0 for q in "VSTGY"}
     seq = []
@@ -587,23 +705,23 @@ def place(ops, pred, succ, prio, gap, backwards):
         first = min(ready, key=lambda i: (max(ready_at[i], free[ops[i]["q"]]), -prio[i], i))
         q = ops[first]["q"]
         t0 = max(ready_at[first], free[q])
-        i = max((i for i in ready if ops[i]["q"] == q and ready_at[i] <= t0 + HOLD), key=lambda i: (prio[i], -i))
+        mine = [i for i in ready if ops[i]["q"] == q]
+        i = max((i for i in mine if ready_at[i] <= t0 + HOLD), key=lambda i: (prio[i], -i))
         if ready_at[i] > t0:
-            fit = [j for j in ready if ops[j]["q"] == q and max(ready_at[j], t0) + ops[j]["dur"] <= ready_at[i] + FIT]
-            now = max((j for j in ready if ops[j]["q"] == q and ready_at[j] <= t0), key=lambda j: (prio[j], -j))
+            fit = [j for j in mine if max(ready_at[j], t0) + dur[j] <= ready_at[i] + FIT]
+            now = max((j for j in mine if ready_at[j] <= t0), key=lambda j: (prio[j], -j))
             if fit:
                 i = max(fit, key=lambda j: (prio[j], -j))
             elif prio[i] - prio[now] < EDGE:
                 i = now
         st = max(ready_at[i], free[q])
         ready.remove(i)
-        o = ops[i]
         start[i] = st
-        free[o["q"]] = st + o["dur"]
+        free[q] = st + dur[i]
         seq.append(i)
         for j in succ[i]:
-            soft = ops[j]["q"] == "T" and o["q"] == "T"
-            ready_at[j] = max(ready_at[j], st + o["dur"] + (ops[j]["lat"] if backwards else o["lat"]) + (0.0 if soft else gap))
+            soft = ops[j]["q"] == "T" and q == "T"
+            ready_at[j] = max(ready_at[j], st + dur[i] + (lat[j] if backwards else lat[i]) + (0.0 if soft else gap))
             left[j] -= 1
             if left[j] == 0:
                 ready.append(j)
@@ -614,18 +732,13 @@ def rank_program(g, core, T, topo):
     rank = T.rank_of(core)
     if rank is None:
         return
-    nxt = T.cores[(rank + 1) % len(T.cores)]
-    ops = build_ops(g, T, topo, core, nxt)
+    n = len(T.cores)
+    ops = build_ops(g, T, topo, core, T.cores[(rank + 1) % n], T.cores[(rank - (NV - 1)) % n])
     seq = order_ops(ops)
     queue = {"V": g.vector, "S": g.scalar, "T": g.tensor, "G": g, "Y": g.sync}
 
     def needs_wait(d, o):
-        p = ops[d]
-        if p["q"] == "T" and o["q"] == "T":
-            return False
-        if o["loose"] and p["q"] == o["q"] and set(p["wr"]) == set(o["wr"]):
-            return False
-        return True
+        return not (ops[d]["q"] == "T" and o["q"] == "T")
 
     signals = set(d for o in ops for d in o["deps"] if needs_wait(d, o))
     count = {q: 0 for q in COUNTER}

@@ -1,3 +1,4 @@
+import math
 from concourse.bass import DstId, RemoteDMATransfer
 from concourse.mybir import dt, AluOpType, AxisListType, ActivationFunctionType
 
@@ -5,18 +6,28 @@ A = AluOpType
 F = ActivationFunctionType
 V_, Q_, NV = 4096, 256, 3
 TH, TAU = 1020, (1020, 1530, 1275)
-WN = V_ + 16
-WE = WN + 512
-BASE = (0, WE + WN, WE + 2 * WN, WE)
-AT = (0, 2, 3, 1)
-SPLIT = False
-LOG_BY_S = False
-NC = 8192 + WN - 256
+HV = 2
+MH = 16 // HV
+EH = 16 * MH
+DUP = 512 // EH
+SEG = 18
+KW = SEG * MH
+PAIR = 2
+WN = V_ + 32
+VB = V_ + 256
+WE = VB + 512
+BASE = (0, WE, WE + WN, WE + 2 * WN)
+LATE = 2
+TSEP = False
+ECH_ON_S = True
+FILL_ON_V = ("ctau", "cmid", "csum")
+XGW = 2
 H16, B16, F32 = "float16", "bfloat16", "float32"
 WALK_ON_V = ((1,), (0, 1), (0, 1))
-CUT_ON_S = (3, 2, 2)
-BUILD_ON_S = 0
-PAIR_ON_V = False
+CUT_ON_S = ((3, 3), (3, 3), (3, 3))
+XSEND = True
+ZH = 1
+LASTH = 2
 FIN = ("Lg", "Ln", "Lp", "Lr", "Lrow", "msk", "m1", "m2", "zo", "Lo", "vo")
 SUMQ = 2
 
@@ -26,47 +37,46 @@ def _sb(n, d):
 
 
 SCRATCH = {
-    "Xs": _sb(V_, B16), "Eraw": _sb(V_, "int32"), "Win": _sb(WE + 3 * WN, F32), "ident": _sb(WE, F32),
+    "Xs": _sb(V_, B16), "Eraw": _sb(V_, "int32"), "Win": _sb(BASE[3] + WN, F32), "ident": _sb(WE, F32),
     "xg": _sb(V_, B16), "absd": ("sbuf", [128, 16, 256], B16), "mH": _sb(V_, B16), "mL": _sb(V_, B16),
-    "mid": _sb(2048, B16), "R1": _sb(512, B16), "Wt": _sb(2048, B16),
+    "mid": _sb(1024, B16), "R1": _sb(512, B16), "Wt": _sb(2048, B16),
     "nI": _sb(128, B16), "hI": _sb(128, H16), "I32": _sb(128, F32), "I": _sb(128, B16), "ones": _sb(256, B16),
-    "pi": _sb(8, "int32"), "col": _sb(40, F32), "cols": _sb(144, F32),
+    "pi": _sb(8, "int32"), "col": _sb(48, F32), "cols": _sb(144, F32),
     "WK": _sb(144, B16), "WP": _sb(144, B16), "WM": _sb(144, B16), "Wh": _sb(144, B16), "Wf": _sb(144, B16),
     "W1": _sb(144, B16), "Wr0": _sb(144, B16), "Wr1": _sb(144, B16), "Wr2": _sb(144, B16), "Ws": _sb(144, B16),
-    "Rot": _sb(128, B16), "W32": _sb(144, F32), "Wp0": _sb(144, F32), "Wp1": _sb(144, F32),
-    "dm": _sb(528, F32), "dn": _sb(32, F32),
-    "kcb": _sb(256, B16), "kcM": _sb(256, F32), "rK": _sb(256, F32), "rG": _sb(256, F32),
-    "c16": _sb(256, "uint16"), "cmid": _sb(128, B16), "csum": _sb(128, B16), "ctau": _sb(384, B16), "cneg": _sb(16, B16), "nc": _sb(80, F32),
-    "fi": _sb(192, "int32"), "lists": _sb(112, "uint16"),
-    "raw": _sb(768, "int32"), "t1": _sb(768, F32), "t2": _sb(768, F32), "offE": _sb(512, "uint16"), "S0": _sb(256, F32),
+    "Rot": _sb(128, B16), "W32": _sb(144, F32),
+    "dm": _sb(528, F32), "df": _sb(64, F32),
+    "kcb": _sb(256, B16), "kcM": _sb(256, F32), "rK": _sb(256, F32), "rG": _sb(KW, F32),
+    "c16": _sb(256, "uint16"), "cmid": _sb(128, B16), "csum": _sb(128, B16), "ctau": _sb(384, B16), "nc": _sb(64, F32), "cbig": _sb(16, B16), "Ht": _sb(512, B16),
+    "fi": _sb(192, "int32"), "lists": _sb(128, "uint16"), "sig": _sb(32, "uint16"),
+    "raw": _sb(768, "int32"), "t1": _sb(768, F32), "t2": _sb(768, F32), "offE": _sb(512, "uint16"), "S0": _sb(512, F32),
     "cf": _sb(256, F32), "cfr": _sb(256, F32), "nzW": _sb(256, B16), "neq": _sb(256, B16),
-    "scK": _sb(256, F32), "ki": _sb(80, "int32"), "k16": _sb(16, "uint16"), "selc": _sb(256, H16), "xv": _sb(256, B16),
-    "Lf": _sb(256, F32), "key": _sb(256, F32), "keyT": _sb(256, F32), "scG": _sb(256, F32), "Ht": _sb(512, B16),
-    "sm": _sb(160, F32), "si": _sb(48, "int32"), "s16": _sb(64, "uint16"), "ech": _sb(256, H16),
-    "eq": _sb(256, F32), "dl": _sb(256, F32), "ur": _sb(256, F32), "eq2": _sb(256, B16),
-    "o16": _sb(64, "uint16"), "An": _sb(768, B16), "vals": ("sbuf", [128, 16, 64], F32),
+    "scK": _sb(256, F32), "ki": _sb(80, "int32"), "k16": _sb(16, "uint16"), "selc": _sb(256, H16),
+    "Lf": _sb(288, F32), "key": _sb(288, F32), "keyT": _sb(288, F32), "scG": _sb(288, F32), "hf": _sb(256, H16),
+    "sm": _sb(144, F32), "si": _sb(48, "int32"), "s16": _sb(64, "uint16"), "ech": _sb(256, H16),
+    "eq": _sb(256, F32), "dl": _sb(256, F32), "ur": _sb(256, F32), "eq2": _sb(512, B16),
+    "o16": _sb(32 * NV, "uint16"), "vals": _sb(1024, F32), "vs": _sb(256 * NV, F32),
     "fin": _sb(256 * len(FIN), F32),
     "Lfin": _sb(256, F32), "zfin": _sb(768, B16), "fz": _sb(32, "uint16"), "fzin": _sb(32, "uint16"), "vin": _sb(16, "uint16"),
+    "vq": _sb(16 * (NV + 1), "uint16"),
+    "wa": _sb(16 * NV, "uint16"), "wain": _sb(16 * NV, "uint16"),
+    "lb": _sb(16 * NV, B16), "lbin": _sb(16 * NV, B16),
+    "hs": _sb(16 * NV, "uint16"), "hin": _sb(16 * NV, "uint16"),
+    "mb": _sb(512 * (1 if XSEND else NV), B16),
 }
-for _t in range(NV + 1):
-    SCRATCH["vq%d" % _t] = _sb(16, "uint16")
 for _t in range(NV):
     SCRATCH["zq%d" % _t] = _sb(256, B16)
     SCRATCH["Lq%d" % _t] = _sb(256, "uint16")
-    SCRATCH["zin%d" % _t] = _sb(1024, B16)
+    SCRATCH["zd%d" % _t] = ("sbuf", [128, HV, 512], B16)
+    SCRATCH["zc%d" % _t] = _sb(768, B16)
     SCRATCH["Lin%d" % _t] = _sb(256, "uint16")
-    SCRATCH["a%d" % _t] = _sb(16, "uint16")
-    SCRATCH["ain%d" % _t] = _sb(16, "uint16")
-    SCRATCH["lb%d" % _t] = _sb(16, B16)
-    SCRATCH["lbin%d" % _t] = _sb(16, B16)
-    SCRATCH["h%d" % _t] = _sb(16, "uint16")
-    SCRATCH["hin%d" % _t] = _sb(16, "uint16")
-    SCRATCH["b%d" % _t] = _sb(512, B16)
-BANKS = ("pA0", "pA1", "pB0", "pB1", "pK", "pG", "pM0", "pM1")
+    SCRATCH["xv%d" % _t] = _sb(256, B16)
+    SCRATCH["xin%d" % _t] = _sb(256, B16)
+BANKS = ("pA0", "pA1", "pB0", "pB1", "pK", "pG0", "pG1", "pM")
 for _n in BANKS:
     SCRATCH[_n] = ("psum", [128, 512], F32)
 
-SEMAPHORES = (["cV", "cS", "cT", "cG", "sent", "mv", "mf", "mzo", "mLo"] + ["dma%d" % _i for _i in range(16)]
+SEMAPHORES = (["cV", "cS", "cT", "cG", "sent", "mv", "mf", "mzo", "mLo"] + ["dma%d" % _i for _i in range(24)]
               + ["%s_%d" % (_n, _i) for _n in ("m1", "mz", "m2a", "m2b", "mh") for _i in range(NV)])
 
 ROUGH = ((0.0009, 1.5, 3.6, 0.00046, 0.12, 0.55, 2.0, 25.0, 2.8),
@@ -74,7 +84,11 @@ ROUGH = ((0.0009, 1.5, 3.6, 0.00046, 0.12, 0.55, 2.0, 25.0, 2.8),
          (0.001, 1.3, 4.5, 0.0005, 0.18, 0.7, 2.4, 30.0, 2.8),
          (0.0012, 1.9, 5.0, 0.0006, 0.1, 0.5, 2.0, 22.0, 3.3))
 HOLD, FIT, EDGE, ROUNDS, TRIES, JITTER = 0.3, 0.05, 1.0, 4, 4, 0.6
-STEPS, SLACK = 4000, 0.001
+STEPS = 60000
+SEED = 1
+PULL = 0.3
+HOT = 0.002
+COLD = 0.0001
 CG, CS, DI = "gather", "scatter", 0.15
 KEPT = {}
 COUNTER = {"V": "cV", "S": "cS", "T": "cT", "G": "cG"}
@@ -89,8 +103,9 @@ def build_ops(g, T, topo, core, nxt, own):
     nd = [0]
     early = [False]
 
-    def op(q, fn, rd, wr, fix, n=0, c=1.0, kind="c", sem=None, inc=1, mb=0.0):
-        ops.append(dict(q=q, fn=fn, rd=list(rd), wr=list(wr), fix=fix, cyc=n if c in (CG, CS) else max(64, n * c), c=c, kind=kind, sem=sem, n=inc, mb=mb, early=early[0]))
+    def op(q, fn, rd, wr, fix, n=0, c=1.0, kind="c", sem=None, inc=1, mb=0.0, acc=None, stop=None):
+        ops.append(dict(q=q, fn=fn, rd=list(rd), wr=list(wr), fix=fix, cyc=n if c in (CG, CS) else max(64, n * c), c=c, kind=kind, sem=sem, n=inc, mb=mb,
+                        early=early[0], acc=acc, stop=stop))
 
     def ts(out, in0, s1, s2, o0, o1, rd, wr, n=16, c=1.0):
         if o1 is None:
@@ -110,17 +125,27 @@ def build_ops(g, T, topo, core, nxt, own):
     def turn(out, in_, rd, wr):
         op("V", lambda: v.transpose(out, in_), rd, wr, 0.05, 256)
 
-    def scan(out, d0, d1, o0, o1, rd, wr):
-        op("V", lambda: v.tensor_tensor_scan(out, d0, d1, 0.0, o0, o1), rd, wr, 0.05, 256)
+    def scan(out, d0, d1, o0, o1, rd, wr, n=256):
+        op("V", lambda: v.tensor_tensor_scan(out, d0, d1, 0.0, o0, o1), rd, wr, 0.05, n)
 
     def act(out, in_, f, rd, wr, n, c=1.0, scale=1.0, bias=0.0):
         op("S", lambda: s.activation(out, in_, f, bias=bias, scale=scale), rd, wr, 0.065, n, c)
 
-    def mm(items, rd, wr, first=True, last=True, x=1):
+    def mm(items, rd, wr, first=True, last=True, x=1, acc=None):
+        stop = [last and acc is None]
+
         def fn():
             ins = None
             for i, (o, l, r, _n) in enumerate(items):
-                ins = te.matmul(o, l, r, first and i == 0, last and i == len(items) - 1)
+                ins = te.matmul(o, l, r, first and acc is None and i == 0, stop[0] and i == len(items) - 1)
+            return ins
+        op("T", fn, rd, wr, 0.02, sum(max(64, it[3]) * x for it in items), acc=acc, stop=stop)
+
+    def mms(items, rd, wr, x=1):
+        def fn():
+            ins = None
+            for o, l, r, _n in items:
+                ins = te.matmul(o, l, r, True, True)
             return ins
         op("T", fn, rd, wr, 0.02, sum(max(64, it[3]) * x for it in items))
 
@@ -160,8 +185,11 @@ def build_ops(g, T, topo, core, nxt, own):
                                     for (o, i), m in zip(pairs, masks)], local_sem=T.sem.sent)
         op("G", fn, rd, wr, 0.0, 0, 1.0, "r", sem, len(es), mb)
 
-    def ch(name, n=8):
-        return ["%s%d" % (name, i) for i in range(n)]
+    def ch(name, n=8, a=0):
+        return ["%s%d" % (name, i) for i in range(a, n)]
+
+    def units(name, a, b):
+        return ch(name, (b + 127) // 128, a // 128)
 
     def wsl(w, b):
         return w[:, 15 - b:143 - b]
@@ -172,10 +200,15 @@ def build_ops(g, T, topo, core, nxt, own):
     def fin(name, a=0, b=256):
         return T.fin[:, 256 * FIN.index(name) + a:256 * FIN.index(name) + b]
 
+    def n2l(out, w, kw_, src, ksrc, bank, const=None, kconst=(), a0=0, n=256, x=1, acc=None):
+        items = [(out, const, T.ones[:, 0:n // 16], n // 16)] if const is not None else []
+        items += [(out, wsl(w, b), src[:, a0 + b:a0 + n:16], n // 16) for b in range(16)]
+        mm(items, [kw_, "onesa"] + list(ksrc) + list(kconst), [bank], True, True, x, acc)
+
     dma("Y", [(T.raw[:, 256 + 128 * u:256 + 128 * u + 128], T.E[16 * u::32, :]) for u in range(2)], [], ["rawE0"], 0.15)
     dma("S", [(T.raw[:, 512 + 128 * u:512 + 128 * u + 128], T.E[16 * u + 1::32, :]) for u in range(2)], [], ["rawE1"], 0.25)
     dma("Y", [(T.Xs[:], T.X[:, :])], [], ["X"], 1.3)
-    dma("S", [(T.zq0[:], T.z0[:, :])], [], ["z0"], 1.3)
+    dma("S", [(T.zq0[:], T.z0[:, :])], [], ch("z0_", ZH), 1.3)
     dma("Y", [(T.ki[:, 64:80], T.v0[:, :])], [], ["v0i"], 1.35)
     for c in range(2):
         dma("Y", [(T.Eraw[:, 2048 * c:2048 * c + 2048], T.E[:, 2048 * c:2048 * c + 2048])], [], ["Eraw%d" % (2 * c), "Eraw%d" % (2 * c + 1)], 2.35 + c)
@@ -184,10 +217,12 @@ def build_ops(g, T, topo, core, nxt, own):
     early[0] = True
     col = T.col
     iota(T.pi[:, 0:1], [[0, 1]], 0, 1, ["pi0"], 1, False)
-    names = ("p1", "xm", "p2", "pE", "sig", "iL", "x16")
-    pats = ([[16, 8], [128, 2]], [[0, 16]], [[16, 2], [32, 8]], [[2, 16]], [[1, 16]], [[1, 8], [128, 2]], [[1, 16]])
+    names = ("p1", "p2", "pE", "x16", "x2", "xm", "pL", "iL")
+    two = HV == 2
+    pats = ([[16, 8], [128, 2]], [[16, 2], [32, 8]], [[2, 16]], [[1, 16]], [[2, 8], [0, 2]],
+            [[8, 2], [0, 8]] if two else [[0, 16]], [[1, 2], [4, 8]] if two else [[2, 16]], [[1, 8], [64 if two else 128, 2]])
     lists = {name: T.lists[:, 16 * j:16 * j + 16] for j, name in enumerate(names)}
-    for j in (0, 3, 1, 2):
+    for j in (0, 2, 1):
         iota(T.fi[:, 16 * j:16 * j + 16], pats[j], 0, 0, ["fi" + names[j]], 16, False)
     iota(T.cols[:], [[1, 144]], 0, 0, ["cols"], 144)
     ts(T.pi[:, 1:2], T.pi[:, 0:1], 15, None, A.bitwise_and, None, ["pi0"], ["pi1"])
@@ -207,8 +242,8 @@ def build_ops(g, T, topo, core, nxt, own):
 
     c32b, k32b = column(cB, 32.0, 0.0)
     cE, kE = column(cB3, -255.0, c32b, [k32b])
-    ts(T.lists[:, 0:48], T.fi[:, 0:48], cB, None, A.add, None, ["fip1", "fixm", "fip2", "colb"], ["lp1", "lxm", "lp2"], 48)
-    ts(lists["pE"], T.fi[:, 48:64], cE, None, A.add, None, ["fipE", kE], ["lpE"])
+    ts(T.lists[:, 0:32], T.fi[:, 0:32], cB, None, A.add, None, ["fip1", "fip2", "colb"], ["lp1", "lp2"], 32)
+    ts(lists["pE"], T.fi[:, 32:48], cE, None, A.add, None, ["fipE", kE], ["lpE"])
     cg, kg = column(cB, -1.0, cP)
     cG15, kG15 = column(cg, 1.0, 15.0, [kg])
     ts(T.W1[:], T.cols[:], cG15, None, A.is_equal, None, ["cols", kG15], ["W1"], 144)
@@ -219,106 +254,121 @@ def build_ops(g, T, topo, core, nxt, own):
     iota(T.mid[:, 0:512], [[1, 32], [0, 16]], 0, 0, ["mid0"], 512)
     c32p, k32p = column(cU, 16.0, cB)
     ts(T.R1[:], T.mid[:, 0:512], c32p, None, A.is_equal, None, ["mid0", k32p], ["R1"], 512, 0.5)
-    ms(T.mH[:, 0:256], 0.0, ["mH0"], 256, 0.5)
     ts(T.rK[:], T.kcb[:], 0.0, 2.0 ** 25, A.is_equal, A.mult, ["kcb"], ["rK"], 256)
-    act(T.rG[:], T.rK[:], F.Identity, ["rK"], ["rG"], 256, 1.0, 512.0, -8192.0)
-    for j in (4, 5, 6):
+    for j in (3, 4, 5, 6, 7):
         iota(T.fi[:, 16 * j:16 * j + 16], pats[j], 0, 0, ["fi" + names[j]], 16, False)
-    iota(T.fi[:, 112:144], [[-512, 2], [16, 16]], NC + 512, 0, ["finc0"], 32, False)
-    iota(T.fi[:, 144:192], [[-8192, NV], [16, 16]], NC + 256 + 8192 * 15, 0, ["finc1"], 48, False)
-    c16b, k16b = column(cB, 16.0, 0.0)
+    iota(T.fi[:, 128:176], [[256, 3], [16, 16]], VB - 256, 0, ["finc"], 48, False)
     c8b, k8b = column(cB, 8.0, 0.0)
     cn2, kn2 = column(cB1, -2.0, cB)
-    cev, kev = column(cn2, -1.0, 1.0, [kn2])
     cw, kw = column(cz, 16.0, cB, ["dm0"])
     cr1, kr1 = column(cw, 1.0, cg, [kw, kg])
     crot, krot = column(cr1, 1.0, -1.0, [kr1])
     ch_, kh = column(cB, 2.0, 1.0)
     cs, ks = column(cB, 1.0, 1.0)
-    cdum, kdum = column(cB, 1.0, float(V_))
+    cdum = [column(cB, 1.0, float(V_ + 16 * u)) for u in range(PAIR)]
     cmid, kmid = column(cB, 0.0, -2048.0)
-    cq1, kq1 = column(cU, -8.0, cg, [kg])
-    cq3, kq3 = column(cB1, 1.0, cq1, [kq1])
-    cq2, kq2 = column(cq3, 1.0, 16.0, [kq3])
+    c1k, k1k = column(cB, 0.0, 1024.0)
+    if two:
+        cxm, kxm = column(cB3, -8.0, cB)
+        cpL, kpL = column(cB3, -254.0, c32b, [k32b])
+        c4b, k4b = column(cB, 4.0, 0.0)
+        ciL, kiL = column(cn2, 124.0, c4b, [kn2, k4b])
+    else:
+        (cxm, kxm), (cpL, kpL), (ciL, kiL) = (cB, "colb"), (cE, kE), (c8b, k8b)
     for name, val, kk in (("WK", 1024.0, ()), ("WP", 2.0 ** 19, ()), ("WM", -2.0 ** 19, ()), ("Wf", 32.0, ()), ("Wh", ch_, [kh]), ("W32", cs, [ks]),
                           ("Wr0", cz, ["dm0"]), ("Wr1", c1, ["dm0"]), ("Wr2", c2, ["dm0"]), ("Ws", cw, [kw])):
         act(T[name][:], T.W1[:], F.Copy, ["W1"] + list(kk), [name], 144, 1.0, val)
-    ts(lists["sig"], T.fi[:, 64:80], c16b, None, A.add, None, ["fisig", k16b], ["lsig"])
-    ts(lists["iL"], T.fi[:, 80:96], c8b, None, A.add, None, ["fiiL", k8b], ["liL"])
-    cp(lists["x16"], T.fi[:, 96:112], ["fix16"], ["lx16"])
-    ts(T.nc[:], T.fi[:, 112:192], cB, None, A.add, None, ["finc0", "finc1", "colb"], ["nc"], 80)
-    for name, val, kk in (("Wp0", cev, kev), ("Wp1", cn2, kn2)):
-        ts(T[name][:], T.cols[:], cq2, val, A.is_equal, A.mult, ["cols", kq2, kk], [name], 144)
+    early[0] = False
+    cp(T.lists[:, 48:80], T.fi[:, 48:80], ["fix16", "fix2"], ["lx16"], 32)
+    for name, cc_, kk in (("xm", cxm, kxm), ("pL", cpL, kpL), ("iL", ciL, kiL)):
+        j = names.index(name)
+        ts(lists[name], T.fi[:, 16 * j:16 * j + 16], cc_, None, A.add, None, ["fi" + name, kk], ["l" + name])
+    ts(T.nc[:, 0:48], T.fi[:, 128:176], cB, None, A.add, None, ["finc", "colb"], ["nc"], 48)
+    if TSEP:
+        ts(T.nc[:, 48:64], T.fi[:, 160:176], cB, -8192.0 * 17, A.add, A.add, ["finc", "colb"], ["ncl"])
+        ms(T.mH[:, 0:256], 0.0, units("mH", 0, 256), 256, 0.5)
+    iota(T.cbig[:], [[0, 16]], 2 ** 23, 0, ["cbig"], 16)
     ts(T.Rot[:], T.cols[:, 0:128], crot, None, A.is_equal, None, ["cols", krot], ["Rot"], 128)
     ts(T.hI[:], T.I[:], 0.5 - 2.0 ** -11, None, A.mult, None, ["I"], ["hI"], 128, 0.5)
     act(T.nI[:], T.I[:], F.Copy, ["I"], ["nI"], 128, 1.0, -1.0)
     act(T.I32[:], T.I[:], F.Copy, ["I"], ["I32"], 128)
-    act(T.dn[:], T.dm[:, 0:32], F.Identity, ["dm0"], ["dn"], 32, 1.0, -1.0, 1.0)
-    ts(T.col[:, 24:40], T.cols[:, 0:16], cB, 2.0 ** 19, A.is_gt, A.mult, ["cols", "colb"], ["tri"])
+    ts(T.df[:, 0:32], T.cols[:, 0:32], cs, None, A.is_equal, None, ["cols", ks], ["df0"], 32)
+    act(T.df[:, 32:64], T.df[:, 0:32], F.Identity, ["df0"], ["df1"], 32, 1.0, -1.0, 1.0)
+    ts(T.col[:, 32:48], T.cols[:, 0:16], cB, 2.0 ** 19, A.is_gt, A.mult, ["cols", "colb"], ["tri"])
     for b in range(1, 16):
-        ts(T.Wt[:, 128 * b:128 * b + 128], wsl(T.W1, b), T.col[:, 24 + b:25 + b], None, A.mult, None, ["W1", "tri"], ["Wt%d" % b], 128, 0.5)
+        ts(T.Wt[:, 128 * b:128 * b + 128], wsl(T.W1, b), T.col[:, 32 + b:33 + b], None, A.mult, None, ["W1", "tri"], ["Wt%d" % b], 128, 0.5)
+    iota(T.keyT[:, 0:KW], [[1, MH], [MH, SEG]], 0, 0, ch("keyT", HV), KW)
+    n2l(T.pM[:, 0:KW // 16], T.W32, "W32", T.keyT, ch("keyT", HV), "pM", None, (), 0, KW, 4)
+    ts(T.sig[:, 0:KW // 16], T.pM[:, 0:KW // 16], 1.0 / 136, None, A.mult, None, ["pM"], ["lsig"])
+    ms(T.scG[:, 0:KW], -8192.0, ch("scG", HV), KW)
+    sel(T.rG[:], T.scG[:, 0:KW], [[0, MH], [1, SEG]], A.not_equal, 2.0 ** 34, 0, 0, ch("scG", HV), ["rG"], KW)
     early[0] = False
 
     for c in range(8):
         w = WE // 8
         iota(T.ident[:, c * w:c * w + w], [[1, w]], c * w, 0, ["id%d" % c], w)
-    iota(T.dm[:, 32:528], [[0, 496]], 0, 0, ["dm"], 496)
+
+    def fill(ap, val, key, n, c=1.0):
+        if key.rstrip("0123456789ab") in FILL_ON_V:
+            ms(ap, float(val), [key], n, c)
+        else:
+            iota(ap, [[0, n]], val, 0, [key], n)
+
+    fill(T.dm[:, 32:528], 0, "dm", 496)
     act(T.dm[:, 32::32], T.ones[:, 0:16], F.Copy, ["onesa", "dm0"], ["dm"], 16, 1.0, cz)
-    iota(T.cmid[:], [[0, 128]], 16, 0, ["cmid"], 128)
-    iota(T.csum[:], [[0, 128]], 17 * 128, 0, ["csum"], 128)
-    iota(T.cneg[:], [[0, 16]], -2 ** 23, 0, ["cneg"], 16)
+    fill(T.cmid[:], 16, "cmid", 128, 0.5)
+    fill(T.csum[:], 17 * 128, "csum", 128, 0.5)
     for t in range(NV):
         top = 16 * ((2 * TAU[t] + 1 + 15) // 16)
-        iota(T.ctau[:, 128 * t:128 * t + 128], [[0, 128]], 4096 * (2 * TAU[t] + 1 - top), 0, ["ctau%d" % t], 128)
-        iota(T.ctau[0:64, 128 * t:128 * t + 128], [[0, 128]], 4096 * top, 0, ["ctau%d" % t], 128)
-    iota(T.kcM[:], [[1, 16], [0, 16]], -15, 0, ["kcM"], 256)
+        fill(T.ctau[64:128, 128 * t:128 * t + 128], 4096 * (2 * TAU[t] + 1 - top), "ctau%da" % t, 128, 0.5)
+        fill(T.ctau[0:64, 128 * t:128 * t + 128], 4096 * top, "ctau%db" % t, 128, 0.5)
+    iota(T.kcM[:], [[0, HV], [1, 16], [0, MH]], -16, 0, ["kcM"], 256)
     for r in range(4):
-        iota(T.Win[:, BASE[r] + V_:BASE[r] + WN], [[0, 16]], 0, 0, ["dum%d" % r], 16)
+        n = VB - V_ if r == 0 else WN - V_
+        fill(T.Win[:, BASE[r] + V_:BASE[r] + V_ + n], 0, "dum%d" % r, n)
+    for h in range(HV):
+        gcopy(T.Lf[:, KW * h:KW * h + MH], T.nc[:, 32 + MH * h:32 + MH * h + MH], ["nc"], ["Lfc%d" % h], MH)
+        gcopy(T.key[:, KW * h + 17 * MH:KW * h + KW], T.nc[:, 16 + MH * h:16 + MH * h + MH], ["nc"], ["keyc%d" % h], MH)
 
-    for r, src, out, ko in ((1, "rawE0", T.offE[:, 0:256], "offE0"), (2, "rawE1", T.offE[:, 256:512], "offE1"), (0, "rawL", T.Lq0[:], "L0")):
+    for r, src, out, ko, lst in ((1, "rawE0", T.offE[:, 0:256], "offE0", "pE"), (2, "rawE1", T.offE[:, 256:512], "offE1", "pE"), (0, "rawL", T.Lq0[:], "L0", "pL")):
         sl = slice(256 * r, 256 * r + 256)
         early[0] = 2 if r else False
         cp(T.t1[:, sl], T.raw[:, sl].indirect(lists["p1"]), [src, "lp1"], ["t1%d" % r], 256, CG)
         turn(T.t2[:, sl], T.t1[:, sl], ["t1%d" % r], ["t2%d" % r])
-        cp(out, T.t2[:, sl].indirect(lists["pE"]), ["t2%d" % r, "lpE"], [ko], 256, CG)
-    cp(T.vq0[:], T.ki[:, 64:80], ["v0i"], ["v0"])
+        cp(out, T.t2[:, sl].indirect(lists[lst]), ["t2%d" % r, "l" + lst], [ko], 256, CG)
+    cp(T.vq[:, 0:16], T.ki[:, 64:80], ["v0i"], ch("v0_", HV))
 
     for c in range(8):
-        act(T.mL[:, 512 * c:512 * c + 512], T.Xs[:].indirect(T.offE[:, 32 * c:32 * c + 32]), F.Copy, ["X", "offE0"], ["mL%d" % c], 512, CG)
-    for c in range(8 - BUILD_ON_S, 8):
-        sl = slice(512 * c, 512 * c + 512)
-        Bc, Rc = T.mid[:, 0:512], T.mid[:, 512:1024]
-        act(Bc, T.Xs[:].indirect(T.offE[:, 256 + 32 * c:256 + 32 * c + 32]), F.Copy, ["X", "offE1"], ["mid0"], 512, CG)
-        mm([(T.pB0[:], T.I[:], Bc, 512), (T.pB0[:], T.nI[:], T.mL[:, sl], 512)], ["I", "nI", "mid0", "mL%d" % c], ["pB0"])
-        act(Rc, T.pB0[:], F.Relu, ["pB0"], ["mid1"], 512)
-        mm([(T.pB1[:], T.I[:], T.mL[:, sl], 512), (T.pB1[:], T.I[:], Rc, 512)], ["I", "mL%d" % c, "mid1"], ["pB1"])
-        act(T.Win[:, BASE[1] + 512 * c:BASE[1] + 512 * c + 512], T.pB1[:], F.Copy, ["pB1"], ["H%d" % c], 512)
-        mm([(T.pB0[:], T.I[:], Bc, 512), (T.pB0[:], T.nI[:], Rc, 512)], ["I", "nI", "mid0", "mid1"], ["pB0"])
-        act(T.Win[:, BASE[2] + 512 * c:BASE[2] + 512 * c + 512], T.pB0[:], F.Copy, ["pB0"], ["Lw%d" % c], 512)
+        act(T.mL[:, 512 * c:512 * c + 512], T.Xs[:].indirect(T.offE[:, 32 * c:32 * c + 32]), F.Copy, ["X", "offE0"], units("mL", 512 * c, 512 * c + 512), 512, CG)
     for c0, c1_ in ((0, 1), (1, 2), (2, 4), (4, 6), (6, 8)):
-        c1_ = min(c1_, 8 - BUILD_ON_S)
-        if c1_ <= c0:
-            continue
         for r, o, kk in ((1, A.max, "H"), (2, A.min, "Lw")):
             tt(T.Win[:, BASE[r] + 512 * c0:BASE[r] + 512 * c1_], T.Xs[:].indirect(T.offE[:, 256 + 32 * c0:256 + 32 * c1_]), T.mL[:, 512 * c0:512 * c1_], o,
-               ["X", "offE1"] + ["mL%d" % c for c in range(c0, c1_)], ["%s%d" % (kk, c) for c in range(c0, c1_)], 512 * (c1_ - c0), CG)
+               ["X", "offE1"] + units("mL", 512 * c0, 512 * c1_), ch(kk, c1_, c0), 512 * (c1_ - c0), CG)
     for c in range(8):
         gcopy(T.Win[:, 512 * c:512 * c + 512], T.Eraw[:, 512 * c:512 * c + 512], ["Eraw%d" % (c // 2)], ["E%d" % c], 512)
-    kE_, kH, kL, kS = ch("E"), ch("H") + ["dum1"], ch("Lw") + ["dum2"], ["S", "dum3"]
+    kE_, kH, kL, kS = ch("E"), ch("H") + ["dum1"], ch("Lw") + ["dum2"], ["S0", "S1", "dum3"]
     kEall = kE_ + ["dum0", "VNh", "VNw"]
     kid = ch("id", 8)
     kdm = ["dm0", "dm"]
 
-    for b in range(16):
-        mm([(T.pM1[:, 0:256], wsl(T.W32, b), T.Win[:, 256 * b:256 * b + 256], 256)], ["W32", "E%d" % (b // 2)], ["pM1"], b == 0, b == 15, 4)
-    act(T.S0[:], T.pM1[:, 0:256], F.Copy, ["pM1"], ["S0"], 256)
-    dma("Y", [(T.Win[0::16, BASE[3]:BASE[3] + V_], T.S0[:])], ["S0"], ["S"], 0.2)
+    def edge_sums():
+        for c in range(8):
+            mms([(T.pM[:, 128 * (c // 4) + j % 16:128 * (c // 4) + 128:16], T.Win[:, 128 * j:128 * j + 128], T.W32[:, 15:143:16], 8) for j in range(4 * c, 4 * c + 4)],
+                ["W32", "E%d" % c], ["pM"], 4)
+        act(T.S0[:, 0:256], T.pM[:, 0:256], F.Copy, ["pM"], ["Sa"], 256)
+        for u in range(2):
+            op("T", lambda u=u: te.transpose(T.pM[:, 256 + 128 * u:384 + 128 * u], T.S0[:, 128 * u:128 * u + 128], T.I32[:]), ["Sa", "I32"], ["pM"], 0.02, 512)
+        act(T.S0[:, 256:512], T.pM[:, 256:512], F.Copy, ["pM"], ["Sb"], 256)
+        dma("Y", [(T.Win[0::16, BASE[3] + 2048 * u:BASE[3] + 2048 * u + 2048], T.S0[:, 256 + 128 * u:384 + 128 * u]) for u in range(2)], ["Sb"], ["S0", "S1"], 0.2)
+
+    if not LATE:
+        edge_sums()
 
     def sm(i):
         return T.sm[:, 16 * i:16 * i + 16]
 
-    def si(i):
-        return T.si[:, 16 * i:16 * i + 16]
+    def si(i, h=None):
+        return T.si[:, 16 * i:16 * i + 16] if h is None else T.si[:, 16 * i + MH * h:16 * i + MH * h + MH]
 
     def ki(i):
         return T.ki[:, 16 * i:16 * i + 16]
@@ -326,204 +376,271 @@ def build_ops(g, T, topo, core, nxt, own):
     def s16(i, n=1):
         return T.s16[:, 16 * i:16 * (i + n)]
 
-    def n2l(out, w, kw_, src, ksrc, bank, const=None, kconst=(), first=True, last=True, a0=0):
-        items = [(out, const, T.ones[:, 0:16], 16)] if const is not None else []
-        items += [(out, wsl(w, b), src[:, a0 + b:a0 + 256:16], 16) for b in range(16)]
-        mm(items, [kw_, ksrc, "onesa"] + list(kconst), [bank], first, last)
+    def part(ap16, a0, h, parts=HV):
+        w = 16 // parts
+        return ap16[:, a0 + w * h:a0 + w * h + w]
 
     flip = [0]
     mid2k = (T.cmid[:], ["cmid"])
     for t in range(NV):
-        z, L16, v16 = T["zq%d" % t], T["Lq%d" % t], T["vq%d" % t]
-        zw, Lin, ain, ma, mb = T["zin%d" % t], T["Lin%d" % t], T["ain%d" % t], T["a%d" % t], T["b%d" % t]
-        lb, lbin, hs, hin = T["lb%d" % t], T["lbin%d" % t], T["h%d" % t], T["hin%d" % t]
-        zin0, zin1, zin2 = zw[:, 256:512], zw[:, 512:1024], zw[:, 256:1024]
-        kz_, kv, kzi, kLi, kai, kbi, khi = "z%d" % t, "v%d" % t, "zin%d" % t, "Lin%d" % t, "ain%d" % t, "bin%d" % t, "hin%d" % t
-        ctau, ktau = T.ctau[:, 128 * t:128 * t + 128], ["ctau%d" % t]
+        z, L16, zd, zc, Lin, xv, xin = [T["%s%d" % (name, t)] for name in ("zq", "Lq", "zd", "zc", "Lin", "xv", "xin")]
+        v16, ma, ain, lb, lbin, hs, hin = [T[name][:, 16 * t:16 * t + 16] for name in ("vq", "wa", "wain", "lb", "lbin", "hs", "hin")]
+        m0_ = 0 if XSEND else 512 * t
+        mba, mbb = T.mb[:, m0_:m0_ + 256], T.mb[:, m0_ + 256:m0_ + 512]
+        kz_, kv, kzi, kLi, kai, khi = ch("z%d_" % t, ZH), ch("v%d_" % t, HV), "zin%d" % t, "Lin%d" % t, "ain%d" % t, "hin%d" % t
+        kbi = ["bina%d" % t, "binb%d" % t]
+        ctau, ktau = T.ctau[:, 128 * t:128 * t + 128], ["ctau%da" % t, "ctau%db" % t]
         last = t == NV - 1
-        send([(zin0, z[:])], "mz_%d" % t, [kz_], [kzi], 0.065)
+        send([(zd[:, h, 0:EH], z[:, EH * h:EH * h + EH]) for h in range(HV)], "mz_%d" % t, kz_, [kzi], 0.065)
         send([(Lin[:], L16[:])], "m1_%d" % t, ["L%d" % t], [kLi], 0.065)
         if last:
-            send([(T.zfin[:, 0:256], z[:])], "mzo", [kz_], ["zfin0"], 0.03, own)
+            send([(T.zfin[:, 0:256], z[:])], "mzo", kz_, ["zfin0"], 0.03, own)
 
         for h in range(2):
-            mm([(T.pA1[:, 128 * h:128 * h + 128], z[:, 128 * h:128 * h + 128], T.I[:], 128)], [kz_, "I"], ["pA1"])
-        act(T.nzW[:], T.pA1[:, 0:256], F.Copy, ["pA1"], ["nzW"], 256, 1.0, -1.0)
+            mm([(T.pA1[:, 128 * h:128 * h + 128], z[:, 128 * h:128 * h + 128], T.I[:], 128)], [kz_[h * ZH // 2], "I"], ["pA1"])
+            if ZH == 2 or h == 1:
+                a_ = 128 * h if ZH == 2 else 0
+                act(T.nzW[:, a_:128 * h + 128], T.pA1[:, a_:128 * h + 128], F.Copy, ["pA1"], ["nzW%d" % h] if ZH == 2 else ch("nzW", 2), 128 * h + 128 - a_, 1.0, -1.0)
+        kc16 = ch("c16_", HV)
         if t == 0:
-            cp(T.c16[:], T.Eraw[:].indirect(v16[:]), ch("Eraw", 4) + [kv], ["c16"], 256, CG)
-        gcopy(T.cfr[:], T.c16[:], ["c16"], ["cfr"], 256)
+            cp(T.c16[:], T.Eraw[:].indirect(v16), ch("Eraw", 4) + kv, kc16, 256, CG)
+        gcopy(T.cfr[:], T.c16[:], kc16, ["cfr"], 256)
         act(T.cf[:], T.cfr[:], F.Identity, ["cfr", kmid], ["cf"], 256, 1.0, 1.0, cmid)
-        if t > 0:
-            tt(T.neq[:], win(0, V_).indirect(v16[:]), T.cfr[:], A.not_equal, kE_ + [kv, "cfr"], ["neq"], 256, CG)
         mm([(T.pK[:, 0:256], T.I[:], T.kcb[:], 256)], ["I", "kcb"], ["pK"], True, False)
+        if t > 0:
+            tt(T.neq[:], win(0, V_).indirect(v16), T.cfr[:], A.not_equal, kE_ + kv + ["cfr"], ["neq"], 256, CG)
+            n2l(T.pK[:, 0:256:16], T.Wf, "Wf", T.neq, ["neq"], "pK", acc="K%d" % t)
         for c in range(8):
             sl = slice(512 * c, 512 * c + 512)
             bank = "pA%d" % (c % 2)
             src = T.Xs[:].indirect(T.c16[:, 32 * c:32 * c + 32])
+            kc = kc16[c * HV // 8]
             if c in WALK_ON_V[t]:
-                cp(T.xg[:, sl], src, ["X", "c16"], ["xg%d" % c], 512, CG)
-            else:
-                act(T.xg[:, sl], src, F.Copy, ["X", "c16"], ["xg%d" % c], 512, CG)
+                cp(T.xg[:, sl], src, ["X", kc], ["xg%d" % c], 512, CG)
+            elif XGW == 2 and c % 2 == 0 and c + 1 not in WALK_ON_V[t]:
+                act(T.xg[:, 512 * c:512 * c + 1024], T.Xs[:].indirect(T.c16[:, 32 * c:32 * c + 64]), F.Copy, ["X", kc], ["xg%d" % c, "xg%d" % (c + 1)], 1024, CG)
+            elif XGW == 1 or c % 2 == 0 or c - 1 in WALK_ON_V[t]:
+                act(T.xg[:, sl], src, F.Copy, ["X", kc], ["xg%d" % c], 512, CG)
             h, cc = c // 4, c % 4
             mm([(T[bank][:], T.nzW[32 * cc:32 * cc + 32, 128 * h:128 * h + 128], T.R1[32 * cc:32 * cc + 32, :], 512), (T[bank][:], T.I[:], T.xg[:, sl], 512)],
-               ["nzW", "R1", "I", "xg%d" % c], [bank])
+               ["nzW%d" % h, "R1", "I", "xg%d" % c], [bank])
             act(T.absd[:, 2 * c:2 * c + 2, :], T[bank][:], F.Abs, [bank], ["ab%d" % c], 512)
             if (c + 1) % SUMQ == 0:
                 m0, m1 = 2 * (c + 1 - SUMQ), 2 * (c + 1)
-                if c == 7 and t > 0:
-                    n2l(T.pK[:, 0:256:16], T.Wf, "Wf", T.neq, "neq", "pK", None, (), False, False)
                 mm([(T.pK[:, 16 * m0:16 * m1], wsl(T.WK, b), T.absd[:, m0:m1, 16 * b:16 * b + 16], 32 * SUMQ) for b in range(16)],
-                   ["WK"] + ["ab%d" % j for j in range(c + 1 - SUMQ, c + 1)], ["pK"], False, c == 7)
+                   ["WK"] + ["ab%d" % j for j in range(c + 1 - SUMQ, c + 1)], ["pK"], acc="K%d" % t)
         scan(T.scK[:], T.rK[:], T.pK[:, 0:256], A.add, A.min, ["rK", "pK"], ["scK"])
         cp(ki(0), T.scK[:, 15::16], ["scK"], ["ki0"])
         ts(ki(1), ki(0), 1023, None, A.bitwise_and, None, ["ki0"], ["ki1"])
         cp(T.k16[:], ki(1), ["ki1"], ["k16"])
         tt(T.selc[:], T.dm[:, 0:528 if t else 32].indirect(T.k16[:]), T.cf[:], A.mult, kdm[0:2 if t else 1] + ["k16", "cf"], ["selc"], 256, CG)
-        n2l(T.pK[:, 256:272], T.W1, "W1", T.selc, "selc", "pK", *mid2k)
-        act(lb[:], T.scK[:, 15::16], F.Identity, ["scK"], ["lb%d" % t], 16, 1.0, -2.0 ** 19, (TH * 1024 + 1023.5) * 2.0 ** 19)
-        cp(ma[:], T.pK[:, 256:272], ["pK"], ["ma%d" % t])
-        send([(ain[:], ma[:]), (lbin[:], lb[:])], "m2a_%d" % t, ["ma%d" % t, "lb%d" % t], [kai], 0.02)
-        act(T.xv[:], T.Xs[:].indirect(ma[:]), F.Copy, ["X", "ma%d" % t], ["xv"], 256, CG)
-        mm([(T.pA1[:, 0:256], T.hI[:], z[:], 256), (T.pA1[:, 0:256], T.hI[:], T.xv[:], 256)], ["hI", kz_, "xv"], ["pA1"])
-        mm([(T.pA0[:, 0:256], T.I[:], z[:], 256), (T.pA0[:, 0:256], T.nI[:], T.xv[:], 256)], ["I", "nI", kz_, "xv"], ["pA0"])
-        ts(mb[:, 0:256], T.pA1[:, 0:256], 1.5 * 2.0 ** 23, -1.5 * 2.0 ** 23, A.add, A.add, ["pA1"], ["mba%d" % t], 256)
-        act(mb[:, 256:512], T.pA0[:, 0:256], F.Abs, ["pA0"], ["mbb%d" % t], 256)
-        n2l(T.pA1[:, 256:272], T.Wh, "Wh", mb, "mba%d" % t, "pA1")
+        n2l(T.pK[:, 256:272], T.W1, "W1", T.selc, ["selc"], "pK", *mid2k)
+        act(lb, T.scK[:, 15::16], F.Identity, ["scK"], ["lb%d" % t], 16, 1.0, 2.0 ** 31, -(TH * 1024 + 1023.5) * 2.0 ** 31)
+        cp(ma, T.pK[:, 256:272], ["pK"], ["ma%d" % t])
+        send([(ain, ma), (lbin, lb)], "m2a_%d" % t, ["ma%d" % t, "lb%d" % t], [kai], 0.02)
+        act(xv[:], T.Xs[:].indirect(ma), F.Copy, ["X", "ma%d" % t], ["xv%d" % t], 256, CG)
+
+        def results(zs, kzs, xs, kx, half, khalf, like, klike, b0, b1):
+            for h, za in enumerate(zs):
+                w_ = 256 // len(zs)
+                sl = slice(w_ * h, w_ * h + w_)
+                mm([(T[b0][:, sl], T.hI[:], za, w_), (T[b0][:, sl], T.hI[:], xs[:, sl], w_)], ["hI", kx] + kzs, [b0])
+            ts(half, T[b0][:, 0:256], 1.5 * 2.0 ** 23, -1.5 * 2.0 ** 23, A.add, A.add, [b0], [khalf], 256)
+            for h, za in enumerate(zs):
+                w_ = 256 // len(zs)
+                sl = slice(w_ * h, w_ * h + w_)
+                mm([(T[b1][:, sl], T.I[:], za, w_), (T[b1][:, sl], T.nI[:], xs[:, sl], w_)], ["I", "nI", kx] + kzs, [b1])
+            act(like, T[b1][:, 0:256], F.Abs, [b1], [klike], 256)
+
+        if XSEND and not last:
+            send([(xin[:], xv[:])], "m2b_%d" % t, ["xv%d" % t], ["xin%d" % t], 0.065)
+            mm([(T.pA1[:, 0:256], T.hI[:], z[:], 256), (T.pA1[:, 0:256], T.hI[:], xv[:], 256)], ["hI", "xv%d" % t] + kz_, ["pA1"])
+            act(T.hf[:], T.pA1[:, 0:256], F.Identity, ["pA1", k1k], ["hf"], 256, 1.0, 1.0, c1k)
+            n2l(T.pA1[:, 256:272], T.Wh, "Wh", T.hf, ["hf"], "pA1")
+        else:
+            results([z[:]], kz_, xv, "xv%d" % t, mba, "mba%d" % t, mbb, "mbb%d" % t, "pA1", "pA0")
+            n2l(T.pA1[:, 256:272], T.Wh, "Wh", T.mb, ["mba%d" % t], "pA1", a0=m0_)
         cp(ki(2), T.pA1[:, 256:272], ["pA1"], ["ki2"])
         ts(ki(3), ki(2), 4095, None, A.bitwise_and, None, ["ki2"], ["ki3"])
-        gcopy(hs[:], ki(3), ["ki3"], ["h%d" % t], 16)
-        send([(hin[:], hs[:])], "mh_%d" % t, ["h%d" % t], [khi], 0.01)
+        gcopy(hs, ki(3), ["ki3"], ["h%d" % t], 16)
+        send([(hin, hs)], "mh_%d" % t, ["h%d" % t], [khi], 0.01)
         if not last:
-            send([(zin1, mb[:])], "m2b_%d" % t, ["mba%d" % t, "mbb%d" % t, "h%d" % t], [kbi], 0.13)
+            if not XSEND:
+                send([(zc[:, 256:768], T.mb[:, m0_:m0_ + 512])], "m2b_%d" % t, ["mba%d" % t, "mbb%d" % t, "h%d" % t], kbi, 0.13)
         else:
-            send([(T.zfin[:, 256:768], mb[:])], "m2b_%d" % t, ["mba%d" % t, "mbb%d" % t, "h%d" % t], ["zfin1"], 0.06, own)
-            if not LOG_BY_S:
-                gcopy(fin("Lg"), L16[:], ["L%d" % t], ["Lg"], 256)
-            gcopy(fin("Lg", 16 * t, 16 * t + 16), ma[:], ["ma%d" % t], ["Lg"], 16)
+            send([(T.zfin[:, 256:768], T.mb[:, m0_:m0_ + 512])], "m2b_%d" % t, ["mba%d" % t, "mbb%d" % t, "h%d" % t], ["zfin1"], 0.06, own)
+            gcopy(fin("Lg"), L16[:], ["L%d" % t], ["Lg"], 256)
+            for h in range(HV):
+                gcopy(fin("Lg", EH * h + MH * t, EH * h + MH * t + MH), part(T.wa, 16 * t, h), ["ma%d" % t], ["Lg"], MH)
             act(fin("Ln"), fin("Lg").indirect(lists["iL"]), F.Copy, ["Lg", "liL"], ["Ln"], 256, CG)
             turn(fin("Lp"), fin("Ln"), ["Ln"], ["Lp"])
             act(fin("Lr"), fin("Lp").indirect(lists["p2"]), F.Copy, ["Lp", "lp2"], ["Lr"], 256, CG)
-            for sg, w in enumerate((T.Wp0, T.Wp1)):
-                mm([(T.pA0[:, 256 + 128 * sg:384 + 128 * sg], w[:, 16 - 16 * u:144 - 16 * u], fin("Lr", 128 * u, 128 * u + 128), 128) for u in range(2)],
-                   ["Wp0", "Wp1", "Lr"], ["pA0"], True, True, 4)
-            act(fin("Lrow"), T.pA0[:, 256:512], F.Copy, ["pA0"], ["Lrow"], 256)
+            r0, l0 = 256 * FIN.index("Lrow"), 256 * FIN.index("Lr")
+            dma("Y", [(T.fin[16 * gi:16 * gi + 16, r0:r0 + 256], T.fin[32 * (gi // 2):32 * (gi // 2) + 32, l0 + 128 * (gi % 2):l0 + 128 * (gi % 2) + 128]) for gi in range(8)],
+                ["Lr"], ["Lrow"], 0.1)
             send([(T.Lfin[:], fin("Lrow"))], "mLo", ["Lrow"], ["Lfin"], 0.06, own)
 
-        gcopy(zw[:, 0:256], zin0, [kzi], ["zd%d" % t], 256)
-        gcopy(T.Lf[:], Lin[:], [kLi], ["Lf"], 256)
-        slot = T.Lf[:, 16 * t:16 * t + 16]
-        gcopy(slot, T.nc[:, 16 * (2 + t):16 * (3 + t)], ["nc"], ["Lf"], 16)
-        mm([(T.pG[:, 0:256], ctau, T.ones[:], 256), (T.pG[:, 16 * t:16 * t + 16], T.cmid[:], T.cneg[:], 16)], ["onesa", "cmid", "cneg"] + ktau, ["pG"], True, False)
-        for c in range(8):
-            k0, k1_ = 2 * c + (2 * c == t), 2 * c + 2 - (2 * c + 1 == t)
-            w_ = 256 * (k1_ - k0)
-            sl = slice(256 * k0, 256 * k1_)
-            offs = Lin[:, 16 * k0:16 * k1_]
-            zt, zrd = zw[:, 512 - w_:512], [kzi] + (["zd%d" % t] if w_ > 256 else [])
-            if c >= 8 - CUT_ON_S[t]:
-                for r, kr, out, ko in ((1, kH, T.mH, "mH"), (2, kL, T.mL, "mL")):
-                    j = flip[0] % 4
-                    flip[0] += 1
-                    bank, mid = "pB%d" % (j % 2), T.mid[:, 512 * j:512 * j + w_]
-                    act(mid, win(r).indirect(offs), F.Copy, kr + [kLi], ["mid%d" % j], w_, CG)
-                    mm([(T[bank][:, 0:w_], T.nI[:], zt, w_), (T[bank][:, 0:w_], T.I[:], mid, w_)], zrd + ["I", "nI", "mid%d" % j], [bank])
-                    act(out[:, sl], T[bank][:, 0:w_], F.Relu, [bank], ["%s%d" % (ko, c)], w_)
-            else:
-                tt(T.mH[:, sl], win(1).indirect(offs), zt, A.max, kH + [kLi] + zrd, ["mH%d" % c], w_, CG)
-                tt(T.mL[:, sl], win(2).indirect(offs), zt, A.max, kL + [kLi] + zrd, ["mL%d" % c], w_, CG)
-            if c % 2 == 1:
-                qd = c // 2
-                for w, kw_, src, ks_ in ((T.WM, "WM", T.mH, "mH"), (T.WP, "WP", T.mL, "mL")):
-                    mm([(T.pG[:, 64 * qd:64 * qd + 64], wsl(w, b), src[:, 1024 * qd + b:1024 * qd + 1024:16], 64) for b in range(16)],
-                       [kw_, "%s%d" % (ks_, c - 1), "%s%d" % (ks_, c)], ["pG"], False, c == 7 and kw_ == "WP")
-        tt(T.key[:], T.pG[:, 0:256], T.Lf[:], A.max, ["pG", "Lf"], ["key"], 256, 1.0)
-        act(T.keyT[:], T.key[:].indirect(lists["sig"]), F.Copy, ["key", "lsig"], ["keyT"], 256, CG)
-        scan(T.scG[:], T.rG[:], T.keyT[:], A.add, A.min, ["rG", "keyT"], ["scG"])
-
-        tt(T.Ht[:, 0:256], win(1).indirect(ain[:]), zin0, A.max, kH + [kai, kzi], ["Hta"], 256, CG)
-        tt(T.Ht[:, 256:512], win(2).indirect(ain[:]), zin0, A.max, kL + [kai, kzi], ["Htb"], 256, CG)
-        n2l(T.pM0[:, 0:16], T.WM, "WM", T.Ht, "Hta", "pM0", ctau, ktau, True, False)
-        n2l(T.pM0[:, 0:16], T.WP, "WP", T.Ht, "Htb", "pM0", None, (), False, True, 256)
-        act(T.Win[:, WN + 256:WN + 512], T.ident[:].indirect(ain[:]), F.Copy, kid + [kai] , ["VNw"], 256, CG)
-        act(T.Win[:, WN:WN + 256], T.ident[:].indirect(hin[:]), F.Copy, kid + [khi], ["VNh"], 256, CG)
-        gcopy(sm(0), ain[:], [kai], ["sm0"], 16)
-        act(sm(1), sm(0), F.Identity, ["sm0"], ["sm1"], 16, 1.0, 1.0, -8192.0 * (15 - t))
-        tt(sm(2), sm(1), lbin[:], A.max, ["sm1", kai], ["sm2"])
-        tt(sm(3), lbin[:], T.nc[:, 0:16], A.min, [kai, "nc"], ["sm3"])
-        tt(sm(4), T.scG[:, 15::16], sm(3), A.max, ["scG", "sm3"], ["sm4"])
-        tt(sm(5), T.pM0[:, 0:16], sm(2), A.max, ["pM0", "sm2"], ["sm5"])
-        tt(si(0), sm(5), sm(4), A.min, ["sm4", "sm5"], ["si0"])
-        ts(si(1), si(0), 8191, None, A.bitwise_and, None, ["si0"], ["u"])
-        cp(s16(0), si(1), ["u"], ["u16"])
-        ts(T.ech[:], win(0, WE).indirect(s16(0)), -2048.0, None, A.add, None, kEall + ["u16"], ["ech"], 256, CG)
-        n2l(T.pM0[:, 16:32], T.Wr0, "Wr0", T.ech, "ech", "pM0", *mid2k)
-        vn, kvn = T["vq%d" % (t + 1)], "v%d" % (t + 1)
-        cp(vn[:], T.pM0[:, 16:32], ["pM0"], [kvn])
-        ts(si(2), si(0), 13, None, A.arith_shift_right, None, ["si0"], ["f"])
-        tt(sm(6), si(0), T.nc[:, 16:32], A.max, ["si0", "nc"], ["sm6"])
-        if last:
-            ts(T.fz[:, 0:16], si(2), 15.0, None, A.add, None, ["f"], ["fza"])
-            ts(T.fz[:, 16:32], sm(6), -float(NC), None, A.add, None, ["sm6"], ["fzb"])
-            send([(T.fzin[:], T.fz[:])], "mf", ["fza", "fzb"], ["fzin"], 0.01)
-            send([(T.vin[:], vn[:])], "mv", [kvn], ["vin"], 0.01)
-        else:
-            cp(T.c16[:], win(0, V_).indirect(vn[:]), kE_ + [kvn], ["c16"], 256, CG)
-            ts(s16(1), sm(6), -float(NC), None, A.add, None, ["sm6"], ["zo16"])
-            act(T["zq%d" % (t + 1)][:], zin2.indirect(s16(1)), F.Copy, [kzi, kbi, "zo16"], ["z%d" % (t + 1)], 256, CG)
-            gcopy(slot, ain[:], [kai], ["Lf"], 16)
-            tt(T.eq[:], si(2).indirect(lists["xm"]), T.kcM[:], A.is_equal, ["f", "lxm", "kcM"], ["eq"], 256, CG)
-            tt(sm(7), T.pM0[:, 16:32], si(1), A.subtract, ["pM0", "u"], ["sm7"])
-            tt(T.dl[:], sm(7).indirect(lists["xm"]), T.eq[:], A.mult, ["sm7", "lxm", "eq"], ["dl"], 256, CG)
-            mm([(T.pB0[:, 0:256], T.I32[:], T.Lf[:], 256)], ["I32", "Lf"], ["pB0"], True, False, 4)
-            mm([(T.pB0[:, 0:256], T.I32[:], T.dl[:], 256)], ["I32", "dl"], ["pB0"], False, True, 4)
-            if LOG_BY_S:
-                act(fin("Lg"), T.pB0[:, 0:256], F.Copy, ["pB0"], ["Lg"], 256)
-                gcopy(T["Lq%d" % (t + 1)][:], fin("Lg"), ["Lg"], ["L%d" % (t + 1)], 256)
-            else:
-                cp(T["Lq%d" % (t + 1)][:], T.pB0[:, 0:256], ["pB0"], ["L%d" % (t + 1)], 256)
-
-        act(T.ur[:], T.ident[:].indirect(s16(0)), F.Copy, kid + ["u16"], ["ur"], 256, CG)
-        tt(T.eq2[:], si(1).indirect(lists["x16"]), T.ur[:], A.is_equal, ["u", "lx16", "ur"], ["eq2"], 256, CG)
-        gcopy(sm(8), s16(0), ["u16"], ["sm8"], 16)
-        y = T.pG[:, 288:304]
-        mm([(y, T.I32[:], sm(8), 16)], ["I32", "sm8"], ["pG"], True, False, 4)
-        mm([(y, T.Wt[:, 128 * b:128 * b + 128], T.eq2[:, b::16], 16) for b in range(1, 16)], ch("Wt", 16) + ["eq2"], ["pG"], False, True)
-        mm([(T.pM1[:, 256:512], T.csum[:], T.ones[:], 256), (T.pM1[:, 256:512], wsl(T.Ws, 0), T.ech[:], 256)], ["onesa", "csum", "Ws", "ech"], ["pM1"])
+        n_ = EH
+        kzd = {1: [kzi]}
+        while n_ < 512:
+            gcopy(zd[:, :, n_:2 * n_], zd[:, :, 0:n_], kzd[n_ // EH], ["zd%d_%d" % (t, n_)], HV * n_)
+            for j in range(n_ // EH + 1, 2 * n_ // EH + 1):
+                kzd[j] = kzd[n_ // EH] + ["zd%d_%d" % (t, n_)]
+            n_ *= 2
         if not last:
-            for r in range(4):
-                ts(T.o16[:, AT[r]:64:4], y, cdum, float(BASE[r] - (BASE[1] if SPLIT and AT[r] > 1 else 0)), A.min, A.add, ["pG", kdum], ["o%d" % r])
-            mm([(T.pM1[:, 0:256], T.cmid[:], T.ones[:], 256), (T.pM1[:, 0:256], T.Rot[:], T.ech[:], 256)], ["onesa", "cmid", "Rot", "ech"], ["pM1"])
-            act(T.vals[:, :, 0:16], T.pM1[:, 0:256], F.Copy, ["pM1"], ["val0"], 256)
-            act(T.vals[:, :, 16:32], T.pM1[:, 256:512], F.Copy, ["pM1"], ["val3"], 256)
-            n2l(T.pB1[:, 0:16], T.Wr1, "Wr1", T.ech, "ech", "pB1", *mid2k)
-            n2l(T.pB1[:, 16:32], T.Wr2, "Wr2", T.ech, "ech", "pB1", *mid2k)
-            cp(s16(2, 2), T.pB1[:, 0:32], ["pB1"], ["ab16"])
-            act(T.An[:, 0:512], T.Xs[:].indirect(s16(2, 2)), F.Copy, ["X", "ab16"], ["An"], 512, CG)
-            An, Bn, Rn = T.An[:, 0:256], T.An[:, 256:512], T.An[:, 512:768]
-            mm([(T.pB1[:, 0:256], T.I[:], Bn, 256), (T.pB1[:, 0:256], T.nI[:], An, 256)], ["I", "nI", "An"], ["pB1"])
-            act(Rn, T.pB1[:, 0:256], F.Relu, ["pB1"], ["Rn"], 256)
-            mm([(T.pB1[:, 0:256], T.I[:], An, 256), (T.pB1[:, 0:256], T.I[:], Rn, 256)], ["I", "An", "Rn"], ["pB1"])
-            mm([(T.pB1[:, 256:512], T.I[:], Bn, 256), (T.pB1[:, 256:512], T.nI[:], Rn, 256)], ["I", "nI", "An", "Rn"], ["pB1"])
-            act(T.vals[:, :, 32:48], T.pB1[:, 0:256], F.Copy, ["pB1"], ["val1"], 256)
-            act(T.vals[:, :, 48:64], T.pB1[:, 256:512], F.Copy, ["pB1"], ["val2"], 256)
-            for m in range(16):
-                if SPLIT:
-                    cp(T.Win[:, BASE[1]:].indirect(T.o16[:, 4 * m + 2:4 * m + 4]), T.vals[:, m, 32:64], ["val1", "val2", "o1", "o2"], kH + kL, 32, CS)
-                    cp(T.Win[:, 0:BASE[1]].indirect(T.o16[:, 4 * m:4 * m + 2]), T.vals[:, m, 0:32], ["val0", "val3", "o0", "o3"], kEall + kS, 32, CS)
+            gcopy(zc[:, 0:256], zd[:, :, 0:EH], [kzi], ["zc%d" % t], 256)
+            if XSEND:
+                results([zd[:, h, 0:EH] for h in range(HV)], [kzi], xin, "xin%d" % t, zc[:, 256:512], kbi[0], zc[:, 512:768], kbi[1], "pM", "pM")
+        act(T.Win[:, VB + 256:VB + 512], T.ident[:].indirect(ain), F.Copy, kid + [kai], ["VNw"], 256, CG)
+        act(T.Win[:, VB:VB + 256], T.ident[:].indirect(hin), F.Copy, kid + [khi], ["VNh"], 256, CG)
+        vn = T.vq[:, 16 * (t + 1):16 * (t + 2)]
+        kvn = ch("v%d_" % (t + 1), HV)
+        for h in range(HV):
+            pG, kG, grp = T["pG%d" % h], "pG%d" % h, "G%d_%d" % (t, h)
+            lf0 = KW * h + MH
+            gcopy(T.Lf[:, lf0:lf0 + EH], Lin[:, EH * h:EH * h + EH], [kLi], ["Lf%d" % h], EH)
+            if not TSEP:
+                gcopy(T.Lf[:, lf0 + MH * t:lf0 + MH * t + MH], part(T.wain, 16 * t, h), [kai], ["Lf%d" % h], MH)
+            mm([(pG[:, a_:min(a_ + 256, 17 * MH)], ctau, T.ones[:, 0:min(256, 17 * MH - a_)], min(256, 17 * MH - a_)) for a_ in range(0, 17 * MH, 256)]
+               + [(pG[:, a_:a_ + MH], T.cmid[:], T.cbig[:, 0:MH], MH) for a_ in ((0, MH + MH * t) if TSEP else ())], ["onesa", "cmid", "cbig"] + ktau, [kG], True, False)
+            if not TSEP:
+                mm([(pG[:, 0:MH], T.I[:], part(T.lbin, 16 * t, h), MH)], ["I", kai], [kG], acc=grp)
+            kg_ = 64 // MH
+            pieces = []
+            for k0 in range(0, 16, kg_):
+                runs = [(k0, k0 + kg_)] if not k0 <= t < k0 + kg_ else [(k0, t), (t + 1, k0 + kg_)]
+                pieces += [(a_, min(a_ + DUP, b_)) for a0_, b_ in runs for a_ in range(a0_, b_, DUP)]
+            on_s = pieces[len(pieces) - CUT_ON_S[t][h]:] if CUT_ON_S[t][h] else []
+            top = on_s[0][0] if on_s else 16
+            for k0, k1_ in pieces + ([] if TSEP else [(t, t + 1)]):
+                e0, w_ = 16 * EH * h + EH * k0, EH * (k1_ - k0)
+                sl = slice(e0, e0 + w_)
+                if k0 == t:
+                    offs, ko = part(T.wain, 16 * t, h), kai
                 else:
-                    cp(T.Win[:].indirect(T.o16[:, 4 * m:4 * m + 4]), T.vals[:, m, :], ch("val", 4) + ch("o", 4), kEall + kH + kL + kS, 64, CS)
+                    offs, ko = Lin[:, EH * h + MH * k0:EH * h + MH * k1_], kLi
+                zt, zrd = zd[:, h, 0:w_], kzd[k1_ - k0]
+                tt(T.mL[:, sl], win(2).indirect(offs), zt, A.max, kL + [ko] + zrd, units("mL", e0, e0 + w_), w_, CG)
+                if (k0, k1_) in on_s:
+                    j = flip[0] % 2
+                    flip[0] += 1
+                    bank, mid = "pB%d" % j, T.mid[:, 512 * j:512 * j + w_]
+                    act(mid, win(1).indirect(offs), F.Copy, kH + [ko], ["mid%d" % j], w_, CG)
+                    mm([(T[bank][:, 0:w_], T.I[:], mid, w_), (T[bank][:, 0:w_], T.nI[:], T.mL[:, sl], w_)], ["I", "nI", "mid%d" % j] + units("mL", e0, e0 + w_), [bank])
+                    act(T.mH[:, sl], T[bank][:, 0:w_], F.Relu, [bank], units("mH", e0, e0 + w_), w_)
+                else:
+                    tt(T.mH[:, sl], win(1).indirect(offs), zt, A.max, kH + [ko] + zrd, units("mH", e0, e0 + w_), w_, CG)
+            low = [(k0, k0 + kg_) for k0 in range(0, top - kg_ + 1, kg_)] or [(0, top)]
+            low[-1] = (low[-1][0], top)
+            for w, kw_, src, ks_, spans in ((T.WM, "WM", T.mH, "mH", [(k0, k0 + kg_) for k0 in range(0, 16, kg_)]), (T.WP, "WP", T.mL, "mL", low)):
+                for k0, k1_ in spans:
+                    e0, e1 = 16 * EH * h + EH * k0, 16 * EH * h + EH * k1_
+                    mm([(pG[:, MH + MH * k0:MH + MH * k1_], wsl(w, b), src[:, e0 + b:e1:16], MH * (k1_ - k0)) for b in range(16)],
+                       [kw_] + units(ks_, e0, e1), [kG], acc=grp)
+            k0 = KW * h
+            tt(T.key[:, k0:k0 + 17 * MH], pG[:, 0:17 * MH], T.Lf[:, k0:k0 + 17 * MH], A.max, [kG, "Lf%d" % h, "Lfc%d" % h], ["key%d" % h], 17 * MH, 1.0)
+            act(T.keyT[:, k0:k0 + KW], T.key[:, k0:k0 + KW].indirect(T.sig[:, 0:KW // 16]), F.Copy, ["key%d" % h, "keyc%d" % h, "lsig"], ["keyT%d" % h], KW, CG)
+            scan(T.scG[:, k0:k0 + KW], T.rG[:], T.keyT[:, k0:k0 + KW], A.add, A.min, ["rG", "keyT%d" % h], ["scG%d" % h], KW)
+            if TSEP:
+                gcopy(T.Lf[:, lf0 + MH * t:lf0 + MH * t + MH], ain, [kai], ["Lf%d" % h], MH)
+                tt(T.Ht[:, 0:256], win(2).indirect(ain), zd[:, 0, 0:256], A.max, kL + [kai, kzi], ["Hta"], 256, CG)
+                tt(T.Ht[:, 256:512], win(1).indirect(ain), zd[:, 0, 0:256], A.max, kH + [kai, kzi], ["Htb"], 256, CG)
+                mm([(T.pG1[:, 0:16], ctau, T.ones[:, 0:16], 16)], ["onesa"] + ktau, ["pG1"], True, False)
+                n2l(T.pG1[:, 0:16], T.WP, "WP", T.Ht, ["Hta"], "pG1", acc="Gt%d" % t)
+                n2l(T.pG1[:, 0:16], T.WM, "WM", T.Ht, ["Htb"], "pG1", a0=256, acc="Gt%d" % t)
+                gcopy(sm(4), ain, [kai], ["sm4"], 16)
+                act(sm(5), sm(4), F.Identity, ["sm4"], ["sm5"], 16, 1.0, 1.0, -8192.0 * (16 - t))
+                tt(sm(6), lbin, T.nc[:, 48:64], A.max, [kai, "ncl"], ["sm6"])
+                tt(sm(7), T.scG[:, SEG - 1:KW:SEG], sm(6), A.min, ["scG0", "sm6"], ["sm7"])
+                tt(sm(8), T.pG1[:, 0:16], sm(5), A.max, ["pG1", "sm5"], ["sm8"], 16, 1.0)
+                tt(si(0), sm(8), sm(7), A.min, ["sm7", "sm8"], ["si0_0"])
+            else:
+                cp(si(0, h), T.scG[:, k0 + SEG - 1:k0 + KW:SEG], ["scG%d" % h], ["si0_%d" % h])
+            ts(si(1, h), si(0, h), 8191, None, A.bitwise_and, None, ["si0_%d" % h], ["u%d" % h])
+            cp(part(T.s16, 0, h), si(1, h), ["u%d" % h], ["u16_%d" % h])
+            if ECH_ON_S:
+                act(T.ech[:, EH * h:EH * h + EH], win(0, WE).indirect(part(T.s16, 0, h)), F.Identity, kEall + ["u16_%d" % h, kmid], ["ech%d" % h], EH, CG, 1.0, cmid)
+            else:
+                ts(T.ech[:, EH * h:EH * h + EH], win(0, WE).indirect(part(T.s16, 0, h)), -2048.0, None, A.add, None, kEall + ["u16_%d" % h], ["ech%d" % h], EH, CG)
+            n2l(pG[:, 288:288 + MH], T.Wr0, "Wr0", T.ech, ["ech%d" % h], kG, *mid2k, a0=EH * h, n=EH)
+            cp(part(T.vq, 16 * (t + 1), h), pG[:, 288:288 + MH], [kG], [kvn[h]])
+            if not last:
+                cp(T.c16[:, EH * h:EH * h + EH], win(0, V_).indirect(part(T.vq, 16 * (t + 1), h)), kE_ + [kvn[h]], [kc16[h]], EH, CG)
+        ku, ku16, ksi, kech = ch("u", HV), ch("u16_", HV), ch("si0_", HV), ch("ech", HV)
+        ts(si(2), si(0), 13, None, A.arith_shift_right, None, ksi, ["f"])
+        if last:
+            tt(sm(0), si(1), T.nc[:, 0:16], A.max, ku + ["nc"], ["sm0"])
+            ts(T.fz[:, 0:16], si(2), 17.0, None, A.add, None, ["f"], ["fza"])
+            ts(T.fz[:, 16:32], sm(0), -float(VB - 256), None, A.add, None, ["sm0"], ["fzb"])
+            send([(T.fzin[:], T.fz[:])], "mf", ["fza", "fzb"], ["fzin"], 0.01)
+            send([(T.vin[:], vn)], "mv", kvn, ["vin"], 0.01)
         else:
-            ts(T.o16[:, 0:64:4], y, cdum, None, A.min, None, ["pG", kdum], ["o0"])
-            act(T.vals[:, :, 48:64], T.pM1[:, 256:512], F.Copy, ["pM1"], ["val3"], 256)
-            for m in range(16):
-                cp(win(3).indirect(T.o16[:, 4 * m:4 * m + 1]), T.vals[:, m, 48:64], ["val3", "o0"], kS, 16, CS)
+            for h in range(ZH):
+                w_ = 256 // ZH
+                kk = [ku[h]] if ZH == HV else ku
+                tt(part(T.sm, 0, h, ZH), part(T.si, 16, h, ZH), part(T.nc, 0, h, ZH), A.max, kk + ["nc"], ["sm0_%d" % h])
+                ts(part(T.s16, 16, h, ZH), part(T.sm, 0, h, ZH), -float(VB - 256), None, A.add, None, ["sm0_%d" % h], ["zo16_%d" % h])
+                act(T["zq%d" % (t + 1)][:, w_ * h:w_ * h + w_], zc[:].indirect(part(T.s16, 16, h, ZH)), F.Copy, ["zc%d" % t, "zo16_%d" % h] + kbi, ["z%d_%d" % (t + 1, h)], w_, CG)
+            tt(T.eq[:], si(2).indirect(lists["xm"]), T.kcM[:], A.is_equal, ["f", "lxm", "kcM"], ["eq"], 256, CG)
+            gcopy(sm(2), vn, kvn, ["sm2"], 16)
+            tt(sm(1), sm(2), si(1), A.subtract, ["sm2"] + ku, ["sm1"])
+            tt(T.dl[:], sm(1).indirect(lists["xm"]), T.eq[:], A.mult, ["sm1", "lxm", "eq"], ["dl"], 256, CG)
+            mm([(T.pB0[:, EH * h:EH * h + EH], T.I32[:], T.Lf[:, KW * h + MH:KW * h + MH + EH], EH) for h in range(HV)], ["I32"] + ch("Lf", HV), ["pB0"], True, False, 4)
+            mm([(T.pB0[:, 0:256], T.I32[:], T.dl[:], 256)], ["I32", "dl"], ["pB0"], False, True, 4)
+            cp(T["Lq%d" % (t + 1)][:], T.pB0[:, 0:256], ["pB0"], ["L%d" % (t + 1)], 256)
+
+        np_ = LASTH if last else 1
+        for h in range(np_):
+            w_, mw = 256 // np_, 16 // np_
+            sl = slice(w_ * h, w_ * h + w_)
+            pick = (lambda ks_: [ks_[h]]) if np_ == HV else (lambda ks_: ks_)
+            kY = "pG%d" % (h if np_ > 1 else 0)
+            y = T[kY][:, 320:320 + mw]
+            uw, grp = part(T.si, 16, h, np_), "Y%d_%d" % (t, h)
+            act(T.ur[:, sl], T.ident[:].indirect(part(T.s16, 0, h, np_)), F.Copy, kid + pick(ku16), ["ur%d" % h], w_, CG)
+            tt(T.eq2[:, sl], uw.indirect(T.lists[:, 48:48 + mw]), T.ur[:, sl], A.is_equal, pick(ku) + ["lx16", "ur%d" % h], ["eq2%d" % h], w_, CG)
+            gcopy(part(T.sm, 48, h, np_), part(T.s16, 0, h, np_), pick(ku16), ["sm3%d" % h], mw)
+            mm([(y, T.I32[:], part(T.sm, 48, h, np_), mw)], ["I32", "sm3%d" % h], [kY], True, False, 4)
+            mm([(y, T.Wt[:, 128 * b:128 * b + 128], T.eq2[:, w_ * h + b:w_ * h + w_:16], mw) for b in range(1, 16)], ch("Wt", 16, 1) + ["eq2%d" % h], [kY], acc=grp)
+            if PAIR == 2:
+                e0 = 256 + w_ * h
+                tt(T.eq2[:, e0:e0 + w_], uw.indirect(T.lists[:, 64:64 + mw]), T.ur[:, sl], A.is_equal, pick(ku) + ["lx16", "ur%d" % h], ["eq3%d" % h], w_, CG)
+                mm([(T[kY][:, 321:320 + mw:2], wsl(T.WP, b), T.eq2[:, e0 + 16 + b:e0 + w_:32], mw // 2) for b in range(16)], ["WP", "eq3%d" % h], [kY], acc=grp)
+            if t >= LATE:
+                ys = T.pM[:, 256 + w_ * h:256 + w_ * h + w_]
+                mm([(ys, T.csum[:], T.ones[:, 0:w_], w_), (ys, wsl(T.Ws, 0), T.ech[:, sl], w_)], ["onesa", "csum", "Ws"] + pick(kech), ["pM"])
+                act(T.vs[:, 256 * t + w_ * h:256 * t + w_ * h + w_], ys, F.Copy, ["pM"], ["vs%d_%d" % (t, h)], w_)
+            ko = ["o%d_%d_%d" % (t, h, u) for u in range(PAIR)]
+            o0 = 32 * t
+            for u in range(PAIR):
+                ts(T.o16[:, o0 + 2 * mw * h // PAIR + u:o0 + 2 * mw * (h + 1) // PAIR:2], T[kY][:, 320 + u:320 + mw:PAIR], cdum[u][0], None, A.min, None, [kY, cdum[u][1]], [ko[u]])
+            if t >= LATE:
+                for m in range(mw * h, mw * h + mw, PAIR):
+                    cp(win(3).indirect(T.o16[:, o0 + 2 * m // PAIR:o0 + 2 * m // PAIR + PAIR]), T.vs[:, 256 * t + 16 * m:256 * t + 16 * (m + PAIR)],
+                       ["vs%d_%d" % (t, h)] + ko, kS, 16 * PAIR, CS)
+        if last:
             dma("Y", [(T.ya[:, :], T.Win[0::16, BASE[3]:BASE[3] + V_])], kS, ["ya"], 0.2)
+            continue
+        mm([(T.pM[:, 0:256], T.cmid[:], T.ones[:], 256), (T.pM[:, 0:256], T.Rot[:], T.ech[:], 256)], ["onesa", "cmid", "Rot"] + kech, ["pM"])
+        act(T.vals[:, 0:256], T.pM[:, 0:256], F.Copy, ["pM"], ["val0"], 256)
+        n2l(T.pB1[:, 0:16], T.Wr1, "Wr1", T.ech, kech, "pB1", *mid2k)
+        n2l(T.pB1[:, 16:32], T.Wr2, "Wr2", T.ech, kech, "pB1", *mid2k)
+        cp(s16(2, 2), T.pB1[:, 0:32], ["pB1"], ["ab16"])
+        act(T.vals[:, 256:768], T.Xs[:].indirect(s16(2, 2)), F.Copy, ["X", "ab16"], ["An"], 512, CG)
+        tt(T.vals[:, 768:1024], T.Xs[:].indirect(s16(3)), T.vals[:, 256:512], A.min, ["X", "ab16", "An"], ["val2"], 256, CG)
+        for m in range(0, 16, PAIR):
+            offs, n_ = T.o16[:, o0 + 2 * m // PAIR:o0 + 2 * m // PAIR + PAIR], 16 * PAIR
+            tt(win(1).indirect(offs), T.vals[:, 256 + 16 * m:256 + 16 * m + n_], T.vals[:, 512 + 16 * m:512 + 16 * m + n_], A.max, ["An"] + ko, kH, n_, CS)
+            cp(win(2).indirect(offs), T.vals[:, 768 + 16 * m:768 + 16 * m + n_], ["val2"] + ko, kL, n_, CS)
+            cp(win(0).indirect(offs), T.vals[:, 16 * m:16 * m + n_], ["val0"] + ko, kE_ + ["dum0"], n_, CS)
+        if t == LATE - 1:
+            edge_sums()
 
     fl, zl = T.fzin[:, 0:16], T.fzin[:, 16:32]
     act(fin("zo"), T.zfin[:].indirect(zl), F.Copy, ["zfin0", "zfin1", "fzin"], ["zo"], 256, CG)
     dma("Y", [(T.yz[:, :], fin("zo"))], ["zo"], ["yz"], 0.1)
-    act(fin("msk"), T.dm[:].indirect(fl), F.Copy, kdm + ["fzin"], ["msk"], 256, CG)
-    tt(fin("m2"), T.dn[:].indirect(fl), T.Lfin[:], A.mult, ["dn", "fzin", "Lfin"], ["m2"], 256, CG)
+    act(fin("msk"), T.df[:, 0:32].indirect(fl), F.Copy, ["df0", "fzin"], ["msk"], 256, CG)
+    tt(fin("m2"), T.df[:, 32:64].indirect(fl), T.Lfin[:], A.mult, ["df1", "fzin", "Lfin"], ["m2"], 256, CG)
     tt(fin("m1"), T.ident[:].indirect(T.vin[:]), fin("msk"), A.mult, kid + ["vin", "msk"], ["m1"], 256, CG)
     tt(fin("Lo"), fin("m1"), fin("m2"), A.add, ["m1", "m2"], ["Lo"], 256)
     dma("Y", [(T.yl[:, :], fin("Lo"))], ["Lo"], ["yl"], 0.1)
@@ -566,21 +683,35 @@ def order_ops(ops):
         deps = set()
         wr = set(o["wr"]) | set(k for k in o["rd"] if k in BANKS)
         for k in o["rd"]:
-            if k in writer:
-                deps.add(writer[k])
+            deps.update(writer.get(k, ()))
         for k in wr:
-            if k in writer:
-                deps.add(writer[k])
-            deps.update(readers.get(k, ()))
+            if o["acc"] and k in BANKS:
+                deps.add(writer[k][0])
+            else:
+                deps.update(writer.get(k, ()))
+                deps.update(readers.get(k, ()))
         deps.discard(i)
         for k in o["rd"]:
             readers.setdefault(k, []).append(i)
         for k in wr:
-            writer[k] = i
-            readers[k] = []
+            if o["acc"] and k in BANKS:
+                writer[k].append(i)
+            else:
+                writer[k] = [i]
+                readers[k] = []
         o["deps"] = sorted(deps)
-    if "seq" in KEPT:
-        return KEPT["seq"]
+    if "seq" not in KEPT:
+        KEPT["seq"] = find_order(ops)
+    closer = {}
+    for i in KEPT["seq"]:
+        if ops[i]["acc"]:
+            closer[ops[i]["acc"]] = i
+    for i in closer.values():
+        ops[i]["stop"][0] = True
+    return KEPT["seq"]
+
+
+def find_order(ops):
     n = len(ops)
     succ = [[] for _ in range(n)]
     for i, o in enumerate(ops):
@@ -609,86 +740,109 @@ def order_ops(ops):
                 best = (score, seq)
             _s, back = place(ops, succ, pred, [start[i] + dur[i] for i in range(n)], size, True)
             prio = [back[i] + dur[i] for i in range(n)]
-    KEPT["seq"] = improve(ops, best[1], succ, sizes)
-    return KEPT["seq"]
+    return improve(ops, best[1], succ, sizes)
 
 
 def improve(ops, seq, succ, sizes):
     n = len(ops)
+    qi = ["VSTGY".index(o["q"]) for o in ops]
     direct = []
     for o in ops:
         far = set(e for d in o["deps"] for e in ops[d]["deps"] if ops[e]["kind"] == "c")
-        direct.append([(d, o["q"] == "T" == ops[d]["q"]) for d in o["deps"] if d not in far])
-    line = {q: [i for i in seq if ops[i]["q"] == q] for q in "VSTGY"}
+        direct.append([d for d in o["deps"] if d not in far])
+    tabs = [(dur, [[(d, lat[d] + (0.0 if o["q"] == "T" == ops[d]["q"] else gap)) for d in direct[i]] for i, o in enumerate(ops)], lat) for dur, lat, gap in sizes]
+    fixed = [o["kind"] == "d" and not o["deps"] for o in ops]
+    tails = [i for i in range(n) if not succ[i]]
+    dset, sset = [set(o["deps"]) for o in ops], [set(x) for x in succ]
+    seq = list(seq)
 
-    def run():
-        before, after = [-1] * n, [-1] * n
-        for l in line.values():
-            for a, b in zip(l, l[1:]):
-                before[b], after[a] = a, b
-        left = [len(ops[i]["deps"]) + (before[i] >= 0) for i in range(n)]
-        order = [i for i in range(n) if left[i] == 0]
-        for i in order:
-            for j in succ[i]:
-                left[j] -= 1
-                if left[j] == 0:
-                    order.append(j)
-            j = after[i]
-            if j >= 0:
-                left[j] -= 1
-                if left[j] == 0:
-                    order.append(j)
-        if len(order) < n:
-            return None
-        score, paths = 0.0, []
-        for (dur, lat, gap), row in zip(sizes, ROUGH):
-            free, done, why = [0.0] * n, [0.0] * n, [-1] * n
-            for i in order:
-                w = before[i]
-                st = free[w] if w >= 0 else 0.0
-                for d, soft in direct[i]:
-                    x = done[d] if soft else done[d] + gap
+    def run(p0, old):
+        score, out = 0.0, []
+        for r, (dur, dep, lat) in enumerate(tabs):
+            end, why = (list(old[r][0]), list(old[r][1])) if old else ([0.0] * n, [-1] * n)
+            last, need, p = [-1] * 5, 5, p0 - 1
+            while p >= 0 and need:
+                if last[qi[seq[p]]] < 0:
+                    last[qi[seq[p]]] = seq[p]
+                    need -= 1
+                p -= 1
+            for p in range(p0, n):
+                i = seq[p]
+                q = qi[i]
+                w = last[q]
+                st = end[w] if w >= 0 else 0.0
+                for d, x in dep[i]:
+                    x += end[d]
                     if x > st:
                         st, w = x, d
                 why[i] = w
-                free[i] = st + dur[i]
-                done[i] = st + dur[i] + lat[i]
-            end = max(done)
-            score += end / row[0]
-            paths.append((why, done.index(end)))
-        return score, order, paths, before
+                end[i] = st + dur[i]
+                last[q] = i
+            top, at = max((end[i] + lat[i], i) for i in tails)
+            score += (top + PULL * sum(end) / n) / ROUGH[r][0]
+            out.append((end, why, at))
+        return score, out
 
-    now = run()
-    best = (now[0], now[1])
-    x = 12345
+    state = [SEED]
+
+    def draw(k):
+        state[0] = (state[0] * 1103515245 + 12345) % 2147483648
+        return (state[0] >> 8) % k
+
+    now = run(0, None)
+    best = (now[0], list(seq))
+    pos = [0] * n
+    for p, i in enumerate(seq):
+        pos[i] = p
     for step in range(STEPS):
-        x = (x * 1103515245 + 12345) % 2147483648
-        why, i = now[2][(x >> 8) % len(sizes)]
+        end, why, i = now[1][draw(len(tabs))]
         held = []
         while i >= 0:
-            if why[i] >= 0 and why[i] == now[3][i] and why[i] not in ops[i]["deps"] and ops[i]["kind"] != "d":
+            w = why[i]
+            if w >= 0 and qi[w] == qi[i] and w not in dset[i] and not fixed[i] and not fixed[w]:
                 held.append(i)
-            i = why[i]
+            i = w
         if not held:
             continue
-        x = (x * 1103515245 + 12345) % 2147483648
-        b = held[(x >> 8) % len(held)]
-        l = line[ops[b]["q"]]
-        p = l.index(b)
-        x = (x * 1103515245 + 12345) % 2147483648
-        k = 1 + (x >> 8) % 4
-        old = list(l)
-        if (x >> 16) % 2:
-            l.insert(max(0, p - k), l.pop(p))
+        b = held[draw(len(held))]
+        a, q, k = why[b], qi[b], 1 + draw(4)
+        if draw(2):
+            lo, hi, move = pos[b], pos[b] + 1, {b}
+            while lo > 0 and k:
+                lo -= 1
+                k -= qi[seq[lo]] == q
+            for p in range(hi - 2, lo - 1, -1):
+                if sset[seq[p]] & move:
+                    move.add(seq[p])
+            part = seq[lo:hi]
+            if part[0] in move:
+                continue
+            new = [j for j in part if j in move] + [j for j in part if j not in move]
         else:
-            l.insert(min(len(l) - 1, p - 1 + k), l.pop(p - 1))
-        new = run()
-        if new is not None and new[0] <= now[0] * (1.0 + SLACK * (1.0 - step / STEPS)):
-            now = new
+            lo, hi, move = pos[a], pos[a], {a}
+            while hi < n - 1 and k:
+                hi += 1
+                k -= qi[seq[hi]] == q
+            hi += 1
+            for p in range(lo + 1, hi):
+                if dset[seq[p]] & move:
+                    move.add(seq[p])
+            if b in move:
+                continue
+            part = seq[lo:hi]
+            new = [j for j in part if j not in move] + [j for j in part if j in move]
+        if any(fixed[j] for j in move):
+            continue
+        seq[lo:hi] = new
+        got = run(lo, now[1])
+        if got[0] <= now[0] * (1.0 - HOT * (COLD / HOT) ** (step / STEPS) * math.log((draw(10000) + 1) / 10001.0)):
+            now = got
+            for p in range(lo, hi):
+                pos[seq[p]] = p
             if now[0] < best[0]:
-                best = (now[0], now[1])
+                best = (now[0], list(seq))
         else:
-            l[:] = old
+            seq[lo:hi] = part
     return best[1]
 
 

@@ -9,27 +9,34 @@ TH, TAU = 1020, (1020, 1530, 1275)
 HV = 2
 MH = 16 // HV
 EH = 16 * MH
-DUP = 512 // EH
+DUP = 4
 SEG = 18
 KW = SEG * MH
 PAIR = 2
-WN = V_ + 32
-VB = V_ + 256
-WE = VB + 512
-BASE = (0, WE, WE + WN, WE + 2 * WN)
+PAD = 16 * PAIR
+WN = V_ + 2 * PAD
+B_H, B_ID, B_E, B_L, B_S = 0, WN, WN + V_, 2 * WN + V_, 3 * WN + V_
+CUT0 = V_ + PAD
 LATE = 2
-TSEP = False
-ECH_ON_S = True
-FILL_ON_V = ("ctau", "cmid", "csum")
-XGW = 2
 H16, B16, F32 = "float16", "bfloat16", "float32"
-WALK_ON_V = ((1,), (0, 1), (0, 1))
-CUT_ON_S = ((3, 3), (3, 3), (3, 3))
-XSEND = True
+XG = ((1, 1, 2, 2, 2), (1, 1, 2, 2, 2), (1, 1, 2, 2, 2))
+TOP = ((12, 12), (12, 12), (8, 12))
+LOW = ((4, 8, 12), (4, 8, 12), (4, 8, 12))
+NBW = 4
+MIDW = (8, 8)
+HALF_S = (0, 1)
+OLD_S = True
+SCANI = True
+XV = ((), (6,), (6,))
+STAG = (0, 0, 0)
+WTG = 2
+CHAIN = None
+SETA = (1, 1, 2, 2, 2)
+SETB = (1, 1, 2, 2, 2)
 ZH = 1
 LASTH = 2
-FIN = ("Lg", "Ln", "Lp", "Lr", "Lrow", "msk", "m1", "m2", "zo", "Lo", "vo")
-SUMQ = 2
+FIN = ("Lg", "Ln", "Lp", "Lr", "Lrow", "m1", "zo", "Lo", "vo")
+BIG = 2.0 ** 24
 
 
 def _sb(n, d):
@@ -37,59 +44,68 @@ def _sb(n, d):
 
 
 SCRATCH = {
-    "Xs": _sb(V_, B16), "Eraw": _sb(V_, "int32"), "Win": _sb(BASE[3] + WN, F32), "ident": _sb(WE, F32),
-    "xg": _sb(V_, B16), "absd": ("sbuf", [128, 16, 256], B16), "mH": _sb(V_, B16), "mL": _sb(V_, B16),
-    "mid": _sb(1024, B16), "R1": _sb(512, B16), "Wt": _sb(2048, B16),
+    "Xs": _sb(V_, B16), "Eraw": _sb(V_, "int32"), "Win": _sb(B_S + WN, F32),
+    "xg": _sb(V_, B16), "absd": ("sbuf", [128, 256, 16], B16),
+    "mH": ("sbuf", [128, HV, 16 * EH], B16), "mL": ("sbuf", [128, HV, 16 * EH], B16),
+    "mid": ("sbuf", [128, HV, 16 * EH], B16), "mt": _sb(512, B16), "cI": _sb(128, B16), "ect": _sb(256, H16), "ein": _sb(256, H16), "Sh0": _sb(160, B16), "Sh1": _sb(160, B16), "Bc": _sb(128, B16), "Wt": _sb(2048, B16),
     "nI": _sb(128, B16), "hI": _sb(128, H16), "I32": _sb(128, F32), "I": _sb(128, B16), "ones": _sb(256, B16),
-    "pi": _sb(8, "int32"), "col": _sb(48, F32), "cols": _sb(144, F32),
+    "pi": _sb(8, "int32"), "col": _sb(48, F32), "cols": _sb(160, F32),
     "WK": _sb(144, B16), "WP": _sb(144, B16), "WM": _sb(144, B16), "Wh": _sb(144, B16), "Wf": _sb(144, B16),
-    "W1": _sb(144, B16), "Wr0": _sb(144, B16), "Wr1": _sb(144, B16), "Wr2": _sb(144, B16), "Ws": _sb(144, B16),
+    "W1": _sb(144, B16), "Ws": _sb(144, B16),
     "Rot": _sb(128, B16), "W32": _sb(144, F32),
     "dm": _sb(528, F32), "df": _sb(64, F32),
-    "kcb": _sb(256, B16), "kcM": _sb(256, F32), "rK": _sb(256, F32), "rG": _sb(KW, F32),
-    "c16": _sb(256, "uint16"), "cmid": _sb(128, B16), "csum": _sb(128, B16), "ctau": _sb(384, B16), "nc": _sb(64, F32), "cbig": _sb(16, B16), "Ht": _sb(512, B16),
-    "fi": _sb(192, "int32"), "lists": _sb(128, "uint16"), "sig": _sb(32, "uint16"),
+    "kcb": _sb(256, B16), "kcM": _sb(256, F32), "rK": _sb(256, F32), "rG": _sb(HV * KW, F32),
+    "c16": _sb(256, "uint16"), "cmid": _sb(128, B16), "cneg": _sb(128, B16), "csum": _sb(128, B16), "ctau": _sb(384, B16), "hk": _sb(32, B16),
+    "fi": _sb(128, "int32"), "lists": _sb(128, "uint16"), "sig": _sb(32, "uint16"),
     "raw": _sb(768, "int32"), "t1": _sb(768, F32), "t2": _sb(768, F32), "offE": _sb(512, "uint16"), "S0": _sb(512, F32),
-    "cf": _sb(256, F32), "cfr": _sb(256, F32), "nzW": _sb(256, B16), "neq": _sb(256, B16),
+    "cf": _sb(256, F32), "cfr": _sb(256, F32), "neq": _sb(256, B16),
     "scK": _sb(256, F32), "ki": _sb(80, "int32"), "k16": _sb(16, "uint16"), "selc": _sb(256, H16),
-    "Lf": _sb(288, F32), "key": _sb(288, F32), "keyT": _sb(288, F32), "scG": _sb(288, F32), "hf": _sb(256, H16),
-    "sm": _sb(144, F32), "si": _sb(48, "int32"), "s16": _sb(64, "uint16"), "ech": _sb(256, H16),
-    "eq": _sb(256, F32), "dl": _sb(256, F32), "ur": _sb(256, F32), "eq2": _sb(512, B16),
+    "Lf": ("sbuf", [128, HV, KW], F32), "key": _sb(288, F32), "keyT": _sb(288, F32), "scG": _sb(288, F32), "hf": _sb(256, H16),
+    "sm": _sb(64, F32), "si": _sb(64, "int32"), "s16": _sb(64, "uint16"), "ech": _sb(256, H16),
+    "eq": _sb(256, B16), "dl": _sb(256, F32), "ur": _sb(256, F32), "eq2": _sb(512, B16),
     "o16": _sb(32 * NV, "uint16"), "vals": _sb(1024, F32), "vs": _sb(256 * NV, F32),
-    "fin": _sb(256 * len(FIN), F32),
-    "Lfin": _sb(256, F32), "zfin": _sb(768, B16), "fz": _sb(32, "uint16"), "fzin": _sb(32, "uint16"), "vin": _sb(16, "uint16"),
-    "vq": _sb(16 * (NV + 1), "uint16"),
+    "fin": _sb(256 * len(FIN), F32), "nm": _sb(256, B16),
+    "Lfin": _sb(256, F32), "zfin": _sb(768, B16), "fz": _sb(32, "uint16"), "fzin": _sb(32, "uint16"),
+    "vq": _sb(16 * NV, "uint16"),
     "wa": _sb(16 * NV, "uint16"), "wain": _sb(16 * NV, "uint16"),
     "lb": _sb(16 * NV, B16), "lbin": _sb(16 * NV, B16),
-    "hs": _sb(16 * NV, "uint16"), "hin": _sb(16 * NV, "uint16"),
-    "mb": _sb(512 * (1 if XSEND else NV), B16),
+    "hs": _sb(16 * NV, "int32"), "hin": _sb(16 * NV, "int32"),
+    "mb": _sb(512, B16),
 }
 for _t in range(NV):
     SCRATCH["zq%d" % _t] = _sb(256, B16)
     SCRATCH["Lq%d" % _t] = _sb(256, "uint16")
-    SCRATCH["zd%d" % _t] = ("sbuf", [128, HV, 512], B16)
-    SCRATCH["zc%d" % _t] = _sb(768, B16)
+    SCRATCH["zd%d" % _t] = ("sbuf", [128, HV, DUP * EH], B16)
     SCRATCH["Lin%d" % _t] = _sb(256, "uint16")
     SCRATCH["xv%d" % _t] = _sb(256, B16)
+    SCRATCH["zc%d" % _t] = _sb(768, B16)
+for _t in range(NV - 1):
     SCRATCH["xin%d" % _t] = _sb(256, B16)
-BANKS = ("pA0", "pA1", "pB0", "pB1", "pK", "pG0", "pG1", "pM")
+BANKS = ("pA0", "pA1", "pA2", "pA3", "pK", "pG0", "pG1", "pM")
 for _n in BANKS:
     SCRATCH[_n] = ("psum", [128, 512], F32)
 
-SEMAPHORES = (["cV", "cS", "cT", "cG", "sent", "mv", "mf", "mzo", "mLo"] + ["dma%d" % _i for _i in range(24)]
-              + ["%s_%d" % (_n, _i) for _n in ("m1", "mz", "m2a", "m2b", "mh") for _i in range(NV)])
+SEMAPHORES = (["cV", "cS", "cT", "cG", "sent", "mv0", "mv1", "mf", "mzo", "mLo"] + ["dma%d" % _i for _i in range(24)]
+              + ["%s_%d" % (_n, _i) for _n in ("m1", "mz", "ml", "m2a", "m2b", "mh") for _i in range(NV)])
 
 ROUGH = ((0.0009, 1.5, 3.6, 0.00046, 0.12, 0.55, 2.0, 25.0, 2.8),
          (0.00085, 1.1, 2.0, 0.00042, 0.1, 0.5, 1.8, 20.0, 2.5),
-         (0.001, 1.3, 4.5, 0.0005, 0.18, 0.7, 2.4, 30.0, 2.8),
-         (0.0012, 1.9, 5.0, 0.0006, 0.1, 0.5, 2.0, 22.0, 3.3))
+         (0.0009, 1.3, 4.5, 0.00055, 0.2, 0.9, 3.0, 35.0, 2.8),
+         (0.00124, 2.0, 5.5, 0.00062, 0.12, 0.6, 2.2, 25.0, 3.3))
 HOLD, FIT, EDGE, ROUNDS, TRIES, JITTER = 0.3, 0.05, 1.0, 4, 4, 0.6
-STEPS = 60000
+AHEAD = {"sums": 3}
+STEPS = 500000
+SWAP = 5
+SORT, SPAN = 150, 150
+QS = "VSTGYNM"
+ROWS = 0.012
+LOAD = (0.5, 0.2, 0.0, 0.0, 0.0, 0.0, 0.0)
 SEED = 1
-PULL = 0.3
-HOT = 0.002
-COLD = 0.0001
+PULL = 1.0
+HOT = 0.001
+WARM, COLD, STARTS = 0.0004, 0.0001, 3
 CG, CS, DI = "gather", "scatter", 0.15
+FIX = {"V": 0.05, "S": 0.065, "G": 0.12}
 KEPT = {}
 COUNTER = {"V": "cV", "S": "cS", "T": "cT", "G": "cG"}
 
@@ -101,35 +117,69 @@ def build_ops(g, T, topo, core, nxt, own):
     free = [e for e in topo.engines(core, own) if e not in eng]
     eng_own = free if len(free) == len(eng) else [e for e in topo.engines(core, own) if e in eng]
     nd = [0]
-    early = [False]
+    early, tag = [False], ["start"]
 
-    def op(q, fn, rd, wr, fix, n=0, c=1.0, kind="c", sem=None, inc=1, mb=0.0, acc=None, stop=None):
-        ops.append(dict(q=q, fn=fn, rd=list(rd), wr=list(wr), fix=fix, cyc=n if c in (CG, CS) else max(64, n * c), c=c, kind=kind, sem=sem, n=inc, mb=mb,
-                        early=early[0], acc=acc, stop=stop))
+    def way(q, fn, fix, n, c=1.0):
+        return dict(q=q, fn=fn, fix=fix, cyc=n if c in (CG, CS) else max(64, n * c), c=c)
+
+    def op(q, fn, rd, wr, fix, n=0, c=1.0, kind="c", sem=None, inc=1, mb=0.0, acc=None, stop=None, alt=None):
+        ops.append(dict(way(q, fn, fix, n, c), rd=list(rd), wr=list(wr), kind=kind, sem=sem, n=inc, mb=mb, early=early[0], tag=tag[0], acc=acc, stop=stop, alt=alt))
+
+    def either(first, other, rd, wr):
+        op(first["q"], first["fn"], rd, wr, first["fix"], first["cyc"], first["c"] if first["c"] in (CG, CS) else 1.0, alt=other)
+
+    def w_ts(out, in0, s1, s2, o0, o1, n, c=1.0):
+        if o1 is None:
+            return way("V", lambda: v.tensor_scalar(out, in0, s1, None, o0), FIX["V"], n, c)
+        return way("V", lambda: v.tensor_scalar(out, in0, s1, s2, o0, o1), FIX["V"], n, c)
+
+    def w_cp(out, in_, n, c=1.0):
+        return way("V", lambda: v.tensor_copy(out, in_), FIX["V"], n, c)
+
+    def w_act(out, in_, f, n, c=1.0, scale=1.0, bias=0.0):
+        return way("S", lambda: s.activation(out, in_, f, bias=bias, scale=scale), FIX["S"], n, c)
+
+    def w_sel(out, in_, pat, o, fill, base, cm, n):
+        return way("G", lambda: g.affine_select(out, in_, pat, o, fill, base, cm), FIX["G"], 2 * n + 64)
+
+    def w_gcp(out, in_, n):
+        return w_sel(out, in_, [[0, n]], A.is_equal, 0.0, 0, 0, n)
+
+    def w_iota(out, pat, base, cm, n, small=True):
+        if small:
+            return way("G", lambda: g.iota(out, pat, base, cm, allow_small_or_imprecise_dtypes=True), 0.08, 2 * n + 64)
+        return way("G", lambda: g.iota(out, pat, base, cm), 0.08, 2 * n + 64)
 
     def ts(out, in0, s1, s2, o0, o1, rd, wr, n=16, c=1.0):
-        if o1 is None:
-            op("V", lambda: v.tensor_scalar(out, in0, s1, None, o0), rd, wr, 0.05, n, c)
-        else:
-            op("V", lambda: v.tensor_scalar(out, in0, s1, s2, o0, o1), rd, wr, 0.05, n, c)
+        either(w_ts(out, in0, s1, s2, o0, o1, n, c), None, rd, wr)
 
     def tt(out, in0, in1, o, rd, wr, n=16, c=2.0):
-        op("V", lambda: v.tensor_tensor(out, in0, in1, o), rd, wr, 0.05, n, c)
+        op("V", lambda: v.tensor_tensor(out, in0, in1, o), rd, wr, FIX["V"], n, c)
 
     def cp(out, in_, rd, wr, n=16, c=1.0):
-        op("V", lambda: v.tensor_copy(out, in_), rd, wr, 0.05, n, c)
+        either(w_cp(out, in_, n, c), None, rd, wr)
 
-    def ms(ap, val, wr, n=16, c=1.0):
-        op("V", lambda: v.memset(ap, val), [], wr, 0.05, n, c)
+    def conv(out, in_, rd, wr, n=16, q="V", c=1.0):
+        ways = [w_cp(out, in_, n, c), w_gcp(out, in_, n) if q else None]
+        either(ways[q == "G"], ways[q != "G"], rd, wr)
 
-    def turn(out, in_, rd, wr):
-        op("V", lambda: v.transpose(out, in_), rd, wr, 0.05, 256)
+    def lin(out, in_, rd, wr, n, scale=1.0, bias=0.0, q="S", c=1.0, cv=None):
+        f = F.Copy if isinstance(bias, float) and bias == 0.0 else F.Identity
+        ways = [w_act(out, in_, f, n, c, scale, bias), w_ts(out, in_, scale, bias, A.mult, A.add, n, cv or c)]
+        either(ways[q == "V"], ways[q != "V"], rd, wr)
+
+    def fill(ap, val, key, n, c=1.0, q="V"):
+        ways = [way("V", lambda: v.memset(ap, float(val)), FIX["V"], n, c), w_iota(ap, [[0, n]], int(val), 0, n) if q else None]
+        either(ways[q == "G"], ways[q != "G"], [], [key])
+
+    def turn(out, in_, rd, wr, n=256):
+        op("V", lambda: v.transpose(out, in_), rd, wr, FIX["V"], n)
 
     def scan(out, d0, d1, o0, o1, rd, wr, n=256):
-        op("V", lambda: v.tensor_tensor_scan(out, d0, d1, 0.0, o0, o1), rd, wr, 0.05, n)
+        op("V", lambda: v.tensor_tensor_scan(out, d0, d1, 0.0, o0, o1), rd, wr, FIX["V"], n)
 
     def act(out, in_, f, rd, wr, n, c=1.0, scale=1.0, bias=0.0):
-        op("S", lambda: s.activation(out, in_, f, bias=bias, scale=scale), rd, wr, 0.065, n, c)
+        either(w_act(out, in_, f, n, c, scale, bias), None, rd, wr)
 
     def mm(items, rd, wr, first=True, last=True, x=1, acc=None):
         stop = [last and acc is None]
@@ -150,16 +200,10 @@ def build_ops(g, T, topo, core, nxt, own):
         op("T", fn, rd, wr, 0.02, sum(max(64, it[3]) * x for it in items))
 
     def iota(out, pat, base, cm, wr, n, small=True):
-        if small:
-            op("G", lambda: g.iota(out, pat, base, cm, allow_small_or_imprecise_dtypes=True), [], wr, 0.08, 2 * n + 64)
-        else:
-            op("G", lambda: g.iota(out, pat, base, cm), [], wr, 0.08, 2 * n + 64)
+        either(w_iota(out, pat, base, cm, n, small), None, [], wr)
 
-    def sel(out, in_, pat, o, fill, base, cm, rd, wr, n):
-        op("G", lambda: g.affine_select(out, in_, pat, o, fill, base, cm), rd, wr, 0.12, 2 * n + 64)
-
-    def gcopy(out, in_, rd, wr, n):
-        sel(out, in_, [[0, n]], A.is_equal, 0.0, 0, 0, rd, wr, n)
+    def sel(out, in_, pat, o, fill_, base, cm, rd, wr, n):
+        either(w_sel(out, in_, pat, o, fill_, base, cm, n), None, rd, wr)
 
     def dma(q, pairs, rd, wr, mb):
         name = "dma%d" % nd[0]
@@ -183,27 +227,35 @@ def build_ops(g, T, topo, core, nxt, own):
             else:
                 g.remote_dma_fused([RemoteDMATransfer(dst_ids=[DstId(rid=rid, pnc=pid)], dma_engine_mask=m, remote_sem=T.sem[sem], src=i, dst=o)
                                     for (o, i), m in zip(pairs, masks)], local_sem=T.sem.sent)
-        op("G", fn, rd, wr, 0.0, 0, 1.0, "r", sem, len(es), mb)
+        op("G", fn, rd, ["issued" + sem], 0.0, 0, 1.0, "r", "sent", len(es))
+        op("N" if to == nxt else "M", None, ["issued" + sem], wr, 0.0, 0, 1.0, "n", sem, len(es), mb + ROWS * len(pairs))
 
     def ch(name, n=8, a=0):
         return ["%s%d" % (name, i) for i in range(a, n)]
 
-    def units(name, a, b):
-        return ch(name, (b + 127) // 128, a // 128)
+    def units(name, h, a, b):
+        return ch(name, 16 * h + b, 16 * h + a)
 
     def wsl(w, b):
         return w[:, 15 - b:143 - b]
 
-    def win(r, n=WN):
-        return T.Win[:, BASE[r]:BASE[r] + n]
+    def tab(base, a=0, b=V_):
+        return T.Win[:, base + PAD + a:base + PAD + b]
+
+    def wide(base):
+        return T.Win[:, base:base + WN]
 
     def fin(name, a=0, b=256):
         return T.fin[:, 256 * FIN.index(name) + a:256 * FIN.index(name) + b]
 
+    def spans(sizes):
+        ends = [sum(sizes[:j + 1]) for j in range(len(sizes))]
+        return list(zip([0] + ends[:-1], ends))
+
     def n2l(out, w, kw_, src, ksrc, bank, const=None, kconst=(), a0=0, n=256, x=1, acc=None):
-        items = [(out, const, T.ones[:, 0:n // 16], n // 16)] if const is not None else []
+        items = [(out, const[0], const[1], n // 16)] if const is not None else []
         items += [(out, wsl(w, b), src[:, a0 + b:a0 + n:16], n // 16) for b in range(16)]
-        mm(items, [kw_, "onesa"] + list(ksrc) + list(kconst), [bank], True, True, x, acc)
+        mm(items, [kw_] + list(ksrc) + list(kconst), [bank], True, True, x, acc)
 
     dma("Y", [(T.raw[:, 256 + 128 * u:256 + 128 * u + 128], T.E[16 * u::32, :]) for u in range(2)], [], ["rawE0"], 0.15)
     dma("S", [(T.raw[:, 512 + 128 * u:512 + 128 * u + 128], T.E[16 * u + 1::32, :]) for u in range(2)], [], ["rawE1"], 0.25)
@@ -218,26 +270,24 @@ def build_ops(g, T, topo, core, nxt, own):
     col = T.col
     iota(T.pi[:, 0:1], [[0, 1]], 0, 1, ["pi0"], 1, False)
     names = ("p1", "p2", "pE", "x16", "x2", "xm", "pL", "iL")
-    two = HV == 2
-    pats = ([[16, 8], [128, 2]], [[16, 2], [32, 8]], [[2, 16]], [[1, 16]], [[2, 8], [0, 2]],
-            [[8, 2], [0, 8]] if two else [[0, 16]], [[1, 2], [4, 8]] if two else [[2, 16]], [[1, 8], [64 if two else 128, 2]])
+    pats = ([[16, 8], [128, 2]], [[16, 2], [32, 8]], [[2, 16]], [[1, 16]], [[2, 8], [0, 2]], [[8, 2], [0, 8]], [[1, 2], [4, 8]], [[1, 8], [64, 2]])
     lists = {name: T.lists[:, 16 * j:16 * j + 16] for j, name in enumerate(names)}
     for j in (0, 2, 1):
         iota(T.fi[:, 16 * j:16 * j + 16], pats[j], 0, 0, ["fi" + names[j]], 16, False)
-    iota(T.cols[:], [[1, 144]], 0, 0, ["cols"], 144)
+    iota(T.cols[:], [[1, 160]], 0, 0, ["cols"], 160)
     ts(T.pi[:, 1:2], T.pi[:, 0:1], 15, None, A.bitwise_and, None, ["pi0"], ["pi1"])
     ts(T.pi[:, 2:3], T.pi[:, 0:1], 15, 1, A.bitwise_and, A.arith_shift_right, ["pi0"], ["pi2"])
-    ts(T.pi[:, 3:4], T.pi[:, 0:1], 4, 1, A.arith_shift_right, A.bitwise_and, ["pi0"], ["pi3"])
-    ts(T.pi[:, 4:5], T.pi[:, 0:1], 3, 1, A.arith_shift_right, A.bitwise_and, ["pi0"], ["pi4"])
-    cp(col[:, 0:5], T.pi[:, 0:5], ch("pi", 5), ["colb"])
-    cP, cB, cB1, cU, cB3 = [col[:, j:j + 1] for j in range(5)]
-    ms(T.ones[:, 0:256], 1.0, ["onesa"], 256, 0.5)
+    ts(T.pi[:, 3:4], T.pi[:, 0:1], 3, 1, A.arith_shift_right, A.bitwise_and, ["pi0"], ["pi3"])
+    ts(T.pi[:, 4:5], T.pi[:, 0:1], 4, 1, A.arith_shift_right, A.bitwise_and, ["pi0"], ["pi4"])
+    conv(col[:, 0:5], T.pi[:, 0:5], ch("pi", 5), ["colb"], 5)
+    cP, cB, cB1, cB3, cU = [col[:, j:j + 1] for j in range(5)]
+    fill(T.ones[:, 0:256], 1, "ones", 256, 0.5)
     made = [5]
 
     def column(in0, scale, bias, rd=()):
         j = made[0]
         made[0] += 1
-        act(col[:, j:j + 1], in0, F.Identity, ["colb"] + list(rd), ["col%d" % j], 1, 1.0, scale, bias)
+        lin(col[:, j:j + 1], in0, ["colb"] + list(rd), ["col%d" % j], 1, scale, bias)
         return col[:, j:j + 1], "col%d" % j
 
     c32b, k32b = column(cB, 32.0, 0.0)
@@ -246,89 +296,77 @@ def build_ops(g, T, topo, core, nxt, own):
     ts(lists["pE"], T.fi[:, 32:48], cE, None, A.add, None, ["fipE", kE], ["lpE"])
     cg, kg = column(cB, -1.0, cP)
     cG15, kG15 = column(cg, 1.0, 15.0, [kg])
-    ts(T.W1[:], T.cols[:], cG15, None, A.is_equal, None, ["cols", kG15], ["W1"], 144)
+    ts(T.W1[:], T.cols[:, 0:144], cG15, None, A.is_equal, None, ["cols", kG15], ["W1"], 144)
     ts(T.dm[:, 0:32], T.cols[:, 0:32], cB, None, A.is_equal, None, ["cols", "colb"], ["dm0"], 32)
-    cz, c1, c2 = [T.dm[:, j:j + 1] for j in range(3)]
-    sel(T.I[:], T.ones[:, 0:128], [[-1, 128]], A.is_equal, 0.0, 0, 1, ["onesa"], ["I"], 128)
+    cz = T.dm[:, 0:1]
+    sel(T.I[:], T.ones[:, 0:128], [[-1, 128]], A.is_equal, 0.0, 0, 1, ["ones"], ["I"], 128)
     iota(T.kcb[:], [[0, 16], [1, 16]], 0, 0, ["kcb"], 256)
-    iota(T.mid[:, 0:512], [[1, 32], [0, 16]], 0, 0, ["mid0"], 512)
-    c32p, k32p = column(cU, 16.0, cB)
-    ts(T.R1[:], T.mid[:, 0:512], c32p, None, A.is_equal, None, ["mid0", k32p], ["R1"], 512, 0.5)
     ts(T.rK[:], T.kcb[:], 0.0, 2.0 ** 25, A.is_equal, A.mult, ["kcb"], ["rK"], 256)
     for j in (3, 4, 5, 6, 7):
         iota(T.fi[:, 16 * j:16 * j + 16], pats[j], 0, 0, ["fi" + names[j]], 16, False)
-    iota(T.fi[:, 128:176], [[256, 3], [16, 16]], VB - 256, 0, ["finc"], 48, False)
-    c8b, k8b = column(cB, 8.0, 0.0)
     cn2, kn2 = column(cB1, -2.0, cB)
     cw, kw = column(cz, 16.0, cB, ["dm0"])
     cr1, kr1 = column(cw, 1.0, cg, [kw, kg])
     crot, krot = column(cr1, 1.0, -1.0, [kr1])
     ch_, kh = column(cB, 2.0, 1.0)
     cs, ks = column(cB, 1.0, 1.0)
-    cdum = [column(cB, 1.0, float(V_ + 16 * u)) for u in range(PAIR)]
-    cmid, kmid = column(cB, 0.0, -2048.0)
-    c1k, k1k = column(cB, 0.0, 1024.0)
-    if two:
-        cxm, kxm = column(cB3, -8.0, cB)
-        cpL, kpL = column(cB3, -254.0, c32b, [k32b])
-        c4b, k4b = column(cB, 4.0, 0.0)
-        ciL, kiL = column(cn2, 124.0, c4b, [kn2, k4b])
-    else:
-        (cxm, kxm), (cpL, kpL), (ciL, kiL) = (cB, "colb"), (cE, kE), (c8b, k8b)
-    for name, val, kk in (("WK", 1024.0, ()), ("WP", 2.0 ** 19, ()), ("WM", -2.0 ** 19, ()), ("Wf", 32.0, ()), ("Wh", ch_, [kh]), ("W32", cs, [ks]),
-                          ("Wr0", cz, ["dm0"]), ("Wr1", c1, ["dm0"]), ("Wr2", c2, ["dm0"]), ("Ws", cw, [kw])):
-        act(T[name][:], T.W1[:], F.Copy, ["W1"] + list(kk), [name], 144, 1.0, val)
+    clo = [(cB, "colb")] + [column(cB, 1.0, 16.0 * u) for u in range(1, PAIR)]
+    chi = [column(cB, 1.0, float(CUT0 + 16 * u)) for u in range(PAIR)]
+    cxm, kxm = column(cB3, -8.0, cB)
+    cpL, kpL = column(cB3, -254.0, c32b, [k32b])
+    c4b, k4b = column(cB, 4.0, 0.0)
+    ciL, kiL = column(cn2, 124.0, c4b, [kn2, k4b])
+    for name, val, kk in (("WK", 1024.0, ()), ("WP", BIG, ()), ("WM", -BIG, ()), ("Wf", 32.0, ()), ("Wh", ch_, [kh]), ("W32", cs, [ks]), ("Ws", cw, [kw])):
+        lin(T[name][:], T.W1[:], ["W1"] + list(kk), [name], 144, val, cv=1.0 if name == "W32" else 0.5)
     early[0] = False
-    cp(T.lists[:, 48:80], T.fi[:, 48:80], ["fix16", "fix2"], ["lx16"], 32)
+    c16p, k16p = column(cP, 1.0, 16.0)
+    cU0, kU0 = column(cU, -1.0, 1.0)
+    ts(T.Sh0[:], T.cols[:], c16p, cU0, A.is_equal, A.mult, ["cols", k16p, kU0], ["Sh0"], 160)
+    ts(T.Sh1[:], T.cols[:], c16p, cU, A.is_equal, A.mult, ["cols", k16p, "colb"], ["Sh1"], 160)
+    iota(T.nm[:, 0:128], [[16, 8], [0, 16]], 0, 0, ["nm"], 128)
+    ts(T.Bc[:], T.nm[:, 0:128], cg, cz, A.is_equal, A.mult, ["nm", kg, "dm0"], ["Bc"], 128, 0.5)
+    conv(T.lists[:, 48:80], T.fi[:, 48:80], ["fix16", "fix2"], ["lx16"], 32)
     for name, cc_, kk in (("xm", cxm, kxm), ("pL", cpL, kpL), ("iL", ciL, kiL)):
         j = names.index(name)
         ts(lists[name], T.fi[:, 16 * j:16 * j + 16], cc_, None, A.add, None, ["fi" + name, kk], ["l" + name])
-    ts(T.nc[:, 0:48], T.fi[:, 128:176], cB, None, A.add, None, ["finc", "colb"], ["nc"], 48)
-    if TSEP:
-        ts(T.nc[:, 48:64], T.fi[:, 160:176], cB, -8192.0 * 17, A.add, A.add, ["finc", "colb"], ["ncl"])
-        ms(T.mH[:, 0:256], 0.0, units("mH", 0, 256), 256, 0.5)
-    iota(T.cbig[:], [[0, 16]], 2 ** 23, 0, ["cbig"], 16)
     ts(T.Rot[:], T.cols[:, 0:128], crot, None, A.is_equal, None, ["cols", krot], ["Rot"], 128)
-    ts(T.hI[:], T.I[:], 0.5 - 2.0 ** -11, None, A.mult, None, ["I"], ["hI"], 128, 0.5)
-    act(T.nI[:], T.I[:], F.Copy, ["I"], ["nI"], 128, 1.0, -1.0)
-    act(T.I32[:], T.I[:], F.Copy, ["I"], ["I32"], 128)
-    ts(T.df[:, 0:32], T.cols[:, 0:32], cs, None, A.is_equal, None, ["cols", ks], ["df0"], 32)
-    act(T.df[:, 32:64], T.df[:, 0:32], F.Identity, ["df0"], ["df1"], 32, 1.0, -1.0, 1.0)
+    lin(T.hI[:], T.I[:], ["I"], ["hI"], 128, 0.5 - 2.0 ** -11, cv=0.5)
+    lin(T.nI[:], T.I[:], ["I"], ["nI"], 128, -1.0, cv=0.5)
+    lin(T.I32[:], T.I[:], ["I"], ["I32"], 128)
+    lin(T.cI[:], T.I[:], ["I"], ["cI"], 128, float(CUT0), cv=0.5)
+    ts(T.df[:, 0:32], T.cols[:, 0:32], cs, -float(V_), A.not_equal, A.mult, ["cols", ks], ["df0"], 32)
+    ts(T.df[:, 32:64], T.cols[:, 0:32], cs, -float(V_), A.is_equal, A.mult, ["cols", ks], ["df1"], 32)
     ts(T.col[:, 32:48], T.cols[:, 0:16], cB, 2.0 ** 19, A.is_gt, A.mult, ["cols", "colb"], ["tri"])
     for b in range(1, 16):
-        ts(T.Wt[:, 128 * b:128 * b + 128], wsl(T.W1, b), T.col[:, 32 + b:33 + b], None, A.mult, None, ["W1", "tri"], ["Wt%d" % b], 128, 0.5)
+        if b % WTG:
+            lin(T.Wt[:, 128 * b:128 * b + 128], wsl(T.W1, b), ["W1", "tri"], ["Wt%d" % b], 128, T.col[:, 32 + b:33 + b], q="V", cv=0.5)
+        else:
+            sel(T.Wt[:, 128 * b:128 * b + 128], wsl(T.WP, b), [[1, 128]], A.is_gt, 0.0, 0, -1, ["WP"], ["Wt%d" % b], 128)
     iota(T.keyT[:, 0:KW], [[1, MH], [MH, SEG]], 0, 0, ch("keyT", HV), KW)
     n2l(T.pM[:, 0:KW // 16], T.W32, "W32", T.keyT, ch("keyT", HV), "pM", None, (), 0, KW, 4)
     ts(T.sig[:, 0:KW // 16], T.pM[:, 0:KW // 16], 1.0 / 136, None, A.mult, None, ["pM"], ["lsig"])
-    ms(T.scG[:, 0:KW], -8192.0, ch("scG", HV), KW)
-    sel(T.rG[:], T.scG[:, 0:KW], [[0, MH], [1, SEG]], A.not_equal, 2.0 ** 34, 0, 0, ch("scG", HV), ["rG"], KW)
-    early[0] = False
+    fill(T.rG[:], -2 ** 14, "rG", HV * KW, q="G")
+    either(way("V", lambda: v.memset(T.rG[:, 0::SEG], 2.0 ** 40), FIX["V"], 16), None, [], ["rG"])
+    fill(T.rG[:, 1::SEG], -(2 ** 22 + CUT0), "rG", 16, q="G")
+    lin(T.rG[:, SEG - 1::SEG], T.cols[:, 0:16], ["cols"], ["rG"], 16, 2.0 ** 18, float(2 ** 22 + 15 * 2 ** 14 + CUT0))
+    iota(T.hk[:, 0:18], [[128, 18]], 31 * 128, 0, ["hk"], 18)
 
     for c in range(8):
-        w = WE // 8
-        iota(T.ident[:, c * w:c * w + w], [[1, w]], c * w, 0, ["id%d" % c], w)
-
-    def fill(ap, val, key, n, c=1.0):
-        if key.rstrip("0123456789ab") in FILL_ON_V:
-            ms(ap, float(val), [key], n, c)
-        else:
-            iota(ap, [[0, n]], val, 0, [key], n)
-
-    fill(T.dm[:, 32:528], 0, "dm", 496)
-    act(T.dm[:, 32::32], T.ones[:, 0:16], F.Copy, ["onesa", "dm0"], ["dm"], 16, 1.0, cz)
+        iota(T.Win[:, B_ID + 512 * c:B_ID + 512 * c + 512], [[1, 512]], 512 * c, 0, ["id%d" % c], 512)
+    fill(T.dm[:, 32:528], 0, "dm", 496, q="G")
+    lin(T.dm[:, 32::32], T.ones[:, 0:16], ["ones", "dm0"], ["dm"], 16, cz)
     fill(T.cmid[:], 16, "cmid", 128, 0.5)
+    fill(T.cneg[:], -32, "cneg", 128, 0.5)
     fill(T.csum[:], 17 * 128, "csum", 128, 0.5)
     for t in range(NV):
         top = 16 * ((2 * TAU[t] + 1 + 15) // 16)
-        fill(T.ctau[64:128, 128 * t:128 * t + 128], 4096 * (2 * TAU[t] + 1 - top), "ctau%da" % t, 128, 0.5)
-        fill(T.ctau[0:64, 128 * t:128 * t + 128], 4096 * top, "ctau%db" % t, 128, 0.5)
-    iota(T.kcM[:], [[0, HV], [1, 16], [0, MH]], -16, 0, ["kcM"], 256)
-    for r in range(4):
-        n = VB - V_ if r == 0 else WN - V_
-        fill(T.Win[:, BASE[r] + V_:BASE[r] + V_ + n], 0, "dum%d" % r, n)
+        fill(T.ctau[64:128, 128 * t:128 * t + 128], BIG / 128 * (2 * TAU[t] + 1 - top), "ctau%da" % t, 128, 0.5, None)
+        fill(T.ctau[0:64, 128 * t:128 * t + 128], BIG / 128 * top, "ctau%db" % t, 128, 0.5, None)
+    iota(T.kcM[:], [[0, HV], [1, 16], [0, MH]], 256, 0, ["kcM"], 256)
+    fill(T.Win[:, B_ID - PAD:B_ID], 0, "dumH", PAD, q="G")
+    fill(T.Win[:, B_E:B_E + PAD], 0, "dumE", PAD, q="G")
     for h in range(HV):
-        gcopy(T.Lf[:, KW * h:KW * h + MH], T.nc[:, 32 + MH * h:32 + MH * h + MH], ["nc"], ["Lfc%d" % h], MH)
-        gcopy(T.key[:, KW * h + 17 * MH:KW * h + KW], T.nc[:, 16 + MH * h:16 + MH * h + MH], ["nc"], ["keyc%d" % h], MH)
+        fill(T.key[:, KW * h + 17 * MH:KW * h + KW], 2 ** 24 - 1, "keyc%d" % h, MH, q="G")
 
     for r, src, out, ko, lst in ((1, "rawE0", T.offE[:, 0:256], "offE0", "pE"), (2, "rawE1", T.offE[:, 256:512], "offE1", "pE"), (0, "rawL", T.Lq0[:], "L0", "pL")):
         sl = slice(256 * r, 256 * r + 256)
@@ -336,32 +374,35 @@ def build_ops(g, T, topo, core, nxt, own):
         cp(T.t1[:, sl], T.raw[:, sl].indirect(lists["p1"]), [src, "lp1"], ["t1%d" % r], 256, CG)
         turn(T.t2[:, sl], T.t1[:, sl], ["t1%d" % r], ["t2%d" % r])
         cp(out, T.t2[:, sl].indirect(lists[lst]), ["t2%d" % r, "l" + lst], [ko], 256, CG)
-    cp(T.vq[:, 0:16], T.ki[:, 64:80], ["v0i"], ch("v0_", HV))
+    conv(T.vq[:, 0:16], T.ki[:, 64:80], ["v0i"], ch("v0_", HV))
 
+    tag[0] = "tables"
+    for c0, c1_ in spans(SETA):
+        lin(T.mL[:, c0 // 4, 512 * (c0 % 4):512 * (c0 % 4 + c1_ - c0)], T.Xs[:].indirect(T.offE[:, 32 * c0:32 * c1_]), ["X", "offE0"], units("mL", 0, 4 * c0, 4 * c1_), 512 * (c1_ - c0), c=CG)
+    for c0, c1_ in spans(SETB):
+        for base, o, kk in ((B_H, A.max, "H"), (B_L, A.min, "Lw")):
+            tt(tab(base, 512 * c0, 512 * c1_), T.Xs[:].indirect(T.offE[:, 256 + 32 * c0:256 + 32 * c1_]), T.mL[:, c0 // 4, 512 * (c0 % 4):512 * (c0 % 4 + c1_ - c0)], o,
+               ["X", "offE1"] + units("mL", 0, 4 * c0, 4 * c1_), ch(kk, c1_, c0), 512 * (c1_ - c0), CG)
+    tag[0] = "edges"
     for c in range(8):
-        act(T.mL[:, 512 * c:512 * c + 512], T.Xs[:].indirect(T.offE[:, 32 * c:32 * c + 32]), F.Copy, ["X", "offE0"], units("mL", 512 * c, 512 * c + 512), 512, CG)
-    for c0, c1_ in ((0, 1), (1, 2), (2, 4), (4, 6), (6, 8)):
-        for r, o, kk in ((1, A.max, "H"), (2, A.min, "Lw")):
-            tt(T.Win[:, BASE[r] + 512 * c0:BASE[r] + 512 * c1_], T.Xs[:].indirect(T.offE[:, 256 + 32 * c0:256 + 32 * c1_]), T.mL[:, 512 * c0:512 * c1_], o,
-               ["X", "offE1"] + units("mL", 512 * c0, 512 * c1_), ch(kk, c1_, c0), 512 * (c1_ - c0), CG)
-    for c in range(8):
-        gcopy(T.Win[:, 512 * c:512 * c + 512], T.Eraw[:, 512 * c:512 * c + 512], ["Eraw%d" % (c // 2)], ["E%d" % c], 512)
-    kE_, kH, kL, kS = ch("E"), ch("H") + ["dum1"], ch("Lw") + ["dum2"], ["S0", "S1", "dum3"]
-    kEall = kE_ + ["dum0", "VNh", "VNw"]
+        conv(tab(B_E, 512 * c, 512 * c + 512), T.Eraw[:, 512 * c:512 * c + 512], ["Eraw%d" % (c // 2)], ["E%d" % c], 512, "G")
+    kE_, kH, kL, kS = ch("E"), ch("H"), ch("Lw"), ["S0", "S1"]
     kid = ch("id", 8)
     kdm = ["dm0", "dm"]
 
     def edge_sums():
         for c in range(8):
-            mms([(T.pM[:, 128 * (c // 4) + j % 16:128 * (c // 4) + 128:16], T.Win[:, 128 * j:128 * j + 128], T.W32[:, 15:143:16], 8) for j in range(4 * c, 4 * c + 4)],
+            mms([(T.pM[:, 128 * (c // 4) + j % 16:128 * (c // 4) + 128:16], tab(B_E, 128 * j, 128 * j + 128), T.W32[:, 15:143:16], 8) for j in range(4 * c, 4 * c + 4)],
                 ["W32", "E%d" % c], ["pM"], 4)
-        act(T.S0[:, 0:256], T.pM[:, 0:256], F.Copy, ["pM"], ["Sa"], 256)
+        lin(T.S0[:, 0:256], T.pM[:, 0:256], ["pM"], ["Sa"], 256)
         for u in range(2):
             op("T", lambda u=u: te.transpose(T.pM[:, 256 + 128 * u:384 + 128 * u], T.S0[:, 128 * u:128 * u + 128], T.I32[:]), ["Sa", "I32"], ["pM"], 0.02, 512)
-        act(T.S0[:, 256:512], T.pM[:, 256:512], F.Copy, ["pM"], ["Sb"], 256)
-        dma("Y", [(T.Win[0::16, BASE[3] + 2048 * u:BASE[3] + 2048 * u + 2048], T.S0[:, 256 + 128 * u:384 + 128 * u]) for u in range(2)], ["Sb"], ["S0", "S1"], 0.2)
+        lin(T.S0[:, 256:512], T.pM[:, 256:512], ["pM"], ["Sb"], 256)
+        s0 = B_S + PAD
+        dma("Y", [(T.Win[0::16, s0 + 2048 * u:s0 + 2048 * u + 2048], T.S0[:, 256 + 128 * u:384 + 128 * u]) for u in range(2)], ["Sb"], ["S0", "S1"], 0.2)
 
     if not LATE:
+        tag[0] = "sums"
         edge_sums()
 
     def sm(i):
@@ -380,271 +421,279 @@ def build_ops(g, T, topo, core, nxt, own):
         w = 16 // parts
         return ap16[:, a0 + w * h:a0 + w * h + w]
 
+    def mid2k(n):
+        return (T.cmid[:], T.ones[:, 0:n]), ["cmid", "ones"]
+
+    def edge_list(bank, c0, k, a_, b_):
+        n_ = (b_ - a_) // 32
+        return [(T[bank][:, c0 + m:c0 + 2 * n_:2], T["Sh%d" % m][:, 16 + 16 * (m - u):144 + 16 * (m - u)], T.ect[:, a_ + 16 * u + k:b_:32], n_) for m in range(2) for u in range(2)]
+
     flip = [0]
-    mid2k = (T.cmid[:], ["cmid"])
     for t in range(NV):
-        z, L16, zd, zc, Lin, xv, xin = [T["%s%d" % (name, t)] for name in ("zq", "Lq", "zd", "zc", "Lin", "xv", "xin")]
+        z, L16, zd, Lin, xv, zc = [T["%s%d" % (name, t)] for name in ("zq", "Lq", "zd", "Lin", "xv", "zc")]
         v16, ma, ain, lb, lbin, hs, hin = [T[name][:, 16 * t:16 * t + 16] for name in ("vq", "wa", "wain", "lb", "lbin", "hs", "hin")]
-        m0_ = 0 if XSEND else 512 * t
-        mba, mbb = T.mb[:, m0_:m0_ + 256], T.mb[:, m0_ + 256:m0_ + 512]
         kz_, kv, kzi, kLi, kai, khi = ch("z%d_" % t, ZH), ch("v%d_" % t, HV), "zin%d" % t, "Lin%d" % t, "ain%d" % t, "hin%d" % t
         kbi = ["bina%d" % t, "binb%d" % t]
         ctau, ktau = T.ctau[:, 128 * t:128 * t + 128], ["ctau%da" % t, "ctau%db" % t]
         last = t == NV - 1
-        send([(zd[:, h, 0:EH], z[:, EH * h:EH * h + EH]) for h in range(HV)], "mz_%d" % t, kz_, [kzi], 0.065)
+        tag[0] = "send%d" % t
+        send([(zc[:, 256:512], z[:])], "mz_%d" % t, kz_, [kzi], 0.065)
         send([(Lin[:], L16[:])], "m1_%d" % t, ["L%d" % t], [kLi], 0.065)
         if last:
-            send([(T.zfin[:, 0:256], z[:])], "mzo", kz_, ["zfin0"], 0.03, own)
+            send([(T.zfin[:, 256:512], z[:])], "mzo", kz_, ["zfin0"], 0.03, own)
 
-        for h in range(2):
-            mm([(T.pA1[:, 128 * h:128 * h + 128], z[:, 128 * h:128 * h + 128], T.I[:], 128)], [kz_[h * ZH // 2], "I"], ["pA1"])
-            if ZH == 2 or h == 1:
-                a_ = 128 * h if ZH == 2 else 0
-                act(T.nzW[:, a_:128 * h + 128], T.pA1[:, a_:128 * h + 128], F.Copy, ["pA1"], ["nzW%d" % h] if ZH == 2 else ch("nzW", 2), 128 * h + 128 - a_, 1.0, -1.0)
+        tag[0] = "walk%d" % t
         kc16 = ch("c16_", HV)
         if t == 0:
             cp(T.c16[:], T.Eraw[:].indirect(v16), ch("Eraw", 4) + kv, kc16, 256, CG)
-        gcopy(T.cfr[:], T.c16[:], kc16, ["cfr"], 256)
-        act(T.cf[:], T.cfr[:], F.Identity, ["cfr", kmid], ["cf"], 256, 1.0, 1.0, cmid)
+        conv(T.cfr[:], T.c16[:], kc16, ["cfr"], 256, "G")
+        lin(T.cf[:], T.cfr[:], ["cfr"], ["cf"], 256, 1.0, -2048.0)
         mm([(T.pK[:, 0:256], T.I[:], T.kcb[:], 256)], ["I", "kcb"], ["pK"], True, False)
         if t > 0:
-            tt(T.neq[:], win(0, V_).indirect(v16), T.cfr[:], A.not_equal, kE_ + kv + ["cfr"], ["neq"], 256, CG)
+            tt(T.neq[:], tab(B_E).indirect(v16), T.cfr[:], A.not_equal, kE_ + kv + ["cfr"], ["neq"], 256, CG)
             n2l(T.pK[:, 0:256:16], T.Wf, "Wf", T.neq, ["neq"], "pK", acc="K%d" % t)
-        for c in range(8):
-            sl = slice(512 * c, 512 * c + 512)
-            bank = "pA%d" % (c % 2)
-            src = T.Xs[:].indirect(T.c16[:, 32 * c:32 * c + 32])
-            kc = kc16[c * HV // 8]
-            if c in WALK_ON_V[t]:
-                cp(T.xg[:, sl], src, ["X", kc], ["xg%d" % c], 512, CG)
-            elif XGW == 2 and c % 2 == 0 and c + 1 not in WALK_ON_V[t]:
-                act(T.xg[:, 512 * c:512 * c + 1024], T.Xs[:].indirect(T.c16[:, 32 * c:32 * c + 64]), F.Copy, ["X", kc], ["xg%d" % c, "xg%d" % (c + 1)], 1024, CG)
-            elif XGW == 1 or c % 2 == 0 or c - 1 in WALK_ON_V[t]:
-                act(T.xg[:, sl], src, F.Copy, ["X", kc], ["xg%d" % c], 512, CG)
-            h, cc = c // 4, c % 4
-            mm([(T[bank][:], T.nzW[32 * cc:32 * cc + 32, 128 * h:128 * h + 128], T.R1[32 * cc:32 * cc + 32, :], 512), (T[bank][:], T.I[:], T.xg[:, sl], 512)],
-               ["nzW%d" % h, "R1", "I", "xg%d" % c], [bank])
-            act(T.absd[:, 2 * c:2 * c + 2, :], T[bank][:], F.Abs, [bank], ["ab%d" % c], 512)
-            if (c + 1) % SUMQ == 0:
-                m0, m1 = 2 * (c + 1 - SUMQ), 2 * (c + 1)
-                mm([(T.pK[:, 16 * m0:16 * m1], wsl(T.WK, b), T.absd[:, m0:m1, 16 * b:16 * b + 16], 32 * SUMQ) for b in range(16)],
-                   ["WK"] + ["ab%d" % j for j in range(c + 1 - SUMQ, c + 1)], ["pK"], acc="K%d" % t)
-        scan(T.scK[:], T.rK[:], T.pK[:, 0:256], A.add, A.min, ["rK", "pK"], ["scK"])
-        cp(ki(0), T.scK[:, 15::16], ["scK"], ["ki0"])
-        ts(ki(1), ki(0), 1023, None, A.bitwise_and, None, ["ki0"], ["ki1"])
-        cp(T.k16[:], ki(1), ["ki1"], ["k16"])
+        for c0, c1_ in spans(XG[t]):
+            tag[0] = "walk%d_%d" % (t, c0 // 4)
+            lin(T.xg[:, 512 * c0:512 * c1_], T.Xs[:].indirect(T.c16[:, 32 * c0:32 * c1_]), ["X"] + kc16[c0 * HV // 8:(c1_ - 1) * HV // 8 + 1], ch("xg", c1_, c0), 512 * (c1_ - c0), c=CG,
+                q="V" if c0 in XV[t] else "S")
+        for c in range(4):
+            qs = slice(64 * c, 64 * c + 64)
+            tag[0] = "walk%d_%d" % (t, c // 2)
+            for j in range(2):
+                bank = "pA%d" % ((2 * c + j) % NBW)
+                mm([(T[bank][:, k::8], T.nI[:], z[:, qs], 64) for k in range(8)], ["nI", kz_[c * ZH // 4]], [bank], True, False)
+                mm([(T[bank][:, k::8], T.I[:], T.xg[:, 1024 * c + 8 * j + k:1024 * c + 1024:16], 64) for k in range(8)], ["I"] + ch("xg", 2 * c + 2, 2 * c), [bank], False, True)
+                act(T.absd[:, qs, 8 * j:8 * j + 8], T[bank][:], F.Abs, [bank], ["ab%d" % (2 * c + j)], 512)
+            mm([(T.pK[:, qs], wsl(T.WK, b), T.absd[:, 64 * c + b:64 * c + 64:16, :], 64) for b in range(16)], ["WK"] + ch("ab", 2 * c + 2, 2 * c), ["pK"], acc="K%d" % t)
+        tag[0] = "pick%d" % t
+        if SCANI:
+            scan(T.raw[:, 0:256], T.rK[:], T.pK[:, 0:256], A.add, A.min, ["rK", "pK"], ["scK", "rawL"])
+            ts(ki(1), T.raw[:, 15:256:16], 1023, None, A.bitwise_and, None, ["scK"], ["ki1"])
+        else:
+            scan(T.scK[:], T.rK[:], T.pK[:, 0:256], A.add, A.min, ["rK", "pK"], ["scK"])
+            conv(ki(0), T.scK[:, 15::16], ["scK"], ["ki0"], 16, CHAIN)
+            ts(ki(1), ki(0), 1023, None, A.bitwise_and, None, ["ki0"], ["ki1"])
+        conv(T.k16[:], ki(1), ["ki1"], ["k16"], 16, CHAIN)
         tt(T.selc[:], T.dm[:, 0:528 if t else 32].indirect(T.k16[:]), T.cf[:], A.mult, kdm[0:2 if t else 1] + ["k16", "cf"], ["selc"], 256, CG)
-        n2l(T.pK[:, 256:272], T.W1, "W1", T.selc, ["selc"], "pK", *mid2k)
-        act(lb, T.scK[:, 15::16], F.Identity, ["scK"], ["lb%d" % t], 16, 1.0, 2.0 ** 31, -(TH * 1024 + 1023.5) * 2.0 ** 31)
+        n2l(T.pK[:, 256:272], T.W1, "W1", T.selc, ["selc"], "pK", *mid2k(16))
+        lin(lb, T.raw[:, 15:256:16] if SCANI else T.scK[:, 15::16], ["scK"], ["lb%d" % t], 16, 2.0 ** 38, -(TH * 1024 + 1023.5) * 2.0 ** 38)
         cp(ma, T.pK[:, 256:272], ["pK"], ["ma%d" % t])
-        send([(ain, ma), (lbin, lb)], "m2a_%d" % t, ["ma%d" % t, "lb%d" % t], [kai], 0.02)
-        act(xv[:], T.Xs[:].indirect(ma), F.Copy, ["X", "ma%d" % t], ["xv%d" % t], 256, CG)
+        send([(lbin, lb)], "ml_%d" % t, ["lb%d" % t], ["lbin%d" % t], 0.004)
+        send([(ain, ma)], "m2a_%d" % t, ["ma%d" % t], [kai], 0.004)
+        tag[0] = "hash%d" % t
+        lin(xv[:], T.Xs[:].indirect(ma), ["X", "ma%d" % t], ["xv%d" % t], 256, c=CG)
 
-        def results(zs, kzs, xs, kx, half, khalf, like, klike, b0, b1):
+        def results(zs, kzs, xs, kx, half, khalf, like, klike, b0, b1, between=lambda: None):
             for h, za in enumerate(zs):
                 w_ = 256 // len(zs)
                 sl = slice(w_ * h, w_ * h + w_)
                 mm([(T[b0][:, sl], T.hI[:], za, w_), (T[b0][:, sl], T.hI[:], xs[:, sl], w_)], ["hI", kx] + kzs, [b0])
-            ts(half, T[b0][:, 0:256], 1.5 * 2.0 ** 23, -1.5 * 2.0 ** 23, A.add, A.add, [b0], [khalf], 256)
+            if t in HALF_S:
+                lin(T.t2[:, 0:256], T[b0][:, 0:256], [b0], ["t20"], 256, 1.0, 1.5 * 2.0 ** 23)
+                lin(half, T.t2[:, 0:256], ["t20"], [khalf], 256, 1.0, -1.5 * 2.0 ** 23)
+            else:
+                ts(half, T[b0][:, 0:256], 1.5 * 2.0 ** 23, -1.5 * 2.0 ** 23, A.add, A.add, [b0], [khalf], 256)
+            between()
             for h, za in enumerate(zs):
                 w_ = 256 // len(zs)
                 sl = slice(w_ * h, w_ * h + w_)
                 mm([(T[b1][:, sl], T.I[:], za, w_), (T[b1][:, sl], T.nI[:], xs[:, sl], w_)], ["I", "nI", kx] + kzs, [b1])
             act(like, T[b1][:, 0:256], F.Abs, [b1], [klike], 256)
 
-        if XSEND and not last:
-            send([(xin[:], xv[:])], "m2b_%d" % t, ["xv%d" % t], ["xin%d" % t], 0.065)
-            mm([(T.pA1[:, 0:256], T.hI[:], z[:], 256), (T.pA1[:, 0:256], T.hI[:], xv[:], 256)], ["hI", "xv%d" % t] + kz_, ["pA1"])
-            act(T.hf[:], T.pA1[:, 0:256], F.Identity, ["pA1", k1k], ["hf"], 256, 1.0, 1.0, c1k)
-            n2l(T.pA1[:, 256:272], T.Wh, "Wh", T.hf, ["hf"], "pA1")
-        else:
-            results([z[:]], kz_, xv, "xv%d" % t, mba, "mba%d" % t, mbb, "mbb%d" % t, "pA1", "pA0")
-            n2l(T.pA1[:, 256:272], T.Wh, "Wh", T.mb, ["mba%d" % t], "pA1", a0=m0_)
-        cp(ki(2), T.pA1[:, 256:272], ["pA1"], ["ki2"])
-        ts(ki(3), ki(2), 4095, None, A.bitwise_and, None, ["ki2"], ["ki3"])
-        gcopy(hs, ki(3), ["ki3"], ["h%d" % t], 16)
-        send([(hin, hs)], "mh_%d" % t, ["h%d" % t], [khi], 0.01)
         if not last:
-            if not XSEND:
-                send([(zc[:, 256:768], T.mb[:, m0_:m0_ + 512])], "m2b_%d" % t, ["mba%d" % t, "mbb%d" % t, "h%d" % t], kbi, 0.13)
+            xin = T["xin%d" % t]
+            send([(xin[:], xv[:])], "m2b_%d" % t, ["xv%d" % t], ["xin%d" % t], 0.065)
+            mm([(T.pK[:, 0:256], T.hI[:], z[:], 256), (T.pK[:, 0:256], T.hI[:], xv[:], 256)], ["hI", "xv%d" % t] + kz_, ["pK"])
+            lin(T.hf[:], T.pK[:, 0:256], ["pK"], ["hf"], 256, 1.0, 1024.0)
+            n2l(T.pK[:, 256:272], T.Wh, "Wh", T.hf, ["hf"], "pK", (T.cmid[:], T.hk[:, 0:16]), ["cmid", "hk"])
+            cp(ki(2), T.pK[:, 256:272], ["pK"], ["ki2"])
         else:
-            send([(T.zfin[:, 256:768], T.mb[:, m0_:m0_ + 512])], "m2b_%d" % t, ["mba%d" % t, "mbb%d" % t, "h%d" % t], ["zfin1"], 0.06, own)
-            gcopy(fin("Lg"), L16[:], ["L%d" % t], ["Lg"], 256)
+            def hashed():
+                n2l(T.pK[:, 256:272], T.Wh, "Wh", T.mb, ["mba"], "pK", (T.cmid[:], T.hk[:, 1:17]), ["cmid", "hk"], a0=256)
+                cp(ki(2), T.pK[:, 256:272], ["pK"], ["ki2"])
+            results([z[:]], kz_, xv, "xv%d" % t, T.mb[:, 256:512], "mba", T.mb[:, 0:256], "mbb", "pK", "pK", hashed)
+        ts(hs, ki(2), 63 * 2 ** 18 + V_ - 1, None, A.bitwise_and, None, ["ki2"], ["h%d" % t])
+        send([(hin, hs)], "mh_%d" % t, ["h%d" % t], [khi], 0.015)
+        if last:
+            send([(T.zfin[:, 512 * u:512 * u + 256], T.mb[:, 256 * u:256 * u + 256]) for u in range(2)], "m2b_%d" % t, ["mba", "mbb", "h%d" % t], ["zfin1"], 0.06, own)
+            tag[0] = "rows"
+            conv(fin("Lg"), L16[:], ["L%d" % t], ["Lg"], 256, "G")
             for h in range(HV):
-                gcopy(fin("Lg", EH * h + MH * t, EH * h + MH * t + MH), part(T.wa, 16 * t, h), ["ma%d" % t], ["Lg"], MH)
-            act(fin("Ln"), fin("Lg").indirect(lists["iL"]), F.Copy, ["Lg", "liL"], ["Ln"], 256, CG)
+                conv(fin("Lg", EH * h + MH * t, EH * h + MH * t + MH), part(T.wa, 16 * t, h), ["ma%d" % t], ["Lg"], MH, "G")
+            lin(fin("Ln"), fin("Lg").indirect(lists["iL"]), ["Lg", "liL"], ["Ln"], 256, c=CG)
             turn(fin("Lp"), fin("Ln"), ["Ln"], ["Lp"])
-            act(fin("Lr"), fin("Lp").indirect(lists["p2"]), F.Copy, ["Lp", "lp2"], ["Lr"], 256, CG)
+            lin(fin("Lr"), fin("Lp").indirect(lists["p2"]), ["Lp", "lp2"], ["Lr"], 256, c=CG)
             r0, l0 = 256 * FIN.index("Lrow"), 256 * FIN.index("Lr")
             dma("Y", [(T.fin[16 * gi:16 * gi + 16, r0:r0 + 256], T.fin[32 * (gi // 2):32 * (gi // 2) + 32, l0 + 128 * (gi % 2):l0 + 128 * (gi % 2) + 128]) for gi in range(8)],
                 ["Lr"], ["Lrow"], 0.1)
             send([(T.Lfin[:], fin("Lrow"))], "mLo", ["Lrow"], ["Lfin"], 0.06, own)
 
+        tag[0] = "copies%d" % t
         n_ = EH
-        kzd = {1: [kzi]}
-        while n_ < 512:
-            gcopy(zd[:, :, n_:2 * n_], zd[:, :, 0:n_], kzd[n_ // EH], ["zd%d_%d" % (t, n_)], HV * n_)
+        kzd = {1: ["zd%d" % t]}
+        conv(zd[:, :, 0:EH], zc[:, 256:512], [kzi], kzd[1], 256, "G", 0.5)
+        while n_ < DUP * EH:
+            conv(zd[:, :, n_:2 * n_], zd[:, :, 0:n_], kzd[n_ // EH], ["zd%d_%d" % (t, n_)], HV * n_, "G", 0.5)
             for j in range(n_ // EH + 1, 2 * n_ // EH + 1):
                 kzd[j] = kzd[n_ // EH] + ["zd%d_%d" % (t, n_)]
             n_ *= 2
         if not last:
-            gcopy(zc[:, 0:256], zd[:, :, 0:EH], [kzi], ["zc%d" % t], 256)
-            if XSEND:
-                results([zd[:, h, 0:EH] for h in range(HV)], [kzi], xin, "xin%d" % t, zc[:, 256:512], kbi[0], zc[:, 512:768], kbi[1], "pM", "pM")
-        act(T.Win[:, VB + 256:VB + 512], T.ident[:].indirect(ain), F.Copy, kid + [kai], ["VNw"], 256, CG)
-        act(T.Win[:, VB:VB + 256], T.ident[:].indirect(hin), F.Copy, kid + [khi], ["VNh"], 256, CG)
-        vn = T.vq[:, 16 * (t + 1):16 * (t + 2)]
-        kvn = ch("v%d_" % (t + 1), HV)
+            results([zc[:, 256:512]], [kzi], xin, "xin%d" % t, zc[:, 512:768], kbi[0], zc[:, 0:256], kbi[1], "pM", "pM")
+        kvn, done = ch("v%d_" % (t + 1), HV), []
+
+        def gap(out, kout, low, klow, mid, kmid, bank, w_):
+            mm([(T[bank][:, 0:w_], T.I[:], mid, w_), (T[bank][:, 0:w_], T.nI[:], low, w_)], ["I", "nI"] + kmid + klow, [bank])
+            either(w_act(out, T[bank][:, 0:w_], F.Relu, w_), w_ts(out, T[bank][:, 0:w_], 0.0, None, A.max, None, w_), [bank], kout)
+
+        tag[0] = "late%d" % t
+        tt(T.mt[:, 0:256], tab(B_L).indirect(ain), zc[:, 256:512], A.max, kL + [kai, kzi], ["lowt"], 256, CG)
+        lin(T.mt[:, 256:512], tab(B_H).indirect(ain), kH + [kai], ["midt"], 256, c=CG)
+        gap(T.mH[:, :, EH * t:EH * t + EH], units("mH", 0, t, t + 1) + units("mH", 1, t, t + 1), T.mt[:, 0:256], ["lowt"], T.mt[:, 256:512], ["midt"], "pK", 256)
+        flip[0] = 0
         for h in range(HV):
             pG, kG, grp = T["pG%d" % h], "pG%d" % h, "G%d_%d" % (t, h)
-            lf0 = KW * h + MH
-            gcopy(T.Lf[:, lf0:lf0 + EH], Lin[:, EH * h:EH * h + EH], [kLi], ["Lf%d" % h], EH)
-            if not TSEP:
-                gcopy(T.Lf[:, lf0 + MH * t:lf0 + MH * t + MH], part(T.wain, 16 * t, h), [kai], ["Lf%d" % h], MH)
-            mm([(pG[:, a_:min(a_ + 256, 17 * MH)], ctau, T.ones[:, 0:min(256, 17 * MH - a_)], min(256, 17 * MH - a_)) for a_ in range(0, 17 * MH, 256)]
-               + [(pG[:, a_:a_ + MH], T.cmid[:], T.cbig[:, 0:MH], MH) for a_ in ((0, MH + MH * t) if TSEP else ())], ["onesa", "cmid", "cbig"] + ktau, [kG], True, False)
-            if not TSEP:
-                mm([(pG[:, 0:MH], T.I[:], part(T.lbin, 16 * t, h), MH)], ["I", kai], [kG], acc=grp)
-            kg_ = 64 // MH
-            pieces = []
-            for k0 in range(0, 16, kg_):
-                runs = [(k0, k0 + kg_)] if not k0 <= t < k0 + kg_ else [(k0, t), (t + 1, k0 + kg_)]
-                pieces += [(a_, min(a_ + DUP, b_)) for a0_, b_ in runs for a_ in range(a0_, b_, DUP)]
-            on_s = pieces[len(pieces) - CUT_ON_S[t][h]:] if CUT_ON_S[t][h] else []
-            top = on_s[0][0] if on_s else 16
-            for k0, k1_ in pieces + ([] if TSEP else [(t, t + 1)]):
-                e0, w_ = 16 * EH * h + EH * k0, EH * (k1_ - k0)
-                sl = slice(e0, e0 + w_)
-                if k0 == t:
-                    offs, ko = part(T.wain, 16 * t, h), kai
-                else:
-                    offs, ko = Lin[:, EH * h + MH * k0:EH * h + MH * k1_], kLi
-                zt, zrd = zd[:, h, 0:w_], kzd[k1_ - k0]
-                tt(T.mL[:, sl], win(2).indirect(offs), zt, A.max, kL + [ko] + zrd, units("mL", e0, e0 + w_), w_, CG)
-                if (k0, k1_) in on_s:
-                    j = flip[0] % 2
-                    flip[0] += 1
-                    bank, mid = "pB%d" % j, T.mid[:, 512 * j:512 * j + w_]
-                    act(mid, win(1).indirect(offs), F.Copy, kH + [ko], ["mid%d" % j], w_, CG)
-                    mm([(T[bank][:, 0:w_], T.I[:], mid, w_), (T[bank][:, 0:w_], T.nI[:], T.mL[:, sl], w_)], ["I", "nI", "mid%d" % j] + units("mL", e0, e0 + w_), [bank])
-                    act(T.mH[:, sl], T[bank][:, 0:w_], F.Relu, [bank], units("mH", e0, e0 + w_), w_)
-                else:
-                    tt(T.mH[:, sl], win(1).indirect(offs), zt, A.max, kH + [ko] + zrd, units("mH", e0, e0 + w_), w_, CG)
-            low = [(k0, k0 + kg_) for k0 in range(0, top - kg_ + 1, kg_)] or [(0, top)]
-            low[-1] = (low[-1][0], top)
-            for w, kw_, src, ks_, spans in ((T.WM, "WM", T.mH, "mH", [(k0, k0 + kg_) for k0 in range(0, 16, kg_)]), (T.WP, "WP", T.mL, "mL", low)):
-                for k0, k1_ in spans:
-                    e0, e1 = 16 * EH * h + EH * k0, 16 * EH * h + EH * k1_
-                    mm([(pG[:, MH + MH * k0:MH + MH * k1_], wsl(w, b), src[:, e0 + b:e1:16], MH * (k1_ - k0)) for b in range(16)],
-                       [kw_] + units(ks_, e0, e1), [kG], acc=grp)
+            top = TOP[t][h]
+            tag[0] = "cut%d_%d" % (t, h)
+            conv(T.Lf[:, h, MH:MH + EH], Lin[:, EH * h:EH * h + EH], [kLi], ["Lf%d" % h], EH, "G")
+            conv(T.Lf[:, h, MH + MH * t:2 * MH + MH * t], part(T.wain, 16 * t, h), [kai], ["Lf%d" % h], MH, "G")
+            conv(T.Lf[:, h, 0:MH], part(T.wain, 16 * t, h), [kai], ["Lfc%d" % h], MH, "G")
+            mm([(pG[:, 0:17 * MH], ctau, T.ones[:, 0:17 * MH], 17 * MH)], ["ones"] + ktau, [kG], True, False)
+            mm([(pG[:, 0:MH], T.I[:], part(T.lbin, 16 * t, h), MH)], ["I", "lbin%d" % t], [kG], acc=grp)
+
+            def pieces(cuts, a_, b_):
+                at = sorted(set([a_, b_] + [x for x in list(cuts) + [t, t + 1] if a_ < x < b_]))
+                return [x for x in zip(at[:-1], at[1:]) if x[0] != t]
+
+            def ahead(name, k0):
+                if h or k0 == t or not STAG[t]:
+                    return []
+                done.append("done%d%s%d" % (t, name, k0))
+                return done[-1:]
+
+            def behind(k0):
+                return list(done) if h and k0 != t else []
+
+            for name, base, kk, cuts, a_ in (("mL", B_L, kL, LOW[t], 0), ("mH", B_H, kH, range(top, 16, DUP), top)):
+                for k0, k1_ in pieces(cuts, a_, 16):
+                    e0, e1, w_ = EH * k0, EH * k1_, EH * (k1_ - k0)
+                    tt(T[name][:, h, e0:e1], tab(base).indirect(Lin[:, EH * h + MH * k0:EH * h + MH * k1_]), zd[:, h, 0:w_], A.max,
+                       kk + [kLi] + kzd[k1_ - k0] + behind(k0), units(name, h, k0, k1_) + ahead(name, k0), w_, CG)
+            for k0, k1_ in pieces(range(top - MIDW[h], t, -MIDW[h]), 0, top):
+                lin(T.mid[:, h, EH * k0:EH * k1_], tab(B_H).indirect(Lin[:, EH * h + MH * k0:EH * h + MH * k1_]), kH + [kLi], units("mid", h, k0, k1_), EH * (k1_ - k0), c=CG)
+            for k0, k1_ in pieces(range(top - 4, t, -4), 0, top):
+                sl = slice(EH * k0, EH * k1_)
+                gap(T.mH[:, h, sl], units("mH", h, k0, k1_), T.mL[:, h, sl], units("mL", h, k0, k1_), T.mid[:, h, sl], units("mid", h, k0, k1_), "pA%d" % (flip[0] % 4), EH * (k1_ - k0))
+                flip[0] += 1
+            for w, kw_, name, sums in ((T.WM, "WM", "mH", [(0, 8), (8, 16)]), (T.WP, "WP", "mL", [(top, 16)] if top < 16 else [])):
+                for k0, k1_ in sums:
+                    mm([(pG[:, MH + MH * k0:MH + MH * k1_], wsl(w, b), T[name][:, h, EH * k0 + b:EH * k1_:16], MH * (k1_ - k0)) for b in range(16)],
+                       [kw_] + units(name, h, k0, k1_), [kG], acc=grp)
             k0 = KW * h
-            tt(T.key[:, k0:k0 + 17 * MH], pG[:, 0:17 * MH], T.Lf[:, k0:k0 + 17 * MH], A.max, [kG, "Lf%d" % h, "Lfc%d" % h], ["key%d" % h], 17 * MH, 1.0)
-            act(T.keyT[:, k0:k0 + KW], T.key[:, k0:k0 + KW].indirect(T.sig[:, 0:KW // 16]), F.Copy, ["key%d" % h, "keyc%d" % h, "lsig"], ["keyT%d" % h], KW, CG)
-            scan(T.scG[:, k0:k0 + KW], T.rG[:], T.keyT[:, k0:k0 + KW], A.add, A.min, ["rG", "keyT%d" % h], ["scG%d" % h], KW)
-            if TSEP:
-                gcopy(T.Lf[:, lf0 + MH * t:lf0 + MH * t + MH], ain, [kai], ["Lf%d" % h], MH)
-                tt(T.Ht[:, 0:256], win(2).indirect(ain), zd[:, 0, 0:256], A.max, kL + [kai, kzi], ["Hta"], 256, CG)
-                tt(T.Ht[:, 256:512], win(1).indirect(ain), zd[:, 0, 0:256], A.max, kH + [kai, kzi], ["Htb"], 256, CG)
-                mm([(T.pG1[:, 0:16], ctau, T.ones[:, 0:16], 16)], ["onesa"] + ktau, ["pG1"], True, False)
-                n2l(T.pG1[:, 0:16], T.WP, "WP", T.Ht, ["Hta"], "pG1", acc="Gt%d" % t)
-                n2l(T.pG1[:, 0:16], T.WM, "WM", T.Ht, ["Htb"], "pG1", a0=256, acc="Gt%d" % t)
-                gcopy(sm(4), ain, [kai], ["sm4"], 16)
-                act(sm(5), sm(4), F.Identity, ["sm4"], ["sm5"], 16, 1.0, 1.0, -8192.0 * (16 - t))
-                tt(sm(6), lbin, T.nc[:, 48:64], A.max, [kai, "ncl"], ["sm6"])
-                tt(sm(7), T.scG[:, SEG - 1:KW:SEG], sm(6), A.min, ["scG0", "sm6"], ["sm7"])
-                tt(sm(8), T.pG1[:, 0:16], sm(5), A.max, ["pG1", "sm5"], ["sm8"], 16, 1.0)
-                tt(si(0), sm(8), sm(7), A.min, ["sm7", "sm8"], ["si0_0"])
+            tag[0] = "first%d_%d" % (t, h)
+            tt(T.key[:, k0:k0 + 17 * MH], pG[:, 0:17 * MH], T.Lf[:, h, 0:17 * MH], A.max, [kG, "Lf%d" % h, "Lfc%d" % h], ["key%d" % h], 17 * MH, 1.0)
+            lin(T.keyT[:, k0:k0 + KW], T.key[:, k0:k0 + KW].indirect(T.sig[:, 0:KW // 16]), ["key%d" % h, "keyc%d" % h, "lsig"], ["keyT%d" % h], KW, c=CG)
+            scan(T.scG[:, k0:k0 + KW], T.rG[:, k0:k0 + KW], T.keyT[:, k0:k0 + KW], A.add, A.min, ["rG", "keyT%d" % h], ["scG%d" % h], KW)
+            tt(si(0, h), T.scG[:, k0 + SEG - 1:k0 + KW:SEG], part(T.hin, 16 * t, h), A.min, ["scG%d" % h, khi], ["si0_%d" % h], MH)
+            ts(si(1, h), si(0, h), 2 ** 14 - 1, None, A.bitwise_and, None, ["si0_%d" % h], ["u%d" % h])
+            conv(part(T.s16, 0, h), si(1, h), ["u%d" % h], ["u16_%d" % h], MH, CHAIN)
+            lin(T.ech[:, EH * h:EH * h + EH], T.Win[:, B_ID:B_ID + CUT0 + V_].indirect(part(T.s16, 0, h)), kE_ + kid + ["dumE", "u16_%d" % h], ["ech%d" % h], EH, 1.0, -2048.0, c=CG)
+            if last:
+                send([(T.ein[:, EH * h:EH * h + EH], T.ech[:, EH * h:EH * h + EH])], "mv%d" % h, ["ech%d" % h], ["ein%d" % h], 0.03)
             else:
-                cp(si(0, h), T.scG[:, k0 + SEG - 1:k0 + KW:SEG], ["scG%d" % h], ["si0_%d" % h])
-            ts(si(1, h), si(0, h), 8191, None, A.bitwise_and, None, ["si0_%d" % h], ["u%d" % h])
-            cp(part(T.s16, 0, h), si(1, h), ["u%d" % h], ["u16_%d" % h])
-            if ECH_ON_S:
-                act(T.ech[:, EH * h:EH * h + EH], win(0, WE).indirect(part(T.s16, 0, h)), F.Identity, kEall + ["u16_%d" % h, kmid], ["ech%d" % h], EH, CG, 1.0, cmid)
-            else:
-                ts(T.ech[:, EH * h:EH * h + EH], win(0, WE).indirect(part(T.s16, 0, h)), -2048.0, None, A.add, None, kEall + ["u16_%d" % h], ["ech%d" % h], EH, CG)
-            n2l(pG[:, 288:288 + MH], T.Wr0, "Wr0", T.ech, ["ech%d" % h], kG, *mid2k, a0=EH * h, n=EH)
-            cp(part(T.vq, 16 * (t + 1), h), pG[:, 288:288 + MH], [kG], [kvn[h]])
-            if not last:
-                cp(T.c16[:, EH * h:EH * h + EH], win(0, V_).indirect(part(T.vq, 16 * (t + 1), h)), kE_ + [kvn[h]], [kc16[h]], EH, CG)
+                turn(T.ect[:, EH * h:EH * h + EH], T.ech[:, EH * h:EH * h + EH], ["ech%d" % h], ["ect%d" % h], EH // 2)
+                mm([(pG[:, 288:288 + MH], T.cmid[:], T.ones[:, 0:MH], MH)] + edge_list(kG, 288, 0, EH * h, EH * h + EH), ["cmid", "ones", "Sh0", "Sh1", "ect%d" % h], [kG])
+                cp(part(T.vq, 16 * (t + 1), h), pG[:, 288:288 + MH], [kG], [kvn[h]])
+                cp(T.c16[:, EH * h:EH * h + EH], tab(B_E).indirect(part(T.vq, 16 * (t + 1), h)), kE_ + [kvn[h]], [kc16[h]], EH, CG)
+        tag[0] = "new%d" % t
         ku, ku16, ksi, kech = ch("u", HV), ch("u16_", HV), ch("si0_", HV), ch("ech", HV)
-        ts(si(2), si(0), 13, None, A.arith_shift_right, None, ksi, ["f"])
+        ts(si(2), si(0), 14, 0x30F, A.arith_shift_right, A.bitwise_and, ksi, ["f"])
         if last:
-            tt(sm(0), si(1), T.nc[:, 0:16], A.max, ku + ["nc"], ["sm0"])
-            ts(T.fz[:, 0:16], si(2), 17.0, None, A.add, None, ["f"], ["fza"])
-            ts(T.fz[:, 16:32], sm(0), -float(VB - 256), None, A.add, None, ["sm0"], ["fzb"])
+            ts(si(3), si(0), 14, 0x3F0, A.arith_shift_right, A.bitwise_and, ksi, ["zo"])
+            ts(T.fz[:, 0:16], si(2), -255.0, 17.0, A.add, A.min, ["f"], ["fza"])
+            ts(T.fz[:, 16:32], si(3), cB, None, A.add, None, ["zo", "colb"], ["fzb"])
             send([(T.fzin[:], T.fz[:])], "mf", ["fza", "fzb"], ["fzin"], 0.01)
-            send([(T.vin[:], vn)], "mv", kvn, ["vin"], 0.01)
         else:
             for h in range(ZH):
                 w_ = 256 // ZH
-                kk = [ku[h]] if ZH == HV else ku
-                tt(part(T.sm, 0, h, ZH), part(T.si, 16, h, ZH), part(T.nc, 0, h, ZH), A.max, kk + ["nc"], ["sm0_%d" % h])
-                ts(part(T.s16, 16, h, ZH), part(T.sm, 0, h, ZH), -float(VB - 256), None, A.add, None, ["sm0_%d" % h], ["zo16_%d" % h])
-                act(T["zq%d" % (t + 1)][:, w_ * h:w_ * h + w_], zc[:].indirect(part(T.s16, 16, h, ZH)), F.Copy, ["zc%d" % t, "zo16_%d" % h] + kbi, ["z%d_%d" % (t + 1, h)], w_, CG)
+                ts(part(T.si, 48, h, ZH), part(T.si, 0, h, ZH), 14, 0x3F0, A.arith_shift_right, A.bitwise_and, [ksi[h]] if ZH == HV else ksi, ["zo_%d" % h])
+                ts(part(T.s16, 16, h, ZH), part(T.si, 48, h, ZH), cB, None, A.add, None, ["zo_%d" % h, "colb"], ["zo16_%d" % h])
+                lin(T["zq%d" % (t + 1)][:, w_ * h:w_ * h + w_], zc[:].indirect(part(T.s16, 16, h, ZH)), [kzi, "zo16_%d" % h] + kbi, ["z%d_%d" % (t + 1, h)], w_, c=CG)
+            tag[0] = "turn%d" % t
+            mm([(T.pG0[:, 320:352], T.cmid[:], T.ones[:, 0:32], 32)] + edge_list("pG0", 320, 1, 0, 256) + edge_list("pG0", 336, 2, 0, 256), ["cmid", "ones", "Sh0", "Sh1"] + ch("ect", HV), ["pG0"])
+            cp(s16(2, 2), T.pG0[:, 320:352], ["pG0"], ["ab16"])
+            tag[0] = "logs%d" % t
             tt(T.eq[:], si(2).indirect(lists["xm"]), T.kcM[:], A.is_equal, ["f", "lxm", "kcM"], ["eq"], 256, CG)
-            gcopy(sm(2), vn, kvn, ["sm2"], 16)
+            conv(sm(2), T.vq[:, 16 * (t + 1):16 * (t + 2)], kvn, ["sm2"], 16, "G")
             tt(sm(1), sm(2), si(1), A.subtract, ["sm2"] + ku, ["sm1"])
             tt(T.dl[:], sm(1).indirect(lists["xm"]), T.eq[:], A.mult, ["sm1", "lxm", "eq"], ["dl"], 256, CG)
-            mm([(T.pB0[:, EH * h:EH * h + EH], T.I32[:], T.Lf[:, KW * h + MH:KW * h + MH + EH], EH) for h in range(HV)], ["I32"] + ch("Lf", HV), ["pB0"], True, False, 4)
-            mm([(T.pB0[:, 0:256], T.I32[:], T.dl[:], 256)], ["I32", "dl"], ["pB0"], False, True, 4)
-            cp(T["Lq%d" % (t + 1)][:], T.pB0[:, 0:256], ["pB0"], ["L%d" % (t + 1)], 256)
+            mm([(T.pG0[:, EH * h:EH * h + EH], T.I32[:], T.Lf[:, h, MH:MH + EH], EH) for h in range(HV)], ["I32"] + ch("Lf", HV), ["pG0"], True, False, 4)
+            mm([(T.pG0[:, 0:256], T.cI[:], T.eq[:], 256)], ["cI", "eq"], ["pG0"], False, False)
+            mm([(T.pG0[:, 0:256], T.I32[:], T.dl[:], 256)], ["I32", "dl"], ["pG0"], False, True, 4)
+            cp(T["Lq%d" % (t + 1)][:], T.pG0[:, 0:256], ["pG0"], ["L%d" % (t + 1)], 256)
 
+        tag[0] = "turn%d" % t
         np_ = LASTH if last else 1
         for h in range(np_):
             w_, mw = 256 // np_, 16 // np_
             sl = slice(w_ * h, w_ * h + w_)
             pick = (lambda ks_: [ks_[h]]) if np_ == HV else (lambda ks_: ks_)
-            kY = "pG%d" % (h if np_ > 1 else 0)
+            kY = "pG%d" % (h if np_ > 1 else 1)
             y = T[kY][:, 320:320 + mw]
             uw, grp = part(T.si, 16, h, np_), "Y%d_%d" % (t, h)
-            act(T.ur[:, sl], T.ident[:].indirect(part(T.s16, 0, h, np_)), F.Copy, kid + pick(ku16), ["ur%d" % h], w_, CG)
+            lin(T.ur[:, sl], T.Win[:, PAD:PAD + CUT0 + V_].indirect(part(T.s16, 0, h, np_)), kH + kid + ["dumH"] + pick(ku16), ["ur%d" % h], w_, 1.0, float(CUT0), c=CG)
             tt(T.eq2[:, sl], uw.indirect(T.lists[:, 48:48 + mw]), T.ur[:, sl], A.is_equal, pick(ku) + ["lx16", "ur%d" % h], ["eq2%d" % h], w_, CG)
-            gcopy(part(T.sm, 48, h, np_), part(T.s16, 0, h, np_), pick(ku16), ["sm3%d" % h], mw)
-            mm([(y, T.I32[:], part(T.sm, 48, h, np_), mw)], ["I32", "sm3%d" % h], [kY], True, False, 4)
+            conv(part(T.sm, 48, h, np_), part(T.s16, 0, h, np_), pick(ku16), ["sm3%d" % h], mw, "G")
+            mm([(y, T.I32[:], part(T.sm, 48, h, np_), 4 * 64), (y, T.cneg[:], T.ones[:, 0:mw], mw)], ["I32", "sm3%d" % h, "cneg", "ones"], [kY], True, False)
             mm([(y, T.Wt[:, 128 * b:128 * b + 128], T.eq2[:, w_ * h + b:w_ * h + w_:16], mw) for b in range(1, 16)], ch("Wt", 16, 1) + ["eq2%d" % h], [kY], acc=grp)
-            if PAIR == 2:
-                e0 = 256 + w_ * h
-                tt(T.eq2[:, e0:e0 + w_], uw.indirect(T.lists[:, 64:64 + mw]), T.ur[:, sl], A.is_equal, pick(ku) + ["lx16", "ur%d" % h], ["eq3%d" % h], w_, CG)
-                mm([(T[kY][:, 321:320 + mw:2], wsl(T.WP, b), T.eq2[:, e0 + 16 + b:e0 + w_:32], mw // 2) for b in range(16)], ["WP", "eq3%d" % h], [kY], acc=grp)
+            e0 = 256 + w_ * h
+            tt(T.eq2[:, e0:e0 + w_], uw.indirect(T.lists[:, 64:64 + mw]), T.ur[:, sl], A.is_equal, pick(ku) + ["lx16", "ur%d" % h], ["eq3%d" % h], w_, CG)
+            mm([(T[kY][:, 321:320 + mw:2], wsl(T.WP, b), T.eq2[:, e0 + 16 + b:e0 + w_:32], mw // 2) for b in range(16)], ["WP", "eq3%d" % h], [kY], acc=grp)
             if t >= LATE:
                 ys = T.pM[:, 256 + w_ * h:256 + w_ * h + w_]
-                mm([(ys, T.csum[:], T.ones[:, 0:w_], w_), (ys, wsl(T.Ws, 0), T.ech[:, sl], w_)], ["onesa", "csum", "Ws"] + pick(kech), ["pM"])
-                act(T.vs[:, 256 * t + w_ * h:256 * t + w_ * h + w_], ys, F.Copy, ["pM"], ["vs%d_%d" % (t, h)], w_)
+                mm([(ys, T.csum[:], T.ones[:, 0:w_], w_), (ys, wsl(T.Ws, 0), T.ech[:, sl], w_)], ["ones", "csum", "Ws"] + pick(kech), ["pM"])
+                lin(T.vs[:, 256 * t + w_ * h:256 * t + w_ * h + w_], ys, ["pM"], ["vs%d_%d" % (t, h)], w_)
             ko = ["o%d_%d_%d" % (t, h, u) for u in range(PAIR)]
             o0 = 32 * t
             for u in range(PAIR):
-                ts(T.o16[:, o0 + 2 * mw * h // PAIR + u:o0 + 2 * mw * (h + 1) // PAIR:2], T[kY][:, 320 + u:320 + mw:PAIR], cdum[u][0], None, A.min, None, [kY, cdum[u][1]], [ko[u]])
+                ts(T.o16[:, o0 + mw * h + u:o0 + mw * (h + 1):2], T[kY][:, 320 + u:320 + mw:PAIR], clo[u][0], chi[u][0], A.max, A.min, [kY, clo[u][1], chi[u][1]], [ko[u]])
             if t >= LATE:
                 for m in range(mw * h, mw * h + mw, PAIR):
-                    cp(win(3).indirect(T.o16[:, o0 + 2 * m // PAIR:o0 + 2 * m // PAIR + PAIR]), T.vs[:, 256 * t + 16 * m:256 * t + 16 * (m + PAIR)],
-                       ["vs%d_%d" % (t, h)] + ko, kS, 16 * PAIR, CS)
+                    cp(wide(B_S).indirect(T.o16[:, o0 + m:o0 + m + PAIR]), T.vs[:, 256 * t + 16 * m:256 * t + 16 * (m + PAIR)], ["vs%d_%d" % (t, h)] + ko, kS, 16 * PAIR, CS)
         if last:
-            dma("Y", [(T.ya[:, :], T.Win[0::16, BASE[3]:BASE[3] + V_])], kS, ["ya"], 0.2)
+            dma("Y", [(T.ya[:, :], T.Win[0::16, B_S + PAD:B_S + PAD + V_])], kS, ["ya"], 0.2)
             continue
-        mm([(T.pM[:, 0:256], T.cmid[:], T.ones[:], 256), (T.pM[:, 0:256], T.Rot[:], T.ech[:], 256)], ["onesa", "cmid", "Rot"] + kech, ["pM"])
-        act(T.vals[:, 0:256], T.pM[:, 0:256], F.Copy, ["pM"], ["val0"], 256)
-        n2l(T.pB1[:, 0:16], T.Wr1, "Wr1", T.ech, kech, "pB1", *mid2k)
-        n2l(T.pB1[:, 16:32], T.Wr2, "Wr2", T.ech, kech, "pB1", *mid2k)
-        cp(s16(2, 2), T.pB1[:, 0:32], ["pB1"], ["ab16"])
-        act(T.vals[:, 256:768], T.Xs[:].indirect(s16(2, 2)), F.Copy, ["X", "ab16"], ["An"], 512, CG)
+        mm([(T.pM[:, 0:256], T.cmid[:], T.ones[:], 256), (T.pM[:, 0:256], T.Rot[:], T.ech[:], 256)], ["ones", "cmid", "Rot"] + kech, ["pM"])
+        lin(T.vals[:, 0:256], T.pM[:, 0:256], ["pM"], ["val0"], 256)
+        lin(T.vals[:, 256:768], T.Xs[:].indirect(s16(2, 2)), ["X", "ab16"], ["An"], 512, c=CG)
         tt(T.vals[:, 768:1024], T.Xs[:].indirect(s16(3)), T.vals[:, 256:512], A.min, ["X", "ab16", "An"], ["val2"], 256, CG)
         for m in range(0, 16, PAIR):
-            offs, n_ = T.o16[:, o0 + 2 * m // PAIR:o0 + 2 * m // PAIR + PAIR], 16 * PAIR
-            tt(win(1).indirect(offs), T.vals[:, 256 + 16 * m:256 + 16 * m + n_], T.vals[:, 512 + 16 * m:512 + 16 * m + n_], A.max, ["An"] + ko, kH, n_, CS)
-            cp(win(2).indirect(offs), T.vals[:, 768 + 16 * m:768 + 16 * m + n_], ["val2"] + ko, kL, n_, CS)
-            cp(win(0).indirect(offs), T.vals[:, 16 * m:16 * m + n_], ["val0"] + ko, kE_ + ["dum0"], n_, CS)
+            offs, n_ = T.o16[:, o0 + m:o0 + m + PAIR], 16 * PAIR
+            tt(wide(B_H).indirect(offs), T.vals[:, 256 + 16 * m:256 + 16 * m + n_], T.vals[:, 512 + 16 * m:512 + 16 * m + n_], A.max, ["An"] + ko, kH + ["dumH"], n_, CS)
+            cp(wide(B_L).indirect(offs), T.vals[:, 768 + 16 * m:768 + 16 * m + n_], ["val2"] + ko, kL, n_, CS)
+            cp(wide(B_E).indirect(offs), T.vals[:, 16 * m:16 * m + n_], ["val0"] + ko, kE_ + ["dumE"], n_, CS)
         if t == LATE - 1:
+            tag[0] = "sums"
             edge_sums()
+    tag[0] = "owner"
 
     fl, zl = T.fzin[:, 0:16], T.fzin[:, 16:32]
-    act(fin("zo"), T.zfin[:].indirect(zl), F.Copy, ["zfin0", "zfin1", "fzin"], ["zo"], 256, CG)
-    dma("Y", [(T.yz[:, :], fin("zo"))], ["zo"], ["yz"], 0.1)
-    act(fin("msk"), T.df[:, 0:32].indirect(fl), F.Copy, ["df0", "fzin"], ["msk"], 256, CG)
-    tt(fin("m2"), T.df[:, 32:64].indirect(fl), T.Lfin[:], A.mult, ["df1", "fzin", "Lfin"], ["m2"], 256, CG)
-    tt(fin("m1"), T.ident[:].indirect(T.vin[:]), fin("msk"), A.mult, kid + ["vin", "msk"], ["m1"], 256, CG)
-    tt(fin("Lo"), fin("m1"), fin("m2"), A.add, ["m1", "m2"], ["Lo"], 256)
+    lin(fin("zo"), T.zfin[:].indirect(zl), ["zfin0", "zfin1", "fzin"], ["zo_f"], 256, c=CG)
+    dma("Y", [(T.yz[:, :], fin("zo"))], ["zo_f"], ["yz"], 0.1)
+    lin(T.nm[:], T.df[:, 0:32].indirect(fl), ["df0", "fzin"], ["nm"], 256, c=CG)
+    if OLD_S:
+        lin(T.neq[:], T.df[:, 32:64].indirect(fl), ["df1", "fzin"], ["neq"], 256, c=CG)
+        mm([(T.pA2[:, 0:256], T.I32[:], T.Lfin[:], 1024)], ["I32", "Lfin"], ["pA2"], True, False)
+        mm([(T.pA2[:, 0:256], T.I[:], T.neq[:], 256)], ["I", "neq"], ["pA2"], False, True)
+        lin(fin("m1"), T.pA2[:, 0:256], ["pA2"], ["m1"], 256)
+    else:
+        tt(fin("m1"), T.df[:, 32:64].indirect(fl), T.Lfin[:], A.add, ["df1", "fzin", "Lfin"], ["m1"], 256, CG)
+    mm([(T.pA1[:, 0:256], T.cmid[:], T.ones[:], 256)], ["cmid", "ones"], ["pA1"], True, False)
+    mm([(T.pA1[:, 0:256], T.I[:], T.nm[:], 256)], ["I", "nm"], ["pA1"], acc="own")
+    for h in range(HV):
+        mm([(T.pA1[:, EH * h:EH * h + EH], T.Bc[:], T.ein[:, EH * h:EH * h + EH], EH)], ["Bc", "ein%d" % h], ["pA1"], acc="own")
+    tt(fin("Lo"), T.pA1[:, 0:256], fin("m1"), A.max, ["m1", "pA1"], ["Lo"], 256, 1.0)
     dma("Y", [(T.yl[:, :], fin("Lo"))], ["Lo"], ["yl"], 0.1)
-    act(fin("vo"), T.ident[:].indirect(T.vin[:]), F.Copy, kid + ["vin"], ["vo"], 256, CG)
+    lin(fin("vo"), T.ein[:], ch("ein", HV), ["vo"], 256, 1.0, 2048.0)
     dma("S", [(T.yv[:, :], T.fin[0::16, 256 * FIN.index("vo"):256 * FIN.index("vo") + 256])], ["vo"], ["yv"], 0.05)
     return ops
 
@@ -653,12 +702,15 @@ def lengths(ops, row):
     cyc, cg, cs, tc, gap, ri, rl, rmb, lmb = row
     dur, lat = [], []
     for o in ops:
-        if o["kind"] == "c":
+        if o.get("kind", "c") == "c":
             dur.append(o["fix"] + o["cyc"] * (tc if o["q"] == "T" else cyc * {CG: cg, CS: cs}.get(o["c"], 1.0)))
             lat.append(0.0)
         elif o["kind"] == "r":
             dur.append(ri)
-            lat.append(rl + rmb * o["mb"])
+            lat.append(0.0)
+        elif o["kind"] == "n":
+            dur.append(rmb * o["mb"])
+            lat.append(rl - rmb * ROWS - gap)
         else:
             dur.append(o["fix"])
             lat.append(1.9 + lmb * o["mb"])
@@ -667,7 +719,7 @@ def lengths(ops, row):
 
 def replay(ops, seq, size):
     dur, lat, gap = size
-    free = {q: 0.0 for q in "VSTGY"}
+    free = {q: 0.0 for q in QS}
     done = [0.0] * len(ops)
     for i in seq:
         o = ops[i]
@@ -701,7 +753,9 @@ def order_ops(ops):
                 readers[k] = []
         o["deps"] = sorted(deps)
     if "seq" not in KEPT:
-        KEPT["seq"] = find_order(ops)
+        KEPT["seq"], KEPT["moved"] = find_order(ops)
+    for i in KEPT["moved"]:
+        ops[i].update(ops[i]["alt"])
     closer = {}
     for i in KEPT["seq"]:
         if ops[i]["acc"]:
@@ -732,83 +786,166 @@ def find_order(ops):
                     prio[i] = 1e6 - i
                 elif ops[i]["early"]:
                     prio[i] = 1e5 * ops[i]["early"] - i
-                elif k:
-                    prio[i] += JITTER * (((i + 1) * 2654435761 + (k * ROUNDS + r) * 40503 * (i + 7)) % 1000) / 1000.0
+                else:
+                    prio[i] += AHEAD.get(ops[i]["tag"], 0.0) + (k > 0) * JITTER * (((i + 1) * 2654435761 + (k * ROUNDS + r) * 40503 * (i + 7)) % 1000) / 1000.0
             seq, start = place(ops, pred, succ, prio, size, False)
             score = sum(replay(ops, seq, sz) / row[0] for sz, row in zip(sizes, ROUGH))
             if best is None or score < best[0]:
                 best = (score, seq)
             _s, back = place(ops, succ, pred, [start[i] + dur[i] for i in range(n)], size, True)
             prio = [back[i] + dur[i] for i in range(n)]
-    return improve(ops, best[1], succ, sizes)
+    short = min(improve(ops, best[1], [], succ, sizes, STEPS // 8, HOT, WARM, SEED + k) for k in range(STARTS))
+    return improve(ops, short[1], short[2], succ, sizes, STEPS - STARTS * (STEPS // 8), WARM, COLD, SEED)[1:]
 
 
-def improve(ops, seq, succ, sizes):
+def improve(ops, seq, given, succ, sizes, steps, hot, cold, seed):
     n = len(ops)
-    qi = ["VSTGY".index(o["q"]) for o in ops]
+    qi = [QS.index(o["q"]) for o in ops]
+    qo = [QS.index((o["alt"] or o)["q"]) for o in ops]
+    other = [lengths([o["alt"] or o for o in ops], row)[0] for row in ROUGH]
     direct = []
     for o in ops:
         far = set(e for d in o["deps"] for e in ops[d]["deps"] if ops[e]["kind"] == "c")
         direct.append([d for d in o["deps"] if d not in far])
-    tabs = [(dur, [[(d, lat[d] + (0.0 if o["q"] == "T" == ops[d]["q"] else gap)) for d in direct[i]] for i, o in enumerate(ops)], lat) for dur, lat, gap in sizes]
+    dep = [[tuple([d] + [lat[d] + (0.0 if o["q"] == "T" == ops[d]["q"] else gap) for dur, lat, gap in sizes]) for d in direct[i]] for i, o in enumerate(ops)]
+    durs = [tuple(size[0][i] for size in sizes) for i in range(n)]
+    other = list(zip(*other))
     fixed = [o["kind"] == "d" and not o["deps"] for o in ops]
     tails = [i for i in range(n) if not succ[i]]
     dset, sset = [set(o["deps"]) for o in ops], [set(x) for x in succ]
     seq = list(seq)
+    moved, load = set(), [0.0]
+
+    fol = [[] for _ in range(n)]
+    for i in range(n):
+        for x in dep[i]:
+            fol[x[0]].append((i,) + x[1:])
+    view = dict(a=0, b=n, last=[n] * len(QS), exits=[(i, [size[1][i] for size in sizes]) for i in tails], queue=[[0.0] * len(QS)] * 4, rest=[0.0] * 4)
+
+    def look(a, b):
+        rem, nxt, queue = [[0.0] * (n + 1) for _ in range(4)], [n] * len(QS), None
+        for i in reversed(seq[b:]):
+            for r, m in enumerate(rem):
+                m[i] = durs[i][r] + max([m[nxt[qi[i]]], sizes[r][1][i]] + [x[1 + r] + m[x[0]] for x in fol[i]])
+            nxt[qi[i]] = i
+        exits, rest = [], [0.0] * 4
+        for p in range(b):
+            i = seq[p]
+            far = [x for x in fol[i] if pos[x[0]] >= b]
+            if far or not succ[i]:
+                out = [max([sizes[r][1][i]] + [x[1 + r] + rem[r][x[0]] for x in far]) for r in range(4)]
+                if p >= a:
+                    exits.append((i, out))
+                else:
+                    rest = [max(rest[r], now[1][r][i] + out[r]) for r in range(4)]
+        last = [n] * len(QS)
+        for i in seq[:a]:
+            last[qi[i]] = i
+        view.update(a=a, b=b, last=last, exits=exits, queue=[[m[j] for j in nxt] for m in rem], rest=rest)
 
     def run(p0, old):
-        score, out = 0.0, []
-        for r, (dur, dep, lat) in enumerate(tabs):
-            end, why = (list(old[r][0]), list(old[r][1])) if old else ([0.0] * n, [-1] * n)
-            last, need, p = [-1] * 5, 5, p0 - 1
-            while p >= 0 and need:
-                if last[qi[seq[p]]] < 0:
-                    last[qi[seq[p]]] = seq[p]
-                    need -= 1
-                p -= 1
-            for p in range(p0, n):
-                i = seq[p]
-                q = qi[i]
-                w = last[q]
-                st = end[w] if w >= 0 else 0.0
-                for d, x in dep[i]:
-                    x += end[d]
-                    if x > st:
-                        st, w = x, d
-                why[i] = w
-                end[i] = st + dur[i]
-                last[q] = i
-            top, at = max((end[i] + lat[i], i) for i in tails)
-            score += (top + PULL * sum(end) / n) / ROUGH[r][0]
-            out.append((end, why, at))
-        return score, out
+        last = list(view["last"])
+        for i in seq[view["a"]:p0]:
+            last[qi[i]] = i
+        e0, e1, e2, e3 = ends = [list(e) for e in old]
+        for i in seq[p0:view["b"]]:
+            q = qi[i]
+            w = last[q]
+            last[q] = i
+            s0, s1, s2, s3 = e0[w], e1[w], e2[w], e3[w]
+            for d, x0, x1, x2, x3 in dep[i]:
+                x0 += e0[d]
+                if x0 > s0:
+                    s0 = x0
+                x1 += e1[d]
+                if x1 > s1:
+                    s1 = x1
+                x2 += e2[d]
+                if x2 > s2:
+                    s2 = x2
+                x3 += e3[d]
+                if x3 > s3:
+                    s3 = x3
+            x0, x1, x2, x3 = durs[i]
+            e0[i], e1[i], e2[i], e3[i] = s0 + x0, s1 + x1, s2 + x2, s3 + x3
+        tops = [max([(e[i] + out[r], i) for i, out in view["exits"]] + [(e[i] + x, i) for i, x in zip(last, view["queue"][r])] + [(view["rest"][r], n)])
+                for r, e in enumerate(ends)]
+        return sum((tops[r][0] + PULL * sum(e) / n) / ROUGH[r][0] for r, e in enumerate(ends)) + load[0], ends, tops
 
-    state = [SEED]
+    def longest(r):
+        e, held, path = now[1][r], [], []
+        i = now[2][r][1]
+        while i < n and pos[i] >= view["a"]:
+            if qi[i] != qo[i]:
+                path.append(i)
+            p = pos[i] - 1
+            while p >= 0 and qi[seq[p]] != qi[i]:
+                p -= 1
+            w = seq[p] if p >= 0 else n
+            st = e[w]
+            for x in dep[i]:
+                if e[x[0]] + x[1 + r] > st:
+                    st, w = e[x[0]] + x[1 + r], x[0]
+            if w < n and pos[w] >= view["a"] and qi[w] == qi[i] and w not in dset[i] and not fixed[i] and not fixed[w]:
+                held.append((i, w))
+            i = w
+        return held, path
+
+    def swap(i):
+        load[0] += sum((LOAD[qo[i]] * other[i][r] - LOAD[qi[i]] * durs[i][r]) / ROUGH[r][0] for r in range(4))
+        qi[i], qo[i] = qo[i], qi[i]
+        durs[i], other[i] = other[i], durs[i]
+        moved.symmetric_difference_update([i])
+
+    for i in given:
+        swap(i)
+    state = [seed]
 
     def draw(k):
         state[0] = (state[0] * 1103515245 + 12345) % 2147483648
         return (state[0] >> 8) % k
 
-    now = run(0, None)
-    best = (now[0], list(seq))
+    now = list(run(0, [[0.0] * (n + 1)] * 4))
+    best = (now[0], list(seq), sorted(moved))
     pos = [0] * n
     for p, i in enumerate(seq):
         pos[i] = p
-    for step in range(STEPS):
-        end, why, i = now[1][draw(len(tabs))]
-        held = []
-        while i >= 0:
-            w = why[i]
-            if w >= 0 and qi[w] == qi[i] and w not in dset[i] and not fixed[i] and not fixed[w]:
-                held.append(i)
-            i = w
+    known, whole = {}, dict(view)
+    for step in range(steps):
+        if step % SORT == 0:
+            view.update(whole)
+            now[:] = run(0, now[1])
+            if now[0] < best[0]:
+                best = (now[0], list(seq), sorted(moved))
+            seq.sort(key=lambda i: now[1][0][i] - durs[i][0])
+            for p, i in enumerate(seq):
+                pos[i] = p
+            a = draw(n + SPAN) - SPAN
+            look(max(a, 0), min(a + SPAN, n))
+            now[:] = run(view["b"], now[1])
+            known.clear()
+        r = draw(4)
+        if r not in known:
+            known[r] = longest(r)
+        held, path = known[r]
+        bar = now[0] * (1.0 - hot * (cold / hot) ** (step / steps) * math.log((draw(10000) + 1) / 10001.0))
+        if path and not draw(SWAP):
+            a = path[draw(len(path))]
+            swap(a)
+            got = run(pos[a], now[1])
+            if got[0] <= bar:
+                now[:] = got
+                known.clear()
+            else:
+                swap(a)
+            continue
         if not held:
             continue
-        b = held[draw(len(held))]
-        a, q, k = why[b], qi[b], 1 + draw(4)
+        b, a = held[draw(len(held))]
+        q, k = qi[b], 1 + draw(4)
         if draw(2):
             lo, hi, move = pos[b], pos[b] + 1, {b}
-            while lo > 0 and k:
+            while lo > view["a"] and k:
                 lo -= 1
                 k -= qi[seq[lo]] == q
             for p in range(hi - 2, lo - 1, -1):
@@ -820,7 +957,7 @@ def improve(ops, seq, succ, sizes):
             new = [j for j in part if j in move] + [j for j in part if j not in move]
         else:
             lo, hi, move = pos[a], pos[a], {a}
-            while hi < n - 1 and k:
+            while hi < view["b"] - 1 and k:
                 hi += 1
                 k -= qi[seq[hi]] == q
             hi += 1
@@ -835,15 +972,14 @@ def improve(ops, seq, succ, sizes):
             continue
         seq[lo:hi] = new
         got = run(lo, now[1])
-        if got[0] <= now[0] * (1.0 - HOT * (COLD / HOT) ** (step / STEPS) * math.log((draw(10000) + 1) / 10001.0)):
-            now = got
+        if got[0] <= bar:
+            now[:] = got
+            known.clear()
             for p in range(lo, hi):
                 pos[seq[p]] = p
-            if now[0] < best[0]:
-                best = (now[0], list(seq))
         else:
             seq[lo:hi] = part
-    return best[1]
+    return best
 
 
 def place(ops, pred, succ, prio, size, backwards):
@@ -853,7 +989,7 @@ def place(ops, pred, succ, prio, size, backwards):
     left = [len(p) for p in pred]
     ready_at = [lat[i] if backwards else 0.0 for i in range(n)]
     ready = [i for i in range(n) if left[i] == 0]
-    free = {q: 0.0 for q in "VSTGY"}
+    free = {q: 0.0 for q in QS}
     seq = []
     while ready:
         first = min(ready, key=lambda i: (max(ready_at[i], free[ops[i]["q"]]), -prio[i], i))
@@ -900,6 +1036,10 @@ def rank_program(g, core, T, topo):
     total = {}
     for i in seq:
         o = ops[i]
+        if o["kind"] == "n":
+            o["mark"] = (o["sem"], o["n"])
+            total[o["sem"]] = o["n"]
+            continue
         want = {}
         for d in o["deps"]:
             if needs_wait(d, o):
@@ -916,11 +1056,11 @@ def rank_program(g, core, T, topo):
                 ins.then_inc(T.sem[COUNTER[o["q"]]], 1)
                 o["mark"] = (COUNTER[o["q"]], count[o["q"]])
                 total[COUNTER[o["q"]]] = count[o["q"]]
+        elif o["kind"] == "r":
+            total["sent"] = total.get("sent", 0) + o["n"]
         else:
             o["mark"] = (o["sem"], o["n"])
             total[o["sem"]] = o["n"]
-            if o["kind"] == "r":
-                total["sent"] = total.get("sent", 0) + o["n"]
     for name in sorted(total):
         if seen["G"].get(name, 0) < total[name]:
             g.wait_ge(T.sem[name], total[name])

import math
from concourse.bass import DstId, RemoteDMATransfer
from concourse.mybir import dt, AluOpType, AxisListType, ActivationFunctionType

A = AluOpType
F = ActivationFunctionType
V_, Q_, NV = 4096, 256, 3
TH, TAU = 1020, (1020, 1530, 1275)
HV = 2
MH = 16 // HV
EH = 16 * MH
DUP = 4
SEG = 18
KW = SEG * MH
PAIR = 2
PAD = 16 * PAIR
WN = V_ + 2 * PAD
B_H, B_ID, B_E, B_L, B_S = 0, WN, WN + V_, 2 * WN + V_, 3 * WN + V_
CUT0 = V_ + PAD
LATE = 2
H16, B16, F32 = "float16", "bfloat16", "float32"
XG = ((1, 1, 2, 2, 2), (1, 1, 2, 2, 2), (1, 1, 2, 2, 2))
TOP = ((12, 12), (12, 12), (8, 12))
LOW = ((4, 8, 12), (4, 8, 12), (4, 8, 12))
NBW = 4
MIDW = (8, 8)
HALF_S = (0, 1)
OLD_S = True
SCANI = True
XV = ((), (6,), (6,))
STAG = (0, 0, 0)
WTG = 2
CHAIN = None
SETA = (1, 1, 2, 2, 2)
SETB = (1, 1, 2, 2, 2)
ZH = 1
LASTH = 2
FIN = ("Lg", "Ln", "Lp", "Lr", "Lrow", "m1", "zo", "Lo", "vo")
BIG = 2.0 ** 24


def _sb(n, d):
    return ("sbuf", [128, n], d)


SCRATCH = {
    "Xs": _sb(V_, B16), "Eraw": _sb(V_, "int32"), "Win": _sb(B_S + WN, F32),
    "xg": _sb(V_, B16), "absd": ("sbuf", [128, 256, 16], B16),
    "mH": ("sbuf", [128, HV, 16 * EH], B16), "mL": ("sbuf", [128, HV, 16 * EH], B16),
    "mid": ("sbuf", [128, HV, 16 * EH], B16), "mt": _sb(512, B16), "cI": _sb(128, B16), "ect": _sb(256, H16), "ein": _sb(256, H16), "Sh0": _sb(160, B16), "Sh1": _sb(160, B16), "Bc": _sb(128, B16), "Wt": _sb(2048, B16),
    "nI": _sb(128, B16), "hI": _sb(128, H16), "I32": _sb(128, F32), "I": _sb(128, B16), "ones": _sb(256, B16),
    "pi": _sb(8, "int32"), "col": _sb(48, F32), "cols": _sb(160, F32),
    "WK": _sb(144, B16), "WP": _sb(144, B16), "WM": _sb(144, B16), "Wh": _sb(144, B16), "Wf": _sb(144, B16),
    "W1": _sb(144, B16), "Ws": _sb(144, B16),
    "Rot": _sb(128, B16), "W32": _sb(144, F32),
    "dm": _sb(528, F32), "df": _sb(64, F32),
    "kcb": _sb(256, B16), "kcM": _sb(256, F32), "rK": _sb(256, F32), "rG": _sb(HV * KW, F32),
    "c16": _sb(256, "uint16"), "cmid": _sb(128, B16), "cneg": _sb(128, B16), "csum": _sb(128, B16), "ctau": _sb(384, B16), "hk": _sb(32, B16),
    "fi": _sb(128, "int32"), "lists": _sb(128, "uint16"), "sig": _sb(32, "uint16"),
    "raw": _sb(768, "int32"), "t1": _sb(768, F32), "t2": _sb(768, F32), "offE": _sb(512, "uint16"), "S0": _sb(512, F32),
    "cf": _sb(256, F32), "cfr": _sb(256, F32), "neq": _sb(256, B16),
    "scK": _sb(256, F32), "ki": _sb(80, "int32"), "k16": _sb(16, "uint16"), "selc": _sb(256, H16),
    "Lf": ("sbuf", [128, HV, KW], F32), "key": _sb(288, F32), "keyT": _sb(288, F32), "scG": _sb(288, F32), "hf": _sb(256, H16),
    "sm": _sb(64, F32), "si": _sb(64, "int32"), "s16": _sb(64, "uint16"), "ech": _sb(256, H16),
    "eq": _sb(256, B16), "dl": _sb(256, F32), "ur": _sb(256, F32), "eq2": _sb(512, B16),
    "o16": _sb(32 * NV, "uint16"), "vals": _sb(1024, F32), "vs": _sb(256 * NV, F32),
    "fin": _sb(256 * len(FIN), F32), "nm": _sb(256, B16),
    "Lfin": _sb(256, F32), "zfin": _sb(768, B16), "fz": _sb(32, "uint16"), "fzin": _sb(32, "uint16"),
    "vq": _sb(16 * NV, "uint16"),
    "wa": _sb(16 * NV, "uint16"), "wain": _sb(16 * NV, "uint16"),
    "lb": _sb(16 * NV, B16), "lbin": _sb(16 * NV, B16),
    "hs": _sb(16 * NV, "int32"), "hin": _sb(16 * NV, "int32"),
    "mb": _sb(512, B16),
}
for _t in range(NV):
    SCRATCH["zq%d" % _t] = _sb(256, B16)
    SCRATCH["Lq%d" % _t] = _sb(256, "uint16")
    SCRATCH["zd%d" % _t] = ("sbuf", [128, HV, DUP * EH], B16)
    SCRATCH["Lin%d" % _t] = _sb(256, "uint16")
    SCRATCH["xv%d" % _t] = _sb(256, B16)
    SCRATCH["zc%d" % _t] = _sb(768, B16)
for _t in range(NV - 1):
    SCRATCH["xin%d" % _t] = _sb(256, B16)
BANKS = ("pA0", "pA1", "pA2", "pA3", "pK", "pG0", "pG1", "pM")
for _n in BANKS:
    SCRATCH[_n] = ("psum", [128, 512], F32)

SEMAPHORES = (["cV", "cS", "cT", "cG", "sent", "mv0", "mv1", "mf", "mzo", "mLo"] + ["dma%d" % _i for _i in range(24)]
              + ["%s_%d" % (_n, _i) for _n in ("m1", "mz", "ml", "m2a", "m2b", "mh") for _i in range(NV)])

ROUGH = ((0.0009, 1.5, 3.6, 0.00046, 0.12, 0.55, 2.0, 25.0, 2.8),
         (0.00085, 1.1, 2.0, 0.00042, 0.1, 0.5, 1.8, 20.0, 2.5),
         (0.0009, 1.3, 4.5, 0.00055, 0.2, 0.9, 3.0, 35.0, 2.8),
         (0.00124, 2.0, 5.5, 0.00062, 0.12, 0.6, 2.2, 25.0, 3.3))
HOLD, FIT, EDGE, ROUNDS, TRIES, JITTER = 0.3, 0.05, 1.0, 4, 4, 0.6
AHEAD = {"sums": 3}
STEPS = 500000
SWAP = 5
SORT, SPAN = 150, 150
QS = "VSTGYNM"
ROWS = 0.012
LOAD = (0.5, 0.2, 0.0, 0.0, 0.0, 0.0, 0.0)
SEED = 1
PULL = 1.0
HOT = 0.001
WARM, COLD, STARTS = 0.0004, 0.0001, 3
CG, CS, DI = "gather", "scatter", 0.15
FIX = {"V": 0.05, "S": 0.065, "G": 0.12}
KEPT = {}
COUNTER = {"V": "cV", "S": "cS", "T": "cT", "G": "cG"}


def build_ops(g, T, topo, core, nxt, own):
    ops = []
    v, s, te = g.vector, g.scalar, g.tensor
    eng = topo.engines(core, nxt)
    free = [e for e in topo.engines(core, own) if e not in eng]
    eng_own = free if len(free) == len(eng) else [e for e in topo.engines(core, own) if e in eng]
    nd = [0]
    early, tag = [False], ["start"]

    def way(q, fn, fix, n, c=1.0):
        return dict(q=q, fn=fn, fix=fix, cyc=n if c in (CG, CS) else max(64, n * c), c=c)

    def op(q, fn, rd, wr, fix, n=0, c=1.0, kind="c", sem=None, inc=1, mb=0.0, acc=None, stop=None, alt=None):
        ops.append(dict(way(q, fn, fix, n, c), rd=list(rd), wr=list(wr), kind=kind, sem=sem, n=inc, mb=mb, early=early[0], tag=tag[0], acc=acc, stop=stop, alt=alt))

    def either(first, other, rd, wr):
        op(first["q"], first["fn"], rd, wr, first["fix"], first["cyc"], first["c"] if first["c"] in (CG, CS) else 1.0, alt=other)

    def w_ts(out, in0, s1, s2, o0, o1, n, c=1.0):
        if o1 is None:
            return way("V", lambda: v.tensor_scalar(out, in0, s1, None, o0), FIX["V"], n, c)
        return way("V", lambda: v.tensor_scalar(out, in0, s1, s2, o0, o1), FIX["V"], n, c)

    def w_cp(out, in_, n, c=1.0):
        return way("V", lambda: v.tensor_copy(out, in_), FIX["V"], n, c)

    def w_act(out, in_, f, n, c=1.0, scale=1.0, bias=0.0):
        return way("S", lambda: s.activation(out, in_, f, bias=bias, scale=scale), FIX["S"], n, c)

    def w_sel(out, in_, pat, o, fill, base, cm, n):
        return way("G", lambda: g.affine_select(out, in_, pat, o, fill, base, cm), FIX["G"], 2 * n + 64)

    def w_gcp(out, in_, n):
        return w_sel(out, in_, [[0, n]], A.is_equal, 0.0, 0, 0, n)

    def w_iota(out, pat, base, cm, n, small=True):
        if small:
            return way("G", lambda: g.iota(out, pat, base, cm, allow_small_or_imprecise_dtypes=True), 0.08, 2 * n + 64)
        return way("G", lambda: g.iota(out, pat, base, cm), 0.08, 2 * n + 64)

    def ts(out, in0, s1, s2, o0, o1, rd, wr, n=16, c=1.0):
        either(w_ts(out, in0, s1, s2, o0, o1, n, c), None, rd, wr)

    def tt(out, in0, in1, o, rd, wr, n=16, c=2.0):
        op("V", lambda: v.tensor_tensor(out, in0, in1, o), rd, wr, FIX["V"], n, c)

    def cp(out, in_, rd, wr, n=16, c=1.0):
        either(w_cp(out, in_, n, c), None, rd, wr)

    def conv(out, in_, rd, wr, n=16, q="V", c=1.0):
        ways = [w_cp(out, in_, n, c), w_gcp(out, in_, n) if q else None]
        either(ways[q == "G"], ways[q != "G"], rd, wr)

    def lin(out, in_, rd, wr, n, scale=1.0, bias=0.0, q="S", c=1.0, cv=None):
        f = F.Copy if isinstance(bias, float) and bias == 0.0 else F.Identity
        ways = [w_act(out, in_, f, n, c, scale, bias), w_ts(out, in_, scale, bias, A.mult, A.add, n, cv or c)]
        either(ways[q == "V"], ways[q != "V"], rd, wr)

    def fill(ap, val, key, n, c=1.0, q="V"):
        ways = [way("V", lambda: v.memset(ap, float(val)), FIX["V"], n, c), w_iota(ap, [[0, n]], int(val), 0, n) if q else None]
        either(ways[q == "G"], ways[q != "G"], [], [key])

    def turn(out, in_, rd, wr, n=256):
        op("V", lambda: v.transpose(out, in_), rd, wr, FIX["V"], n)

    def scan(out, d0, d1, o0, o1, rd, wr, n=256):
        op("V", lambda: v.tensor_tensor_scan(out, d0, d1, 0.0, o0, o1), rd, wr, FIX["V"], n)

    def act(out, in_, f, rd, wr, n, c=1.0, scale=1.0, bias=0.0):
        either(w_act(out, in_, f, n, c, scale, bias), None, rd, wr)

    def mm(items, rd, wr, first=True, last=True, x=1, acc=None):
        stop = [last and acc is None]

        def fn():
            ins = None
            for i, (o, l, r, _n) in enumerate(items):
                ins = te.matmul(o, l, r, first and acc is None and i == 0, stop[0] and i == len(items) - 1)
            return ins
        op("T", fn, rd, wr, 0.02, sum(max(64, it[3]) * x for it in items), acc=acc, stop=stop)

    def mms(items, rd, wr, x=1):
        def fn():
            ins = None
            for o, l, r, _n in items:
                ins = te.matmul(o, l, r, True, True)
            return ins
        op("T", fn, rd, wr, 0.02, sum(max(64, it[3]) * x for it in items))

    def iota(out, pat, base, cm, wr, n, small=True):
        either(w_iota(out, pat, base, cm, n, small), None, [], wr)

    def sel(out, in_, pat, o, fill_, base, cm, rd, wr, n):
        either(w_sel(out, in_, pat, o, fill_, base, cm, n), None, rd, wr)

    def dma(q, pairs, rd, wr, mb):
        name = "dma%d" % nd[0]
        nd[0] += 1
        queue = g.sync if q == "Y" else s

        def fn():
            for o, i in pairs:
                queue.dma_start(o, i).then_inc(T.sem[name], 16)
        op(q, fn, rd, wr, DI * len(pairs), 0, 1.0, "d", name, 16 * len(pairs), mb)

    def send(pairs, sem, rd, wr, mb, to=nxt):
        rid, pid, _ = topo.addr(to)
        es = eng if to == nxt else eng_own
        k = len(es) // len(pairs)
        masks = [sum(1 << e for e in es[k * j:k * j + k]) for j in range(len(pairs))]

        def fn():
            if len(pairs) == 1:
                g.remote_dma(pairs[0][0], pairs[0][1], T.sem[sem], T.sem.sent, pid, rid, masks[0])
            else:
                g.remote_dma_fused([RemoteDMATransfer(dst_ids=[DstId(rid=rid, pnc=pid)], dma_engine_mask=m, remote_sem=T.sem[sem], src=i, dst=o)
                                    for (o, i), m in zip(pairs, masks)], local_sem=T.sem.sent)
        op("G", fn, rd, ["issued" + sem], 0.0, 0, 1.0, "r", "sent", len(es))
        op("N" if to == nxt else "M", None, ["issued" + sem], wr, 0.0, 0, 1.0, "n", sem, len(es), mb + ROWS * len(pairs))

    def ch(name, n=8, a=0):
        return ["%s%d" % (name, i) for i in range(a, n)]

    def units(name, h, a, b):
        return ch(name, 16 * h + b, 16 * h + a)

    def wsl(w, b):
        return w[:, 15 - b:143 - b]

    def tab(base, a=0, b=V_):
        return T.Win[:, base + PAD + a:base + PAD + b]

    def wide(base):
        return T.Win[:, base:base + WN]

    def fin(name, a=0, b=256):
        return T.fin[:, 256 * FIN.index(name) + a:256 * FIN.index(name) + b]

    def spans(sizes):
        ends = [sum(sizes[:j + 1]) for j in range(len(sizes))]
        return list(zip([0] + ends[:-1], ends))

    def n2l(out, w, kw_, src, ksrc, bank, const=None, kconst=(), a0=0, n=256, x=1, acc=None):
        items = [(out, const[0], const[1], n // 16)] if const is not None else []
        items += [(out, wsl(w, b), src[:, a0 + b:a0 + n:16], n // 16) for b in range(16)]
        mm(items, [kw_] + list(ksrc) + list(kconst), [bank], True, True, x, acc)

    dma("Y", [(T.raw[:, 256 + 128 * u:256 + 128 * u + 128], T.E[16 * u::32, :]) for u in range(2)], [], ["rawE0"], 0.15)
    dma("S", [(T.raw[:, 512 + 128 * u:512 + 128 * u + 128], T.E[16 * u + 1::32, :]) for u in range(2)], [], ["rawE1"], 0.25)
    dma("Y", [(T.Xs[:], T.X[:, :])], [], ["X"], 1.3)
    dma("S", [(T.zq0[:], T.z0[:, :])], [], ch("z0_", ZH), 1.3)
    dma("Y", [(T.ki[:, 64:80], T.v0[:, :])], [], ["v0i"], 1.35)
    for c in range(2):
        dma("Y", [(T.Eraw[:, 2048 * c:2048 * c + 2048], T.E[:, 2048 * c:2048 * c + 2048])], [], ["Eraw%d" % (2 * c), "Eraw%d" % (2 * c + 1)], 2.35 + c)
    dma("Y", [(T.raw[32 * (gi // 2):32 * (gi // 2) + 32, 128 * (gi % 2):128 * (gi % 2) + 128], T.L0[16 * gi:16 * gi + 16, :]) for gi in range(8)], [], ["rawL"], 3.5)

    early[0] = True
    col = T.col
    iota(T.pi[:, 0:1], [[0, 1]], 0, 1, ["pi0"], 1, False)
    names = ("p1", "p2", "pE", "x16", "x2", "xm", "pL", "iL")
    pats = ([[16, 8], [128, 2]], [[16, 2], [32, 8]], [[2, 16]], [[1, 16]], [[2, 8], [0, 2]], [[8, 2], [0, 8]], [[1, 2], [4, 8]], [[1, 8], [64, 2]])
    lists = {name: T.lists[:, 16 * j:16 * j + 16] for j, name in enumerate(names)}
    for j in (0, 2, 1):
        iota(T.fi[:, 16 * j:16 * j + 16], pats[j], 0, 0, ["fi" + names[j]], 16, False)
    iota(T.cols[:], [[1, 160]], 0, 0, ["cols"], 160)
    ts(T.pi[:, 1:2], T.pi[:, 0:1], 15, None, A.bitwise_and, None, ["pi0"], ["pi1"])
    ts(T.pi[:, 2:3], T.pi[:, 0:1], 15, 1, A.bitwise_and, A.arith_shift_right, ["pi0"], ["pi2"])
    ts(T.pi[:, 3:4], T.pi[:, 0:1], 3, 1, A.arith_shift_right, A.bitwise_and, ["pi0"], ["pi3"])
    ts(T.pi[:, 4:5], T.pi[:, 0:1], 4, 1, A.arith_shift_right, A.bitwise_and, ["pi0"], ["pi4"])
    conv(col[:, 0:5], T.pi[:, 0:5], ch("pi", 5), ["colb"], 5)
    cP, cB, cB1, cB3, cU = [col[:, j:j + 1] for j in range(5)]
    fill(T.ones[:, 0:256], 1, "ones", 256, 0.5)
    made = [5]

    def column(in0, scale, bias, rd=()):
        j = made[0]
        made[0] += 1
        lin(col[:, j:j + 1], in0, ["colb"] + list(rd), ["col%d" % j], 1, scale, bias)
        return col[:, j:j + 1], "col%d" % j

    c32b, k32b = column(cB, 32.0, 0.0)
    cE, kE = column(cB3, -255.0, c32b, [k32b])
    ts(T.lists[:, 0:32], T.fi[:, 0:32], cB, None, A.add, None, ["fip1", "fip2", "colb"], ["lp1", "lp2"], 32)
    ts(lists["pE"], T.fi[:, 32:48], cE, None, A.add, None, ["fipE", kE], ["lpE"])
    cg, kg = column(cB, -1.0, cP)
    cG15, kG15 = column(cg, 1.0, 15.0, [kg])
    ts(T.W1[:], T.cols[:, 0:144], cG15, None, A.is_equal, None, ["cols", kG15], ["W1"], 144)
    ts(T.dm[:, 0:32], T.cols[:, 0:32], cB, None, A.is_equal, None, ["cols", "colb"], ["dm0"], 32)
    cz = T.dm[:, 0:1]
    sel(T.I[:], T.ones[:, 0:128], [[-1, 128]], A.is_equal, 0.0, 0, 1, ["ones"], ["I"], 128)
    iota(T.kcb[:], [[0, 16], [1, 16]], 0, 0, ["kcb"], 256)
    ts(T.rK[:], T.kcb[:], 0.0, 2.0 ** 25, A.is_equal, A.mult, ["kcb"], ["rK"], 256)
    for j in (3, 4, 5, 6, 7):
        iota(T.fi[:, 16 * j:16 * j + 16], pats[j], 0, 0, ["fi" + names[j]], 16, False)
    cn2, kn2 = column(cB1, -2.0, cB)
    cw, kw = column(cz, 16.0, cB, ["dm0"])
    cr1, kr1 = column(cw, 1.0, cg, [kw, kg])
    crot, krot = column(cr1, 1.0, -1.0, [kr1])
    ch_, kh = column(cB, 2.0, 1.0)
    cs, ks = column(cB, 1.0, 1.0)
    clo = [(cB, "colb")] + [column(cB, 1.0, 16.0 * u) for u in range(1, PAIR)]
    chi = [column(cB, 1.0, float(CUT0 + 16 * u)) for u in range(PAIR)]
    cxm, kxm = column(cB3, -8.0, cB)
    cpL, kpL = column(cB3, -254.0, c32b, [k32b])
    c4b, k4b = column(cB, 4.0, 0.0)
    ciL, kiL = column(cn2, 124.0, c4b, [kn2, k4b])
    for name, val, kk in (("WK", 1024.0, ()), ("WP", BIG, ()), ("WM", -BIG, ()), ("Wf", 32.0, ()), ("Wh", ch_, [kh]), ("W32", cs, [ks]), ("Ws", cw, [kw])):
        lin(T[name][:], T.W1[:], ["W1"] + list(kk), [name], 144, val, cv=1.0 if name == "W32" else 0.5)
    early[0] = False
    c16p, k16p = column(cP, 1.0, 16.0)
    cU0, kU0 = column(cU, -1.0, 1.0)
    ts(T.Sh0[:], T.cols[:], c16p, cU0, A.is_equal, A.mult, ["cols", k16p, kU0], ["Sh0"], 160)
    ts(T.Sh1[:], T.cols[:], c16p, cU, A.is_equal, A.mult, ["cols", k16p, "colb"], ["Sh1"], 160)
    iota(T.nm[:, 0:128], [[16, 8], [0, 16]], 0, 0, ["nm"], 128)
    ts(T.Bc[:], T.nm[:, 0:128], cg, cz, A.is_equal, A.mult, ["nm", kg, "dm0"], ["Bc"], 128, 0.5)
    conv(T.lists[:, 48:80], T.fi[:, 48:80], ["fix16", "fix2"], ["lx16"], 32)
    for name, cc_, kk in (("xm", cxm, kxm), ("pL", cpL, kpL), ("iL", ciL, kiL)):
        j = names.index(name)
        ts(lists[name], T.fi[:, 16 * j:16 * j + 16], cc_, None, A.add, None, ["fi" + name, kk], ["l" + name])
    ts(T.Rot[:], T.cols[:, 0:128], crot, None, A.is_equal, None, ["cols", krot], ["Rot"], 128)
    lin(T.hI[:], T.I[:], ["I"], ["hI"], 128, 0.5 - 2.0 ** -11, cv=0.5)
    lin(T.nI[:], T.I[:], ["I"], ["nI"], 128, -1.0, cv=0.5)
    lin(T.I32[:], T.I[:], ["I"], ["I32"], 128)
    lin(T.cI[:], T.I[:], ["I"], ["cI"], 128, float(CUT0), cv=0.5)
    ts(T.df[:, 0:32], T.cols[:, 0:32], cs, -float(V_), A.not_equal, A.mult, ["cols", ks], ["df0"], 32)
    ts(T.df[:, 32:64], T.cols[:, 0:32], cs, -float(V_), A.is_equal, A.mult, ["cols", ks], ["df1"], 32)
    ts(T.col[:, 32:48], T.cols[:, 0:16], cB, 2.0 ** 19, A.is_gt, A.mult, ["cols", "colb"], ["tri"])
    for b in range(1, 16):
        if b % WTG:
            lin(T.Wt[:, 128 * b:128 * b + 128], wsl(T.W1, b), ["W1", "tri"], ["Wt%d" % b], 128, T.col[:, 32 + b:33 + b], q="V", cv=0.5)
        else:
            sel(T.Wt[:, 128 * b:128 * b + 128], wsl(T.WP, b), [[1, 128]], A.is_gt, 0.0, 0, -1, ["WP"], ["Wt%d" % b], 128)
    iota(T.keyT[:, 0:KW], [[1, MH], [MH, SEG]], 0, 0, ch("keyT", HV), KW)
    n2l(T.pM[:, 0:KW // 16], T.W32, "W32", T.keyT, ch("keyT", HV), "pM", None, (), 0, KW, 4)
    ts(T.sig[:, 0:KW // 16], T.pM[:, 0:KW // 16], 1.0 / 136, None, A.mult, None, ["pM"], ["lsig"])
    fill(T.rG[:], -2 ** 14, "rG", HV * KW, q="G")
    either(way("V", lambda: v.memset(T.rG[:, 0::SEG], 2.0 ** 40), FIX["V"], 16), None, [], ["rG"])
    fill(T.rG[:, 1::SEG], -(2 ** 22 + CUT0), "rG", 16, q="G")
    lin(T.rG[:, SEG - 1::SEG], T.cols[:, 0:16], ["cols"], ["rG"], 16, 2.0 ** 18, float(2 ** 22 + 15 * 2 ** 14 + CUT0))
    iota(T.hk[:, 0:18], [[128, 18]], 31 * 128, 0, ["hk"], 18)

    for c in range(8):
        iota(T.Win[:, B_ID + 512 * c:B_ID + 512 * c + 512], [[1, 512]], 512 * c, 0, ["id%d" % c], 512)
    fill(T.dm[:, 32:528], 0, "dm", 496, q="G")
    lin(T.dm[:, 32::32], T.ones[:, 0:16], ["ones", "dm0"], ["dm"], 16, cz)
    fill(T.cmid[:], 16, "cmid", 128, 0.5)
    fill(T.cneg[:], -32, "cneg", 128, 0.5)
    fill(T.csum[:], 17 * 128, "csum", 128, 0.5)
    for t in range(NV):
        top = 16 * ((2 * TAU[t] + 1 + 15) // 16)
        fill(T.ctau[64:128, 128 * t:128 * t + 128], BIG / 128 * (2 * TAU[t] + 1 - top), "ctau%da" % t, 128, 0.5, None)
        fill(T.ctau[0:64, 128 * t:128 * t + 128], BIG / 128 * top, "ctau%db" % t, 128, 0.5, None)
    iota(T.kcM[:], [[0, HV], [1, 16], [0, MH]], 256, 0, ["kcM"], 256)
    fill(T.Win[:, B_ID - PAD:B_ID], 0, "dumH", PAD, q="G")
    fill(T.Win[:, B_E:B_E + PAD], 0, "dumE", PAD, q="G")
    for h in range(HV):
        fill(T.key[:, KW * h + 17 * MH:KW * h + KW], 2 ** 24 - 1, "keyc%d" % h, MH, q="G")

    for r, src, out, ko, lst in ((1, "rawE0", T.offE[:, 0:256], "offE0", "pE"), (2, "rawE1", T.offE[:, 256:512], "offE1", "pE"), (0, "rawL", T.Lq0[:], "L0", "pL")):
        sl = slice(256 * r, 256 * r + 256)
        early[0] = 2 if r else False
        cp(T.t1[:, sl], T.raw[:, sl].indirect(lists["p1"]), [src, "lp1"], ["t1%d" % r], 256, CG)
        turn(T.t2[:, sl], T.t1[:, sl], ["t1%d" % r], ["t2%d" % r])
        cp(out, T.t2[:, sl].indirect(lists[lst]), ["t2%d" % r, "l" + lst], [ko], 256, CG)
    conv(T.vq[:, 0:16], T.ki[:, 64:80], ["v0i"], ch("v0_", HV))

    tag[0] = "tables"
    for c0, c1_ in spans(SETA):
        lin(T.mL[:, c0 // 4, 512 * (c0 % 4):512 * (c0 % 4 + c1_ - c0)], T.Xs[:].indirect(T.offE[:, 32 * c0:32 * c1_]), ["X", "offE0"], units("mL", 0, 4 * c0, 4 * c1_), 512 * (c1_ - c0), c=CG)
    for c0, c1_ in spans(SETB):
        for base, o, kk in ((B_H, A.max, "H"), (B_L, A.min, "Lw")):
            tt(tab(base, 512 * c0, 512 * c1_), T.Xs[:].indirect(T.offE[:, 256 + 32 * c0:256 + 32 * c1_]), T.mL[:, c0 // 4, 512 * (c0 % 4):512 * (c0 % 4 + c1_ - c0)], o,
               ["X", "offE1"] + units("mL", 0, 4 * c0, 4 * c1_), ch(kk, c1_, c0), 512 * (c1_ - c0), CG)
    tag[0] = "edges"
    for c in range(8):
        conv(tab(B_E, 512 * c, 512 * c + 512), T.Eraw[:, 512 * c:512 * c + 512], ["Eraw%d" % (c // 2)], ["E%d" % c], 512, "G")
    kE_, kH, kL, kS = ch("E"), ch("H"), ch("Lw"), ["S0", "S1"]
    kid = ch("id", 8)
    kdm = ["dm0", "dm"]

    def edge_sums():
        for c in range(8):
            mms([(T.pM[:, 128 * (c // 4) + j % 16:128 * (c // 4) + 128:16], tab(B_E, 128 * j, 128 * j + 128), T.W32[:, 15:143:16], 8) for j in range(4 * c, 4 * c + 4)],
                ["W32", "E%d" % c], ["pM"], 4)
        lin(T.S0[:, 0:256], T.pM[:, 0:256], ["pM"], ["Sa"], 256)
        for u in range(2):
            op("T", lambda u=u: te.transpose(T.pM[:, 256 + 128 * u:384 + 128 * u], T.S0[:, 128 * u:128 * u + 128], T.I32[:]), ["Sa", "I32"], ["pM"], 0.02, 512)
        lin(T.S0[:, 256:512], T.pM[:, 256:512], ["pM"], ["Sb"], 256)
        s0 = B_S + PAD
        dma("Y", [(T.Win[0::16, s0 + 2048 * u:s0 + 2048 * u + 2048], T.S0[:, 256 + 128 * u:384 + 128 * u]) for u in range(2)], ["Sb"], ["S0", "S1"], 0.2)

    if not LATE:
        tag[0] = "sums"
        edge_sums()

    def sm(i):
        return T.sm[:, 16 * i:16 * i + 16]

    def si(i, h=None):
        return T.si[:, 16 * i:16 * i + 16] if h is None else T.si[:, 16 * i + MH * h:16 * i + MH * h + MH]

    def ki(i):
        return T.ki[:, 16 * i:16 * i + 16]

    def s16(i, n=1):
        return T.s16[:, 16 * i:16 * (i + n)]

    def part(ap16, a0, h, parts=HV):
        w = 16 // parts
        return ap16[:, a0 + w * h:a0 + w * h + w]

    def mid2k(n):
        return (T.cmid[:], T.ones[:, 0:n]), ["cmid", "ones"]

    def edge_list(bank, c0, k, a_, b_):
        n_ = (b_ - a_) // 32
        return [(T[bank][:, c0 + m:c0 + 2 * n_:2], T["Sh%d" % m][:, 16 + 16 * (m - u):144 + 16 * (m - u)], T.ect[:, a_ + 16 * u + k:b_:32], n_) for m in range(2) for u in range(2)]

    flip = [0]
    for t in range(NV):
        z, L16, zd, Lin, xv, zc = [T["%s%d" % (name, t)] for name in ("zq", "Lq", "zd", "Lin", "xv", "zc")]
        v16, ma, ain, lb, lbin, hs, hin = [T[name][:, 16 * t:16 * t + 16] for name in ("vq", "wa", "wain", "lb", "lbin", "hs", "hin")]
        kz_, kv, kzi, kLi, kai, khi = ch("z%d_" % t, ZH), ch("v%d_" % t, HV), "zin%d" % t, "Lin%d" % t, "ain%d" % t, "hin%d" % t
        kbi = ["bina%d" % t, "binb%d" % t]
        ctau, ktau = T.ctau[:, 128 * t:128 * t + 128], ["ctau%da" % t, "ctau%db" % t]
        last = t == NV - 1
        tag[0] = "send%d" % t
        send([(zc[:, 256:512], z[:])], "mz_%d" % t, kz_, [kzi], 0.065)
        send([(Lin[:], L16[:])], "m1_%d" % t, ["L%d" % t], [kLi], 0.065)
        if last:
            send([(T.zfin[:, 256:512], z[:])], "mzo", kz_, ["zfin0"], 0.03, own)

        tag[0] = "walk%d" % t
        kc16 = ch("c16_", HV)
        if t == 0:
            cp(T.c16[:], T.Eraw[:].indirect(v16), ch("Eraw", 4) + kv, kc16, 256, CG)
        conv(T.cfr[:], T.c16[:], kc16, ["cfr"], 256, "G")
        lin(T.cf[:], T.cfr[:], ["cfr"], ["cf"], 256, 1.0, -2048.0)
        mm([(T.pK[:, 0:256], T.I[:], T.kcb[:], 256)], ["I", "kcb"], ["pK"], True, False)
        if t > 0:
            tt(T.neq[:], tab(B_E).indirect(v16), T.cfr[:], A.not_equal, kE_ + kv + ["cfr"], ["neq"], 256, CG)
            n2l(T.pK[:, 0:256:16], T.Wf, "Wf", T.neq, ["neq"], "pK", acc="K%d" % t)
        for c0, c1_ in spans(XG[t]):
            tag[0] = "walk%d_%d" % (t, c0 // 4)
            lin(T.xg[:, 512 * c0:512 * c1_], T.Xs[:].indirect(T.c16[:, 32 * c0:32 * c1_]), ["X"] + kc16[c0 * HV // 8:(c1_ - 1) * HV // 8 + 1], ch("xg", c1_, c0), 512 * (c1_ - c0), c=CG,
                q="V" if c0 in XV[t] else "S")
        for c in range(4):
            qs = slice(64 * c, 64 * c + 64)
            tag[0] = "walk%d_%d" % (t, c // 2)
            for j in range(2):
                bank = "pA%d" % ((2 * c + j) % NBW)
                mm([(T[bank][:, k::8], T.nI[:], z[:, qs], 64) for k in range(8)], ["nI", kz_[c * ZH // 4]], [bank], True, False)
                mm([(T[bank][:, k::8], T.I[:], T.xg[:, 1024 * c + 8 * j + k:1024 * c + 1024:16], 64) for k in range(8)], ["I"] + ch("xg", 2 * c + 2, 2 * c), [bank], False, True)
                act(T.absd[:, qs, 8 * j:8 * j + 8], T[bank][:], F.Abs, [bank], ["ab%d" % (2 * c + j)], 512)
            mm([(T.pK[:, qs], wsl(T.WK, b), T.absd[:, 64 * c + b:64 * c + 64:16, :], 64) for b in range(16)], ["WK"] + ch("ab", 2 * c + 2, 2 * c), ["pK"], acc="K%d" % t)
        tag[0] = "pick%d" % t
        if SCANI:
            scan(T.raw[:, 0:256], T.rK[:], T.pK[:, 0:256], A.add, A.min, ["rK", "pK"], ["scK", "rawL"])
            ts(ki(1), T.raw[:, 15:256:16], 1023, None, A.bitwise_and, None, ["scK"], ["ki1"])
        else:
            scan(T.scK[:], T.rK[:], T.pK[:, 0:256], A.add, A.min, ["rK", "pK"], ["scK"])
            conv(ki(0), T.scK[:, 15::16], ["scK"], ["ki0"], 16, CHAIN)
            ts(ki(1), ki(0), 1023, None, A.bitwise_and, None, ["ki0"], ["ki1"])
        conv(T.k16[:], ki(1), ["ki1"], ["k16"], 16, CHAIN)
        tt(T.selc[:], T.dm[:, 0:528 if t else 32].indirect(T.k16[:]), T.cf[:], A.mult, kdm[0:2 if t else 1] + ["k16", "cf"], ["selc"], 256, CG)
        n2l(T.pK[:, 256:272], T.W1, "W1", T.selc, ["selc"], "pK", *mid2k(16))
        lin(lb, T.raw[:, 15:256:16] if SCANI else T.scK[:, 15::16], ["scK"], ["lb%d" % t], 16, 2.0 ** 38, -(TH * 1024 + 1023.5) * 2.0 ** 38)
        cp(ma, T.pK[:, 256:272], ["pK"], ["ma%d" % t])
        send([(lbin, lb)], "ml_%d" % t, ["lb%d" % t], ["lbin%d" % t], 0.004)
        send([(ain, ma)], "m2a_%d" % t, ["ma%d" % t], [kai], 0.004)
        tag[0] = "hash%d" % t
        lin(xv[:], T.Xs[:].indirect(ma), ["X", "ma%d" % t], ["xv%d" % t], 256, c=CG)

        def results(zs, kzs, xs, kx, half, khalf, like, klike, b0, b1, between=lambda: None):
            for h, za in enumerate(zs):
                w_ = 256 // len(zs)
                sl = slice(w_ * h, w_ * h + w_)
                mm([(T[b0][:, sl], T.hI[:], za, w_), (T[b0][:, sl], T.hI[:], xs[:, sl], w_)], ["hI", kx] + kzs, [b0])
            if t in HALF_S:
                lin(T.t2[:, 0:256], T[b0][:, 0:256], [b0], ["t20"], 256, 1.0, 1.5 * 2.0 ** 23)
                lin(half, T.t2[:, 0:256], ["t20"], [khalf], 256, 1.0, -1.5 * 2.0 ** 23)
            else:
                ts(half, T[b0][:, 0:256], 1.5 * 2.0 ** 23, -1.5 * 2.0 ** 23, A.add, A.add, [b0], [khalf], 256)
            between()
            for h, za in enumerate(zs):
                w_ = 256 // len(zs)
                sl = slice(w_ * h, w_ * h + w_)
                mm([(T[b1][:, sl], T.I[:], za, w_), (T[b1][:, sl], T.nI[:], xs[:, sl], w_)], ["I", "nI", kx] + kzs, [b1])
            act(like, T[b1][:, 0:256], F.Abs, [b1], [klike], 256)

        if not last:
            xin = T["xin%d" % t]
            send([(xin[:], xv[:])], "m2b_%d" % t, ["xv%d" % t], ["xin%d" % t], 0.065)
            mm([(T.pK[:, 0:256], T.hI[:], z[:], 256), (T.pK[:, 0:256], T.hI[:], xv[:], 256)], ["hI", "xv%d" % t] + kz_, ["pK"])
            lin(T.hf[:], T.pK[:, 0:256], ["pK"], ["hf"], 256, 1.0, 1024.0)
            n2l(T.pK[:, 256:272], T.Wh, "Wh", T.hf, ["hf"], "pK", (T.cmid[:], T.hk[:, 0:16]), ["cmid", "hk"])
            cp(ki(2), T.pK[:, 256:272], ["pK"], ["ki2"])
        else:
            def hashed():
                n2l(T.pK[:, 256:272], T.Wh, "Wh", T.mb, ["mba"], "pK", (T.cmid[:], T.hk[:, 1:17]), ["cmid", "hk"], a0=256)
                cp(ki(2), T.pK[:, 256:272], ["pK"], ["ki2"])
            results([z[:]], kz_, xv, "xv%d" % t, T.mb[:, 256:512], "mba", T.mb[:, 0:256], "mbb", "pK", "pK", hashed)
        ts(hs, ki(2), 63 * 2 ** 18 + V_ - 1, None, A.bitwise_and, None, ["ki2"], ["h%d" % t])
        send([(hin, hs)], "mh_%d" % t, ["h%d" % t], [khi], 0.015)
        if last:
            send([(T.zfin[:, 512 * u:512 * u + 256], T.mb[:, 256 * u:256 * u + 256]) for u in range(2)], "m2b_%d" % t, ["mba", "mbb", "h%d" % t], ["zfin1"], 0.06, own)
            tag[0] = "rows"
            conv(fin("Lg"), L16[:], ["L%d" % t], ["Lg"], 256, "G")
            for h in range(HV):
                conv(fin("Lg", EH * h + MH * t, EH * h + MH * t + MH), part(T.wa, 16 * t, h), ["ma%d" % t], ["Lg"], MH, "G")
            lin(fin("Ln"), fin("Lg").indirect(lists["iL"]), ["Lg", "liL"], ["Ln"], 256, c=CG)
            turn(fin("Lp"), fin("Ln"), ["Ln"], ["Lp"])
            lin(fin("Lr"), fin("Lp").indirect(lists["p2"]), ["Lp", "lp2"], ["Lr"], 256, c=CG)
            r0, l0 = 256 * FIN.index("Lrow"), 256 * FIN.index("Lr")
            dma("Y", [(T.fin[16 * gi:16 * gi + 16, r0:r0 + 256], T.fin[32 * (gi // 2):32 * (gi // 2) + 32, l0 + 128 * (gi % 2):l0 + 128 * (gi % 2) + 128]) for gi in range(8)],
                ["Lr"], ["Lrow"], 0.1)
            send([(T.Lfin[:], fin("Lrow"))], "mLo", ["Lrow"], ["Lfin"], 0.06, own)

        tag[0] = "copies%d" % t
        n_ = EH
        kzd = {1: ["zd%d" % t]}
        conv(zd[:, :, 0:EH], zc[:, 256:512], [kzi], kzd[1], 256, "G", 0.5)
        while n_ < DUP * EH:
            conv(zd[:, :, n_:2 * n_], zd[:, :, 0:n_], kzd[n_ // EH], ["zd%d_%d" % (t, n_)], HV * n_, "G", 0.5)
            for j in range(n_ // EH + 1, 2 * n_ // EH + 1):
                kzd[j] = kzd[n_ // EH] + ["zd%d_%d" % (t, n_)]
            n_ *= 2
        if not last:
            results([zc[:, 256:512]], [kzi], xin, "xin%d" % t, zc[:, 512:768], kbi[0], zc[:, 0:256], kbi[1], "pM", "pM")
        kvn, done = ch("v%d_" % (t + 1), HV), []

        def gap(out, kout, low, klow, mid, kmid, bank, w_):
            mm([(T[bank][:, 0:w_], T.I[:], mid, w_), (T[bank][:, 0:w_], T.nI[:], low, w_)], ["I", "nI"] + kmid + klow, [bank])
            either(w_act(out, T[bank][:, 0:w_], F.Relu, w_), w_ts(out, T[bank][:, 0:w_], 0.0, None, A.max, None, w_), [bank], kout)

        tag[0] = "late%d" % t
        tt(T.mt[:, 0:256], tab(B_L).indirect(ain), zc[:, 256:512], A.max, kL + [kai, kzi], ["lowt"], 256, CG)
        lin(T.mt[:, 256:512], tab(B_H).indirect(ain), kH + [kai], ["midt"], 256, c=CG)
        gap(T.mH[:, :, EH * t:EH * t + EH], units("mH", 0, t, t + 1) + units("mH", 1, t, t + 1), T.mt[:, 0:256], ["lowt"], T.mt[:, 256:512], ["midt"], "pK", 256)
        flip[0] = 0
        for h in range(HV):
            pG, kG, grp = T["pG%d" % h], "pG%d" % h, "G%d_%d" % (t, h)
            top = TOP[t][h]
            tag[0] = "cut%d_%d" % (t, h)
            conv(T.Lf[:, h, MH:MH + EH], Lin[:, EH * h:EH * h + EH], [kLi], ["Lf%d" % h], EH, "G")
            conv(T.Lf[:, h, MH + MH * t:2 * MH + MH * t], part(T.wain, 16 * t, h), [kai], ["Lf%d" % h], MH, "G")
            conv(T.Lf[:, h, 0:MH], part(T.wain, 16 * t, h), [kai], ["Lfc%d" % h], MH, "G")
            mm([(pG[:, 0:17 * MH], ctau, T.ones[:, 0:17 * MH], 17 * MH)], ["ones"] + ktau, [kG], True, False)
            mm([(pG[:, 0:MH], T.I[:], part(T.lbin, 16 * t, h), MH)], ["I", "lbin%d" % t], [kG], acc=grp)

            def pieces(cuts, a_, b_):
                at = sorted(set([a_, b_] + [x for x in list(cuts) + [t, t + 1] if a_ < x < b_]))
                return [x for x in zip(at[:-1], at[1:]) if x[0] != t]

            def ahead(name, k0):
                if h or k0 == t or not STAG[t]:
                    return []
                done.append("done%d%s%d" % (t, name, k0))
                return done[-1:]

            def behind(k0):
                return list(done) if h and k0 != t else []

            for name, base, kk, cuts, a_ in (("mL", B_L, kL, LOW[t], 0), ("mH", B_H, kH, range(top, 16, DUP), top)):
                for k0, k1_ in pieces(cuts, a_, 16):
                    e0, e1, w_ = EH * k0, EH * k1_, EH * (k1_ - k0)
                    tt(T[name][:, h, e0:e1], tab(base).indirect(Lin[:, EH * h + MH * k0:EH * h + MH * k1_]), zd[:, h, 0:w_], A.max,
                       kk + [kLi] + kzd[k1_ - k0] + behind(k0), units(name, h, k0, k1_) + ahead(name, k0), w_, CG)
            for k0, k1_ in pieces(range(top - MIDW[h], t, -MIDW[h]), 0, top):
                lin(T.mid[:, h, EH * k0:EH * k1_], tab(B_H).indirect(Lin[:, EH * h + MH * k0:EH * h + MH * k1_]), kH + [kLi], units("mid", h, k0, k1_), EH * (k1_ - k0), c=CG)
            for k0, k1_ in pieces(range(top - 4, t, -4), 0, top):
                sl = slice(EH * k0, EH * k1_)
                gap(T.mH[:, h, sl], units("mH", h, k0, k1_), T.mL[:, h, sl], units("mL", h, k0, k1_), T.mid[:, h, sl], units("mid", h, k0, k1_), "pA%d" % (flip[0] % 4), EH * (k1_ - k0))
                flip[0] += 1
            for w, kw_, name, sums in ((T.WM, "WM", "mH", [(0, 8), (8, 16)]), (T.WP, "WP", "mL", [(top, 16)] if top < 16 else [])):
                for k0, k1_ in sums:
                    mm([(pG[:, MH + MH * k0:MH + MH * k1_], wsl(w, b), T[name][:, h, EH * k0 + b:EH * k1_:16], MH * (k1_ - k0)) for b in range(16)],
                       [kw_] + units(name, h, k0, k1_), [kG], acc=grp)
            k0 = KW * h
            tag[0] = "first%d_%d" % (t, h)
            tt(T.key[:, k0:k0 + 17 * MH], pG[:, 0:17 * MH], T.Lf[:, h, 0:17 * MH], A.max, [kG, "Lf%d" % h, "Lfc%d" % h], ["key%d" % h], 17 * MH, 1.0)
            lin(T.keyT[:, k0:k0 + KW], T.key[:, k0:k0 + KW].indirect(T.sig[:, 0:KW // 16]), ["key%d" % h, "keyc%d" % h, "lsig"], ["keyT%d" % h], KW, c=CG)
            scan(T.scG[:, k0:k0 + KW], T.rG[:, k0:k0 + KW], T.keyT[:, k0:k0 + KW], A.add, A.min, ["rG", "keyT%d" % h], ["scG%d" % h], KW)
            tt(si(0, h), T.scG[:, k0 + SEG - 1:k0 + KW:SEG], part(T.hin, 16 * t, h), A.min, ["scG%d" % h, khi], ["si0_%d" % h], MH)
            ts(si(1, h), si(0, h), 2 ** 14 - 1, None, A.bitwise_and, None, ["si0_%d" % h], ["u%d" % h])
            conv(part(T.s16, 0, h), si(1, h), ["u%d" % h], ["u16_%d" % h], MH, CHAIN)
            lin(T.ech[:, EH * h:EH * h + EH], T.Win[:, B_ID:B_ID + CUT0 + V_].indirect(part(T.s16, 0, h)), kE_ + kid + ["dumE", "u16_%d" % h], ["ech%d" % h], EH, 1.0, -2048.0, c=CG)
            if last:
                send([(T.ein[:, EH * h:EH * h + EH], T.ech[:, EH * h:EH * h + EH])], "mv%d" % h, ["ech%d" % h], ["ein%d" % h], 0.03)
            else:
                turn(T.ect[:, EH * h:EH * h + EH], T.ech[:, EH * h:EH * h + EH], ["ech%d" % h], ["ect%d" % h], EH // 2)
                mm([(pG[:, 288:288 + MH], T.cmid[:], T.ones[:, 0:MH], MH)] + edge_list(kG, 288, 0, EH * h, EH * h + EH), ["cmid", "ones", "Sh0", "Sh1", "ect%d" % h], [kG])
                cp(part(T.vq, 16 * (t + 1), h), pG[:, 288:288 + MH], [kG], [kvn[h]])
                cp(T.c16[:, EH * h:EH * h + EH], tab(B_E).indirect(part(T.vq, 16 * (t + 1), h)), kE_ + [kvn[h]], [kc16[h]], EH, CG)
        tag[0] = "new%d" % t
        ku, ku16, ksi, kech = ch("u", HV), ch("u16_", HV), ch("si0_", HV), ch("ech", HV)
        ts(si(2), si(0), 14, 0x30F, A.arith_shift_right, A.bitwise_and, ksi, ["f"])
        if last:
            ts(si(3), si(0), 14, 0x3F0, A.arith_shift_right, A.bitwise_and, ksi, ["zo"])
            ts(T.fz[:, 0:16], si(2), -255.0, 17.0, A.add, A.min, ["f"], ["fza"])
            ts(T.fz[:, 16:32], si(3), cB, None, A.add, None, ["zo", "colb"], ["fzb"])
            send([(T.fzin[:], T.fz[:])], "mf", ["fza", "fzb"], ["fzin"], 0.01)
        else:
            for h in range(ZH):
                w_ = 256 // ZH
                ts(part(T.si, 48, h, ZH), part(T.si, 0, h, ZH), 14, 0x3F0, A.arith_shift_right, A.bitwise_and, [ksi[h]] if ZH == HV else ksi, ["zo_%d" % h])
                ts(part(T.s16, 16, h, ZH), part(T.si, 48, h, ZH), cB, None, A.add, None, ["zo_%d" % h, "colb"], ["zo16_%d" % h])
                lin(T["zq%d" % (t + 1)][:, w_ * h:w_ * h + w_], zc[:].indirect(part(T.s16, 16, h, ZH)), [kzi, "zo16_%d" % h] + kbi, ["z%d_%d" % (t + 1, h)], w_, c=CG)
            tag[0] = "turn%d" % t
            mm([(T.pG0[:, 320:352], T.cmid[:], T.ones[:, 0:32], 32)] + edge_list("pG0", 320, 1, 0, 256) + edge_list("pG0", 336, 2, 0, 256), ["cmid", "ones", "Sh0", "Sh1"] + ch("ect", HV), ["pG0"])
            cp(s16(2, 2), T.pG0[:, 320:352], ["pG0"], ["ab16"])
            tag[0] = "logs%d" % t
            tt(T.eq[:], si(2).indirect(lists["xm"]), T.kcM[:], A.is_equal, ["f", "lxm", "kcM"], ["eq"], 256, CG)
            conv(sm(2), T.vq[:, 16 * (t + 1):16 * (t + 2)], kvn, ["sm2"], 16, "G")
            tt(sm(1), sm(2), si(1), A.subtract, ["sm2"] + ku, ["sm1"])
            tt(T.dl[:], sm(1).indirect(lists["xm"]), T.eq[:], A.mult, ["sm1", "lxm", "eq"], ["dl"], 256, CG)
            mm([(T.pG0[:, EH * h:EH * h + EH], T.I32[:], T.Lf[:, h, MH:MH + EH], EH) for h in range(HV)], ["I32"] + ch("Lf", HV), ["pG0"], True, False, 4)
            mm([(T.pG0[:, 0:256], T.cI[:], T.eq[:], 256)], ["cI", "eq"], ["pG0"], False, False)
            mm([(T.pG0[:, 0:256], T.I32[:], T.dl[:], 256)], ["I32", "dl"], ["pG0"], False, True, 4)
            cp(T["Lq%d" % (t + 1)][:], T.pG0[:, 0:256], ["pG0"], ["L%d" % (t + 1)], 256)

        tag[0] = "turn%d" % t
        np_ = LASTH if last else 1
        for h in range(np_):
            w_, mw = 256 // np_, 16 // np_
            sl = slice(w_ * h, w_ * h + w_)
            pick = (lambda ks_: [ks_[h]]) if np_ == HV else (lambda ks_: ks_)
            kY = "pG%d" % (h if np_ > 1 else 1)
            y = T[kY][:, 320:320 + mw]
            uw, grp = part(T.si, 16, h, np_), "Y%d_%d" % (t, h)
            lin(T.ur[:, sl], T.Win[:, PAD:PAD + CUT0 + V_].indirect(part(T.s16, 0, h, np_)), kH + kid + ["dumH"] + pick(ku16), ["ur%d" % h], w_, 1.0, float(CUT0), c=CG)
            tt(T.eq2[:, sl], uw.indirect(T.lists[:, 48:48 + mw]), T.ur[:, sl], A.is_equal, pick(ku) + ["lx16", "ur%d" % h], ["eq2%d" % h], w_, CG)
            conv(part(T.sm, 48, h, np_), part(T.s16, 0, h, np_), pick(ku16), ["sm3%d" % h], mw, "G")
            mm([(y, T.I32[:], part(T.sm, 48, h, np_), 4 * 64), (y, T.cneg[:], T.ones[:, 0:mw], mw)], ["I32", "sm3%d" % h, "cneg", "ones"], [kY], True, False)
            mm([(y, T.Wt[:, 128 * b:128 * b + 128], T.eq2[:, w_ * h + b:w_ * h + w_:16], mw) for b in range(1, 16)], ch("Wt", 16, 1) + ["eq2%d" % h], [kY], acc=grp)
            e0 = 256 + w_ * h
            tt(T.eq2[:, e0:e0 + w_], uw.indirect(T.lists[:, 64:64 + mw]), T.ur[:, sl], A.is_equal, pick(ku) + ["lx16", "ur%d" % h], ["eq3%d" % h], w_, CG)
            mm([(T[kY][:, 321:320 + mw:2], wsl(T.WP, b), T.eq2[:, e0 + 16 + b:e0 + w_:32], mw // 2) for b in range(16)], ["WP", "eq3%d" % h], [kY], acc=grp)
            if t >= LATE:
                ys = T.pM[:, 256 + w_ * h:256 + w_ * h + w_]
                mm([(ys, T.csum[:], T.ones[:, 0:w_], w_), (ys, wsl(T.Ws, 0), T.ech[:, sl], w_)], ["ones", "csum", "Ws"] + pick(kech), ["pM"])
                lin(T.vs[:, 256 * t + w_ * h:256 * t + w_ * h + w_], ys, ["pM"], ["vs%d_%d" % (t, h)], w_)
            ko = ["o%d_%d_%d" % (t, h, u) for u in range(PAIR)]
            o0 = 32 * t
            for u in range(PAIR):
                ts(T.o16[:, o0 + mw * h + u:o0 + mw * (h + 1):2], T[kY][:, 320 + u:320 + mw:PAIR], clo[u][0], chi[u][0], A.max, A.min, [kY, clo[u][1], chi[u][1]], [ko[u]])
            if t >= LATE:
                for m in range(mw * h, mw * h + mw, PAIR):
                    cp(wide(B_S).indirect(T.o16[:, o0 + m:o0 + m + PAIR]), T.vs[:, 256 * t + 16 * m:256 * t + 16 * (m + PAIR)], ["vs%d_%d" % (t, h)] + ko, kS, 16 * PAIR, CS)
        if last:
            dma("Y", [(T.ya[:, :], T.Win[0::16, B_S + PAD:B_S + PAD + V_])], kS, ["ya"], 0.2)
            continue
        mm([(T.pM[:, 0:256], T.cmid[:], T.ones[:], 256), (T.pM[:, 0:256], T.Rot[:], T.ech[:], 256)], ["ones", "cmid", "Rot"] + kech, ["pM"])
        lin(T.vals[:, 0:256], T.pM[:, 0:256], ["pM"], ["val0"], 256)
        lin(T.vals[:, 256:768], T.Xs[:].indirect(s16(2, 2)), ["X", "ab16"], ["An"], 512, c=CG)
        tt(T.vals[:, 768:1024], T.Xs[:].indirect(s16(3)), T.vals[:, 256:512], A.min, ["X", "ab16", "An"], ["val2"], 256, CG)
        for m in range(0, 16, PAIR):
            offs, n_ = T.o16[:, o0 + m:o0 + m + PAIR], 16 * PAIR
            tt(wide(B_H).indirect(offs), T.vals[:, 256 + 16 * m:256 + 16 * m + n_], T.vals[:, 512 + 16 * m:512 + 16 * m + n_], A.max, ["An"] + ko, kH + ["dumH"], n_, CS)
            cp(wide(B_L).indirect(offs), T.vals[:, 768 + 16 * m:768 + 16 * m + n_], ["val2"] + ko, kL, n_, CS)
            cp(wide(B_E).indirect(offs), T.vals[:, 16 * m:16 * m + n_], ["val0"] + ko, kE_ + ["dumE"], n_, CS)
        if t == LATE - 1:
            tag[0] = "sums"
            edge_sums()
    tag[0] = "owner"

    fl, zl = T.fzin[:, 0:16], T.fzin[:, 16:32]
    lin(fin("zo"), T.zfin[:].indirect(zl), ["zfin0", "zfin1", "fzin"], ["zo_f"], 256, c=CG)
    dma("Y", [(T.yz[:, :], fin("zo"))], ["zo_f"], ["yz"], 0.1)
    lin(T.nm[:], T.df[:, 0:32].indirect(fl), ["df0", "fzin"], ["nm"], 256, c=CG)
    if OLD_S:
        lin(T.neq[:], T.df[:, 32:64].indirect(fl), ["df1", "fzin"], ["neq"], 256, c=CG)
        mm([(T.pA2[:, 0:256], T.I32[:], T.Lfin[:], 1024)], ["I32", "Lfin"], ["pA2"], True, False)
        mm([(T.pA2[:, 0:256], T.I[:], T.neq[:], 256)], ["I", "neq"], ["pA2"], False, True)
        lin(fin("m1"), T.pA2[:, 0:256], ["pA2"], ["m1"], 256)
    else:
        tt(fin("m1"), T.df[:, 32:64].indirect(fl), T.Lfin[:], A.add, ["df1", "fzin", "Lfin"], ["m1"], 256, CG)
    mm([(T.pA1[:, 0:256], T.cmid[:], T.ones[:], 256)], ["cmid", "ones"], ["pA1"], True, False)
    mm([(T.pA1[:, 0:256], T.I[:], T.nm[:], 256)], ["I", "nm"], ["pA1"], acc="own")
    for h in range(HV):
        mm([(T.pA1[:, EH * h:EH * h + EH], T.Bc[:], T.ein[:, EH * h:EH * h + EH], EH)], ["Bc", "ein%d" % h], ["pA1"], acc="own")
    tt(fin("Lo"), T.pA1[:, 0:256], fin("m1"), A.max, ["m1", "pA1"], ["Lo"], 256, 1.0)
    dma("Y", [(T.yl[:, :], fin("Lo"))], ["Lo"], ["yl"], 0.1)
    lin(fin("vo"), T.ein[:], ch("ein", HV), ["vo"], 256, 1.0, 2048.0)
    dma("S", [(T.yv[:, :], T.fin[0::16, 256 * FIN.index("vo"):256 * FIN.index("vo") + 256])], ["vo"], ["yv"], 0.05)
    return ops


def lengths(ops, row):
    cyc, cg, cs, tc, gap, ri, rl, rmb, lmb = row
    dur, lat = [], []
    for o in ops:
        if o.get("kind", "c") == "c":
            dur.append(o["fix"] + o["cyc"] * (tc if o["q"] == "T" else cyc * {CG: cg, CS: cs}.get(o["c"], 1.0)))
            lat.append(0.0)
        elif o["kind"] == "r":
            dur.append(ri)
            lat.append(0.0)
        elif o["kind"] == "n":
            dur.append(rmb * o["mb"])
            lat.append(rl - rmb * ROWS - gap)
        else:
            dur.append(o["fix"])
            lat.append(1.9 + lmb * o["mb"])
    return dur, lat, gap


def replay(ops, seq, size):
    dur, lat, gap = size
    free = {q: 0.0 for q in QS}
    done = [0.0] * len(ops)
    for i in seq:
        o = ops[i]
        st = max([free[o["q"]]] + [done[d] + (0.0 if o["q"] == "T" == ops[d]["q"] else gap) for d in o["deps"]])
        free[o["q"]] = st + dur[i]
        done[i] = st + dur[i] + lat[i]
    return max(done)


def order_ops(ops):
    writer, readers = {}, {}
    for i, o in enumerate(ops):
        deps = set()
        wr = set(o["wr"]) | set(k for k in o["rd"] if k in BANKS)
        for k in o["rd"]:
            deps.update(writer.get(k, ()))
        for k in wr:
            if o["acc"] and k in BANKS:
                deps.add(writer[k][0])
            else:
                deps.update(writer.get(k, ()))
                deps.update(readers.get(k, ()))
        deps.discard(i)
        for k in o["rd"]:
            readers.setdefault(k, []).append(i)
        for k in wr:
            if o["acc"] and k in BANKS:
                writer[k].append(i)
            else:
                writer[k] = [i]
                readers[k] = []
        o["deps"] = sorted(deps)
    if "seq" not in KEPT:
        KEPT["seq"], KEPT["moved"] = find_order(ops)
    for i in KEPT["moved"]:
        ops[i].update(ops[i]["alt"])
    closer = {}
    for i in KEPT["seq"]:
        if ops[i]["acc"]:
            closer[ops[i]["acc"]] = i
    for i in closer.values():
        ops[i]["stop"][0] = True
    return KEPT["seq"]


def find_order(ops):
    n = len(ops)
    succ = [[] for _ in range(n)]
    for i, o in enumerate(ops):
        for d in o["deps"]:
            succ[d].append(i)
    pred = [o["deps"] for o in ops]
    sizes = [lengths(ops, row) for row in ROUGH]
    best = None
    for k in range(TRIES):
        size = sizes[k % len(sizes)] if k >= TRIES // 2 else sizes[0]
        dur, lat, gap = size
        prio = [0.0] * n
        for i in range(n - 1, -1, -1):
            prio[i] = dur[i] + lat[i] + max([gap + prio[j] for j in succ[i]] + [0.0])
        for r in range(ROUNDS):
            for i in range(n):
                if ops[i]["kind"] == "d" and not ops[i]["deps"]:
                    prio[i] = 1e6 - i
                elif ops[i]["early"]:
                    prio[i] = 1e5 * ops[i]["early"] - i
                else:
                    prio[i] += AHEAD.get(ops[i]["tag"], 0.0) + (k > 0) * JITTER * (((i + 1) * 2654435761 + (k * ROUNDS + r) * 40503 * (i + 7)) % 1000) / 1000.0
            seq, start = place(ops, pred, succ, prio, size, False)
            score = sum(replay(ops, seq, sz) / row[0] for sz, row in zip(sizes, ROUGH))
            if best is None or score < best[0]:
                best = (score, seq)
            _s, back = place(ops, succ, pred, [start[i] + dur[i] for i in range(n)], size, True)
            prio = [back[i] + dur[i] for i in range(n)]
    short = min(improve(ops, best[1], [], succ, sizes, STEPS // 8, HOT, WARM, SEED + k) for k in range(STARTS))
    return improve(ops, short[1], short[2], succ, sizes, STEPS - STARTS * (STEPS // 8), WARM, COLD, SEED)[1:]


def improve(ops, seq, given, succ, sizes, steps, hot, cold, seed):
    n = len(ops)
    qi = [QS.index(o["q"]) for o in ops]
    qo = [QS.index((o["alt"] or o)["q"]) for o in ops]
    other = [lengths([o["alt"] or o for o in ops], row)[0] for row in ROUGH]
    direct = []
    for o in ops:
        far = set(e for d in o["deps"] for e in ops[d]["deps"] if ops[e]["kind"] == "c")
        direct.append([d for d in o["deps"] if d not in far])
    dep = [[tuple([d] + [lat[d] + (0.0 if o["q"] == "T" == ops[d]["q"] else gap) for dur, lat, gap in sizes]) for d in direct[i]] for i, o in enumerate(ops)]
    durs = [tuple(size[0][i] for size in sizes) for i in range(n)]
    other = list(zip(*other))
    fixed = [o["kind"] == "d" and not o["deps"] for o in ops]
    tails = [i for i in range(n) if not succ[i]]
    dset, sset = [set(o["deps"]) for o in ops], [set(x) for x in succ]
    seq = list(seq)
    moved, load = set(), [0.0]

    fol = [[] for _ in range(n)]
    for i in range(n):
        for x in dep[i]:
            fol[x[0]].append((i,) + x[1:])
    view = dict(a=0, b=n, last=[n] * len(QS), exits=[(i, [size[1][i] for size in sizes]) for i in tails], queue=[[0.0] * len(QS)] * 4, rest=[0.0] * 4)

    def look(a, b):
        rem, nxt, queue = [[0.0] * (n + 1) for _ in range(4)], [n] * len(QS), None
        for i in reversed(seq[b:]):
            for r, m in enumerate(rem):
                m[i] = durs[i][r] + max([m[nxt[qi[i]]], sizes[r][1][i]] + [x[1 + r] + m[x[0]] for x in fol[i]])
            nxt[qi[i]] = i
        exits, rest = [], [0.0] * 4
        for p in range(b):
            i = seq[p]
            far = [x for x in fol[i] if pos[x[0]] >= b]
            if far or not succ[i]:
                out = [max([sizes[r][1][i]] + [x[1 + r] + rem[r][x[0]] for x in far]) for r in range(4)]
                if p >= a:
                    exits.append((i, out))
                else:
                    rest = [max(rest[r], now[1][r][i] + out[r]) for r in range(4)]
        last = [n] * len(QS)
        for i in seq[:a]:
            last[qi[i]] = i
        view.update(a=a, b=b, last=last, exits=exits, queue=[[m[j] for j in nxt] for m in rem], rest=rest)

    def run(p0, old):
        last = list(view["last"])
        for i in seq[view["a"]:p0]:
            last[qi[i]] = i
        e0, e1, e2, e3 = ends = [list(e) for e in old]
        for i in seq[p0:view["b"]]:
            q = qi[i]
            w = last[q]
            last[q] = i
            s0, s1, s2, s3 = e0[w], e1[w], e2[w], e3[w]
            for d, x0, x1, x2, x3 in dep[i]:
                x0 += e0[d]
                if x0 > s0:
                    s0 = x0
                x1 += e1[d]
                if x1 > s1:
                    s1 = x1
                x2 += e2[d]
                if x2 > s2:
                    s2 = x2
                x3 += e3[d]
                if x3 > s3:
                    s3 = x3
            x0, x1, x2, x3 = durs[i]
            e0[i], e1[i], e2[i], e3[i] = s0 + x0, s1 + x1, s2 + x2, s3 + x3
        tops = [max([(e[i] + out[r], i) for i, out in view["exits"]] + [(e[i] + x, i) for i, x in zip(last, view["queue"][r])] + [(view["rest"][r], n)])
                for r, e in enumerate(ends)]
        return sum((tops[r][0] + PULL * sum(e) / n) / ROUGH[r][0] for r, e in enumerate(ends)) + load[0], ends, tops

    def longest(r):
        e, held, path = now[1][r], [], []
        i = now[2][r][1]
        while i < n and pos[i] >= view["a"]:
            if qi[i] != qo[i]:
                path.append(i)
            p = pos[i] - 1
            while p >= 0 and qi[seq[p]] != qi[i]:
                p -= 1
            w = seq[p] if p >= 0 else n
            st = e[w]
            for x in dep[i]:
                if e[x[0]] + x[1 + r] > st:
                    st, w = e[x[0]] + x[1 + r], x[0]
            if w < n and pos[w] >= view["a"] and qi[w] == qi[i] and w not in dset[i] and not fixed[i] and not fixed[w]:
                held.append((i, w))
            i = w
        return held, path

    def swap(i):
        load[0] += sum((LOAD[qo[i]] * other[i][r] - LOAD[qi[i]] * durs[i][r]) / ROUGH[r][0] for r in range(4))
        qi[i], qo[i] = qo[i], qi[i]
        durs[i], other[i] = other[i], durs[i]
        moved.symmetric_difference_update([i])

    for i in given:
        swap(i)
    state = [seed]

    def draw(k):
        state[0] = (state[0] * 1103515245 + 12345) % 2147483648
        return (state[0] >> 8) % k

    now = list(run(0, [[0.0] * (n + 1)] * 4))
    best = (now[0], list(seq), sorted(moved))
    pos = [0] * n
    for p, i in enumerate(seq):
        pos[i] = p
    known, whole = {}, dict(view)
    for step in range(steps):
        if step % SORT == 0:
            view.update(whole)
            now[:] = run(0, now[1])
            if now[0] < best[0]:
                best = (now[0], list(seq), sorted(moved))
            seq.sort(key=lambda i: now[1][0][i] - durs[i][0])
            for p, i in enumerate(seq):
                pos[i] = p
            a = draw(n + SPAN) - SPAN
            look(max(a, 0), min(a + SPAN, n))
            now[:] = run(view["b"], now[1])
            known.clear()
        r = draw(4)
        if r not in known:
            known[r] = longest(r)
        held, path = known[r]
        bar = now[0] * (1.0 - hot * (cold / hot) ** (step / steps) * math.log((draw(10000) + 1) / 10001.0))
        if path and not draw(SWAP):
            a = path[draw(len(path))]
            swap(a)
            got = run(pos[a], now[1])
            if got[0] <= bar:
                now[:] = got
                known.clear()
            else:
                swap(a)
            continue
        if not held:
            continue
        b, a = held[draw(len(held))]
        q, k = qi[b], 1 + draw(4)
        if draw(2):
            lo, hi, move = pos[b], pos[b] + 1, {b}
            while lo > view["a"] and k:
                lo -= 1
                k -= qi[seq[lo]] == q
            for p in range(hi - 2, lo - 1, -1):
                if sset[seq[p]] & move:
                    move.add(seq[p])
            part = seq[lo:hi]
            if part[0] in move:
                continue
            new = [j for j in part if j in move] + [j for j in part if j not in move]
        else:
            lo, hi, move = pos[a], pos[a], {a}
            while hi < view["b"] - 1 and k:
                hi += 1
                k -= qi[seq[hi]] == q
            hi += 1
            for p in range(lo + 1, hi):
                if dset[seq[p]] & move:
                    move.add(seq[p])
            if b in move:
                continue
            part = seq[lo:hi]
            new = [j for j in part if j not in move] + [j for j in part if j in move]
        if any(fixed[j] for j in move):
            continue
        seq[lo:hi] = new
        got = run(lo, now[1])
        if got[0] <= bar:
            now[:] = got
            known.clear()
            for p in range(lo, hi):
                pos[seq[p]] = p
        else:
            seq[lo:hi] = part
    return best


def place(ops, pred, succ, prio, size, backwards):
    dur, lat, gap = size
    n = len(ops)
    start = [0.0] * n
    left = [len(p) for p in pred]
    ready_at = [lat[i] if backwards else 0.0 for i in range(n)]
    ready = [i for i in range(n) if left[i] == 0]
    free = {q: 0.0 for q in QS}
    seq = []
    while ready:
        first = min(ready, key=lambda i: (max(ready_at[i], free[ops[i]["q"]]), -prio[i], i))
        q = ops[first]["q"]
        t0 = max(ready_at[first], free[q])
        mine = [i for i in ready if ops[i]["q"] == q]
        i = max((i for i in mine if ready_at[i] <= t0 + HOLD), key=lambda i: (prio[i], -i))
        if ready_at[i] > t0:
            fit = [j for j in mine if max(ready_at[j], t0) + dur[j] <= ready_at[i] + FIT]
            now = max((j for j in mine if ready_at[j] <= t0), key=lambda j: (prio[j], -j))
            if fit:
                i = max(fit, key=lambda j: (prio[j], -j))
            elif prio[i] - prio[now] < EDGE:
                i = now
        st = max(ready_at[i], free[q])
        ready.remove(i)
        start[i] = st
        free[q] = st + dur[i]
        seq.append(i)
        for j in succ[i]:
            soft = ops[j]["q"] == "T" and q == "T"
            ready_at[j] = max(ready_at[j], st + dur[i] + (lat[j] if backwards else lat[i]) + (0.0 if soft else gap))
            left[j] -= 1
            if left[j] == 0:
                ready.append(j)
    return seq, start


def rank_program(g, core, T, topo):
    rank = T.rank_of(core)
    if rank is None:
        return
    n = len(T.cores)
    ops = build_ops(g, T, topo, core, T.cores[(rank + 1) % n], T.cores[(rank - (NV - 1)) % n])
    seq = order_ops(ops)
    queue = {"V": g.vector, "S": g.scalar, "T": g.tensor, "G": g, "Y": g.sync}

    def needs_wait(d, o):
        return not (ops[d]["q"] == "T" and o["q"] == "T")

    signals = set(d for o in ops for d in o["deps"] if needs_wait(d, o))
    count = {q: 0 for q in COUNTER}
    seen = {q: {} for q in queue}
    total = {}
    for i in seq:
        o = ops[i]
        if o["kind"] == "n":
            o["mark"] = (o["sem"], o["n"])
            total[o["sem"]] = o["n"]
            continue
        want = {}
        for d in o["deps"]:
            if needs_wait(d, o):
                name, val = ops[d]["mark"]
                want[name] = max(want.get(name, 0), val)
        for name in sorted(want):
            if seen[o["q"]].get(name, 0) < want[name]:
                queue[o["q"]].wait_ge(T.sem[name], want[name])
                seen[o["q"]][name] = want[name]
        ins = o["fn"]()
        if o["kind"] == "c":
            if i in signals:
                count[o["q"]] += 1
                ins.then_inc(T.sem[COUNTER[o["q"]]], 1)
                o["mark"] = (COUNTER[o["q"]], count[o["q"]])
                total[COUNTER[o["q"]]] = count[o["q"]]
        elif o["kind"] == "r":
            total["sent"] = total.get("sent", 0) + o["n"]
        else:
            o["mark"] = (o["sem"], o["n"])
            total[o["sem"]] = o["n"]
    for name in sorted(total):
        if seen["G"].get(name, 0) < total[name]:
            g.wait_ge(T.sem[name], total[name])
